import numpy as np
import ml_dtypes


def mxq(x, axis, fmt="e4m3"):
    dtype, down = {"e4m3": (ml_dtypes.float8_e4m3fn, 7), "e5m2": (ml_dtypes.float8_e5m2, 14)}[fmt]
    v = np.moveaxis(np.asarray(x, np.float32).astype(ml_dtypes.bfloat16).astype(np.float64), axis, -1)
    blocks = v.reshape(v.shape[:-1] + (-1, 32))
    amax = np.abs(blocks).max(-1, keepdims=True)
    byte = np.maximum(np.where(amax > 0, np.frexp(amax)[1] - 1 + 127, 0) - down, 1)
    scale = np.exp2(byte - 127.0)
    codes = (blocks / scale).astype(np.float32).astype(dtype).astype(np.float64)
    return np.moveaxis((codes * scale).reshape(v.shape), -1, axis)


WIDE = False


def mx_kscale(k):
    if not WIDE:
        return np.ones(k)
    levels = np.array([10, -10, 5, -5, 0])
    if k % 512:
        return np.exp2(np.random.permutation(np.resize(levels, k // 32))).repeat(32)
    a = np.empty((k // 512, 16))
    for p in range(k // 512):
        a[p, :8] = np.random.permutation(np.resize(levels, 8))
        for g in range(8):
            far = levels[np.abs(levels - a[p, g]) >= 10]
            a[p, g + 8] = far[np.random.randint(len(far))]
    return np.exp2(a.ravel()).repeat(32)


def f64(x):
    return np.asarray(x).astype(np.float64)


def striped(idx):
    return np.tile(idx.reshape(-1, 16).T, (8, 1)).astype(np.uint16)


def unstriped(offs):
    return offs[:16].T.reshape(-1).astype(np.int64)


E2M1 = np.array([0.0, 0.5, 1.0, 1.5, 2.0, 3.0, 4.0, 6.0, -0.0, -0.5, -1.0, -1.5, -2.0, -3.0, -4.0, -6.0])


def pack_weight(w, fmt):
    k, n = w.shape
    w = f64(np.asarray(w, np.float32).astype(ml_dtypes.bfloat16)).reshape(k // 32, 32, n)
    amax = np.abs(w).max(1)
    if fmt == "e4m3":
        byte = np.frexp(amax)[1] - 1 + 127 - 7
    else:
        mant, ex = np.frexp(amax / 6.0)
        byte = np.where(mant > 0.5, ex, ex - 1) + 127
    byte = np.clip(np.where(amax > 0, byte, 1), 1, 254)
    scaled = (w * np.exp2(127.0 - byte)[:, None, :]).reshape(k, n).astype(np.float32)
    by_word = np.ascontiguousarray(scaled.reshape(k // 512, 128, 4, n).transpose(0, 1, 3, 2))
    if fmt == "e4m3":
        words = by_word.astype(ml_dtypes.float8_e4m3fn).view(np.uint8)
    else:
        c = by_word.astype(ml_dtypes.float4_e2m1fn).view(np.uint8) & 0xF
        words = (c[..., 0::2] | (c[..., 1::2] << 4)).reshape(k // 512, 128, 2 * n)
    return np.ascontiguousarray(words), np.ascontiguousarray(byte.astype(np.uint8).reshape(k // 512, 16, n))


def unpack_weight(words, scales, fmt):
    g, _, n = scales.shape
    words = np.ascontiguousarray(words).reshape(g, 128, n, -1)
    if fmt == "e4m3":
        vals = words.view(ml_dtypes.float8_e4m3fn).astype(np.float64)
    else:
        nib = np.empty((g, 128, n, 4), np.uint8)
        nib[..., 0::2] = words & 0xF
        nib[..., 1::2] = words >> 4
        vals = E2M1[nib]
    vals = vals * np.repeat(np.exp2(scales.astype(np.float64) - 127.0), 8, axis=1)[..., None]
    return vals.transpose(0, 1, 3, 2).reshape(g * 512, n)


def silu(v):
    return v / (1.0 + np.exp(-np.maximum(v, -700.0)))


K, T, E, C, N = 2048, 512, 8, 128, 256
K8 = 1024


def by_expert(wq, xq):
    return np.concatenate([wq[e].T @ xq[:, e * C:(e + 1) * C] for e in range(E)], axis=1)


def setup_inputs():
    n = np.random.standard_normal
    s = mx_kscale(K)[:, None]
    first = np.random.permutation(np.repeat(np.arange(E), T // E))
    second = (first + 1 + np.random.permutation(np.repeat(np.arange(E - 1), -(-T // (E - 1)))[:T])) % E
    while np.bincount(second, minlength=E).max() != T // E:
        load = np.bincount(second, minlength=E); hi, lo = int(load.argmax()), int(load.argmin())
        t = np.flatnonzero((second == hi) & (first != lo))[0]; second[t] = lo
    slot_token = np.empty(E * C, np.int64); pos = np.empty((2, T), np.int64); fill = np.zeros(E, np.int64)
    place = np.stack([np.random.permutation(C) for _ in range(E)])
    for r, deal in enumerate((first, second)):
        for t in np.random.permutation(T):
            e = deal[t]; j = e * C + place[e, fill[e]]; fill[e] += 1; slot_token[j] = t; pos[r, t] = j
    g = np.random.uniform(0.2, 0.8, T)
    w = n((E, K, N)) / np.sqrt(K) / s[None]
    w8 = [pack_weight(m[:K8], "e4m3") for m in w]
    w4 = [pack_weight(m[K8:], "e2m1") for m in w]
    return {
        "xT": (n((K, T)) * s).astype(np.float32),
        "w8_words": np.stack([m[0] for m in w8]),
        "w8_scales": np.stack([m[1] for m in w8]),
        "w4_words": np.stack([m[0] for m in w4]),
        "w4_scales": np.stack([m[1] for m in w4]),
        "b": (0.3 * n((N, E))).astype(np.float32),
        "gate": np.stack([np.tile(g, (N, 1)), np.tile(1.0 - g, (N, 1))]).astype(np.float32),
        "offs": striped(slot_token),
        "pos1": striped(pos[0]),
        "pos2": striped(pos[1]),
    }


def reference(xT, w8_words, w8_scales, w4_words, w4_scales, b, gate, offs, pos1, pos2):
    idx = unstriped(offs)
    w = np.stack([np.concatenate([unpack_weight(w8_words[e], w8_scales[e], "e4m3"), unpack_weight(w4_words[e], w4_scales[e], "e2m1")]) for e in range(E)])
    xq = mxq(f64(xT)[:, idx], 0, "e4m3")
    y = by_expert(w, xq)
    y = silu(y + np.repeat(f64(b), C, axis=1))
    return f64(gate[0]) * y[:, unstriped(pos1)] + f64(gate[1]) * y[:, unstriped(pos2)]

@@ -1,0 +1,212 @@
+from contextlib import ExitStack
+
+import concourse.mybir as mybir
+
+K, T, E, C, N = 2048, 512, 8, 128, 256
+SLOTS = E * C
+FLOPS = 2 * SLOTS * K * N
+BYTES = 4 * K * T + E * N * (1024 + 512) + 2 * E * 2 * 16 * N + 4 * N * E + 4 * 2 * 128 * T + 2 * 2 * SLOTS * 8 + 4 * N * T
+
+F32 = mybir.dt.float32
+BF16 = mybir.dt.bfloat16
+I32 = mybir.dt.int32
+U32 = mybir.dt.uint32
+U16 = mybir.dt.uint16
+U8 = mybir.dt.uint8
+E4M3 = mybir.dt.float8_e4m3fn_x4
+E2M1 = mybir.dt.float4_e2m1fn_x4
+MULT = mybir.AluOpType.mult
+SILU = mybir.ActivationFunctionType.Silu
+
+P = 128
+PASSES = 4
+ORDER = (0, 2, 1, 3)
+PLANE_ROW = (4, 4, 0, 0)
+WINDOW = 1408
+
+
+def tile_moe_pln_lin_silu_kernel(
+    tc, xT, w8_words, w8_scales, w4_words, w4_scales, b, gate, offs, pos1, pos2, out
+):
+    nc = tc.nc
+    with ExitStack() as ctx:
+        lists = ctx.enter_context(tc.tile_pool(name="lists", bufs=1))
+        keep = ctx.enter_context(tc.tile_pool(name="keep", bufs=1))
+        psum = ctx.enter_context(tc.psum_pool(name="psum", bufs=8))
+
+        offs_sb = lists.tile([P, SLOTS // 16], U16, name="offs_sb")
+        pos1_sb = lists.tile([P, T // 16], U16, name="pos1_sb")
+        pos2_sb = lists.tile([P, T // 16], U16, name="pos2_sb")
+
+        x = [keep.tile([P, 4, T], F32, name="x%d" % g) for g in range(PASSES)]
+        xb = [keep.tile([P, T, 4], BF16, name="xb%d" % g, align_bytes=64) for g in range(PASSES)]
+        words = keep.tile([P, (PASSES - 1) * T + WINDOW], I32, name="words", align_bytes=64)
+        planes = [keep.tile([P, WINDOW], U8, name="plane%d" % i, align_bytes=64) for i in range(2)]
+        slot_words = [keep.tile([P, SLOTS], U32, name="slot_words%d" % g, align_bytes=64) for g in range(PASSES)]
+        slot_planes = [keep.tile([P, SLOTS], U8, name="slot_plane%d" % i, align_bytes=64) for i in range(2)]
+        w8 = [keep.tile([P, E, N], I32, name="w8_%d" % i, align_bytes=64) for i in range(2)]
+        w4 = [keep.tile([P, E, 2 * N], U8, name="w4_%d" % i, align_bytes=64) for i in range(2)]
+        w_planes = keep.tile([P, E * 2 * N], U8, name="w_planes", align_bytes=64)
+        gates = keep.tile([P, 2, T], F32, name="gates")
+        bias = keep.tile([P, 2, E], F32, name="bias")
+        y = [keep.tile([P, SLOTS], F32, name="y%d" % h) for h in range(2)]
+        first = [keep.tile([P, T], F32, name="first%d" % h) for h in range(2)]
+        second = [keep.tile([P, T], F32, name="second%d" % h) for h in range(2)]
+        result = [keep.tile([P, T], F32, name="result%d" % h) for h in range(2)]
+        dummy = keep.tile([P, 2], F32, name="dummy")
+
+        def load_x(g, lo, hi):
+            rows = xT[512 * g : 512 * (g + 1), lo:hi].rearrange("(p j) t -> p j t", j=4)
+            nc.sync.dma_start(out=x[g][:, :, lo:hi], in_=rows)
+
+        def load_scales(k, scales):
+            rows = scales.bitcast(I32).rearrange("e a q n -> q (e a) n")
+            tile_rows = w_planes[:].bitcast(I32).rearrange("p (ea n) -> p ea n", ea=2 * E)
+            for r in range(4):
+                nc.gpsimd.dma_start(out=tile_rows[k + r : P : 32], in_=rows[r:16:4])
+
+        nc.vector.memset(w_planes[:].bitcast(I32), 0)
+        load_scales(4, w8_scales)
+        load_scales(0, w4_scales)
+        nc.gpsimd.dma_start(out=bias[:], in_=b.rearrange("(h p) e -> p h e", h=2))
+        w8_rows = w8_words.rearrange("e a p n t -> (e a) p (n t)").bitcast(I32)
+        w4_rows = w4_words.rearrange("e a p n -> (e a) p n").bitcast(I32)
+        load_x(0, 0, 256)
+        load_x(0, 256, 512)
+        nc.sync.dma_start(offs_sb[:], offs)
+        for g in ORDER[1:]:
+            load_x(g, 0, T)
+        nc.sync.dma_start(pos1_sb[:], pos1)
+        nc.sync.dma_start(pos2_sb[:], pos2)
+        for i in range(2):
+            part = slice(E * i, E * (i + 1))
+            nc.sync.dma_start(out=w8[i][:], in_=w8_rows[part].rearrange("m p n -> p m n"))
+            nc.sync.dma_start(
+                out=w4[i][:].rearrange("p m n -> p (m n)").bitcast(I32).rearrange("p (m n) -> p m n", m=E),
+                in_=w4_rows[part].rearrange("m p n -> p m n"),
+            )
+        for i in range(2):
+            nc.sync.dma_start(out=gates[:, i, :], in_=gate[i, 0:P])
+
+        nc.vector.memset(words[:, PASSES * T :], 0)
+        for plane in planes:
+            nc.vector.memset(plane[:].bitcast(I32), 0)
+        nc.vector.memset(dummy[:], 0.0)
+        nc.scalar.activation(dummy[:, 1:2], dummy[:, 0:1], SILU)
+
+        def interleave(engine_copy, g, lo, hi):
+            engine_copy(out=xb[g][:, lo:hi, :], in_=x[g][:, :, lo:hi].rearrange("p j t -> p t j"))
+
+        def quantize(g, lo, hi):
+            start = T * (PASSES - 1 - ORDER.index(g))
+            nc.vector.quantize_mx(
+                out=words[:, start + lo : start + hi].bitcast(E4M3),
+                scales=planes[g % 2][PLANE_ROW[g] : P, lo:hi],
+                in_=xb[g][:, lo:hi, :].rearrange("p t j -> p (t j)"),
+            )
+
+        def gather_words(g, lo, hi):
+            start = T * (PASSES - 1 - ORDER.index(g))
+            window = words[:, start : start + (WINDOW if g != 3 else 1024)].bitcast(U32)
+            nc.vector.tensor_copy(slot_words[g][:, lo:hi], window.indirect(offs_sb[:, lo // 16 : hi // 16]))
+
+        def gather_bytes(i, lo, hi):
+            window = planes[i][:]
+            nc.vector.tensor_copy(slot_planes[i][:, lo:hi], window.indirect(offs_sb[:, lo // 16 : hi // 16]))
+
+        def multiply(acc, g, h, e, start, stop):
+            a = g % 2
+            i, m = divmod(2 * e + a, E)
+            cols = slice(C * e, C * (e + 1))
+            rows = slice(P * h, P * (h + 1))
+            scale_cols = slice(N * (2 * e + a) + P * h, N * (2 * e + a) + P * (h + 1))
+            if g < 2:
+                k, weights = 4, w8[i][:, m, rows].bitcast(E4M3)
+            else:
+                k, weights = 0, w4[i][:, m, 2 * P * h : 2 * P * (h + 1)].bitcast(E2M1)
+            nc.tensor.matmul_mx(
+                out=acc[:],
+                lhsT=weights,
+                lhsT_scale=w_planes[k:P, scale_cols],
+                rhs=slot_words[g][:, cols].bitcast(E4M3),
+                rhs_scale=slot_planes[a][PLANE_ROW[g] : P, cols],
+                start=start,
+                stop=stop,
+            )
+
+        def finish(acc, h, e):
+            nc.scalar.activation(y[h][:, C * e : C * (e + 1)], acc[:], SILU, bias=bias[:, h, e : e + 1])
+
+        def fetch(into, h, i, lo, hi):
+            places = (pos1_sb, pos2_sb)[i][:, lo // 16 : hi // 16]
+            nc.vector.tensor_tensor(into[h][:, lo:hi], y[h][:].indirect(places), gates[:, i, lo:hi], MULT)
+
+        def add_and_store(h, lo, hi):
+            nc.vector.tensor_add(result[h][:, lo:hi], first[h][:, lo:hi], second[h][:, lo:hi])
+            nc.sync.dma_start(out=out[P * h : P * (h + 1), lo:hi], in_=result[h][:, lo:hi])
+
+        interleave(nc.vector.tensor_copy, 0, 0, 256)
+        quantize(0, 0, 256)
+        interleave(nc.scalar.copy, 0, 416, 512)
+        interleave(nc.vector.tensor_copy, 0, 256, 416)
+        quantize(0, 256, 512)
+        interleave(nc.scalar.copy, 2, 0, 192)
+        interleave(nc.scalar.copy, 1, 0, T)
+        interleave(nc.scalar.copy, 3, 0, T)
+        gather_words(0, 0, 768)
+        interleave(nc.vector.tensor_copy, 2, 192, T)
+        quantize(2, 0, T)
+        gather_words(0, 768, SLOTS)
+        gather_words(2, 0, SLOTS)
+        gather_bytes(0, 0, 512)
+        quantize(1, 0, T)
+        gather_bytes(0, 512, SLOTS)
+        accs = [psum.tile([P, C], F32, name="acc") for e in range(E)]
+        for e in range(4):
+            multiply(accs[e], 0, 0, e, True, False)
+            multiply(accs[e], 2, 0, e, False, False)
+
+        def close_first_half(e):
+            multiply(accs[e], 3, 0, e, False, True)
+            finish(accs[e], 0, e)
+
+        def second_half(e):
+            acc = psum.tile([P, C], F32, name="acc")
+            for g in range(PASSES):
+                multiply(acc, g, 1, e, g == 0, g == PASSES - 1)
+            finish(acc, 1, e)
+
+        gather_words(1, 0, 256)
+        quantize(3, 0, T)
+        gather_words(1, 256, 512)
+        gather_bytes(1, 0, 512)
+        for e in range(4):
+            multiply(accs[e], 1, 0, e, False, False)
+        gather_words(3, 0, 512)
+        for e in range(4):
+            close_first_half(e)
+        for e in range(2):
+            second_half(e)
+        gather_words(1, 512, SLOTS)
+        gather_bytes(1, 512, SLOTS)
+        for e in range(4, E):
+            multiply(accs[e], 0, 0, e, True, False)
+        for g in (2, 1):
+            for e in range(4, E):
+                multiply(accs[e], g, 0, e, False, False)
+        for e in (4, 6):
+            gather_words(3, C * e, C * (e + 2))
+            close_first_half(e)
+            close_first_half(e + 1)
+        fetch(first, 0, 0, 0, T)
+        fetch(second, 0, 1, 0, 384)
+        fetch(second, 0, 1, 384, T)
+        add_and_store(0, 0, 384)
+        for e in range(2, E):
+            second_half(e)
+        fetch(first, 1, 0, 0, T)
+        add_and_store(0, 384, T)
+        fetch(second, 1, 1, 0, 384)
+        fetch(second, 1, 1, 384, T)
+        add_and_store(1, 0, 384)
+        add_and_store(1, 384, T)

@@ -20,9 +20,12 @@ SILU = mybir.ActivationFunctionType.Silu
 
 P = 128
 PASSES = 4
-ORDER = (0, 2, 1, 3)
-PLANE_ROW = (4, 4, 0, 0)
-WINDOW = 1408
+HALF = SLOTS // 2
+SCALE_ROW = (4, 8, 12, 0)
+W8_ROW = 8
+WORD_COLUMN = (3 * T, 2 * T, 0, T)
+WIDE = 1408
+BYTE_WINDOW = 704
 
 
 def tile_moe_pln_lin_silu_kernel(
@@ -38,14 +41,15 @@ def tile_moe_pln_lin_silu_kernel(
         pos1_sb = lists.tile([P, T // 16], U16, name="pos1_sb")
         pos2_sb = lists.tile([P, T // 16], U16, name="pos2_sb")
 
-        x = [keep.tile([P, 4, T], F32, name="x%d" % g) for g in range(PASSES)]
+        x = [[keep.tile([P, 4, T // 2], F32, name="x%d_%d" % (g, u)) for u in range(2)] for g in range(PASSES)]
         xb = [keep.tile([P, T, 4], BF16, name="xb%d" % g, align_bytes=64) for g in range(PASSES)]
-        words = keep.tile([P, (PASSES - 1) * T + WINDOW], I32, name="words", align_bytes=64)
-        planes = [keep.tile([P, WINDOW], U8, name="plane%d" % i, align_bytes=64) for i in range(2)]
+        words = keep.tile([P, (PASSES - 1) * T + WIDE], I32, name="words", align_bytes=64)
+        plane = keep.tile([P, BYTE_WINDOW], U8, name="plane", align_bytes=64)
         slot_words = [keep.tile([P, SLOTS], U32, name="slot_words%d" % g, align_bytes=64) for g in range(PASSES)]
-        slot_planes = [keep.tile([P, SLOTS], U8, name="slot_plane%d" % i, align_bytes=64) for i in range(2)]
-        w8 = [keep.tile([P, E, N], I32, name="w8_%d" % i, align_bytes=64) for i in range(2)]
-        w4 = [keep.tile([P, E, 2 * N], U8, name="w4_%d" % i, align_bytes=64) for i in range(2)]
+        slot_plane = [keep.tile([P, HALF], U8, name="slot_plane%d" % u, align_bytes=64) for u in range(2)]
+        moved = [keep.tile([P, HALF], U8, name="moved%d" % u, align_bytes=64) for u in range(2)]
+        w8 = [[keep.tile([P, E, P], I32, name="w8_%d_%d" % (h, u), align_bytes=64) for u in range(2)] for h in range(2)]
+        w4 = [[keep.tile([P, E, 2 * P], U8, name="w4_%d_%d" % (h, u), align_bytes=64) for u in range(2)] for h in range(2)]
         w_planes = keep.tile([P, E * 2 * N], U8, name="w_planes", align_bytes=64)
         gates = keep.tile([P, 2, T], F32, name="gates")
         bias = keep.tile([P, 2, E], F32, name="bias")
@@ -55,81 +59,97 @@ def tile_moe_pln_lin_silu_kernel(
         result = [keep.tile([P, T], F32, name="result%d" % h) for h in range(2)]
         dummy = keep.tile([P, 2], F32, name="dummy")
 
-        def load_x(g, lo, hi):
-            rows = xT[512 * g : 512 * (g + 1), lo:hi].rearrange("(p j) t -> p j t", j=4)
-            nc.sync.dma_start(out=x[g][:, :, lo:hi], in_=rows)
+        def load_x(g, u):
+            rows = xT[512 * g : 512 * (g + 1), 256 * u : 256 * (u + 1)].rearrange("(p j) t -> p j t", j=4)
+            nc.sync.dma_start(out=x[g][u][:], in_=rows)
 
-        def load_scales(k, scales):
+        def load_scales(k, scales, r):
             rows = scales.bitcast(I32).rearrange("e a q n -> q (e a) n")
             tile_rows = w_planes[:].bitcast(I32).rearrange("p (ea n) -> p ea n", ea=2 * E)
-            for r in range(4):
-                nc.gpsimd.dma_start(out=tile_rows[k + r : P : 32], in_=rows[r:16:4])
+            nc.sync.dma_start(out=tile_rows[k + r : P : 32], in_=rows[r:16:4])
 
-        nc.vector.memset(w_planes[:].bitcast(I32), 0)
-        load_scales(4, w8_scales)
-        load_scales(0, w4_scales)
-        nc.gpsimd.dma_start(out=bias[:], in_=b.rearrange("(h p) e -> p h e", h=2))
         w8_rows = w8_words.rearrange("e a p n t -> (e a) p (n t)").bitcast(I32)
         w4_rows = w4_words.rearrange("e a p n -> (e a) p n").bitcast(I32)
-        load_x(0, 0, 256)
-        load_x(0, 256, 512)
-        nc.sync.dma_start(offs_sb[:], offs)
-        for g in ORDER[1:]:
-            load_x(g, 0, T)
-        nc.sync.dma_start(pos1_sb[:], pos1)
-        nc.sync.dma_start(pos2_sb[:], pos2)
-        for i in range(2):
-            part = slice(E * i, E * (i + 1))
-            nc.sync.dma_start(out=w8[i][:], in_=w8_rows[part].rearrange("m p n -> p m n"))
-            nc.sync.dma_start(
-                out=w4[i][:].rearrange("p m n -> p (m n)").bitcast(I32).rearrange("p (m n) -> p m n", m=E),
-                in_=w4_rows[part].rearrange("m p n -> p m n"),
-            )
-        for i in range(2):
-            nc.sync.dma_start(out=gates[:, i, :], in_=gate[i, 0:P])
 
-        nc.vector.memset(words[:, PASSES * T :], 0)
-        for plane in planes:
-            nc.vector.memset(plane[:].bitcast(I32), 0)
+        def load_w8(h, u):
+            rows = w8_rows[E * u : E * (u + 1), :, P * h : P * (h + 1)]
+            nc.sync.dma_start(out=w8[h][u][:], in_=rows.rearrange("m p n -> p m n"))
+
+        def load_w4(h, u):
+            rows = w4_rows[E * u : E * (u + 1), :, 64 * h : 64 * (h + 1)]
+            into = w4[h][u][:].rearrange("p m n -> p (m n)").bitcast(I32).rearrange("p (m n) -> p m n", m=E)
+            nc.sync.dma_start(out=into, in_=rows.rearrange("m p n -> p m n"))
+
         nc.vector.memset(dummy[:], 0.0)
         nc.scalar.activation(dummy[:, 1:2], dummy[:, 0:1], SILU)
+        nc.vector.memset(plane[:].bitcast(I32), 0)
+        nc.vector.memset(words[:, PASSES * T :], 0)
+        nc.vector.memset(w_planes[:].bitcast(I32), 0)
+        for u in range(2):
+            nc.vector.memset(moved[u][:].bitcast(I32), 0)
+
+        load_x(0, 0)
+        load_x(0, 1)
+        nc.sync.dma_start(offs_sb[:], offs)
+        for g in range(1, PASSES):
+            load_x(g, 0)
+            load_x(g, 1)
+        nc.sync.dma_start(pos1_sb[:], pos1)
+        nc.sync.dma_start(pos2_sb[:], pos2)
+        nc.sync.dma_start(out=bias[:], in_=b.rearrange("(h p) e -> p h e", h=2))
+        for r in range(4):
+            load_scales(W8_ROW, w8_scales, r)
+            load_scales(0, w4_scales, r)
+        load_w8(0, 0)
+        load_w8(0, 1)
+        load_w4(0, 0)
+        load_w4(0, 1)
+        nc.sync.dma_start(out=gates[:], in_=gate[:, 0:P, :].rearrange("i p t -> p i t"))
+        for u in range(2):
+            load_w8(1, u)
+            load_w4(1, u)
 
         def interleave(engine_copy, g, lo, hi):
-            engine_copy(out=xb[g][:, lo:hi, :], in_=x[g][:, :, lo:hi].rearrange("p j t -> p t j"))
+            u = lo // 256
+            rows = x[g][u][:, :, lo - 256 * u : hi - 256 * u]
+            engine_copy(
+                out=xb[g][:, lo:hi, :].rearrange("p (c i) j -> p c j i", i=4),
+                in_=rows.rearrange("p j (c i) -> p c j i", i=4),
+            )
 
         def quantize(g, lo, hi):
-            start = T * (PASSES - 1 - ORDER.index(g))
+            start = WORD_COLUMN[g]
             nc.vector.quantize_mx(
                 out=words[:, start + lo : start + hi].bitcast(E4M3),
-                scales=planes[g % 2][PLANE_ROW[g] : P, lo:hi],
+                scales=plane[SCALE_ROW[g] : P, lo:hi],
                 in_=xb[g][:, lo:hi, :].rearrange("p t j -> p (t j)"),
             )
 
-        def gather_words(g, lo, hi):
-            start = T * (PASSES - 1 - ORDER.index(g))
-            window = words[:, start : start + (WINDOW if g != 3 else 1024)].bitcast(U32)
+        def gather_words(g, lo, hi, width):
+            start = WORD_COLUMN[g]
+            window = words[:, start : start + width].bitcast(U32)
             nc.vector.tensor_copy(slot_words[g][:, lo:hi], window.indirect(offs_sb[:, lo // 16 : hi // 16]))
 
-        def gather_bytes(i, lo, hi):
-            window = planes[i][:]
-            nc.vector.tensor_copy(slot_planes[i][:, lo:hi], window.indirect(offs_sb[:, lo // 16 : hi // 16]))
+        def gather_bytes(u):
+            nc.vector.tensor_copy(slot_plane[u][:], plane[:].indirect(offs_sb[:, 32 * u : 32 * (u + 1)]))
+            k = SCALE_ROW[2]
+            nc.scalar.dma_start(out=moved[u][0:112, :].bitcast(I32), in_=slot_plane[u][k : k + 112, :].bitcast(I32))
 
         def multiply(acc, g, h, e, start, stop):
             a = g % 2
-            i, m = divmod(2 * e + a, E)
-            cols = slice(C * e, C * (e + 1))
-            rows = slice(P * h, P * (h + 1))
+            u, m = divmod(2 * e + a, E)
+            cols = slice(C * (e % 4), C * (e % 4 + 1))
             scale_cols = slice(N * (2 * e + a) + P * h, N * (2 * e + a) + P * (h + 1))
             if g < 2:
-                k, weights = 4, w8[i][:, m, rows].bitcast(E4M3)
+                k, weights = W8_ROW, w8[h][u][:, m, :].bitcast(E4M3)
             else:
-                k, weights = 0, w4[i][:, m, 2 * P * h : 2 * P * (h + 1)].bitcast(E2M1)
+                k, weights = 0, w4[h][u][:, m, :].bitcast(E2M1)
             nc.tensor.matmul_mx(
                 out=acc[:],
                 lhsT=weights,
                 lhsT_scale=w_planes[k:P, scale_cols],
-                rhs=slot_words[g][:, cols].bitcast(E4M3),
-                rhs_scale=slot_planes[a][PLANE_ROW[g] : P, cols],
+                rhs=slot_words[g][:, C * e : C * (e + 1)].bitcast(E4M3),
+                rhs_scale=moved[u][:, cols] if g == 2 else slot_plane[u][SCALE_ROW[g] : P, cols],
                 start=start,
                 stop=stop,
             )
@@ -150,60 +170,41 @@ def tile_moe_pln_lin_silu_kernel(
         interleave(nc.scalar.copy, 0, 416, 512)
         interleave(nc.vector.tensor_copy, 0, 256, 416)
         quantize(0, 256, 512)
-        interleave(nc.scalar.copy, 2, 0, 192)
-        interleave(nc.scalar.copy, 1, 0, T)
-        interleave(nc.scalar.copy, 3, 0, T)
-        gather_words(0, 0, 768)
-        interleave(nc.vector.tensor_copy, 2, 192, T)
-        quantize(2, 0, T)
-        gather_words(0, 768, SLOTS)
-        gather_words(2, 0, SLOTS)
-        gather_bytes(0, 0, 512)
+        for g in range(1, PASSES):
+            interleave(nc.scalar.copy, g, 0, 256)
+            interleave(nc.scalar.copy, g, 256, T)
+        gather_words(0, 0, SLOTS, WIDE)
         quantize(1, 0, T)
-        gather_bytes(0, 512, SLOTS)
-        accs = [psum.tile([P, C], F32, name="acc") for e in range(E)]
-        for e in range(4):
-            multiply(accs[e], 0, 0, e, True, False)
-            multiply(accs[e], 2, 0, e, False, False)
+        gather_words(1, 0, SLOTS, WIDE)
+        quantize(2, 0, T)
+        gather_words(2, 0, 384, T)
+        quantize(3, 0, T)
+        gather_bytes(0)
+        gather_bytes(1)
+        gather_words(3, 0, 512, 2 * T)
+        gather_words(2, 384, SLOTS, 2 * T)
+        gather_words(3, 512, 768, T)
+        gather_words(3, 768, 896, T)
+        gather_words(3, 896, SLOTS, T)
 
-        def close_first_half(e):
+        accs = [psum.tile([P, C], F32, name="acc") for e in range(E)]
+        for e in range(E):
+            multiply(accs[e], 0, 0, e, True, False)
+            multiply(accs[e], 1, 0, e, False, False)
+        for e in range(E):
+            multiply(accs[e], 2, 0, e, False, False)
             multiply(accs[e], 3, 0, e, False, True)
             finish(accs[e], 0, e)
-
-        def second_half(e):
+        for e in range(E):
             acc = psum.tile([P, C], F32, name="acc")
             for g in range(PASSES):
                 multiply(acc, g, 1, e, g == 0, g == PASSES - 1)
             finish(acc, 1, e)
 
-        gather_words(1, 0, 256)
-        quantize(3, 0, T)
-        gather_words(1, 256, 512)
-        gather_bytes(1, 0, 512)
-        for e in range(4):
-            multiply(accs[e], 1, 0, e, False, False)
-        gather_words(3, 0, 512)
-        for e in range(4):
-            close_first_half(e)
-        for e in range(2):
-            second_half(e)
-        gather_words(1, 512, SLOTS)
-        gather_bytes(1, 512, SLOTS)
-        for e in range(4, E):
-            multiply(accs[e], 0, 0, e, True, False)
-        for g in (2, 1):
-            for e in range(4, E):
-                multiply(accs[e], g, 0, e, False, False)
-        for e in (4, 6):
-            gather_words(3, C * e, C * (e + 2))
-            close_first_half(e)
-            close_first_half(e + 1)
         fetch(first, 0, 0, 0, T)
         fetch(second, 0, 1, 0, 384)
         fetch(second, 0, 1, 384, T)
         add_and_store(0, 0, 384)
-        for e in range(2, E):
-            second_half(e)
         fetch(first, 1, 0, 0, T)
         add_and_store(0, 384, T)
         fetch(second, 1, 1, 0, 384)

@@ -48,8 +48,8 @@ def tile_moe_pln_lin_silu_kernel(
         slot_words = [keep.tile([P, SLOTS], U32, name="slot_words%d" % g, align_bytes=64) for g in range(PASSES)]
         slot_plane = [keep.tile([P, HALF], U8, name="slot_plane%d" % u, align_bytes=64) for u in range(2)]
         moved = [keep.tile([P, HALF], U8, name="moved%d" % u, align_bytes=64) for u in range(2)]
-        w8 = [[keep.tile([P, E, P], I32, name="w8_%d_%d" % (h, u), align_bytes=64) for u in range(2)] for h in range(2)]
-        w4 = [[keep.tile([P, E, 2 * P], U8, name="w4_%d_%d" % (h, u), align_bytes=64) for u in range(2)] for h in range(2)]
+        w8 = [keep.tile([P, E, N], I32, name="w8_%d" % u, align_bytes=64) for u in range(2)]
+        w4 = [keep.tile([P, E, 2 * N], U8, name="w4_%d" % u, align_bytes=64) for u in range(2)]
         w_planes = keep.tile([P, E * 2 * N], U8, name="w_planes", align_bytes=64)
         gates = keep.tile([P, 2, T], F32, name="gates")
         bias = keep.tile([P, 2, E], F32, name="bias")
@@ -66,28 +66,31 @@ def tile_moe_pln_lin_silu_kernel(
         def load_scales(k, scales, r):
             rows = scales.bitcast(I32).rearrange("e a q n -> q (e a) n")
             tile_rows = w_planes[:].bitcast(I32).rearrange("p (ea n) -> p ea n", ea=2 * E)
-            nc.sync.dma_start(out=tile_rows[k + r : P : 32], in_=rows[r:16:4])
+            nc.gpsimd.dma_start(out=tile_rows[k + r : P : 32], in_=rows[r:16:4])
 
         w8_rows = w8_words.rearrange("e a p n t -> (e a) p (n t)").bitcast(I32)
         w4_rows = w4_words.rearrange("e a p n -> (e a) p n").bitcast(I32)
 
-        def load_w8(h, u):
-            rows = w8_rows[E * u : E * (u + 1), :, P * h : P * (h + 1)]
-            nc.sync.dma_start(out=w8[h][u][:], in_=rows.rearrange("m p n -> p m n"))
+        def load_w8(u):
+            nc.sync.dma_start(out=w8[u][:], in_=w8_rows[E * u : E * (u + 1)].rearrange("m p n -> p m n"))
 
-        def load_w4(h, u):
-            rows = w4_rows[E * u : E * (u + 1), :, 64 * h : 64 * (h + 1)]
-            into = w4[h][u][:].rearrange("p m n -> p (m n)").bitcast(I32).rearrange("p (m n) -> p m n", m=E)
-            nc.sync.dma_start(out=into, in_=rows.rearrange("m p n -> p m n"))
+        def load_w4(u):
+            into = w4[u][:].rearrange("p m n -> p (m n)").bitcast(I32).rearrange("p (m n) -> p m n", m=E)
+            nc.sync.dma_start(out=into, in_=w4_rows[E * u : E * (u + 1)].rearrange("m p n -> p m n"))
 
+        nc.vector.memset(w_planes[:].bitcast(I32), 0)
         nc.vector.memset(dummy[:], 0.0)
         nc.scalar.activation(dummy[:, 1:2], dummy[:, 0:1], SILU)
         nc.vector.memset(plane[:].bitcast(I32), 0)
         nc.vector.memset(words[:, PASSES * T :], 0)
-        nc.vector.memset(w_planes[:].bitcast(I32), 0)
         for u in range(2):
             nc.vector.memset(moved[u][:].bitcast(I32), 0)
 
+        for r in range(4):
+            load_scales(W8_ROW, w8_scales, r)
+        for r in range(4):
+            load_scales(0, w4_scales, r)
+        nc.gpsimd.dma_start(out=bias[:], in_=b.rearrange("(h p) e -> p h e", h=2))
         load_x(0, 0)
         load_x(0, 1)
         nc.sync.dma_start(offs_sb[:], offs)
@@ -96,18 +99,10 @@ def tile_moe_pln_lin_silu_kernel(
             load_x(g, 1)
         nc.sync.dma_start(pos1_sb[:], pos1)
         nc.sync.dma_start(pos2_sb[:], pos2)
-        nc.sync.dma_start(out=bias[:], in_=b.rearrange("(h p) e -> p h e", h=2))
-        for r in range(4):
-            load_scales(W8_ROW, w8_scales, r)
-            load_scales(0, w4_scales, r)
-        load_w8(0, 0)
-        load_w8(0, 1)
-        load_w4(0, 0)
-        load_w4(0, 1)
-        nc.sync.dma_start(out=gates[:], in_=gate[:, 0:P, :].rearrange("i p t -> p i t"))
         for u in range(2):
-            load_w8(1, u)
-            load_w4(1, u)
+            load_w8(u)
+            load_w4(u)
+        nc.sync.dma_start(out=gates[:], in_=gate[:, 0:P, :].rearrange("i p t -> p i t"))
 
         def interleave(engine_copy, g, lo, hi):
             u = lo // 256
@@ -141,9 +136,9 @@ def tile_moe_pln_lin_silu_kernel(
             cols = slice(C * (e % 4), C * (e % 4 + 1))
             scale_cols = slice(N * (2 * e + a) + P * h, N * (2 * e + a) + P * (h + 1))
             if g < 2:
-                k, weights = W8_ROW, w8[h][u][:, m, :].bitcast(E4M3)
+                k, weights = W8_ROW, w8[u][:, m, P * h : P * (h + 1)].bitcast(E4M3)
             else:
-                k, weights = 0, w4[h][u][:, m, :].bitcast(E2M1)
+                k, weights = 0, w4[u][:, m, 2 * P * h : 2 * P * (h + 1)].bitcast(E2M1)
             nc.tensor.matmul_mx(
                 out=acc[:],
                 lhsT=weights,

@@ -41,7 +41,7 @@ def tile_moe_pln_lin_silu_kernel(
         pos1_sb = lists.tile([P, T // 16], U16, name="pos1_sb")
         pos2_sb = lists.tile([P, T // 16], U16, name="pos2_sb")
 
-        x = [[keep.tile([P, 4, T // 2], F32, name="x%d_%d" % (g, u)) for u in range(2)] for g in range(PASSES)]
+        x = [keep.tile([P, 4, T], F32, name="x%d" % g) for g in range(PASSES)]
         xb = [keep.tile([P, T, 4], BF16, name="xb%d" % g, align_bytes=64) for g in range(PASSES)]
         words = keep.tile([P, (PASSES - 1) * T + WIDE], I32, name="words", align_bytes=64)
         plane = keep.tile([P, BYTE_WINDOW], U8, name="plane", align_bytes=64)
@@ -59,9 +59,8 @@ def tile_moe_pln_lin_silu_kernel(
         result = [keep.tile([P, T], F32, name="result%d" % h) for h in range(2)]
         dummy = keep.tile([P, 2], F32, name="dummy")
 
-        def load_x(g, u):
-            rows = xT[512 * g : 512 * (g + 1), 256 * u : 256 * (u + 1)].rearrange("(p j) t -> p j t", j=4)
-            nc.sync.dma_start(out=x[g][u][:], in_=rows)
+        def load_x(g):
+            nc.sync.dma_start(out=x[g][:], in_=xT[512 * g : 512 * (g + 1), :].rearrange("(p j) t -> p j t", j=4))
 
         def load_scales(k, scales, r):
             rows = scales.bitcast(I32).rearrange("e a q n -> q (e a) n")
@@ -91,12 +90,10 @@ def tile_moe_pln_lin_silu_kernel(
         for r in range(4):
             load_scales(0, w4_scales, r)
         nc.gpsimd.dma_start(out=bias[:], in_=b.rearrange("(h p) e -> p h e", h=2))
-        load_x(0, 0)
-        load_x(0, 1)
+        load_x(0)
         nc.sync.dma_start(offs_sb[:], offs)
         for g in range(1, PASSES):
-            load_x(g, 0)
-            load_x(g, 1)
+            load_x(g)
         nc.sync.dma_start(pos1_sb[:], pos1)
         nc.sync.dma_start(pos2_sb[:], pos2)
         for u in range(2):
@@ -105,8 +102,7 @@ def tile_moe_pln_lin_silu_kernel(
         nc.sync.dma_start(out=gates[:], in_=gate[:, 0:P, :].rearrange("i p t -> p i t"))
 
         def interleave(engine_copy, g, lo, hi):
-            u = lo // 256
-            rows = x[g][u][:, :, lo - 256 * u : hi - 256 * u]
+            rows = x[g][:, :, lo:hi]
             engine_copy(
                 out=xb[g][:, lo:hi, :].rearrange("p (c i) j -> p c j i", i=4),
                 in_=rows.rearrange("p j (c i) -> p c j i", i=4),
@@ -160,41 +156,41 @@ def tile_moe_pln_lin_silu_kernel(
             nc.vector.tensor_add(result[h][:, lo:hi], first[h][:, lo:hi], second[h][:, lo:hi])
             nc.sync.dma_start(out=out[P * h : P * (h + 1), lo:hi], in_=result[h][:, lo:hi])
 
+        interleave(nc.scalar.copy, 0, 336, T)
         interleave(nc.vector.tensor_copy, 0, 0, 256)
+        interleave(nc.vector.tensor_copy, 0, 256, 336)
         quantize(0, 0, 256)
-        interleave(nc.scalar.copy, 0, 416, 512)
-        interleave(nc.vector.tensor_copy, 0, 256, 416)
-        quantize(0, 256, 512)
+        quantize(0, 256, T)
         for g in range(1, PASSES):
-            interleave(nc.scalar.copy, g, 0, 256)
-            interleave(nc.scalar.copy, g, 256, T)
+            interleave(nc.scalar.copy, g, 0, T)
         gather_words(0, 0, SLOTS, WIDE)
         quantize(1, 0, T)
         gather_words(1, 0, SLOTS, WIDE)
         quantize(2, 0, T)
-        gather_words(2, 0, 384, T)
+        gather_words(2, 0, 256, T)
+        gather_words(2, 256, 512, T)
         quantize(3, 0, T)
         gather_bytes(0)
         gather_bytes(1)
         gather_words(3, 0, 512, 2 * T)
-        gather_words(2, 384, SLOTS, 2 * T)
+        gather_words(2, 512, SLOTS, 2 * T)
         gather_words(3, 512, 768, T)
         gather_words(3, 768, 896, T)
         gather_words(3, 896, SLOTS, T)
 
-        accs = [psum.tile([P, C], F32, name="acc") for e in range(E)]
-        for e in range(E):
-            multiply(accs[e], 0, 0, e, True, False)
-            multiply(accs[e], 1, 0, e, False, False)
-        for e in range(E):
-            multiply(accs[e], 2, 0, e, False, False)
-            multiply(accs[e], 3, 0, e, False, True)
-            finish(accs[e], 0, e)
-        for e in range(E):
-            acc = psum.tile([P, C], F32, name="acc")
-            for g in range(PASSES):
-                multiply(acc, g, 1, e, g == 0, g == PASSES - 1)
-            finish(acc, 1, e)
+        for u in range(2):
+            experts = range(4 * u, 4 * u + 4)
+            accs = {(h, e): psum.tile([P, C], F32, name="acc") for h in range(2) for e in experts}
+            for h in range(2):
+                for e in experts:
+                    multiply(accs[h, e], 0, h, e, True, False)
+                    multiply(accs[h, e], 1, h, e, False, False)
+            for h in range(2):
+                for e in experts:
+                    multiply(accs[h, e], 2, h, e, False, False)
+                for e in experts:
+                    multiply(accs[h, e], 3, h, e, False, True)
+                    finish(accs[h, e], h, e)
 
         fetch(first, 0, 0, 0, T)
         fetch(second, 0, 1, 0, 384)

@@ -1,6 +1,7 @@
 from contextlib import ExitStack
 
 import concourse.mybir as mybir
+from concourse.masks import make_identity
 
 K, T, E, C, N = 2048, 512, 8, 128, 256
 SLOTS = E * C
@@ -41,17 +42,18 @@ def tile_moe_pln_lin_silu_kernel(
         pos1_sb = lists.tile([P, T // 16], U16, name="pos1_sb")
         pos2_sb = lists.tile([P, T // 16], U16, name="pos2_sb")
 
-        x = [keep.tile([P, 4, T], F32, name="x%d" % g) for g in range(PASSES)]
+        x = [keep.tile([P, 4, T], F32, name="x%d" % g, align_bytes=64) for g in range(PASSES)]
         xb = [keep.tile([P, T, 4], BF16, name="xb%d" % g, align_bytes=64) for g in range(PASSES)]
         words = keep.tile([P, (PASSES - 1) * T + WIDE], I32, name="words", align_bytes=64)
-        plane = keep.tile([P, BYTE_WINDOW], U8, name="plane", align_bytes=64)
+        plane = keep.tile([P, BYTE_WINDOW], U8, name="plane", tag="plane", align_bytes=64)
         slot_words = [keep.tile([P, SLOTS], U32, name="slot_words%d" % g, align_bytes=64) for g in range(PASSES)]
         slot_plane = [keep.tile([P, HALF], U8, name="slot_plane%d" % u, align_bytes=64) for u in range(2)]
         moved = [keep.tile([P, HALF], U8, name="moved%d" % u, align_bytes=64) for u in range(2)]
-        w8 = [keep.tile([P, E, N], I32, name="w8_%d" % u, align_bytes=64) for u in range(2)]
-        w4 = [keep.tile([P, E, 2 * N], U8, name="w4_%d" % u, align_bytes=64) for u in range(2)]
-        w_planes = keep.tile([P, E * 2 * N], U8, name="w_planes", align_bytes=64)
+        w8, w4 = {}, {}
+        ident = keep.tile([P, P], F32, name="ident")
+        gate_rows = keep.tile([P, 2, 8], F32, name="gate_rows")
         gates = keep.tile([P, 2, T], F32, name="gates")
+        w_planes = keep.tile([P, E * 2 * N], U8, name="w_planes", align_bytes=64)
         bias = keep.tile([P, 2, E], F32, name="bias")
         y = [keep.tile([P, SLOTS], F32, name="y%d" % h) for h in range(2)]
         first = [keep.tile([P, T], F32, name="first%d" % h) for h in range(2)]
@@ -65,17 +67,22 @@ def tile_moe_pln_lin_silu_kernel(
         def load_scales(k, scales, r):
             rows = scales.bitcast(I32).rearrange("e a q n -> q (e a) n")
             tile_rows = w_planes[:].bitcast(I32).rearrange("p (ea n) -> p ea n", ea=2 * E)
-            nc.gpsimd.dma_start(out=tile_rows[k + r : P : 32], in_=rows[r:16:4])
+            nc.sync.dma_start(out=tile_rows[k + r : P : 32], in_=rows[r:16:4])
 
         w8_rows = w8_words.rearrange("e a p n t -> (e a) p (n t)").bitcast(I32)
         w4_rows = w4_words.rearrange("e a p n -> (e a) p n").bitcast(I32)
 
-        def load_w8(u):
-            nc.sync.dma_start(out=w8[u][:], in_=w8_rows[E * u : E * (u + 1)].rearrange("m p n -> p m n"))
+        def load_w8(h, u, into):
+            w8[h, u] = into.rearrange("p (m n) -> p m n", m=E)
+            rows = w8_rows[E * u : E * (u + 1), :, P * h : P * (h + 1)]
+            nc.sync.dma_start(out=w8[h, u], in_=rows.rearrange("m p n -> p m n"))
 
-        def load_w4(u):
-            into = w4[u][:].rearrange("p m n -> p (m n)").bitcast(I32).rearrange("p (m n) -> p m n", m=E)
-            nc.sync.dma_start(out=into, in_=w4_rows[E * u : E * (u + 1)].rearrange("m p n -> p m n"))
+        def load_w4(u, into):
+            w4[u] = into.rearrange("p (m n) -> p m n", m=E)
+            nc.sync.dma_start(out=w4[u], in_=w4_rows[E * u : E * (u + 1)].rearrange("m p n -> p m n"))
+
+        def reuse(name, tag, width):
+            return keep.tile([P, width], I32, name=name, tag=tag, align_bytes=64)[:]
 
         nc.vector.memset(w_planes[:].bitcast(I32), 0)
         nc.vector.memset(dummy[:], 0.0)
@@ -85,21 +92,18 @@ def tile_moe_pln_lin_silu_kernel(
         for u in range(2):
             nc.vector.memset(moved[u][:].bitcast(I32), 0)
 
-        for r in range(4):
-            load_scales(W8_ROW, w8_scales, r)
-        for r in range(4):
-            load_scales(0, w4_scales, r)
-        nc.gpsimd.dma_start(out=bias[:], in_=b.rearrange("(h p) e -> p h e", h=2))
+        make_identity(nc, ident[:])
         load_x(0)
         nc.sync.dma_start(offs_sb[:], offs)
+        nc.sync.dma_start(out=gate_rows[:, :, 0:4], in_=gate[:, 0, :].rearrange("i (p r) -> p i r", r=4))
         for g in range(1, PASSES):
             load_x(g)
+        nc.sync.dma_start(out=bias[:], in_=b.rearrange("(h p) e -> p h e", h=2))
         nc.sync.dma_start(pos1_sb[:], pos1)
         nc.sync.dma_start(pos2_sb[:], pos2)
-        for u in range(2):
-            load_w8(u)
-            load_w4(u)
-        nc.sync.dma_start(out=gates[:], in_=gate[:, 0:P, :].rearrange("i p t -> p i t"))
+        for r in range(4):
+            load_scales(W8_ROW, w8_scales, r)
+            load_scales(0, w4_scales, r)
 
         def interleave(engine_copy, g, lo, hi):
             rows = x[g][:, :, lo:hi]
@@ -124,7 +128,7 @@ def tile_moe_pln_lin_silu_kernel(
         def gather_bytes(u):
             nc.vector.tensor_copy(slot_plane[u][:], plane[:].indirect(offs_sb[:, 32 * u : 32 * (u + 1)]))
             k = SCALE_ROW[2]
-            nc.scalar.dma_start(out=moved[u][0:112, :].bitcast(I32), in_=slot_plane[u][k : k + 112, :].bitcast(I32))
+            nc.sync.dma_start(out=moved[u][0:112, :].bitcast(I32), in_=slot_plane[u][k : k + 112, :].bitcast(I32))
 
         def multiply(acc, g, h, e, start, stop):
             a = g % 2
@@ -132,9 +136,9 @@ def tile_moe_pln_lin_silu_kernel(
             cols = slice(C * (e % 4), C * (e % 4 + 1))
             scale_cols = slice(N * (2 * e + a) + P * h, N * (2 * e + a) + P * (h + 1))
             if g < 2:
-                k, weights = W8_ROW, w8[u][:, m, P * h : P * (h + 1)].bitcast(E4M3)
+                k, weights = W8_ROW, w8[h, u][:, m, :].bitcast(E4M3)
             else:
-                k, weights = 0, w4[u][:, m, 2 * P * h : 2 * P * (h + 1)].bitcast(E2M1)
+                k, weights = 0, w4[u][:, m, 64 * h : 64 * (h + 1)].bitcast(U8).bitcast(E2M1)
             nc.tensor.matmul_mx(
                 out=acc[:],
                 lhsT=weights,
@@ -161,8 +165,15 @@ def tile_moe_pln_lin_silu_kernel(
         interleave(nc.vector.tensor_copy, 0, 256, 336)
         quantize(0, 0, 256)
         quantize(0, 256, T)
+        load_w8(0, 0, reuse("w8_first", "x0", 1024))
+        load_w4(0, reuse("w4_first", "xb0", 1024))
         for g in range(1, PASSES):
             interleave(nc.scalar.copy, g, 0, T)
+        for i in range(2):
+            spread = psum.tile([P, 4, P], F32, name="spread", tag="acc")
+            for r in range(4):
+                nc.tensor.transpose(spread[:, r, :], gate_rows[:, i, r : r + 1].to_broadcast([P, P]), ident[:])
+            nc.scalar.copy(out=gates[:, i, :].rearrange("p (t r) -> p t r", r=4), in_=spread[:].rearrange("p r t -> p t r"))
         gather_words(0, 0, SLOTS, WIDE)
         quantize(1, 0, T)
         gather_words(1, 0, SLOTS, WIDE)
@@ -170,27 +181,31 @@ def tile_moe_pln_lin_silu_kernel(
         gather_words(2, 0, 256, T)
         gather_words(2, 256, 512, T)
         quantize(3, 0, T)
+        load_w8(0, 1, reuse("w8_second", "xb3", 1024))
         gather_bytes(0)
         gather_bytes(1)
+        late = reuse("late", "plane", 3072)
+        load_w4(1, late[:, 0:1024])
+        load_w8(1, 0, late[:, 1024:2048])
+        load_w8(1, 1, late[:, 2048:3072])
         gather_words(3, 0, 512, 2 * T)
         gather_words(2, 512, SLOTS, 2 * T)
         gather_words(3, 512, 768, T)
         gather_words(3, 768, 896, T)
         gather_words(3, 896, SLOTS, T)
 
-        for u in range(2):
-            experts = range(4 * u, 4 * u + 4)
-            accs = {(h, e): psum.tile([P, C], F32, name="acc") for h in range(2) for e in experts}
-            for h in range(2):
+        for h, order in ((0, (0, 1, 2, 3)), (1, (2, 3, 0, 1))):
+            accs = [psum.tile([P, C], F32, name="acc") for e in range(E)]
+            for u in range(2):
+                experts = range(4 * u, 4 * u + 4)
                 for e in experts:
-                    multiply(accs[h, e], 0, h, e, True, False)
-                    multiply(accs[h, e], 1, h, e, False, False)
-            for h in range(2):
+                    multiply(accs[e], order[0], h, e, True, False)
+                    multiply(accs[e], order[1], h, e, False, False)
                 for e in experts:
-                    multiply(accs[h, e], 2, h, e, False, False)
+                    multiply(accs[e], order[2], h, e, False, False)
                 for e in experts:
-                    multiply(accs[h, e], 3, h, e, False, True)
-                    finish(accs[h, e], h, e)
+                    multiply(accs[e], order[3], h, e, False, True)
+                    finish(accs[e], h, e)
 
         fetch(first, 0, 0, 0, T)
         fetch(second, 0, 1, 0, 384)

@@ -72,14 +72,17 @@ def tile_moe_pln_lin_silu_kernel(
         w8_rows = w8_words.rearrange("e a p n t -> (e a) p (n t)").bitcast(I32)
         w4_rows = w4_words.rearrange("e a p n -> (e a) p n").bitcast(I32)
 
-        def load_w8(h, u, into):
-            w8[h, u] = into.rearrange("p (m n) -> p m n", m=E)
-            rows = w8_rows[E * u : E * (u + 1), :, P * h : P * (h + 1)]
-            nc.sync.dma_start(out=w8[h, u], in_=rows.rearrange("m p n -> p m n"))
+        def load_w8(h, lo, hi, into):
+            into = into.rearrange("p (m n) -> p m n", n=P)
+            nc.sync.dma_start(out=into, in_=w8_rows[2 * lo : 2 * hi, :, P * h : P * (h + 1)].rearrange("m p n -> p m n"))
+            for m in range(2 * lo, 2 * hi):
+                w8[h, m] = into[:, m - 2 * lo, :]
 
-        def load_w4(u, into):
-            w4[u] = into.rearrange("p (m n) -> p m n", m=E)
-            nc.sync.dma_start(out=w4[u], in_=w4_rows[E * u : E * (u + 1)].rearrange("m p n -> p m n"))
+        def load_w4(lo, hi, into):
+            into = into.rearrange("p (m n) -> p m n", n=P)
+            nc.sync.dma_start(out=into, in_=w4_rows[2 * lo : 2 * hi].rearrange("m p n -> p m n"))
+            for m in range(2 * lo, 2 * hi):
+                w4[m] = into[:, m - 2 * lo, :]
 
         def reuse(name, tag, width):
             return keep.tile([P, width], I32, name=name, tag=tag, align_bytes=64)[:]
@@ -132,13 +135,13 @@ def tile_moe_pln_lin_silu_kernel(
 
         def multiply(acc, g, h, e, start, stop):
             a = g % 2
-            u, m = divmod(2 * e + a, E)
+            u, m = e // 4, 2 * e + a
             cols = slice(C * (e % 4), C * (e % 4 + 1))
             scale_cols = slice(N * (2 * e + a) + P * h, N * (2 * e + a) + P * (h + 1))
             if g < 2:
-                k, weights = W8_ROW, w8[h, u][:, m, :].bitcast(E4M3)
+                k, weights = W8_ROW, w8[h, m].bitcast(E4M3)
             else:
-                k, weights = 0, w4[u][:, m, 64 * h : 64 * (h + 1)].bitcast(U8).bitcast(E2M1)
+                k, weights = 0, w4[m][:, 64 * h : 64 * (h + 1)].bitcast(U8).bitcast(E2M1)
             nc.tensor.matmul_mx(
                 out=acc[:],
                 lhsT=weights,
@@ -165,8 +168,8 @@ def tile_moe_pln_lin_silu_kernel(
         interleave(nc.vector.tensor_copy, 0, 256, 336)
         quantize(0, 0, 256)
         quantize(0, 256, T)
-        load_w8(0, 0, reuse("w8_first", "x0", 1024))
-        load_w4(0, reuse("w4_first", "xb0", 1024))
+        load_w8(0, 0, 4, reuse("w8_first", "x0", 1024))
+        load_w4(0, 4, reuse("w4_first", "xb0", 1024))
         for g in range(1, PASSES):
             interleave(nc.scalar.copy, g, 0, T)
         for i in range(2):
@@ -181,31 +184,39 @@ def tile_moe_pln_lin_silu_kernel(
         gather_words(2, 0, 256, T)
         gather_words(2, 256, 512, T)
         quantize(3, 0, T)
-        load_w8(0, 1, reuse("w8_second", "xb3", 1024))
+        load_w8(0, 4, 8, reuse("w8_second", "xb3", 1024))
         gather_bytes(0)
         gather_bytes(1)
         late = reuse("late", "plane", 3072)
-        load_w4(1, late[:, 0:1024])
-        load_w8(1, 0, late[:, 1024:2048])
-        load_w8(1, 1, late[:, 2048:3072])
+        load_w4(4, 6, late[:, 0:512])
+        load_w4(6, 8, late[:, 512:1024])
+        load_w8(1, 0, 4, late[:, 1024:2048])
+        load_w8(1, 4, 6, late[:, 2048:2560])
+        load_w8(1, 6, 8, late[:, 2560:3072])
         gather_words(3, 0, 512, 2 * T)
         gather_words(2, 512, SLOTS, 2 * T)
         gather_words(3, 512, 768, T)
         gather_words(3, 768, 896, T)
         gather_words(3, 896, SLOTS, T)
 
-        for h, order in ((0, (0, 1, 2, 3)), (1, (2, 3, 0, 1))):
-            accs = [psum.tile([P, C], F32, name="acc") for e in range(E)]
-            for u in range(2):
-                experts = range(4 * u, 4 * u + 4)
-                for e in experts:
-                    multiply(accs[e], order[0], h, e, True, False)
-                    multiply(accs[e], order[1], h, e, False, False)
-                for e in experts:
-                    multiply(accs[e], order[2], h, e, False, False)
-                for e in experts:
-                    multiply(accs[e], order[3], h, e, False, True)
-                    finish(accs[e], h, e)
+        accs = [psum.tile([P, C], F32, name="acc") for e in range(E)]
+        for u in range(2):
+            experts = range(4 * u, 4 * u + 4)
+            for e in experts:
+                multiply(accs[e], 0, 0, e, True, False)
+                multiply(accs[e], 1, 0, e, False, False)
+            for e in experts:
+                multiply(accs[e], 2, 0, e, False, False)
+                multiply(accs[e], 3, 0, e, False, True)
+                finish(accs[e], 0, e)
+        accs = [psum.tile([P, C], F32, name="acc") for e in range(E)]
+        for e in range(E):
+            multiply(accs[e], 2, 1, e, True, False)
+            multiply(accs[e], 3, 1, e, False, False)
+        for e in range(E):
+            multiply(accs[e], 0, 1, e, False, False)
+            multiply(accs[e], 1, 1, e, False, True)
+            finish(accs[e], 1, e)
 
         fetch(first, 0, 0, 0, T)
         fetch(second, 0, 1, 0, 384)

@@ -52,7 +52,6 @@ def tile_moe_pln_lin_silu_kernel(
         w8, w4 = {}, {}
         ident = keep.tile([P, P], F32, name="ident")
         gate_rows = keep.tile([P, 2, 8], F32, name="gate_rows")
-        gates = keep.tile([P, 2, T], F32, name="gates")
         w_planes = keep.tile([P, E * 2 * N], U8, name="w_planes", align_bytes=64)
         bias = keep.tile([P, 2, E], F32, name="bias")
         y = [keep.tile([P, SLOTS], F32, name="y%d" % h) for h in range(2)]
@@ -172,6 +171,7 @@ def tile_moe_pln_lin_silu_kernel(
         load_w4(0, 4, reuse("w4_first", "xb0", 1024))
         for g in range(1, PASSES):
             interleave(nc.scalar.copy, g, 0, T)
+        gates = keep.tile([P, 2, T], F32, name="gates", tag="x3", align_bytes=64)
         for i in range(2):
             spread = psum.tile([P, 4, P], F32, name="spread", tag="acc")
             for r in range(4):

@@ -184,15 +184,15 @@ def tile_moe_pln_lin_silu_kernel(
         gather_words(2, 0, 256, T)
         gather_words(2, 256, 512, T)
         quantize(3, 0, T)
-        load_w8(0, 4, 8, reuse("w8_second", "xb3", 1024))
+        middle = reuse("middle", "xb3", 2048)
+        load_w8(0, 4, 8, middle[:, 0:1024])
+        load_w4(4, 8, middle[:, 1024:2048])
         gather_bytes(0)
         gather_bytes(1)
-        late = reuse("late", "plane", 3072)
-        load_w4(4, 6, late[:, 0:512])
-        load_w4(6, 8, late[:, 512:1024])
-        load_w8(1, 0, 4, late[:, 1024:2048])
-        load_w8(1, 4, 6, late[:, 2048:2560])
-        load_w8(1, 6, 8, late[:, 2560:3072])
+        late = reuse("late", "plane", 2048)
+        load_w8(1, 0, 4, late[:, 0:1024])
+        load_w8(1, 4, 6, late[:, 1024:1536])
+        load_w8(1, 6, 8, late[:, 1536:2048])
         gather_words(3, 0, 512, 2 * T)
         gather_words(2, 512, SLOTS, 2 * T)
         gather_words(3, 512, 768, T)

@@ -24,7 +24,7 @@ PASSES = 4
 HALF = SLOTS // 2
 SCALE_ROW = (4, 8, 12, 0)
 W8_ROW = 8
-WORD_COLUMN = (3 * T, 2 * T, 0, T)
+WORD_COLUMN = (2 * T, T, 0, 2 * T + 1408)
 WIDE = 1408
 BYTE_WINDOW = 704
 
@@ -44,7 +44,7 @@ def tile_moe_pln_lin_silu_kernel(
 
         x = [keep.tile([P, 4, T], F32, name="x%d" % g, align_bytes=64) for g in range(PASSES)]
         xb = [keep.tile([P, T, 4], BF16, name="xb%d" % g, align_bytes=64) for g in range(PASSES)]
-        words = keep.tile([P, (PASSES - 1) * T + WIDE], I32, name="words", align_bytes=64)
+        words = keep.tile([P, WORD_COLUMN[3] + 704], I32, name="words", align_bytes=64)
         plane = keep.tile([P, BYTE_WINDOW], U8, name="plane", tag="plane", align_bytes=64)
         slot_words = [keep.tile([P, SLOTS], U32, name="slot_words%d" % g, align_bytes=64) for g in range(PASSES)]
         slot_plane = [keep.tile([P, HALF], U8, name="slot_plane%d" % u, align_bytes=64) for u in range(2)]
@@ -90,7 +90,8 @@ def tile_moe_pln_lin_silu_kernel(
         nc.vector.memset(dummy[:], 0.0)
         nc.scalar.activation(dummy[:, 1:2], dummy[:, 0:1], SILU)
         nc.vector.memset(plane[:].bitcast(I32), 0)
-        nc.vector.memset(words[:, PASSES * T :], 0)
+        nc.vector.memset(words[:, 3 * T : WORD_COLUMN[3]], 0)
+        nc.vector.memset(words[:, WORD_COLUMN[3] + T :], 0)
         for u in range(2):
             nc.vector.memset(moved[u][:].bitcast(I32), 0)
 
@@ -181,8 +182,7 @@ def tile_moe_pln_lin_silu_kernel(
         quantize(1, 0, T)
         gather_words(1, 0, SLOTS, WIDE)
         quantize(2, 0, T)
-        gather_words(2, 0, 256, T)
-        gather_words(2, 256, 512, T)
+        gather_words(2, 0, 512, 2 * T)
         quantize(3, 0, T)
         middle = reuse("middle", "xb3", 2048)
         load_w8(0, 4, 8, middle[:, 0:1024])
@@ -193,8 +193,8 @@ def tile_moe_pln_lin_silu_kernel(
         load_w8(1, 0, 4, late[:, 0:1024])
         load_w8(1, 4, 6, late[:, 1024:1536])
         load_w8(1, 6, 8, late[:, 1536:2048])
-        gather_words(3, 0, 512, 2 * T)
-        gather_words(2, 512, SLOTS, 2 * T)
+        gather_words(3, 0, 512, 704)
+        gather_words(2, 512, SLOTS, WORD_COLUMN[3] + T)
         gather_words(3, 512, 768, T)
         gather_words(3, 768, 896, T)
         gather_words(3, 896, SLOTS, T)
@@ -218,12 +218,26 @@ def tile_moe_pln_lin_silu_kernel(
             multiply(accs[e], 1, 1, e, False, True)
             finish(accs[e], 1, e)
 
+        def add_by_transposes(lo):
+            turned = psum.tile([P, 2, P], F32, name="turned", tag="acc")
+            for i in range(2):
+                cols = slice(lo + P * i, lo + P * (i + 1))
+                nc.tensor.matmul(turned[:, i, :], first[0][:, cols], ident[:], start=True, stop=False, is_transpose=True)
+                nc.tensor.matmul(turned[:, i, :], second[0][:, cols], ident[:], start=False, stop=True, is_transpose=True)
+            sums = keep.tile([P, 2, P], F32, name="sums%d" % lo)
+            nc.scalar.copy(out=sums[:], in_=turned[:])
+            back = psum.tile([P, 2, P], F32, name="back", tag="acc")
+            for i in range(2):
+                nc.tensor.transpose(back[:, i, :], sums[:, i, :], ident[:])
+            nc.scalar.copy(out=result[0][:, lo : lo + 2 * P], in_=back[:].rearrange("p i t -> p (i t)"))
+            nc.sync.dma_start(out=out[0:P, lo : lo + 2 * P], in_=result[0][:, lo : lo + 2 * P])
+
         fetch(first, 0, 0, 0, T)
-        fetch(second, 0, 1, 0, 384)
-        fetch(second, 0, 1, 384, T)
-        add_and_store(0, 0, 384)
+        fetch(second, 0, 1, 0, 256)
+        fetch(second, 0, 1, 256, T)
+        add_by_transposes(0)
+        add_by_transposes(256)
         fetch(first, 1, 0, 0, T)
-        add_and_store(0, 384, T)
         fetch(second, 1, 1, 0, 384)
         fetch(second, 1, 1, 384, T)
         add_and_store(1, 0, 384)

@@ -98,11 +98,12 @@ def tile_moe_pln_lin_silu_kernel(
         make_identity(nc, ident[:])
         load_x(0)
         nc.sync.dma_start(offs_sb[:], offs)
+        load_x(1)
+        load_x(2)
         nc.sync.dma_start(out=gate_rows[:, :, 0:4], in_=gate[:, 0, :].rearrange("i (p r) -> p i r", r=4))
-        for g in range(1, PASSES):
-            load_x(g)
         nc.sync.dma_start(out=bias[:], in_=b.rearrange("(h p) e -> p h e", h=2))
         nc.sync.dma_start(pos1_sb[:], pos1)
+        load_x(3)
         nc.sync.dma_start(pos2_sb[:], pos2)
         for r in range(4):
             load_scales(W8_ROW, w8_scales, r)

@@ -46,7 +46,7 @@ def tile_moe_pln_lin_silu_kernel(
         xb = [keep.tile([P, T, 4], BF16, name="xb%d" % g, align_bytes=64) for g in range(PASSES)]
         words = keep.tile([P, WORD_COLUMN[3] + 704], I32, name="words", align_bytes=64)
         plane = keep.tile([P, BYTE_WINDOW], U8, name="plane", tag="plane", align_bytes=64)
-        slot_words = [keep.tile([P, SLOTS], U32, name="slot_words%d" % g, align_bytes=64) for g in range(PASSES)]
+        slot_words = {}
         slot_plane = [keep.tile([P, HALF], U8, name="slot_plane%d" % u, align_bytes=64) for u in range(2)]
         moved = [keep.tile([P, HALF], U8, name="moved%d" % u, align_bytes=64) for u in range(2)]
         w8, w4 = {}, {}
@@ -124,10 +124,14 @@ def tile_moe_pln_lin_silu_kernel(
                 in_=xb[g][:, lo:hi, :].rearrange("p t j -> p (t j)"),
             )
 
-        def gather_words(g, lo, hi, width):
+        def gather_words(g, lo, hi, width, tag=None):
+            name = "slot_words%d_%d" % (g, lo)
+            into = keep.tile([P, hi - lo], U32, name=name, tag=tag or name, align_bytes=64)
             start = WORD_COLUMN[g]
             window = words[:, start : start + width].bitcast(U32)
-            nc.vector.tensor_copy(slot_words[g][:, lo:hi], window.indirect(offs_sb[:, lo // 16 : hi // 16]))
+            nc.vector.tensor_copy(into[:], window.indirect(offs_sb[:, lo // 16 : hi // 16]))
+            for e in range(lo // C, hi // C):
+                slot_words[g, e] = into[:, C * e - lo : C * (e + 1) - lo]
 
         def gather_bytes(u):
             nc.vector.tensor_copy(slot_plane[u][:], plane[:].indirect(offs_sb[:, 32 * u : 32 * (u + 1)]))
@@ -147,7 +151,7 @@ def tile_moe_pln_lin_silu_kernel(
                 out=acc[:],
                 lhsT=weights,
                 lhsT_scale=w_planes[k:P, scale_cols],
-                rhs=slot_words[g][:, C * e : C * (e + 1)].bitcast(E4M3),
+                rhs=slot_words[g, e].bitcast(E4M3),
                 rhs_scale=moved[u][:, cols] if g == 2 else slot_plane[u][SCALE_ROW[g] : P, cols],
                 start=start,
                 stop=stop,
@@ -171,7 +175,9 @@ def tile_moe_pln_lin_silu_kernel(
         quantize(0, 256, T)
         load_w8(0, 0, 4, reuse("w8_first", "x0", 1024))
         load_w4(0, 4, reuse("w4_first", "xb0", 1024))
-        for g in range(1, PASSES):
+        interleave(nc.scalar.copy, 1, 0, 256)
+        interleave(nc.scalar.copy, 1, 256, T)
+        for g in range(2, PASSES):
             interleave(nc.scalar.copy, g, 0, T)
         gates = keep.tile([P, 2, T], F32, name="gates", tag="x3", align_bytes=64)
         for i in range(2):
@@ -180,9 +186,11 @@ def tile_moe_pln_lin_silu_kernel(
                 nc.tensor.transpose(spread[:, r, :], gate_rows[:, i, r : r + 1].to_broadcast([P, P]), ident[:])
             nc.scalar.copy(out=gates[:, i, :].rearrange("p (t r) -> p t r", r=4), in_=spread[:].rearrange("p r t -> p t r"))
         gather_words(0, 0, SLOTS, WIDE)
-        quantize(1, 0, T)
-        gather_words(1, 0, SLOTS, WIDE)
+        quantize(1, 0, 256)
+        quantize(1, 256, T)
+        gather_words(1, 0, 768, 2 * T)
         quantize(2, 0, T)
+        gather_words(1, 768, SLOTS, T, "x2")
         gather_words(2, 0, 512, 2 * T)
         quantize(3, 0, T)
         middle = reuse("middle", "xb3", 2048)

@@ -218,13 +218,13 @@ def tile_moe_pln_lin_silu_kernel(
                 multiply(accs[e], 2, 0, e, False, False)
                 multiply(accs[e], 3, 0, e, False, True)
                 finish(accs[e], 0, e)
-        accs = [psum.tile([P, C], F32, name="acc") for e in range(E)]
-        for e in range(E):
+        accs = {e: psum.tile([P, C], F32, name="acc") for e in (6, 7, 0, 1, 2, 3, 4, 5)}
+        for e in (6, 7, 0, 1, 2, 3):
             multiply(accs[e], 2, 1, e, True, False)
             multiply(accs[e], 3, 1, e, False, False)
         for e in range(E):
-            multiply(accs[e], 0, 1, e, False, False)
-            multiply(accs[e], 1, 1, e, False, True)
+            for g in range(PASSES if e in (4, 5) else 2):
+                multiply(accs[e], g, 1, e, g == 0 and e in (4, 5), g == (3 if e in (4, 5) else 1))
             finish(accs[e], 1, e)
 
         def add_by_transposes(lo):

@@ -173,8 +173,8 @@ def tile_moe_pln_lin_silu_kernel(
         interleave(nc.vector.tensor_copy, 0, 256, 336)
         quantize(0, 0, 256)
         quantize(0, 256, T)
-        load_w8(0, 0, 4, reuse("w8_first", "x0", 1024))
-        load_w4(0, 4, reuse("w4_first", "xb0", 1024))
+        load_w8(0, 0, E, reuse("w8_first", "x0", 2048))
+        load_w4(0, E, reuse("w4_all", "xb0", 2048))
         interleave(nc.scalar.copy, 1, 0, 256)
         interleave(nc.scalar.copy, 1, 256, T)
         for g in range(2, PASSES):
@@ -193,9 +193,6 @@ def tile_moe_pln_lin_silu_kernel(
         gather_words(1, 768, SLOTS, T, "x2")
         gather_words(2, 0, 512, 2 * T)
         quantize(3, 0, T)
-        middle = reuse("middle", "xb3", 2048)
-        load_w8(0, 4, 8, middle[:, 0:1024])
-        load_w4(4, 8, middle[:, 1024:2048])
         gather_bytes(0)
         gather_bytes(1)
         late = reuse("late", "plane", 2048)

@@ -46,6 +46,7 @@ def tile_moe_pln_lin_silu_kernel(
         xb = [keep.tile([P, T, 4], BF16, name="xb%d" % g, align_bytes=64) for g in range(PASSES)]
         words = keep.tile([P, WORD_COLUMN[3] + 704], I32, name="words", align_bytes=64)
         plane = keep.tile([P, BYTE_WINDOW], U8, name="plane", tag="plane", align_bytes=64)
+        plane_copy = keep.tile([P, BYTE_WINDOW], U8, name="plane_copy", tag="plane_copy", align_bytes=64)
         slot_words = {}
         slot_plane = [keep.tile([P, HALF], U8, name="slot_plane%d" % u, align_bytes=64) for u in range(2)]
         moved = [keep.tile([P, HALF], U8, name="moved%d" % u, align_bytes=64) for u in range(2)]
@@ -134,7 +135,7 @@ def tile_moe_pln_lin_silu_kernel(
                 slot_words[g, e] = into[:, C * e - lo : C * (e + 1) - lo]
 
         def gather_bytes(u):
-            nc.vector.tensor_copy(slot_plane[u][:], plane[:].indirect(offs_sb[:, 32 * u : 32 * (u + 1)]))
+            nc.vector.tensor_copy(slot_plane[u][:], (plane, plane_copy)[u][:].indirect(offs_sb[:, 32 * u : 32 * (u + 1)]))
             k = SCALE_ROW[2]
             nc.sync.dma_start(out=moved[u][0:112, :].bitcast(I32), in_=slot_plane[u][k : k + 112, :].bitcast(I32))
 
@@ -174,7 +175,7 @@ def tile_moe_pln_lin_silu_kernel(
         quantize(0, 0, 256)
         quantize(0, 256, T)
         load_w8(0, 0, E, reuse("w8_first", "x0", 2048))
-        load_w4(0, E, reuse("w4_all", "xb0", 2048))
+        load_w4(0, 4, reuse("w4_first", "xb0", 1024))
         interleave(nc.scalar.copy, 1, 0, 256)
         interleave(nc.scalar.copy, 1, 256, T)
         for g in range(2, PASSES):
@@ -193,9 +194,11 @@ def tile_moe_pln_lin_silu_kernel(
         gather_words(1, 768, SLOTS, T, "x2")
         gather_words(2, 0, 512, 2 * T)
         quantize(3, 0, T)
+        nc.vector.tensor_copy(plane_copy[:].bitcast(I32), plane[:].bitcast(I32))
         gather_bytes(0)
+        load_w4(4, 8, reuse("w4_second", "plane", 1024))
         gather_bytes(1)
-        late = reuse("late", "plane", 2048)
+        late = reuse("late", "plane_copy", 2048)
         load_w8(1, 0, 4, late[:, 0:1024])
         load_w8(1, 4, 6, late[:, 1024:1536])
         load_w8(1, 6, 8, late[:, 1536:2048])

@@ -78,6 +78,13 @@ def tile_moe_pln_lin_silu_kernel(
             for m in range(2 * lo, 2 * hi):
                 w8[h, m] = into[:, m - 2 * lo, :]
 
+        def load_w8_whole(lo, hi, into):
+            into = into.rearrange("p (m n) -> p m n", n=N)
+            nc.sync.dma_start(out=into, in_=w8_rows[2 * lo : 2 * hi].rearrange("m p n -> p m n"))
+            for m in range(2 * lo, 2 * hi):
+                for h in range(2):
+                    w8[h, m] = into[:, m - 2 * lo, P * h : P * (h + 1)]
+
         def load_w4(lo, hi, into):
             into = into.rearrange("p (m n) -> p m n", n=P)
             nc.sync.dma_start(out=into, in_=w4_rows[2 * lo : 2 * hi].rearrange("m p n -> p m n"))
@@ -174,7 +181,9 @@ def tile_moe_pln_lin_silu_kernel(
         interleave(nc.vector.tensor_copy, 0, 256, 336)
         quantize(0, 0, 256)
         quantize(0, 256, T)
-        load_w8(0, 0, E, reuse("w8_first", "x0", 2048))
+        early = reuse("w8_first", "x0", 2560)
+        load_w8_whole(0, 2, early[:, 0:1024])
+        load_w8(0, 2, E, early[:, 1024:2560])
         load_w4(0, 4, reuse("w4_first", "xb0", 1024))
         interleave(nc.scalar.copy, 1, 0, 256)
         interleave(nc.scalar.copy, 1, 256, T)
@@ -199,7 +208,7 @@ def tile_moe_pln_lin_silu_kernel(
         load_w4(4, 8, reuse("w4_second", "plane", 1024))
         gather_bytes(1)
         late = reuse("late", "plane_copy", 2048)
-        load_w8(1, 0, 4, late[:, 0:1024])
+        load_w8(1, 2, 4, late[:, 0:512])
         load_w8(1, 4, 6, late[:, 1024:1536])
         load_w8(1, 6, 8, late[:, 1536:2048])
         gather_words(3, 0, 512, 704)

@@ -181,9 +181,9 @@ def tile_moe_pln_lin_silu_kernel(
         interleave(nc.vector.tensor_copy, 0, 256, 336)
         quantize(0, 0, 256)
         quantize(0, 256, T)
-        early = reuse("w8_first", "x0", 2560)
-        load_w8_whole(0, 2, early[:, 0:1024])
-        load_w8(0, 2, E, early[:, 1024:2560])
+        early = reuse("w8_first", "x0", 2816)
+        load_w8_whole(0, 3, early[:, 0:1536])
+        load_w8(0, 3, E, early[:, 1536:2816])
         load_w4(0, 4, reuse("w4_first", "xb0", 1024))
         interleave(nc.scalar.copy, 1, 0, 256)
         interleave(nc.scalar.copy, 1, 256, T)
@@ -208,9 +208,9 @@ def tile_moe_pln_lin_silu_kernel(
         load_w4(4, 8, reuse("w4_second", "plane", 1024))
         gather_bytes(1)
         late = reuse("late", "plane_copy", 2048)
-        load_w8(1, 2, 4, late[:, 0:512])
-        load_w8(1, 4, 6, late[:, 1024:1536])
-        load_w8(1, 6, 8, late[:, 1536:2048])
+        load_w8(1, 3, 6, late[:, 0:768])
+        load_w8(1, 6, 7, late[:, 1024:1280])
+        load_w8(1, 7, 8, late[:, 1536:1792])
         gather_words(3, 0, 512, 704)
         gather_words(2, 512, SLOTS, WORD_COLUMN[3] + T)
         gather_words(3, 512, 768, T)

@@ -27,6 +27,8 @@ W8_ROW = 8
 WORD_COLUMN = (2 * T, T, 0, 2 * T + 1408)
 WIDE = 1408
 BYTE_WINDOW = 704
+GATE_STEP = 64 * T - P
+GATE_START = T + 3 * P
 
 
 def tile_moe_pln_lin_silu_kernel(
@@ -36,7 +38,7 @@ def tile_moe_pln_lin_silu_kernel(
     with ExitStack() as ctx:
         lists = ctx.enter_context(tc.tile_pool(name="lists", bufs=1))
         keep = ctx.enter_context(tc.tile_pool(name="keep", bufs=1))
-        psum = ctx.enter_context(tc.psum_pool(name="psum", bufs=8))
+        psum = ctx.enter_context(tc.psum_pool(name="psum", bufs=1))
 
         offs_sb = lists.tile([P, SLOTS // 16], U16, name="offs_sb")
         pos1_sb = lists.tile([P, T // 16], U16, name="pos1_sb")
@@ -52,7 +54,8 @@ def tile_moe_pln_lin_silu_kernel(
         moved = [keep.tile([P, HALF], U8, name="moved%d" % u, align_bytes=64) for u in range(2)]
         w8, w4 = {}, {}
         ident = keep.tile([P, P], F32, name="ident")
-        gate_rows = keep.tile([P, 2, 8], F32, name="gate_rows")
+        gate_rows = keep.tile([P, P], F32, name="gate_rows")
+        gate_columns = keep.tile([P, 8], F32, name="gate_columns")
         w_planes = keep.tile([P, E * 2 * N], U8, name="w_planes", align_bytes=64)
         bias = keep.tile([P, 2, E], F32, name="bias")
         y = [keep.tile([P, SLOTS], F32, name="y%d" % h) for h in range(2)]
@@ -94,6 +97,7 @@ def tile_moe_pln_lin_silu_kernel(
         def reuse(name, tag, width):
             return keep.tile([P, width], I32, name=name, tag=tag, align_bytes=64)[:]
 
+        nc.vector.memset(gate_rows[:], 0.0)
         nc.vector.memset(w_planes[:].bitcast(I32), 0)
         nc.vector.memset(dummy[:], 0.0)
         nc.scalar.activation(dummy[:, 1:2], dummy[:, 0:1], SILU)
@@ -105,13 +109,14 @@ def tile_moe_pln_lin_silu_kernel(
 
         make_identity(nc, ident[:])
         load_x(0)
+        gate_runs = gate.rearrange("i n t -> (i n t)")[GATE_START : GATE_START + 8 * GATE_STEP]
+        nc.sync.dma_start(out=gate_rows[0:8, :], in_=gate_runs.rearrange("(j s) -> j s", s=GATE_STEP)[:, 0:P])
         nc.sync.dma_start(offs_sb[:], offs)
         load_x(1)
         load_x(2)
-        nc.sync.dma_start(out=gate_rows[:, :, 0:4], in_=gate[:, 0, :].rearrange("i (p r) -> p i r", r=4))
-        nc.sync.dma_start(out=bias[:], in_=b.rearrange("(h p) e -> p h e", h=2))
         nc.sync.dma_start(pos1_sb[:], pos1)
         load_x(3)
+        nc.sync.dma_start(out=bias[:], in_=b.rearrange("(h p) e -> p h e", h=2))
         nc.sync.dma_start(pos2_sb[:], pos2)
         for r in range(4):
             load_scales(W8_ROW, w8_scales, r)
@@ -177,6 +182,9 @@ def tile_moe_pln_lin_silu_kernel(
             nc.sync.dma_start(out=out[P * h : P * (h + 1), lo:hi], in_=result[h][:, lo:hi])
 
         interleave(nc.scalar.copy, 0, 336, T)
+        gate_turned = psum.tile([P, P], F32, name="gate_turned", tag="bank5")
+        nc.tensor.transpose(gate_turned[:], gate_rows[:], ident[:])
+        nc.scalar.copy(out=gate_columns[:], in_=gate_turned[:, 0:8])
         interleave(nc.vector.tensor_copy, 0, 0, 256)
         interleave(nc.vector.tensor_copy, 0, 256, 336)
         quantize(0, 0, 256)
@@ -191,10 +199,11 @@ def tile_moe_pln_lin_silu_kernel(
             interleave(nc.scalar.copy, g, 0, T)
         gates = keep.tile([P, 2, T], F32, name="gates", tag="x3", align_bytes=64)
         for i in range(2):
-            spread = psum.tile([P, 4, P], F32, name="spread", tag="acc")
+            spread = psum.tile([P, 4, P], F32, name="spread", tag="bank%d" % (6 + i))
             for r in range(4):
-                nc.tensor.transpose(spread[:, r, :], gate_rows[:, i, r : r + 1].to_broadcast([P, P]), ident[:])
-            nc.scalar.copy(out=gates[:, i, :].rearrange("p (t r) -> p t r", r=4), in_=spread[:].rearrange("p r t -> p t r"))
+                j = 4 * i + 3 - r
+                nc.tensor.transpose(spread[:, r, :], gate_columns[:, j : j + 1].to_broadcast([P, P]), ident[:])
+            nc.scalar.copy(out=gates[:, i, :], in_=spread[:].rearrange("p r t -> p (r t)"))
         gather_words(0, 0, SLOTS, WIDE)
         quantize(1, 0, 256)
         quantize(1, 256, T)
@@ -217,34 +226,44 @@ def tile_moe_pln_lin_silu_kernel(
         gather_words(3, 768, 896, T)
         gather_words(3, 896, SLOTS, T)
 
-        accs = [psum.tile([P, C], F32, name="acc") for e in range(E)]
-        for u in range(2):
-            experts = range(4 * u, 4 * u + 4)
-            for e in experts:
-                multiply(accs[e], 0, 0, e, True, False)
-                multiply(accs[e], 1, 0, e, False, False)
-            for e in experts:
-                multiply(accs[e], 2, 0, e, False, False)
-                multiply(accs[e], 3, 0, e, False, True)
-                finish(accs[e], 0, e)
-        accs = {e: psum.tile([P, C], F32, name="acc") for e in (6, 7, 0, 1, 2, 3, 4, 5)}
-        for e in (6, 7, 0, 1, 2, 3):
-            multiply(accs[e], 2, 1, e, True, False)
-            multiply(accs[e], 3, 1, e, False, False)
-        for e in range(E):
-            for g in range(PASSES if e in (4, 5) else 2):
-                multiply(accs[e], g, 1, e, g == 0 and e in (4, 5), g == (3 if e in (4, 5) else 1))
-            finish(accs[e], 1, e)
+        accs = {}
 
-        def add_by_transposes(lo):
-            turned = psum.tile([P, 2, P], F32, name="turned", tag="acc")
+        def run(h, e, passes, start, stop, bank=None):
+            if start:
+                accs[h, e] = psum.tile([P, C], F32, name="acc", tag="bank%d" % bank)
+            for g in passes:
+                multiply(accs[h, e], g, h, e, start and g == passes[0], stop and g == passes[-1])
+            if stop:
+                finish(accs[h, e], h, e)
+
+        for bank, (h, e) in enumerate([(0, 0), (0, 1), (0, 2), (0, 3), (1, 0), (1, 1), (1, 2), (0, 4)]):
+            run(h, e, (0, 1), True, False, bank)
+        for e in range(4):
+            run(0, e, (2, 3), False, True)
+        for e in range(3):
+            run(1, e, (2, 3), False, True)
+        for e in range(5, E):
+            run(0, e, (0, 1), True, False, e - 5)
+        run(1, 3, (2, 3), True, False, 3)
+        for e in range(4, E):
+            run(0, e, (2, 3), False, True)
+        for e in range(4, E):
+            run(1, e, (2, 3), True, False, e)
+        for e in range(3, E):
+            run(1, e, (0, 1), False, True)
+
+        def add_turned(lo, bank):
+            turned = psum.tile([P, 2, P], F32, name="turned", tag="bank%d" % bank)
             for i in range(2):
                 cols = slice(lo + P * i, lo + P * (i + 1))
                 nc.tensor.matmul(turned[:, i, :], first[0][:, cols], ident[:], start=True, stop=False, is_transpose=True)
                 nc.tensor.matmul(turned[:, i, :], second[0][:, cols], ident[:], start=False, stop=True, is_transpose=True)
             sums = keep.tile([P, 2, P], F32, name="sums%d" % lo)
             nc.scalar.copy(out=sums[:], in_=turned[:])
-            back = psum.tile([P, 2, P], F32, name="back", tag="acc")
+            return sums
+
+        def turn_back_and_store(sums, lo, bank):
+            back = psum.tile([P, 2, P], F32, name="back", tag="bank%d" % bank)
             for i in range(2):
                 nc.tensor.transpose(back[:, i, :], sums[:, i, :], ident[:])
             nc.scalar.copy(out=result[0][:, lo : lo + 2 * P], in_=back[:].rearrange("p i t -> p (i t)"))
@@ -253,8 +272,9 @@ def tile_moe_pln_lin_silu_kernel(
         fetch(first, 0, 0, 0, T)
         fetch(second, 0, 1, 0, 256)
         fetch(second, 0, 1, 256, T)
-        add_by_transposes(0)
-        add_by_transposes(256)
+        sums = [add_turned(0, 6), add_turned(256, 7)]
+        turn_back_and_store(sums[0], 0, 0)
+        turn_back_and_store(sums[1], 256, 1)
         fetch(first, 1, 0, 0, T)
         fetch(second, 1, 1, 0, 384)
         fetch(second, 1, 1, 384, T)

@@ -27,6 +27,8 @@ W8_ROW = 8
 WORD_COLUMN = (2 * T, T, 0, 2 * T + 1408)
 WIDE = 1408
 BYTE_WINDOW = 704
+WHOLE = 2
+LATE_CUTS = (WHOLE, 5, 7, E)
 GATE_STEP = 64 * T - P
 GATE_START = T + 3 * P
 
@@ -189,9 +191,9 @@ def tile_moe_pln_lin_silu_kernel(
         interleave(nc.vector.tensor_copy, 0, 256, 336)
         quantize(0, 0, 256)
         quantize(0, 256, T)
-        early = reuse("w8_first", "x0", 2816)
-        load_w8_whole(0, 3, early[:, 0:1536])
-        load_w8(0, 3, E, early[:, 1536:2816])
+        early = reuse("w8_first", "x0", 256 * (E + WHOLE))
+        load_w8_whole(0, WHOLE, early[:, 0 : 512 * WHOLE])
+        load_w8(0, WHOLE, E, early[:, 512 * WHOLE :])
         load_w4(0, 4, reuse("w4_first", "xb0", 1024))
         interleave(nc.scalar.copy, 1, 0, 256)
         interleave(nc.scalar.copy, 1, 256, T)
@@ -217,9 +219,8 @@ def tile_moe_pln_lin_silu_kernel(
         load_w4(4, 8, reuse("w4_second", "plane", 1024))
         gather_bytes(1)
         late = reuse("late", "plane_copy", 2048)
-        load_w8(1, 3, 6, late[:, 0:768])
-        load_w8(1, 6, 7, late[:, 1024:1280])
-        load_w8(1, 7, 8, late[:, 1536:1792])
+        for lo, hi in zip(LATE_CUTS, LATE_CUTS[1:]):
+            load_w8(1, lo, hi, late[:, 256 * lo : 256 * hi])
         gather_words(3, 0, 512, 704)
         gather_words(2, 512, SLOTS, WORD_COLUMN[3] + T)
         gather_words(3, 512, 768, T)
@@ -236,20 +237,22 @@ def tile_moe_pln_lin_silu_kernel(
             if stop:
                 finish(accs[h, e], h, e)
 
-        for bank, (h, e) in enumerate([(0, 0), (0, 1), (0, 2), (0, 3), (1, 0), (1, 1), (1, 2), (0, 4)]):
+        opened = [(0, e) for e in range(4)] + [(1, e) for e in range(WHOLE)] + [(0, e) for e in range(4, E - WHOLE)]
+        for bank, (h, e) in enumerate(opened):
             run(h, e, (0, 1), True, False, bank)
         for e in range(4):
             run(0, e, (2, 3), False, True)
-        for e in range(3):
+        for e in range(WHOLE):
             run(1, e, (2, 3), False, True)
-        for e in range(5, E):
-            run(0, e, (0, 1), True, False, e - 5)
-        run(1, 3, (2, 3), True, False, 3)
+        for e in range(E - WHOLE, E):
+            run(0, e, (0, 1), True, False, e - E + WHOLE)
+        for e in range(WHOLE, 4):
+            run(1, e, (2, 3), True, False, e)
         for e in range(4, E):
             run(0, e, (2, 3), False, True)
         for e in range(4, E):
             run(1, e, (2, 3), True, False, e)
-        for e in range(3, E):
+        for e in range(WHOLE, E):
             run(1, e, (0, 1), False, True)
 
         def add_turned(lo, bank):
@@ -267,7 +270,7 @@ def tile_moe_pln_lin_silu_kernel(
             for i in range(2):
                 nc.tensor.transpose(back[:, i, :], sums[:, i, :], ident[:])
             nc.scalar.copy(out=result[0][:, lo : lo + 2 * P], in_=back[:].rearrange("p i t -> p (i t)"))
-            nc.sync.dma_start(out=out[0:P, lo : lo + 2 * P], in_=result[0][:, lo : lo + 2 * P])
+            nc.scalar.dma_start(out=out[0:P, lo : lo + 2 * P], in_=result[0][:, lo : lo + 2 * P])
 
         fetch(first, 0, 0, 0, T)
         fetch(second, 0, 1, 0, 256)
@@ -276,7 +279,7 @@ def tile_moe_pln_lin_silu_kernel(
         turn_back_and_store(sums[0], 0, 0)
         turn_back_and_store(sums[1], 256, 1)
         fetch(first, 1, 0, 0, T)
-        fetch(second, 1, 1, 0, 384)
-        fetch(second, 1, 1, 384, T)
-        add_and_store(1, 0, 384)
-        add_and_store(1, 384, T)
+        fetch(second, 1, 1, 0, 256)
+        fetch(second, 1, 1, 256, T)
+        add_and_store(1, 0, 256)
+        add_and_store(1, 256, T)

@@ -50,7 +50,6 @@ def tile_moe_pln_lin_silu_kernel(
         xb = [keep.tile([P, T, 4], BF16, name="xb%d" % g, align_bytes=64) for g in range(PASSES)]
         words = keep.tile([P, WORD_COLUMN[3] + 704], I32, name="words", align_bytes=64)
         plane = keep.tile([P, BYTE_WINDOW], U8, name="plane", tag="plane", align_bytes=64)
-        plane_copy = keep.tile([P, BYTE_WINDOW], U8, name="plane_copy", tag="plane_copy", align_bytes=64)
         slot_words = {}
         slot_plane = [keep.tile([P, HALF], U8, name="slot_plane%d" % u, align_bytes=64) for u in range(2)]
         moved = [keep.tile([P, HALF], U8, name="moved%d" % u, align_bytes=64) for u in range(2)]
@@ -149,7 +148,7 @@ def tile_moe_pln_lin_silu_kernel(
                 slot_words[g, e] = into[:, C * e - lo : C * (e + 1) - lo]
 
         def gather_bytes(u):
-            nc.vector.tensor_copy(slot_plane[u][:], (plane, plane_copy)[u][:].indirect(offs_sb[:, 32 * u : 32 * (u + 1)]))
+            nc.vector.tensor_copy(slot_plane[u][:], plane[:].indirect(offs_sb[:, 32 * u : 32 * (u + 1)]))
             k = SCALE_ROW[2]
             nc.sync.dma_start(out=moved[u][0:112, :].bitcast(I32), in_=slot_plane[u][k : k + 112, :].bitcast(I32))
 
@@ -214,11 +213,10 @@ def tile_moe_pln_lin_silu_kernel(
         gather_words(1, 768, SLOTS, T, "x2")
         gather_words(2, 0, 512, 2 * T)
         quantize(3, 0, T)
-        nc.vector.tensor_copy(plane_copy[:].bitcast(I32), plane[:].bitcast(I32))
         gather_bytes(0)
-        load_w4(4, 8, reuse("w4_second", "plane", 1024))
+        load_w4(4, 8, reuse("w4_second", "xb3", 1024))
         gather_bytes(1)
-        late = reuse("late", "plane_copy", 2048)
+        late = reuse("late", "plane", 2048)
         for lo, hi in zip(LATE_CUTS, LATE_CUTS[1:]):
             load_w8(1, lo, hi, late[:, 256 * lo : 256 * hi])
         gather_words(3, 0, 512, 704)

@@ -6,7 +6,7 @@ from concourse.masks import make_identity
 K, T, E, C, N = 2048, 512, 8, 128, 256
 SLOTS = E * C
 FLOPS = 2 * SLOTS * K * N
-BYTES = 4 * K * T + E * N * (1024 + 512) + 2 * E * 2 * 16 * N + 4 * N * E + 4 * 2 * 128 * T + 2 * 2 * SLOTS * 8 + 4 * N * T
+BYTES = 4 * K * T + E * N * (1024 + 512) + E * N * K // 32 + 4 * N * E + 4 * 2 * T + 2 * 8 * (SLOTS + 2 * T) + 4 * N * T
 
 F32 = mybir.dt.float32
 BF16 = mybir.dt.bfloat16
@@ -21,15 +21,27 @@ SILU = mybir.ActivationFunctionType.Silu
 
 P = 128
 PASSES = 4
-HALF = SLOTS // 2
-SCALE_ROW = (4, 8, 12, 0)
+K_PASS = K // PASSES
+HALF_T = T // 2
+GROUP = E // 2
+GROUP_SLOTS = GROUP * C
+
+TOKEN_ROW = (4, 8, 12, 0)
+MOVED_PASS = 2
+LIVE_ROWS = 100
 W8_ROW = 8
-WORD_COLUMN = (2 * T, T, 0, 2 * T + 1408)
-WIDE = 1408
-BYTE_WINDOW = 704
+
+WINDOW_1024 = 1408
+WINDOW_768 = 1024
+WINDOW_512 = 704
+WORD_COLUMN = (2 * T, T, 0, 2 * T + WINDOW_1024)
+
+VECTOR_TOKENS = 336
 WHOLE = 2
 LATE_CUTS = (WHOLE, 5, 7, E)
-GATE_STEP = 64 * T - P
+
+GATE_RUNS = 2 * T // P
+GATE_STEP = N * T // 4 - P
 GATE_START = T + 3 * P
 
 
@@ -42,45 +54,46 @@ def tile_moe_pln_lin_silu_kernel(
         keep = ctx.enter_context(tc.tile_pool(name="keep", bufs=1))
         psum = ctx.enter_context(tc.psum_pool(name="psum", bufs=1))
 
+        def in_bank(bank, shape, name):
+            return psum.tile(shape, F32, name=name, tag="bank%d" % bank)
+
+        def raw_words(name, tag, width):
+            return keep.tile([P, width], I32, name=name, tag=tag, align_bytes=64)[:]
+
         offs_sb = lists.tile([P, SLOTS // 16], U16, name="offs_sb")
         pos1_sb = lists.tile([P, T // 16], U16, name="pos1_sb")
         pos2_sb = lists.tile([P, T // 16], U16, name="pos2_sb")
 
         x = [keep.tile([P, 4, T], F32, name="x%d" % g, align_bytes=64) for g in range(PASSES)]
         xb = [keep.tile([P, T, 4], BF16, name="xb%d" % g, align_bytes=64) for g in range(PASSES)]
-        words = keep.tile([P, WORD_COLUMN[3] + 704], I32, name="words", align_bytes=64)
-        plane = keep.tile([P, BYTE_WINDOW], U8, name="plane", tag="plane", align_bytes=64)
-        slot_words = {}
-        slot_plane = [keep.tile([P, HALF], U8, name="slot_plane%d" % u, align_bytes=64) for u in range(2)]
-        moved = [keep.tile([P, HALF], U8, name="moved%d" % u, align_bytes=64) for u in range(2)]
-        w8, w4 = {}, {}
+        words = keep.tile([P, WORD_COLUMN[3] + WINDOW_512], I32, name="words", align_bytes=64)
+        plane = keep.tile([P, WINDOW_512], U8, name="plane", align_bytes=64)
+        slot_plane = [keep.tile([P, GROUP_SLOTS], U8, name="slot_plane%d" % u, align_bytes=64) for u in range(2)]
+        moved = [keep.tile([P, GROUP_SLOTS], U8, name="moved%d" % u, align_bytes=64) for u in range(2)]
         ident = keep.tile([P, P], F32, name="ident")
         gate_rows = keep.tile([P, P], F32, name="gate_rows")
-        gate_columns = keep.tile([P, 8], F32, name="gate_columns")
-        w_planes = keep.tile([P, E * 2 * N], U8, name="w_planes", align_bytes=64)
+        gate_columns = keep.tile([P, GATE_RUNS], F32, name="gate_columns")
+        w_plane = keep.tile([P, E * 2 * N], U8, name="w_plane", align_bytes=64)
         bias = keep.tile([P, 2, E], F32, name="bias")
         y = [keep.tile([P, SLOTS], F32, name="y%d" % h) for h in range(2)]
         first = [keep.tile([P, T], F32, name="first%d" % h) for h in range(2)]
         second = [keep.tile([P, T], F32, name="second%d" % h) for h in range(2)]
         result = [keep.tile([P, T], F32, name="result%d" % h) for h in range(2)]
-        dummy = keep.tile([P, 2], F32, name="dummy")
+        slot_words = {}
+        w8, w4 = {}, {}
+        sums = {}
 
         def load_x(g):
-            nc.sync.dma_start(out=x[g][:], in_=xT[512 * g : 512 * (g + 1), :].rearrange("(p j) t -> p j t", j=4))
+            rows = xT[K_PASS * g : K_PASS * (g + 1), :]
+            nc.sync.dma_start(out=x[g][:], in_=rows.rearrange("(p j) t -> p j t", j=4))
 
-        def load_scales(k, scales, r):
+        def load_scales(first_row, scales, r):
             rows = scales.bitcast(I32).rearrange("e a q n -> q (e a) n")
-            tile_rows = w_planes[:].bitcast(I32).rearrange("p (ea n) -> p ea n", ea=2 * E)
-            nc.sync.dma_start(out=tile_rows[k + r : P : 32], in_=rows[r:16:4])
+            plane_rows = w_plane[:].bitcast(I32).rearrange("p (m n) -> p m n", m=2 * E)
+            nc.sync.dma_start(out=plane_rows[first_row + r : P : 32], in_=rows[r:16:4])
 
         w8_rows = w8_words.rearrange("e a p n t -> (e a) p (n t)").bitcast(I32)
         w4_rows = w4_words.rearrange("e a p n -> (e a) p n").bitcast(I32)
-
-        def load_w8(h, lo, hi, into):
-            into = into.rearrange("p (m n) -> p m n", n=P)
-            nc.sync.dma_start(out=into, in_=w8_rows[2 * lo : 2 * hi, :, P * h : P * (h + 1)].rearrange("m p n -> p m n"))
-            for m in range(2 * lo, 2 * hi):
-                w8[h, m] = into[:, m - 2 * lo, :]
 
         def load_w8_whole(lo, hi, into):
             into = into.rearrange("p (m n) -> p m n", n=N)
@@ -89,195 +102,200 @@ def tile_moe_pln_lin_silu_kernel(
                 for h in range(2):
                     w8[h, m] = into[:, m - 2 * lo, P * h : P * (h + 1)]
 
-        def load_w4(lo, hi, into):
+        def load_w8_half(h, lo, hi, into):
             into = into.rearrange("p (m n) -> p m n", n=P)
-            nc.sync.dma_start(out=into, in_=w4_rows[2 * lo : 2 * hi].rearrange("m p n -> p m n"))
+            rows = w8_rows[2 * lo : 2 * hi, :, P * h : P * (h + 1)]
+            nc.sync.dma_start(out=into, in_=rows.rearrange("m p n -> p m n"))
             for m in range(2 * lo, 2 * hi):
-                w4[m] = into[:, m - 2 * lo, :]
+                w8[h, m] = into[:, m - 2 * lo, :]
 
-        def reuse(name, tag, width):
-            return keep.tile([P, width], I32, name=name, tag=tag, align_bytes=64)[:]
+        def load_w4(u, into):
+            into = into.rearrange("p (m n) -> p m n", n=N // 2)
+            rows = w4_rows[2 * GROUP * u : 2 * GROUP * (u + 1)]
+            nc.sync.dma_start(out=into, in_=rows.rearrange("m p n -> p m n"))
+            for m in range(2 * GROUP):
+                w4[2 * GROUP * u + m] = into[:, m, :]
 
-        nc.vector.memset(gate_rows[:], 0.0)
-        nc.vector.memset(w_planes[:].bitcast(I32), 0)
-        nc.vector.memset(dummy[:], 0.0)
-        nc.scalar.activation(dummy[:, 1:2], dummy[:, 0:1], SILU)
-        nc.vector.memset(plane[:].bitcast(I32), 0)
-        nc.vector.memset(words[:, 3 * T : WORD_COLUMN[3]], 0)
-        nc.vector.memset(words[:, WORD_COLUMN[3] + T :], 0)
-        for u in range(2):
-            nc.vector.memset(moved[u][:].bitcast(I32), 0)
-
-        make_identity(nc, ident[:])
-        load_x(0)
-        gate_runs = gate.rearrange("i n t -> (i n t)")[GATE_START : GATE_START + 8 * GATE_STEP]
-        nc.sync.dma_start(out=gate_rows[0:8, :], in_=gate_runs.rearrange("(j s) -> j s", s=GATE_STEP)[:, 0:P])
-        nc.sync.dma_start(offs_sb[:], offs)
-        load_x(1)
-        load_x(2)
-        nc.sync.dma_start(pos1_sb[:], pos1)
-        load_x(3)
-        nc.sync.dma_start(out=bias[:], in_=b.rearrange("(h p) e -> p h e", h=2))
-        nc.sync.dma_start(pos2_sb[:], pos2)
-        for r in range(4):
-            load_scales(W8_ROW, w8_scales, r)
-            load_scales(0, w4_scales, r)
-
-        def interleave(engine_copy, g, lo, hi):
-            rows = x[g][:, :, lo:hi]
+        def round_and_interleave(engine_copy, g, lo, hi):
             engine_copy(
                 out=xb[g][:, lo:hi, :].rearrange("p (c i) j -> p c j i", i=4),
-                in_=rows.rearrange("p j (c i) -> p c j i", i=4),
+                in_=x[g][:, :, lo:hi].rearrange("p j (c i) -> p c j i", i=4),
             )
 
         def quantize(g, lo, hi):
             start = WORD_COLUMN[g]
             nc.vector.quantize_mx(
                 out=words[:, start + lo : start + hi].bitcast(E4M3),
-                scales=plane[SCALE_ROW[g] : P, lo:hi],
+                scales=plane[TOKEN_ROW[g] : P, lo:hi],
                 in_=xb[g][:, lo:hi, :].rearrange("p t j -> p (t j)"),
             )
 
-        def gather_words(g, lo, hi, width, tag=None):
-            name = "slot_words%d_%d" % (g, lo)
-            into = keep.tile([P, hi - lo], U32, name=name, tag=tag or name, align_bytes=64)
+        def gather_words(g, lo, hi, width, tag):
+            into = keep.tile([P, C * (hi - lo)], U32, name="slot_words%d_%d" % (g, lo), tag=tag, align_bytes=64)
             start = WORD_COLUMN[g]
             window = words[:, start : start + width].bitcast(U32)
-            nc.vector.tensor_copy(into[:], window.indirect(offs_sb[:, lo // 16 : hi // 16]))
-            for e in range(lo // C, hi // C):
-                slot_words[g, e] = into[:, C * e - lo : C * (e + 1) - lo]
+            nc.vector.tensor_copy(into[:], window.indirect(offs_sb[:, C * lo // 16 : C * hi // 16]))
+            for e in range(lo, hi):
+                slot_words[g, e] = into[:, C * (e - lo) : C * (e - lo + 1)]
 
-        def gather_bytes(u):
-            nc.vector.tensor_copy(slot_plane[u][:], plane[:].indirect(offs_sb[:, 32 * u : 32 * (u + 1)]))
-            k = SCALE_ROW[2]
-            nc.sync.dma_start(out=moved[u][0:112, :].bitcast(I32), in_=slot_plane[u][k : k + 112, :].bitcast(I32))
+        def gather_and_move_scales(u):
+            entries = offs_sb[:, GROUP_SLOTS * u // 16 : GROUP_SLOTS * (u + 1) // 16]
+            nc.vector.tensor_copy(slot_plane[u][:], plane[:].indirect(entries))
+            row = TOKEN_ROW[MOVED_PASS]
+            nc.sync.dma_start(
+                out=moved[u][0:LIVE_ROWS, :].bitcast(I32), in_=slot_plane[u][row : row + LIVE_ROWS, :].bitcast(I32)
+            )
 
-        def multiply(acc, g, h, e, start, stop):
-            a = g % 2
-            u, m = e // 4, 2 * e + a
-            cols = slice(C * (e % 4), C * (e % 4 + 1))
-            scale_cols = slice(N * (2 * e + a) + P * h, N * (2 * e + a) + P * (h + 1))
+        def multiply(h, e, g, start, stop):
+            u, m = e // GROUP, 2 * e + g % 2
+            slots = slice(C * (e % GROUP), C * (e % GROUP + 1))
             if g < 2:
-                k, weights = W8_ROW, w8[h, m].bitcast(E4M3)
+                w_row, weights = W8_ROW, w8[h, m].bitcast(E4M3)
             else:
-                k, weights = 0, w4[m][:, 64 * h : 64 * (h + 1)].bitcast(U8).bitcast(E2M1)
+                w_row, weights = 0, w4[m][:, P // 2 * h : P // 2 * (h + 1)].bitcast(U8).bitcast(E2M1)
             nc.tensor.matmul_mx(
-                out=acc[:],
+                out=sums[h, e][:],
                 lhsT=weights,
-                lhsT_scale=w_planes[k:P, scale_cols],
+                lhsT_scale=w_plane[w_row:P, N * m + P * h : N * m + P * (h + 1)],
                 rhs=slot_words[g, e].bitcast(E4M3),
-                rhs_scale=moved[u][:, cols] if g == 2 else slot_plane[u][SCALE_ROW[g] : P, cols],
+                rhs_scale=moved[u][:, slots] if g == MOVED_PASS else slot_plane[u][TOKEN_ROW[g] : P, slots],
                 start=start,
                 stop=stop,
             )
 
-        def finish(acc, h, e):
-            nc.scalar.activation(y[h][:, C * e : C * (e + 1)], acc[:], SILU, bias=bias[:, h, e : e + 1])
+        def open_sum(h, e, passes, bank):
+            sums[h, e] = in_bank(bank, [P, C], "sum")
+            multiply(h, e, passes[0], True, False)
+            multiply(h, e, passes[1], False, False)
+
+        def close_sum(h, e, passes):
+            multiply(h, e, passes[0], False, False)
+            multiply(h, e, passes[1], False, True)
+            nc.scalar.activation(y[h][:, C * e : C * (e + 1)], sums[h, e][:], SILU, bias=bias[:, h, e : e + 1])
 
         def fetch(into, h, i, lo, hi):
             places = (pos1_sb, pos2_sb)[i][:, lo // 16 : hi // 16]
             nc.vector.tensor_tensor(into[h][:, lo:hi], y[h][:].indirect(places), gates[:, i, lo:hi], MULT)
 
-        def add_and_store(h, lo, hi):
-            nc.vector.tensor_add(result[h][:, lo:hi], first[h][:, lo:hi], second[h][:, lo:hi])
-            nc.sync.dma_start(out=out[P * h : P * (h + 1), lo:hi], in_=result[h][:, lo:hi])
-
-        interleave(nc.scalar.copy, 0, 336, T)
-        gate_turned = psum.tile([P, P], F32, name="gate_turned", tag="bank5")
-        nc.tensor.transpose(gate_turned[:], gate_rows[:], ident[:])
-        nc.scalar.copy(out=gate_columns[:], in_=gate_turned[:, 0:8])
-        interleave(nc.vector.tensor_copy, 0, 0, 256)
-        interleave(nc.vector.tensor_copy, 0, 256, 336)
-        quantize(0, 0, 256)
-        quantize(0, 256, T)
-        early = reuse("w8_first", "x0", 256 * (E + WHOLE))
-        load_w8_whole(0, WHOLE, early[:, 0 : 512 * WHOLE])
-        load_w8(0, WHOLE, E, early[:, 512 * WHOLE :])
-        load_w4(0, 4, reuse("w4_first", "xb0", 1024))
-        interleave(nc.scalar.copy, 1, 0, 256)
-        interleave(nc.scalar.copy, 1, 256, T)
-        for g in range(2, PASSES):
-            interleave(nc.scalar.copy, g, 0, T)
-        gates = keep.tile([P, 2, T], F32, name="gates", tag="x3", align_bytes=64)
-        for i in range(2):
-            spread = psum.tile([P, 4, P], F32, name="spread", tag="bank%d" % (6 + i))
-            for r in range(4):
-                j = 4 * i + 3 - r
-                nc.tensor.transpose(spread[:, r, :], gate_columns[:, j : j + 1].to_broadcast([P, P]), ident[:])
-            nc.scalar.copy(out=gates[:, i, :], in_=spread[:].rearrange("p r t -> p (r t)"))
-        gather_words(0, 0, SLOTS, WIDE)
-        quantize(1, 0, 256)
-        quantize(1, 256, T)
-        gather_words(1, 0, 768, 2 * T)
-        quantize(2, 0, T)
-        gather_words(1, 768, SLOTS, T, "x2")
-        gather_words(2, 0, 512, 2 * T)
-        quantize(3, 0, T)
-        gather_bytes(0)
-        load_w4(4, 8, reuse("w4_second", "xb3", 1024))
-        gather_bytes(1)
-        late = reuse("late", "plane", 2048)
-        for lo, hi in zip(LATE_CUTS, LATE_CUTS[1:]):
-            load_w8(1, lo, hi, late[:, 256 * lo : 256 * hi])
-        gather_words(3, 0, 512, 704)
-        gather_words(2, 512, SLOTS, WORD_COLUMN[3] + T)
-        gather_words(3, 512, 768, T)
-        gather_words(3, 768, 896, T)
-        gather_words(3, 896, SLOTS, T)
-
-        accs = {}
-
-        def run(h, e, passes, start, stop, bank=None):
-            if start:
-                accs[h, e] = psum.tile([P, C], F32, name="acc", tag="bank%d" % bank)
-            for g in passes:
-                multiply(accs[h, e], g, h, e, start and g == passes[0], stop and g == passes[-1])
-            if stop:
-                finish(accs[h, e], h, e)
-
-        opened = [(0, e) for e in range(4)] + [(1, e) for e in range(WHOLE)] + [(0, e) for e in range(4, E - WHOLE)]
-        for bank, (h, e) in enumerate(opened):
-            run(h, e, (0, 1), True, False, bank)
-        for e in range(4):
-            run(0, e, (2, 3), False, True)
-        for e in range(WHOLE):
-            run(1, e, (2, 3), False, True)
-        for e in range(E - WHOLE, E):
-            run(0, e, (0, 1), True, False, e - E + WHOLE)
-        for e in range(WHOLE, 4):
-            run(1, e, (2, 3), True, False, e)
-        for e in range(4, E):
-            run(0, e, (2, 3), False, True)
-        for e in range(4, E):
-            run(1, e, (2, 3), True, False, e)
-        for e in range(WHOLE, E):
-            run(1, e, (0, 1), False, True)
+        def fetch_half(h):
+            fetch(first, h, 0, 0, T)
+            fetch(second, h, 1, 0, HALF_T)
+            fetch(second, h, 1, HALF_T, T)
 
         def add_turned(lo, bank):
-            turned = psum.tile([P, 2, P], F32, name="turned", tag="bank%d" % bank)
+            turned = in_bank(bank, [P, 2, P], "turned")
             for i in range(2):
                 cols = slice(lo + P * i, lo + P * (i + 1))
                 nc.tensor.matmul(turned[:, i, :], first[0][:, cols], ident[:], start=True, stop=False, is_transpose=True)
                 nc.tensor.matmul(turned[:, i, :], second[0][:, cols], ident[:], start=False, stop=True, is_transpose=True)
-            sums = keep.tile([P, 2, P], F32, name="sums%d" % lo)
-            nc.scalar.copy(out=sums[:], in_=turned[:])
-            return sums
+            added = keep.tile([P, 2, P], F32, name="added%d" % lo)
+            nc.scalar.copy(out=added[:], in_=turned[:])
+            return added
 
-        def turn_back_and_store(sums, lo, bank):
-            back = psum.tile([P, 2, P], F32, name="back", tag="bank%d" % bank)
+        def turn_back_and_store(added, lo, bank):
+            back = in_bank(bank, [P, 2, P], "back")
             for i in range(2):
-                nc.tensor.transpose(back[:, i, :], sums[:, i, :], ident[:])
-            nc.scalar.copy(out=result[0][:, lo : lo + 2 * P], in_=back[:].rearrange("p i t -> p (i t)"))
-            nc.scalar.dma_start(out=out[0:P, lo : lo + 2 * P], in_=result[0][:, lo : lo + 2 * P])
+                nc.tensor.transpose(back[:, i, :], added[:, i, :], ident[:])
+            nc.scalar.copy(out=result[0][:, lo : lo + HALF_T], in_=back[:].rearrange("p i t -> p (i t)"))
+            nc.scalar.dma_start(out=out[0:P, lo : lo + HALF_T], in_=result[0][:, lo : lo + HALF_T])
 
-        fetch(first, 0, 0, 0, T)
-        fetch(second, 0, 1, 0, 256)
-        fetch(second, 0, 1, 256, T)
-        sums = [add_turned(0, 6), add_turned(256, 7)]
-        turn_back_and_store(sums[0], 0, 0)
-        turn_back_and_store(sums[1], 256, 1)
-        fetch(first, 1, 0, 0, T)
-        fetch(second, 1, 1, 0, 256)
-        fetch(second, 1, 1, 256, T)
-        add_and_store(1, 0, 256)
-        add_and_store(1, 256, T)
+        def add_and_store(lo, hi):
+            nc.vector.tensor_add(result[1][:, lo:hi], first[1][:, lo:hi], second[1][:, lo:hi])
+            nc.sync.dma_start(out=out[P:N, lo:hi], in_=result[1][:, lo:hi])
+
+        nc.vector.memset(gate_rows[:], 0.0)
+        nc.vector.memset(w_plane[:].bitcast(I32), 0)
+        nc.vector.memset(plane[:].bitcast(I32), 0)
+        nc.vector.memset(words[:, WORD_COLUMN[0] + T : WORD_COLUMN[3]], 0)
+        nc.vector.memset(words[:, WORD_COLUMN[3] + T :], 0)
+        for u in range(2):
+            nc.vector.memset(moved[u][:].bitcast(I32), 0)
+        make_identity(nc, ident[:])
+
+        load_x(0)
+        gate_flat = gate.rearrange("i n t -> (i n t)")[GATE_START : GATE_START + GATE_RUNS * GATE_STEP]
+        nc.sync.dma_start(out=gate_rows[0:GATE_RUNS, :], in_=gate_flat.rearrange("(s c) -> s c", c=GATE_STEP)[:, 0:P])
+        nc.sync.dma_start(offs_sb[:], offs)
+        load_x(1)
+        load_x(2)
+        nc.sync.dma_start(pos1_sb[:], pos1)
+        load_x(3)
+        for r in range(4):
+            load_scales(W8_ROW, w8_scales, r)
+            load_scales(0, w4_scales, r)
+        nc.sync.dma_start(out=bias[:], in_=b.rearrange("(h p) e -> p h e", h=2))
+        nc.sync.dma_start(pos2_sb[:], pos2)
+        load_w8_whole(0, WHOLE, raw_words("w8_whole", "w8_whole", 2 * N * WHOLE))
+        load_w8_half(0, WHOLE, E, raw_words("w8_early", "w8_early", 2 * P * (E - WHOLE)))
+        load_w4(0, raw_words("w4_first", "w4_first", N * GROUP))
+
+        round_and_interleave(nc.scalar.copy, 0, VECTOR_TOKENS, T)
+        gate_turned = in_bank(5, [P, P], "gate_turned")
+        nc.tensor.transpose(gate_turned[:], gate_rows[:], ident[:])
+        nc.scalar.copy(out=gate_columns[:], in_=gate_turned[:, 0:GATE_RUNS])
+        round_and_interleave(nc.vector.tensor_copy, 0, 0, HALF_T)
+        round_and_interleave(nc.vector.tensor_copy, 0, HALF_T, VECTOR_TOKENS)
+        quantize(0, 0, HALF_T)
+        quantize(0, HALF_T, T)
+        round_and_interleave(nc.scalar.copy, 1, 0, HALF_T)
+        round_and_interleave(nc.scalar.copy, 1, HALF_T, T)
+        round_and_interleave(nc.scalar.copy, 2, 0, T)
+        round_and_interleave(nc.scalar.copy, 3, 0, T)
+
+        gates = keep.tile([P, 2, T], F32, name="gates", tag="x3", align_bytes=64)
+        for i in range(2):
+            spread = in_bank(6 + i, [P, 4, P], "spread")
+            for r in range(4):
+                s = 4 * i + 3 - r
+                nc.tensor.transpose(spread[:, r, :], gate_columns[:, s : s + 1].to_broadcast([P, P]), ident[:])
+            nc.scalar.copy(out=gates[:, i, :], in_=spread[:].rearrange("p r t -> p (r t)"))
+
+        gather_words(0, 0, E, WINDOW_1024, "slots0")
+        quantize(1, 0, HALF_T)
+        quantize(1, HALF_T, T)
+        gather_words(1, 0, E - 2, WINDOW_768, "slots1")
+        quantize(2, 0, T)
+        gather_words(1, E - 2, E, T, "x2")
+        gather_words(2, 0, GROUP, WINDOW_768, "slots2_first")
+        quantize(3, 0, T)
+
+        gather_and_move_scales(0)
+        load_w4(1, raw_words("w4_second", "xb3", N * GROUP))
+        gather_and_move_scales(1)
+        late = raw_words("w8_late", "plane", 2 * P * (E - WHOLE))
+        for lo, hi in zip(LATE_CUTS, LATE_CUTS[1:]):
+            load_w8_half(1, lo, hi, late[:, 2 * P * (lo - WHOLE) : 2 * P * (hi - WHOLE)])
+
+        gather_words(3, 0, GROUP, WINDOW_512, "slots3_first")
+        gather_words(2, GROUP, E, WORD_COLUMN[3] + T, "slots2_second")
+        gather_words(3, GROUP, E - 2, T, "slots3_second")
+        gather_words(3, E - 2, E - 1, T, "slots3_third")
+        gather_words(3, E - 1, E, T, "slots3_last")
+
+        e4m3_passes, e2m1_passes = (0, 1), (2, 3)
+        first_eight = [(0, e) for e in range(GROUP)] + [(1, e) for e in range(WHOLE)]
+        first_eight = first_eight + [(0, e) for e in range(GROUP, E - WHOLE)]
+        for bank, (h, e) in enumerate(first_eight):
+            open_sum(h, e, e4m3_passes, bank)
+        for e in range(GROUP):
+            close_sum(0, e, e2m1_passes)
+        for e in range(WHOLE):
+            close_sum(1, e, e2m1_passes)
+        for bank, e in enumerate(range(E - WHOLE, E)):
+            open_sum(0, e, e4m3_passes, bank)
+        for e in range(WHOLE, GROUP):
+            open_sum(1, e, e2m1_passes, e)
+        for e in range(GROUP, E):
+            close_sum(0, e, e2m1_passes)
+        for e in range(GROUP, E):
+            open_sum(1, e, e2m1_passes, e)
+        for e in range(WHOLE, E):
+            close_sum(1, e, e4m3_passes)
+
+        fetch_half(0)
+        added = [add_turned(0, E - 2), add_turned(HALF_T, E - 1)]
+        turn_back_and_store(added[0], 0, 0)
+        turn_back_and_store(added[1], HALF_T, 1)
+        fetch_half(1)
+        add_and_store(0, HALF_T)
+        add_and_store(HALF_T, T)

@@ -39,6 +39,7 @@ WORD_COLUMN = (2 * T, T, 0, 2 * T + WINDOW_1024)
 VECTOR_TOKENS = 336
 WHOLE = 2
 LATE_CUTS = (WHOLE, 5, 7, E)
+W4_EARLY = 5
 
 GATE_RUNS = 2 * T // P
 GATE_STEP = N * T // 4 - P
@@ -109,12 +110,11 @@ def tile_moe_pln_lin_silu_kernel(
             for m in range(2 * lo, 2 * hi):
                 w8[h, m] = into[:, m - 2 * lo, :]
 
-        def load_w4(u, into):
+        def load_w4(lo, hi, into):
             into = into.rearrange("p (m n) -> p m n", n=N // 2)
-            rows = w4_rows[2 * GROUP * u : 2 * GROUP * (u + 1)]
-            nc.sync.dma_start(out=into, in_=rows.rearrange("m p n -> p m n"))
-            for m in range(2 * GROUP):
-                w4[2 * GROUP * u + m] = into[:, m, :]
+            nc.sync.dma_start(out=into, in_=w4_rows[2 * lo : 2 * hi].rearrange("m p n -> p m n"))
+            for m in range(2 * lo, 2 * hi):
+                w4[m] = into[:, m - 2 * lo, :]
 
         def round_and_interleave(engine_copy, g, lo, hi):
             engine_copy(
@@ -227,7 +227,7 @@ def tile_moe_pln_lin_silu_kernel(
         nc.sync.dma_start(pos2_sb[:], pos2)
         load_w8_whole(0, WHOLE, raw_words("w8_whole", "w8_whole", 2 * N * WHOLE))
         load_w8_half(0, WHOLE, E, raw_words("w8_early", "w8_early", 2 * P * (E - WHOLE)))
-        load_w4(0, raw_words("w4_first", "w4_first", N * GROUP))
+        load_w4(0, W4_EARLY, raw_words("w4_first", "w4_first", N * W4_EARLY))
 
         round_and_interleave(nc.scalar.copy, 0, VECTOR_TOKENS, T)
         gate_turned = in_bank(5, [P, P], "gate_turned")
@@ -260,7 +260,7 @@ def tile_moe_pln_lin_silu_kernel(
         quantize(3, 0, T)
 
         gather_and_move_scales(0)
-        load_w4(1, raw_words("w4_second", "xb3", N * GROUP))
+        load_w4(W4_EARLY, E, raw_words("w4_second", "xb3", N * (E - W4_EARLY)))
         gather_and_move_scales(1)
         late = raw_words("w8_late", "plane", 2 * P * (E - WHOLE))
         for lo, hi in zip(LATE_CUTS, LATE_CUTS[1:]):

@@ -142,9 +142,11 @@ def tile_moe_pln_lin_silu_kernel(
             entries = offs_sb[:, GROUP_SLOTS * u // 16 : GROUP_SLOTS * (u + 1) // 16]
             nc.vector.tensor_copy(slot_plane[u][:], plane[:].indirect(entries))
             row = TOKEN_ROW[MOVED_PASS]
-            nc.sync.dma_start(
-                out=moved[u][0:LIVE_ROWS, :].bitcast(I32), in_=slot_plane[u][row : row + LIVE_ROWS, :].bitcast(I32)
-            )
+            for lo, count in ((0, 64), (64, 4), (96, 4)):
+                nc.sync.dma_start(
+                    out=moved[u][lo : lo + count, :].bitcast(I32),
+                    in_=slot_plane[u][row + lo : row + lo + count, :].bitcast(I32),
+                )
 
         def multiply(h, e, g, start, stop):
             u, m = e // GROUP, 2 * e + g % 2

@@ -37,9 +37,11 @@ WINDOW_512 = 704
 WORD_COLUMN = (2 * T, T, 0, 2 * T + WINDOW_1024)
 
 VECTOR_TOKENS = 336
-WHOLE = 2
+VECTOR_TOKENS_1 = 64
+WHOLE = 3
 LATE_CUTS = (WHOLE, 5, 7, E)
-W4_EARLY = 5
+W4_EARLY = 4
+W4_MIDDLE = 6
 
 GATE_RUNS = 2 * T // P
 GATE_STEP = N * T // 4 - P
@@ -215,36 +217,34 @@ def tile_moe_pln_lin_silu_kernel(
         make_identity(nc, ident[:])
 
         load_x(0)
-        gate_flat = gate.rearrange("i n t -> (i n t)")[GATE_START : GATE_START + GATE_RUNS * GATE_STEP]
-        nc.sync.dma_start(out=gate_rows[0:GATE_RUNS, :], in_=gate_flat.rearrange("(s c) -> s c", c=GATE_STEP)[:, 0:P])
         nc.sync.dma_start(offs_sb[:], offs)
         load_x(1)
         load_x(2)
-        nc.sync.dma_start(pos1_sb[:], pos1)
         load_x(3)
+        gate_flat = gate.rearrange("i n t -> (i n t)")[GATE_START : GATE_START + GATE_RUNS * GATE_STEP]
+        nc.sync.dma_start(out=gate_rows[0:GATE_RUNS, :], in_=gate_flat.rearrange("(s c) -> s c", c=GATE_STEP)[:, 0:P])
         for r in range(4):
             load_scales(W8_ROW, w8_scales, r)
             load_scales(0, w4_scales, r)
         nc.sync.dma_start(out=bias[:], in_=b.rearrange("(h p) e -> p h e", h=2))
-        nc.sync.dma_start(pos2_sb[:], pos2)
         load_w8_whole(0, WHOLE, raw_words("w8_whole", "w8_whole", 2 * N * WHOLE))
         load_w8_half(0, WHOLE, E, raw_words("w8_early", "w8_early", 2 * P * (E - WHOLE)))
         load_w4(0, W4_EARLY, raw_words("w4_first", "w4_first", N * W4_EARLY))
 
         round_and_interleave(nc.scalar.copy, 0, VECTOR_TOKENS, T)
-        gate_turned = in_bank(5, [P, P], "gate_turned")
-        nc.tensor.transpose(gate_turned[:], gate_rows[:], ident[:])
-        nc.scalar.copy(out=gate_columns[:], in_=gate_turned[:, 0:GATE_RUNS])
         round_and_interleave(nc.vector.tensor_copy, 0, 0, HALF_T)
         round_and_interleave(nc.vector.tensor_copy, 0, HALF_T, VECTOR_TOKENS)
         quantize(0, 0, HALF_T)
         quantize(0, HALF_T, T)
         round_and_interleave(nc.scalar.copy, 1, 0, HALF_T)
-        round_and_interleave(nc.scalar.copy, 1, HALF_T, T)
+        round_and_interleave(nc.scalar.copy, 1, HALF_T, T - VECTOR_TOKENS_1)
         round_and_interleave(nc.scalar.copy, 2, 0, T)
         round_and_interleave(nc.scalar.copy, 3, 0, T)
 
-        gates = keep.tile([P, 2, T], F32, name="gates", tag="x3", align_bytes=64)
+        gate_turned = in_bank(5, [P, P], "gate_turned")
+        nc.tensor.transpose(gate_turned[:], gate_rows[:], ident[:])
+        nc.scalar.copy(out=gate_columns[:], in_=gate_turned[:, 0:GATE_RUNS])
+        gates = keep.tile([P, 2, T], F32, name="gates", align_bytes=64)
         for i in range(2):
             spread = in_bank(6 + i, [P, 4, P], "spread")
             for r in range(4):
@@ -252,39 +252,43 @@ def tile_moe_pln_lin_silu_kernel(
                 nc.tensor.transpose(spread[:, r, :], gate_columns[:, s : s + 1].to_broadcast([P, P]), ident[:])
             nc.scalar.copy(out=gates[:, i, :], in_=spread[:].rearrange("p r t -> p (r t)"))
 
-        gather_words(0, 0, E, WINDOW_1024, "slots0")
+        gather_words(0, 0, E - 1, WINDOW_1024, "slots0")
+        round_and_interleave(nc.vector.tensor_copy, 1, T - VECTOR_TOKENS_1, T)
         quantize(1, 0, HALF_T)
         quantize(1, HALF_T, T)
+        gather_words(0, E - 1, E, T, "x1")
         gather_words(1, 0, E - 2, WINDOW_768, "slots1")
         quantize(2, 0, T)
         gather_words(1, E - 2, E, T, "x2")
         gather_words(2, 0, GROUP, WINDOW_768, "slots2_first")
         quantize(3, 0, T)
+        gather_words(2, GROUP, GROUP + 1, T, "x3")
 
         gather_and_move_scales(0)
-        load_w4(W4_EARLY, E, raw_words("w4_second", "xb3", N * (E - W4_EARLY)))
+        load_w4(W4_EARLY, W4_MIDDLE, raw_words("w4_second", "xb3", N * (W4_MIDDLE - W4_EARLY)))
         gather_and_move_scales(1)
-        late = raw_words("w8_late", "plane", 2 * P * (E - WHOLE))
+        late = raw_words("late", "plane", N * (E - W4_MIDDLE) + 2 * P * (E - WHOLE))
+        load_w4(W4_MIDDLE, E, late[:, 0 : N * (E - W4_MIDDLE)])
+        late = late[:, N * (E - W4_MIDDLE) :]
+        nc.sync.dma_start(pos1_sb[:], pos1)
+        nc.sync.dma_start(pos2_sb[:], pos2)
         for lo, hi in zip(LATE_CUTS, LATE_CUTS[1:]):
             load_w8_half(1, lo, hi, late[:, 2 * P * (lo - WHOLE) : 2 * P * (hi - WHOLE)])
 
         gather_words(3, 0, GROUP, WINDOW_512, "slots3_first")
-        gather_words(2, GROUP, E, WORD_COLUMN[3] + T, "slots2_second")
+        gather_words(2, GROUP + 1, E, WORD_COLUMN[3] + T, "slots2_second")
         gather_words(3, GROUP, E - 2, T, "slots3_second")
         gather_words(3, E - 2, E - 1, T, "slots3_third")
         gather_words(3, E - 1, E, T, "slots3_last")
 
         e4m3_passes, e2m1_passes = (0, 1), (2, 3)
-        first_eight = [(0, e) for e in range(GROUP)] + [(1, e) for e in range(WHOLE)]
-        first_eight = first_eight + [(0, e) for e in range(GROUP, E - WHOLE)]
-        for bank, (h, e) in enumerate(first_eight):
-            open_sum(h, e, e4m3_passes, bank)
+        for e in range(E):
+            open_sum(0, e, e4m3_passes, e)
         for e in range(GROUP):
             close_sum(0, e, e2m1_passes)
         for e in range(WHOLE):
+            open_sum(1, e, e4m3_passes, e)
             close_sum(1, e, e2m1_passes)
-        for bank, e in enumerate(range(E - WHOLE, E)):
-            open_sum(0, e, e4m3_passes, bank)
         for e in range(WHOLE, GROUP):
             open_sum(1, e, e2m1_passes, e)
         for e in range(GROUP, E):

@@ -41,7 +41,6 @@ VECTOR_TOKENS_1 = 64
 WHOLE = 3
 LATE_CUTS = (WHOLE, 5, 7, E)
 W4_EARLY = 4
-W4_MIDDLE = 6
 
 GATE_RUNS = 2 * T // P
 GATE_STEP = N * T // 4 - P
@@ -265,13 +264,11 @@ def tile_moe_pln_lin_silu_kernel(
         gather_words(2, GROUP, GROUP + 1, T, "x3")
 
         gather_and_move_scales(0)
-        load_w4(W4_EARLY, W4_MIDDLE, raw_words("w4_second", "xb3", N * (W4_MIDDLE - W4_EARLY)))
-        gather_and_move_scales(1)
-        late = raw_words("late", "plane", N * (E - W4_MIDDLE) + 2 * P * (E - WHOLE))
-        load_w4(W4_MIDDLE, E, late[:, 0 : N * (E - W4_MIDDLE)])
-        late = late[:, N * (E - W4_MIDDLE) :]
+        load_w4(W4_EARLY, E, raw_words("w4_second", "xb3", N * (E - W4_EARLY)))
         nc.sync.dma_start(pos1_sb[:], pos1)
         nc.sync.dma_start(pos2_sb[:], pos2)
+        gather_and_move_scales(1)
+        late = raw_words("late", "plane", 2 * P * (E - WHOLE))
         for lo, hi in zip(LATE_CUTS, LATE_CUTS[1:]):
             load_w8_half(1, lo, hi, late[:, 2 * P * (lo - WHOLE) : 2 * P * (hi - WHOLE)])
 

@@ -31,10 +31,8 @@ MOVED_PASS = 2
 LIVE_ROWS = 100
 W8_ROW = 8
 
-WINDOW_1024 = 1408
-WINDOW_768 = 1024
+WORD_WIDTH = (1216, 1024, 704, 704)
 WINDOW_512 = 704
-WORD_COLUMN = (2 * T, T, 0, 2 * T + WINDOW_1024)
 
 VECTOR_TOKENS = 336
 VECTOR_TOKENS_1 = 64
@@ -68,7 +66,7 @@ def tile_moe_pln_lin_silu_kernel(
 
         x = [keep.tile([P, 4, T], F32, name="x%d" % g, align_bytes=64) for g in range(PASSES)]
         xb = [keep.tile([P, T, 4], BF16, name="xb%d" % g, align_bytes=64) for g in range(PASSES)]
-        words = keep.tile([P, WORD_COLUMN[3] + WINDOW_512], I32, name="words", align_bytes=64)
+        words = [keep.tile([P, WORD_WIDTH[g]], I32, name="words%d" % g, align_bytes=64) for g in range(PASSES)]
         plane = keep.tile([P, WINDOW_512], U8, name="plane", align_bytes=64)
         slot_plane = [keep.tile([P, GROUP_SLOTS], U8, name="slot_plane%d" % u, align_bytes=64) for u in range(2)]
         moved = [keep.tile([P, GROUP_SLOTS], U8, name="moved%d" % u, align_bytes=64) for u in range(2)]
@@ -124,17 +122,15 @@ def tile_moe_pln_lin_silu_kernel(
             )
 
         def quantize(g, lo, hi):
-            start = WORD_COLUMN[g]
             nc.vector.quantize_mx(
-                out=words[:, start + lo : start + hi].bitcast(E4M3),
+                out=words[g][:, lo:hi].bitcast(E4M3),
                 scales=plane[TOKEN_ROW[g] : P, lo:hi],
                 in_=xb[g][:, lo:hi, :].rearrange("p t j -> p (t j)"),
             )
 
         def gather_words(g, lo, hi, width, tag):
             into = keep.tile([P, C * (hi - lo)], U32, name="slot_words%d_%d" % (g, lo), tag=tag, align_bytes=64)
-            start = WORD_COLUMN[g]
-            window = words[:, start : start + width].bitcast(U32)
+            window = words[g][:, 0:width].bitcast(U32)
             nc.vector.tensor_copy(into[:], window.indirect(offs_sb[:, C * lo // 16 : C * hi // 16]))
             for e in range(lo, hi):
                 slot_words[g, e] = into[:, C * (e - lo) : C * (e - lo + 1)]
@@ -209,8 +205,8 @@ def tile_moe_pln_lin_silu_kernel(
         nc.vector.memset(gate_rows[:], 0.0)
         nc.vector.memset(w_plane[:].bitcast(I32), 0)
         nc.vector.memset(plane[:].bitcast(I32), 0)
-        nc.vector.memset(words[:, WORD_COLUMN[0] + T : WORD_COLUMN[3]], 0)
-        nc.vector.memset(words[:, WORD_COLUMN[3] + T :], 0)
+        for g in range(PASSES):
+            nc.vector.memset(words[g][:, T:], 0)
         for u in range(2):
             nc.vector.memset(moved[u][:].bitcast(I32), 0)
         make_identity(nc, ident[:])
@@ -251,20 +247,20 @@ def tile_moe_pln_lin_silu_kernel(
                 nc.tensor.transpose(spread[:, r, :], gate_columns[:, s : s + 1].to_broadcast([P, P]), ident[:])
             nc.scalar.copy(out=gates[:, i, :], in_=spread[:].rearrange("p r t -> p (r t)"))
 
-        gather_words(0, 0, E - 1, WINDOW_1024, "slots0")
+        gather_words(0, 0, E - 1, WORD_WIDTH[0], "slots0")
         round_and_interleave(nc.vector.tensor_copy, 1, T - VECTOR_TOKENS_1, T)
         quantize(1, 0, HALF_T)
         quantize(1, HALF_T, T)
         gather_words(0, E - 1, E, T, "x1")
-        gather_words(1, 0, E - 2, WINDOW_768, "slots1")
+        gather_words(1, 0, E - 2, WORD_WIDTH[1], "slots1")
         quantize(2, 0, T)
         gather_words(1, E - 2, E, T, "x2")
-        gather_words(2, 0, GROUP, WINDOW_768, "slots2_first")
+        gather_words(2, 0, GROUP, WORD_WIDTH[2], "slots2_first")
         quantize(3, 0, T)
         gather_words(2, GROUP, GROUP + 1, T, "x3")
 
         gather_and_move_scales(0)
-        load_w4(W4_EARLY, E, raw_words("w4_second", "xb3", N * (E - W4_EARLY)))
+        load_w4(W4_EARLY, E, raw_words("w4_second", "w4_second", N * (E - W4_EARLY)))
         nc.sync.dma_start(pos1_sb[:], pos1)
         nc.sync.dma_start(pos2_sb[:], pos2)
         gather_and_move_scales(1)
@@ -273,7 +269,7 @@ def tile_moe_pln_lin_silu_kernel(
             load_w8_half(1, lo, hi, late[:, 2 * P * (lo - WHOLE) : 2 * P * (hi - WHOLE)])
 
         gather_words(3, 0, GROUP, WINDOW_512, "slots3_first")
-        gather_words(2, GROUP + 1, E, WORD_COLUMN[3] + T, "slots2_second")
+        gather_words(2, GROUP + 1, E, T, "xb3")
         gather_words(3, GROUP, E - 2, T, "slots3_second")
         gather_words(3, E - 2, E - 1, T, "slots3_third")
         gather_words(3, E - 1, E, T, "slots3_last")

@@ -58,22 +58,22 @@ def tile_moe_pln_lin_silu_kernel(
             return psum.tile(shape, F32, name=name, tag="bank%d" % bank)
 
         def raw_words(name, tag, width):
-            return keep.tile([P, width], I32, name=name, tag=tag, align_bytes=64)[:]
+            return keep.tile([P, width], I32, name=name, tag=tag, align_bytes=256)[:]
 
         offs_sb = lists.tile([P, SLOTS // 16], U16, name="offs_sb")
         pos1_sb = lists.tile([P, T // 16], U16, name="pos1_sb")
         pos2_sb = lists.tile([P, T // 16], U16, name="pos2_sb")
 
-        x = [keep.tile([P, 4, T], F32, name="x%d" % g, align_bytes=64) for g in range(PASSES)]
-        xb = [keep.tile([P, T, 4], BF16, name="xb%d" % g, align_bytes=64) for g in range(PASSES)]
-        words = [keep.tile([P, WORD_WIDTH[g]], I32, name="words%d" % g, align_bytes=64) for g in range(PASSES)]
-        plane = keep.tile([P, WINDOW_512], U8, name="plane", align_bytes=64)
-        slot_plane = [keep.tile([P, GROUP_SLOTS], U8, name="slot_plane%d" % u, align_bytes=64) for u in range(2)]
-        moved = [keep.tile([P, GROUP_SLOTS], U8, name="moved%d" % u, align_bytes=64) for u in range(2)]
+        x = [keep.tile([P, 4, T], F32, name="x%d" % g, align_bytes=256) for g in range(PASSES)]
+        xb = [keep.tile([P, T, 4], BF16, name="xb%d" % g, align_bytes=256) for g in range(PASSES)]
+        words = [keep.tile([P, WORD_WIDTH[g]], I32, name="words%d" % g, align_bytes=256) for g in range(PASSES)]
+        plane = keep.tile([P, WINDOW_512], U8, name="plane", align_bytes=256)
+        slot_plane = [keep.tile([P, GROUP_SLOTS], U8, name="slot_plane%d" % u, align_bytes=256) for u in range(2)]
+        moved = [keep.tile([P, GROUP_SLOTS], U8, name="moved%d" % u, align_bytes=256) for u in range(2)]
         ident = keep.tile([P, P], F32, name="ident")
         gate_rows = keep.tile([P, P], F32, name="gate_rows")
         gate_columns = keep.tile([P, GATE_RUNS], F32, name="gate_columns")
-        w_plane = keep.tile([P, E * 2 * N], U8, name="w_plane", align_bytes=64)
+        w_plane = keep.tile([P, E * 2 * N], U8, name="w_plane", align_bytes=256)
         bias = keep.tile([P, 2, E], F32, name="bias")
         y = [keep.tile([P, SLOTS], F32, name="y%d" % h) for h in range(2)]
         first = [keep.tile([P, T], F32, name="first%d" % h) for h in range(2)]
@@ -129,7 +129,7 @@ def tile_moe_pln_lin_silu_kernel(
             )
 
         def gather_words(g, lo, hi, width, tag):
-            into = keep.tile([P, C * (hi - lo)], U32, name="slot_words%d_%d" % (g, lo), tag=tag, align_bytes=64)
+            into = keep.tile([P, C * (hi - lo)], U32, name="slot_words%d_%d" % (g, lo), tag=tag, align_bytes=256)
             window = words[g][:, 0:width].bitcast(U32)
             nc.vector.tensor_copy(into[:], window.indirect(offs_sb[:, C * lo // 16 : C * hi // 16]))
             for e in range(lo, hi):
@@ -239,7 +239,7 @@ def tile_moe_pln_lin_silu_kernel(
         gate_turned = in_bank(5, [P, P], "gate_turned")
         nc.tensor.transpose(gate_turned[:], gate_rows[:], ident[:])
         nc.scalar.copy(out=gate_columns[:], in_=gate_turned[:, 0:GATE_RUNS])
-        gates = keep.tile([P, 2, T], F32, name="gates", align_bytes=64)
+        gates = keep.tile([P, 2, T], F32, name="gates", align_bytes=256)
         for i in range(2):
             spread = in_bank(6 + i, [P, 4, P], "spread")
             for r in range(4):

@@ -37,6 +37,7 @@ WINDOW_512 = 704
 VECTOR_TOKENS = 336
 VECTOR_TOKENS_1 = 64
 WHOLE = 3
+EARLY_SUMS = 2
 LATE_CUTS = (WHOLE, 5, 7, E)
 W4_EARLY = 4
 
@@ -170,6 +171,9 @@ def tile_moe_pln_lin_silu_kernel(
         def close_sum(h, e, passes):
             multiply(h, e, passes[0], False, False)
             multiply(h, e, passes[1], False, True)
+            activate(h, e)
+
+        def activate(h, e):
             nc.scalar.activation(y[h][:, C * e : C * (e + 1)], sums[h, e][:], SILU, bias=bias[:, h, e : e + 1])
 
         def fetch(into, h, i, lo, hi):
@@ -279,16 +283,22 @@ def tile_moe_pln_lin_silu_kernel(
             open_sum(0, e, e4m3_passes, e)
         for e in range(GROUP):
             close_sum(0, e, e2m1_passes)
-        for e in range(WHOLE):
+        for e in range(EARLY_SUMS):
             open_sum(1, e, e4m3_passes, e)
             close_sum(1, e, e2m1_passes)
-        for e in range(WHOLE, GROUP):
-            open_sum(1, e, e2m1_passes, e)
         for e in range(GROUP, E):
-            close_sum(0, e, e2m1_passes)
+            multiply(0, e, 2, False, False)
         for e in range(GROUP, E):
+            multiply(0, e, 3, False, True)
+            activate(0, e)
+        open_sum(1, 2, e4m3_passes, 4)
+        close_sum(1, 2, e2m1_passes)
+        for e in (3, 4):
+            open_sum(1, e, e4m3_passes, e - 1)
+            close_sum(1, e, e2m1_passes)
+        for e in range(5, E):
             open_sum(1, e, e2m1_passes, e)
-        for e in range(WHOLE, E):
+        for e in range(5, E):
             close_sum(1, e, e4m3_passes)
 
         fetch_half(0)

@@ -71,15 +71,15 @@ def tile_moe_pln_lin_silu_kernel(
         plane = keep.tile([P, WINDOW_512], U8, name="plane", align_bytes=256)
         slot_plane = [keep.tile([P, GROUP_SLOTS], U8, name="slot_plane%d" % u, align_bytes=256) for u in range(2)]
         moved = [keep.tile([P, GROUP_SLOTS], U8, name="moved%d" % u, align_bytes=256) for u in range(2)]
-        ident = keep.tile([P, P], F32, name="ident")
+        ident = keep.tile([P, P], F32, name="ident", align_bytes=256)
         gate_rows = keep.tile([P, P], F32, name="gate_rows")
         gate_columns = keep.tile([P, GATE_RUNS], F32, name="gate_columns")
         w_plane = keep.tile([P, E * 2 * N], U8, name="w_plane", align_bytes=256)
         bias = keep.tile([P, 2, E], F32, name="bias")
-        y = [keep.tile([P, SLOTS], F32, name="y%d" % h) for h in range(2)]
-        first = [keep.tile([P, T], F32, name="first%d" % h) for h in range(2)]
-        second = [keep.tile([P, T], F32, name="second%d" % h) for h in range(2)]
-        result = [keep.tile([P, T], F32, name="result%d" % h) for h in range(2)]
+        y = [keep.tile([P, SLOTS], F32, name="y%d" % h, align_bytes=256) for h in range(2)]
+        first = [keep.tile([P, T], F32, name="first%d" % h, align_bytes=256) for h in range(2)]
+        second = [keep.tile([P, T], F32, name="second%d" % h, align_bytes=256) for h in range(2)]
+        result = [keep.tile([P, T], F32, name="result%d" % h, align_bytes=256) for h in range(2)]
         slot_words = {}
         w8, w4 = {}, {}
         sums = {}
@@ -191,7 +191,7 @@ def tile_moe_pln_lin_silu_kernel(
                 cols = slice(lo + P * i, lo + P * (i + 1))
                 nc.tensor.matmul(turned[:, i, :], first[0][:, cols], ident[:], start=True, stop=False, is_transpose=True)
                 nc.tensor.matmul(turned[:, i, :], second[0][:, cols], ident[:], start=False, stop=True, is_transpose=True)
-            added = keep.tile([P, 2, P], F32, name="added%d" % lo)
+            added = keep.tile([P, 2, P], F32, name="added%d" % lo, align_bytes=256)
             nc.scalar.copy(out=added[:], in_=turned[:])
             return added
 

@@ -29,16 +29,16 @@ GROUP_SLOTS = GROUP * C
 TOKEN_ROW = (4, 8, 12, 0)
 MOVED_PASS = 2
 LIVE_ROWS = 100
+MOVE_CUTS = (((0, 64), (64, 4), (96, 4)), ((0, 64), (64, 36)))
 W8_ROW = 8
 
-WORD_WIDTH = (1216, 1024, 704, 704)
+WORD_WIDTH = (1216, 1216, 704, 704)
 WINDOW_512 = 704
 
 VECTOR_TOKENS = 336
-VECTOR_TOKENS_1 = 64
 WHOLE = 3
 EARLY_SUMS = 2
-LATE_CUTS = (WHOLE, 5, 7, E)
+LATE_CUTS = (WHOLE, 6, E)
 W4_EARLY = 4
 
 GATE_RUNS = 2 * T // P
@@ -53,6 +53,7 @@ def tile_moe_pln_lin_silu_kernel(
     with ExitStack() as ctx:
         lists = ctx.enter_context(tc.tile_pool(name="lists", bufs=1))
         keep = ctx.enter_context(tc.tile_pool(name="keep", bufs=1))
+        shared = ctx.enter_context(tc.tile_pool(name="shared", bufs=1))
         psum = ctx.enter_context(tc.psum_pool(name="psum", bufs=1))
 
         def in_bank(bank, shape, name):
@@ -65,7 +66,10 @@ def tile_moe_pln_lin_silu_kernel(
         pos1_sb = lists.tile([P, T // 16], U16, name="pos1_sb")
         pos2_sb = lists.tile([P, T // 16], U16, name="pos2_sb")
 
-        x = [keep.tile([P, 4, T], F32, name="x%d" % g, align_bytes=256) for g in range(PASSES)]
+        x = {(g, 0): keep.tile([P, 4, T], F32, name="x%d" % g, align_bytes=256) for g in (0, 2)}
+        x[3, 0] = shared.tile([P, 4, T], F32, name="x3", align_bytes=256, offset=0)
+        x[1, 0] = keep.tile([P, 4, HALF_T], F32, name="x1_first", align_bytes=256)
+        x[1, HALF_T] = keep.tile([P, 4, HALF_T], F32, name="x1", align_bytes=256)
         xb = [keep.tile([P, T, 4], BF16, name="xb%d" % g, align_bytes=256) for g in range(PASSES)]
         words = [keep.tile([P, WORD_WIDTH[g]], I32, name="words%d" % g, align_bytes=256) for g in range(PASSES)]
         plane = keep.tile([P, WINDOW_512], U8, name="plane", align_bytes=256)
@@ -84,9 +88,9 @@ def tile_moe_pln_lin_silu_kernel(
         w8, w4 = {}, {}
         sums = {}
 
-        def load_x(g):
-            rows = xT[K_PASS * g : K_PASS * (g + 1), :]
-            nc.sync.dma_start(out=x[g][:], in_=rows.rearrange("(p j) t -> p j t", j=4))
+        def load_x(g, lo=0, hi=T):
+            rows = xT[K_PASS * g : K_PASS * (g + 1), lo:hi]
+            nc.sync.dma_start(out=x[g, lo][:], in_=rows.rearrange("(p j) t -> p j t", j=4))
 
         def load_scales(first_row, scales, r):
             rows = scales.bitcast(I32).rearrange("e a q n -> q (e a) n")
@@ -116,10 +120,10 @@ def tile_moe_pln_lin_silu_kernel(
             for m in range(2 * lo, 2 * hi):
                 w4[m] = into[:, m - 2 * lo, :]
 
-        def round_and_interleave(engine_copy, g, lo, hi):
+        def round_and_interleave(engine_copy, g, lo, hi, first_token=0):
             engine_copy(
                 out=xb[g][:, lo:hi, :].rearrange("p (c i) j -> p c j i", i=4),
-                in_=x[g][:, :, lo:hi].rearrange("p j (c i) -> p c j i", i=4),
+                in_=x[g, first_token][:, :, lo - first_token : hi - first_token].rearrange("p j (c i) -> p c j i", i=4),
             )
 
         def quantize(g, lo, hi):
@@ -129,8 +133,10 @@ def tile_moe_pln_lin_silu_kernel(
                 in_=xb[g][:, lo:hi, :].rearrange("p t j -> p (t j)"),
             )
 
-        def gather_words(g, lo, hi, width, tag):
-            into = keep.tile([P, C * (hi - lo)], U32, name="slot_words%d_%d" % (g, lo), tag=tag, align_bytes=256)
+        def slot_tile(experts, tag):
+            return keep.tile([P, C * experts], U32, name="slot_words", tag=tag, align_bytes=256)
+
+        def gather_words(g, lo, hi, width, into):
             window = words[g][:, 0:width].bitcast(U32)
             nc.vector.tensor_copy(into[:], window.indirect(offs_sb[:, C * lo // 16 : C * hi // 16]))
             for e in range(lo, hi):
@@ -140,7 +146,7 @@ def tile_moe_pln_lin_silu_kernel(
             entries = offs_sb[:, GROUP_SLOTS * u // 16 : GROUP_SLOTS * (u + 1) // 16]
             nc.vector.tensor_copy(slot_plane[u][:], plane[:].indirect(entries))
             row = TOKEN_ROW[MOVED_PASS]
-            for lo, count in ((0, 64), (64, 4), (96, 4)):
+            for lo, count in MOVE_CUTS[u]:
                 nc.sync.dma_start(
                     out=moved[u][lo : lo + count, :].bitcast(I32),
                     in_=slot_plane[u][row + lo : row + lo + count, :].bitcast(I32),
@@ -216,12 +222,13 @@ def tile_moe_pln_lin_silu_kernel(
         make_identity(nc, ident[:])
 
         load_x(0)
-        nc.sync.dma_start(offs_sb[:], offs)
-        load_x(1)
-        load_x(2)
-        load_x(3)
         gate_flat = gate.rearrange("i n t -> (i n t)")[GATE_START : GATE_START + GATE_RUNS * GATE_STEP]
         nc.sync.dma_start(out=gate_rows[0:GATE_RUNS, :], in_=gate_flat.rearrange("(s c) -> s c", c=GATE_STEP)[:, 0:P])
+        nc.sync.dma_start(offs_sb[:], offs)
+        load_x(1, 0, HALF_T)
+        load_x(1, HALF_T, T)
+        load_x(2)
+        load_x(3)
         for r in range(4):
             load_scales(W8_ROW, w8_scales, r)
             load_scales(0, w4_scales, r)
@@ -231,19 +238,19 @@ def tile_moe_pln_lin_silu_kernel(
         load_w4(0, W4_EARLY, raw_words("w4_first", "w4_first", N * W4_EARLY))
 
         round_and_interleave(nc.scalar.copy, 0, VECTOR_TOKENS, T)
+        gate_turned = in_bank(5, [P, P], "gate_turned")
+        nc.tensor.transpose(gate_turned[:], gate_rows[:], ident[:])
+        nc.scalar.copy(out=gate_columns[:], in_=gate_turned[:, 0:GATE_RUNS])
         round_and_interleave(nc.vector.tensor_copy, 0, 0, HALF_T)
         round_and_interleave(nc.vector.tensor_copy, 0, HALF_T, VECTOR_TOKENS)
         quantize(0, 0, HALF_T)
         quantize(0, HALF_T, T)
         round_and_interleave(nc.scalar.copy, 1, 0, HALF_T)
-        round_and_interleave(nc.scalar.copy, 1, HALF_T, T - VECTOR_TOKENS_1)
+        round_and_interleave(nc.scalar.copy, 1, HALF_T, T, HALF_T)
         round_and_interleave(nc.scalar.copy, 2, 0, T)
         round_and_interleave(nc.scalar.copy, 3, 0, T)
 
-        gate_turned = in_bank(5, [P, P], "gate_turned")
-        nc.tensor.transpose(gate_turned[:], gate_rows[:], ident[:])
-        nc.scalar.copy(out=gate_columns[:], in_=gate_turned[:, 0:GATE_RUNS])
-        gates = keep.tile([P, 2, T], F32, name="gates", align_bytes=256)
+        gates = shared.tile([P, 2, T], F32, name="gates", offset=0)
         for i in range(2):
             spread = in_bank(6 + i, [P, 4, P], "spread")
             for r in range(4):
@@ -251,17 +258,16 @@ def tile_moe_pln_lin_silu_kernel(
                 nc.tensor.transpose(spread[:, r, :], gate_columns[:, s : s + 1].to_broadcast([P, P]), ident[:])
             nc.scalar.copy(out=gates[:, i, :], in_=spread[:].rearrange("p r t -> p (r t)"))
 
-        gather_words(0, 0, E - 1, WORD_WIDTH[0], "slots0")
-        round_and_interleave(nc.vector.tensor_copy, 1, T - VECTOR_TOKENS_1, T)
+        gather_words(0, 0, E - 1, WORD_WIDTH[0], slot_tile(E - 1, "slots0"))
         quantize(1, 0, HALF_T)
         quantize(1, HALF_T, T)
-        gather_words(0, E - 1, E, T, "x1")
-        gather_words(1, 0, E - 2, WORD_WIDTH[1], "slots1")
+        gather_words(0, E - 1, E, T, slot_tile(1, "x1"))
+        gather_words(1, 0, E - 1, WORD_WIDTH[1], slot_tile(E - 1, "slots1"))
         quantize(2, 0, T)
-        gather_words(1, E - 2, E, T, "x2")
-        gather_words(2, 0, GROUP, WORD_WIDTH[2], "slots2_first")
+        gather_words(1, E - 1, E, T, slot_tile(1, "x2"))
+        gather_words(2, 0, GROUP, WORD_WIDTH[2], slot_tile(GROUP, "slots2_first"))
         quantize(3, 0, T)
-        gather_words(2, GROUP, GROUP + 1, T, "x3")
+        gather_words(2, GROUP, GROUP + 1, T, shared.tile([P, C], U32, name="slot_words_x3", align_bytes=256, offset=4096))
 
         gather_and_move_scales(0)
         load_w4(W4_EARLY, E, raw_words("w4_second", "w4_second", N * (E - W4_EARLY)))
@@ -272,11 +278,11 @@ def tile_moe_pln_lin_silu_kernel(
         for lo, hi in zip(LATE_CUTS, LATE_CUTS[1:]):
             load_w8_half(1, lo, hi, late[:, 2 * P * (lo - WHOLE) : 2 * P * (hi - WHOLE)])
 
-        gather_words(3, 0, GROUP, WINDOW_512, "slots3_first")
-        gather_words(2, GROUP + 1, E, T, "xb3")
-        gather_words(3, GROUP, E - 2, T, "slots3_second")
-        gather_words(3, E - 2, E - 1, T, "slots3_third")
-        gather_words(3, E - 1, E, T, "slots3_last")
+        gather_words(3, 0, GROUP, WINDOW_512, slot_tile(GROUP, "slots3_first"))
+        gather_words(2, GROUP + 1, E, T, slot_tile(GROUP - 1, "xb3"))
+        gather_words(3, GROUP, E - 2, T, slot_tile(2, "slots3_second"))
+        gather_words(3, E - 2, E - 1, T, slot_tile(1, "slots3_third"))
+        gather_words(3, E - 1, E, T, slot_tile(1, "slots3_last"))
 
         e4m3_passes, e2m1_passes = (0, 1), (2, 3)
         for e in range(E):

@@ -29,7 +29,7 @@ GROUP_SLOTS = GROUP * C
 TOKEN_ROW = (4, 8, 12, 0)
 MOVED_PASS = 2
 LIVE_ROWS = 100
-MOVE_CUTS = (((0, 64), (64, 4), (96, 4)), ((0, 64), (64, 36)))
+MOVE_CUTS = ((0, 64), (64, 4), (96, 4))
 W8_ROW = 8
 
 WORD_WIDTH = (1216, 1216, 704, 704)
@@ -77,7 +77,6 @@ def tile_moe_pln_lin_silu_kernel(
         moved = [keep.tile([P, GROUP_SLOTS], U8, name="moved%d" % u, align_bytes=256) for u in range(2)]
         ident = keep.tile([P, P], F32, name="ident", align_bytes=256)
         gate_rows = keep.tile([P, P], F32, name="gate_rows")
-        gate_columns = keep.tile([P, GATE_RUNS], F32, name="gate_columns")
         w_plane = keep.tile([P, E * 2 * N], U8, name="w_plane", align_bytes=256)
         bias = keep.tile([P, 2, E], F32, name="bias")
         y = [keep.tile([P, SLOTS], F32, name="y%d" % h, align_bytes=256) for h in range(2)]
@@ -146,7 +145,7 @@ def tile_moe_pln_lin_silu_kernel(
             entries = offs_sb[:, GROUP_SLOTS * u // 16 : GROUP_SLOTS * (u + 1) // 16]
             nc.vector.tensor_copy(slot_plane[u][:], plane[:].indirect(entries))
             row = TOKEN_ROW[MOVED_PASS]
-            for lo, count in MOVE_CUTS[u]:
+            for lo, count in MOVE_CUTS:
                 nc.sync.dma_start(
                     out=moved[u][lo : lo + count, :].bitcast(I32),
                     in_=slot_plane[u][row + lo : row + lo + count, :].bitcast(I32),
@@ -223,7 +222,7 @@ def tile_moe_pln_lin_silu_kernel(
 
         load_x(0)
         gate_flat = gate.rearrange("i n t -> (i n t)")[GATE_START : GATE_START + GATE_RUNS * GATE_STEP]
-        nc.sync.dma_start(out=gate_rows[0:GATE_RUNS, :], in_=gate_flat.rearrange("(s c) -> s c", c=GATE_STEP)[:, 0:P])
+        nc.gpsimd.dma_start(out=gate_rows[0:GATE_RUNS, :], in_=gate_flat.rearrange("(s c) -> s c", c=GATE_STEP)[:, 0:P])
         nc.sync.dma_start(offs_sb[:], offs)
         load_x(1, 0, HALF_T)
         load_x(1, HALF_T, T)
@@ -238,9 +237,6 @@ def tile_moe_pln_lin_silu_kernel(
         load_w4(0, W4_EARLY, raw_words("w4_first", "w4_first", N * W4_EARLY))
 
         round_and_interleave(nc.scalar.copy, 0, VECTOR_TOKENS, T)
-        gate_turned = in_bank(5, [P, P], "gate_turned")
-        nc.tensor.transpose(gate_turned[:], gate_rows[:], ident[:])
-        nc.scalar.copy(out=gate_columns[:], in_=gate_turned[:, 0:GATE_RUNS])
         round_and_interleave(nc.vector.tensor_copy, 0, 0, HALF_T)
         round_and_interleave(nc.vector.tensor_copy, 0, HALF_T, VECTOR_TOKENS)
         quantize(0, 0, HALF_T)
@@ -250,6 +246,10 @@ def tile_moe_pln_lin_silu_kernel(
         round_and_interleave(nc.scalar.copy, 2, 0, T)
         round_and_interleave(nc.scalar.copy, 3, 0, T)
 
+        gate_turned = in_bank(5, [P, P], "gate_turned")
+        nc.tensor.transpose(gate_turned[:], gate_rows[:], ident[:])
+        gate_columns = shared.tile([P, GATE_RUNS], F32, name="gate_columns", offset=4608)
+        nc.scalar.copy(out=gate_columns[:], in_=gate_turned[:, 0:GATE_RUNS])
         gates = shared.tile([P, 2, T], F32, name="gates", offset=0)
         for i in range(2):
             spread = in_bank(6 + i, [P, 4, P], "spread")

@@ -32,7 +32,7 @@ LIVE_ROWS = 100
 MOVE_CUTS = ((0, 64), (64, 4), (96, 4))
 W8_ROW = 8
 
-WORD_WIDTH = (1216, 1216, 704, 704)
+WORD_WIDTH = (1216, 1216, 704, 896)
 WINDOW_512 = 704
 
 VECTOR_TOKENS = 336
@@ -271,46 +271,49 @@ def tile_moe_pln_lin_silu_kernel(
 
         gather_and_move_scales(0)
         load_w4(W4_EARLY, E, raw_words("w4_second", "w4_second", N * (E - W4_EARLY)))
+        gather_and_move_scales(1)
         nc.sync.dma_start(pos1_sb[:], pos1)
         nc.sync.dma_start(pos2_sb[:], pos2)
-        gather_and_move_scales(1)
         late = raw_words("late", "plane", 2 * P * (E - WHOLE))
         for lo, hi in zip(LATE_CUTS, LATE_CUTS[1:]):
             load_w8_half(1, lo, hi, late[:, 2 * P * (lo - WHOLE) : 2 * P * (hi - WHOLE)])
 
-        gather_words(3, 0, GROUP, WINDOW_512, slot_tile(GROUP, "slots3_first"))
+        gather_words(3, 0, GROUP + 1, WORD_WIDTH[3], slot_tile(GROUP + 1, "slots3_first"))
         gather_words(2, GROUP + 1, E, T, slot_tile(GROUP - 1, "xb3"))
-        gather_words(3, GROUP, E - 2, T, slot_tile(2, "slots3_second"))
-        gather_words(3, E - 2, E - 1, T, slot_tile(1, "slots3_third"))
+        gather_words(3, GROUP + 1, E - 1, T, slot_tile(2, "slots3_second"))
         gather_words(3, E - 1, E, T, slot_tile(1, "slots3_last"))
 
         e4m3_passes, e2m1_passes = (0, 1), (2, 3)
-        for e in range(E):
-            open_sum(0, e, e4m3_passes, e)
-        for e in range(GROUP):
-            close_sum(0, e, e2m1_passes)
-        for e in range(EARLY_SUMS):
-            open_sum(1, e, e4m3_passes, e)
-            close_sum(1, e, e2m1_passes)
+        first_eight = [(0, e) for e in range(GROUP)] + [(1, e) for e in range(EARLY_SUMS)]
+        first_eight = first_eight + [(0, e) for e in range(GROUP, E - EARLY_SUMS)]
+        for bank, (h, e) in enumerate(first_eight):
+            open_sum(h, e, e4m3_passes, bank)
+        for h, e in first_eight[: GROUP + EARLY_SUMS]:
+            multiply(h, e, 2, False, False)
+        for h, e in first_eight[: GROUP + EARLY_SUMS]:
+            multiply(h, e, 3, False, True)
+            activate(h, e)
+        for bank, e in enumerate(range(E - EARLY_SUMS, E)):
+            open_sum(0, e, e4m3_passes, bank)
         for e in range(GROUP, E):
             multiply(0, e, 2, False, False)
         for e in range(GROUP, E):
             multiply(0, e, 3, False, True)
             activate(0, e)
-        open_sum(1, 2, e4m3_passes, 4)
+        open_sum(1, 2, e4m3_passes, 6)
         close_sum(1, 2, e2m1_passes)
+        for e, bank in ((5, 7), (6, 0), (7, 1)):
+            open_sum(1, e, e2m1_passes, bank)
         for e in (3, 4):
             open_sum(1, e, e4m3_passes, e - 1)
             close_sum(1, e, e2m1_passes)
         for e in range(5, E):
-            open_sum(1, e, e2m1_passes, e)
-        for e in range(5, E):
             close_sum(1, e, e4m3_passes)
 
         fetch_half(0)
-        added = [add_turned(0, E - 2), add_turned(HALF_T, E - 1)]
-        turn_back_and_store(added[0], 0, 0)
-        turn_back_and_store(added[1], HALF_T, 1)
+        added = [add_turned(0, 0), add_turned(HALF_T, 1)]
+        turn_back_and_store(added[0], 0, 2)
+        turn_back_and_store(added[1], HALF_T, 3)
         fetch_half(1)
         add_and_store(0, HALF_T)
         add_and_store(HALF_T, T)

@@ -33,13 +33,15 @@ MOVE_CUTS = ((0, 64), (64, 4), (96, 4))
 W8_ROW = 8
 
 WORD_WIDTH = (1216, 1216, 704, 896)
+WORD_COLUMN = (3 * T, 2 * T, T, 0)
 WINDOW_512 = 704
 
 VECTOR_TOKENS = 336
+VECTOR_TOKENS_1 = 112
 WHOLE = 3
 EARLY_SUMS = 2
-LATE_CUTS = (WHOLE, 6, E)
-W4_EARLY = 4
+LATE_CUTS = (WHOLE, 5, 7, E)
+W4_EARLY = 6
 
 GATE_RUNS = 2 * T // P
 GATE_STEP = N * T // 4 - P
@@ -66,12 +68,10 @@ def tile_moe_pln_lin_silu_kernel(
         pos1_sb = lists.tile([P, T // 16], U16, name="pos1_sb")
         pos2_sb = lists.tile([P, T // 16], U16, name="pos2_sb")
 
-        x = {(g, 0): keep.tile([P, 4, T], F32, name="x%d" % g, align_bytes=256) for g in (0, 2)}
-        x[3, 0] = shared.tile([P, 4, T], F32, name="x3", align_bytes=256, offset=0)
-        x[1, 0] = keep.tile([P, 4, HALF_T], F32, name="x1_first", align_bytes=256)
-        x[1, HALF_T] = keep.tile([P, 4, HALF_T], F32, name="x1", align_bytes=256)
+        x = [keep.tile([P, 4, T], F32, name="x%d" % g, align_bytes=256) for g in range(PASSES - 1)]
+        x = x + [shared.tile([P, 4, T], F32, name="x3", align_bytes=256, offset=0)]
         xb = [keep.tile([P, T, 4], BF16, name="xb%d" % g, align_bytes=256) for g in range(PASSES)]
-        words = [keep.tile([P, WORD_WIDTH[g]], I32, name="words%d" % g, align_bytes=256) for g in range(PASSES)]
+        words = keep.tile([P, WORD_COLUMN[0] + WORD_WIDTH[0]], I32, name="words", align_bytes=256)
         plane = keep.tile([P, WINDOW_512], U8, name="plane", align_bytes=256)
         slot_plane = [keep.tile([P, GROUP_SLOTS], U8, name="slot_plane%d" % u, align_bytes=256) for u in range(2)]
         moved = [keep.tile([P, GROUP_SLOTS], U8, name="moved%d" % u, align_bytes=256) for u in range(2)]
@@ -87,9 +87,9 @@ def tile_moe_pln_lin_silu_kernel(
         w8, w4 = {}, {}
         sums = {}
 
-        def load_x(g, lo=0, hi=T):
-            rows = xT[K_PASS * g : K_PASS * (g + 1), lo:hi]
-            nc.sync.dma_start(out=x[g, lo][:], in_=rows.rearrange("(p j) t -> p j t", j=4))
+        def load_x(g):
+            rows = xT[K_PASS * g : K_PASS * (g + 1), :]
+            nc.sync.dma_start(out=x[g][:], in_=rows.rearrange("(p j) t -> p j t", j=4))
 
         def load_scales(first_row, scales, r):
             rows = scales.bitcast(I32).rearrange("e a q n -> q (e a) n")
@@ -119,15 +119,15 @@ def tile_moe_pln_lin_silu_kernel(
             for m in range(2 * lo, 2 * hi):
                 w4[m] = into[:, m - 2 * lo, :]
 
-        def round_and_interleave(engine_copy, g, lo, hi, first_token=0):
+        def round_and_interleave(engine_copy, g, lo, hi):
             engine_copy(
                 out=xb[g][:, lo:hi, :].rearrange("p (c i) j -> p c j i", i=4),
-                in_=x[g, first_token][:, :, lo - first_token : hi - first_token].rearrange("p j (c i) -> p c j i", i=4),
+                in_=x[g][:, :, lo:hi].rearrange("p j (c i) -> p c j i", i=4),
             )
 
         def quantize(g, lo, hi):
             nc.vector.quantize_mx(
-                out=words[g][:, lo:hi].bitcast(E4M3),
+                out=words[:, WORD_COLUMN[g] + lo : WORD_COLUMN[g] + hi].bitcast(E4M3),
                 scales=plane[TOKEN_ROW[g] : P, lo:hi],
                 in_=xb[g][:, lo:hi, :].rearrange("p t j -> p (t j)"),
             )
@@ -136,7 +136,7 @@ def tile_moe_pln_lin_silu_kernel(
             return keep.tile([P, C * experts], U32, name="slot_words", tag=tag, align_bytes=256)
 
         def gather_words(g, lo, hi, width, into):
-            window = words[g][:, 0:width].bitcast(U32)
+            window = words[:, WORD_COLUMN[g] : WORD_COLUMN[g] + width].bitcast(U32)
             nc.vector.tensor_copy(into[:], window.indirect(offs_sb[:, C * lo // 16 : C * hi // 16]))
             for e in range(lo, hi):
                 slot_words[g, e] = into[:, C * (e - lo) : C * (e - lo + 1)]
@@ -214,8 +214,7 @@ def tile_moe_pln_lin_silu_kernel(
         nc.vector.memset(gate_rows[:], 0.0)
         nc.vector.memset(w_plane[:].bitcast(I32), 0)
         nc.vector.memset(plane[:].bitcast(I32), 0)
-        for g in range(PASSES):
-            nc.vector.memset(words[g][:, T:], 0)
+        nc.vector.memset(words[:, WORD_COLUMN[0] + T :], 0)
         for u in range(2):
             nc.vector.memset(moved[u][:].bitcast(I32), 0)
         make_identity(nc, ident[:])
@@ -224,16 +223,18 @@ def tile_moe_pln_lin_silu_kernel(
         gate_flat = gate.rearrange("i n t -> (i n t)")[GATE_START : GATE_START + GATE_RUNS * GATE_STEP]
         nc.gpsimd.dma_start(out=gate_rows[0:GATE_RUNS, :], in_=gate_flat.rearrange("(s c) -> s c", c=GATE_STEP)[:, 0:P])
         nc.sync.dma_start(offs_sb[:], offs)
-        load_x(1, 0, HALF_T)
-        load_x(1, HALF_T, T)
+        load_x(1)
         load_x(2)
         load_x(3)
         for r in range(4):
             load_scales(W8_ROW, w8_scales, r)
+        load_w8_whole(0, WHOLE, raw_words("w8_whole", "w8_whole", 2 * N * WHOLE))
+        for r in range(4):
             load_scales(0, w4_scales, r)
         nc.sync.dma_start(out=bias[:], in_=b.rearrange("(h p) e -> p h e", h=2))
-        load_w8_whole(0, WHOLE, raw_words("w8_whole", "w8_whole", 2 * N * WHOLE))
         load_w8_half(0, WHOLE, E, raw_words("w8_early", "w8_early", 2 * P * (E - WHOLE)))
+        nc.sync.dma_start(pos1_sb[:], pos1)
+        nc.sync.dma_start(pos2_sb[:], pos2)
         load_w4(0, W4_EARLY, raw_words("w4_first", "w4_first", N * W4_EARLY))
 
         round_and_interleave(nc.scalar.copy, 0, VECTOR_TOKENS, T)
@@ -242,7 +243,7 @@ def tile_moe_pln_lin_silu_kernel(
         quantize(0, 0, HALF_T)
         quantize(0, HALF_T, T)
         round_and_interleave(nc.scalar.copy, 1, 0, HALF_T)
-        round_and_interleave(nc.scalar.copy, 1, HALF_T, T, HALF_T)
+        round_and_interleave(nc.scalar.copy, 1, HALF_T, T - VECTOR_TOKENS_1)
         round_and_interleave(nc.scalar.copy, 2, 0, T)
         round_and_interleave(nc.scalar.copy, 3, 0, T)
 
@@ -259,6 +260,7 @@ def tile_moe_pln_lin_silu_kernel(
             nc.scalar.copy(out=gates[:, i, :], in_=spread[:].rearrange("p r t -> p (r t)"))
 
         gather_words(0, 0, E - 1, WORD_WIDTH[0], slot_tile(E - 1, "slots0"))
+        round_and_interleave(nc.vector.tensor_copy, 1, T - VECTOR_TOKENS_1, T)
         quantize(1, 0, HALF_T)
         quantize(1, HALF_T, T)
         gather_words(0, E - 1, E, T, slot_tile(1, "x1"))
@@ -272,8 +274,6 @@ def tile_moe_pln_lin_silu_kernel(
         gather_and_move_scales(0)
         load_w4(W4_EARLY, E, raw_words("w4_second", "w4_second", N * (E - W4_EARLY)))
         gather_and_move_scales(1)
-        nc.sync.dma_start(pos1_sb[:], pos1)
-        nc.sync.dma_start(pos2_sb[:], pos2)
         late = raw_words("late", "plane", 2 * P * (E - WHOLE))
         for lo, hi in zip(LATE_CUTS, LATE_CUTS[1:]):
             load_w8_half(1, lo, hi, late[:, 2 * P * (lo - WHOLE) : 2 * P * (hi - WHOLE)])

@@ -41,7 +41,7 @@ VECTOR_TOKENS_1 = 112
 WHOLE = 3
 EARLY_SUMS = 2
 LATE_CUTS = (WHOLE, 5, 7, E)
-W4_EARLY = 6
+W4_EARLY = 4
 
 GATE_RUNS = 2 * T // P
 GATE_STEP = N * T // 4 - P

@@ -228,10 +228,9 @@ def tile_moe_pln_lin_silu_kernel(
         load_x(3)
         for r in range(4):
             load_scales(W8_ROW, w8_scales, r)
-        load_w8_whole(0, WHOLE, raw_words("w8_whole", "w8_whole", 2 * N * WHOLE))
-        for r in range(4):
             load_scales(0, w4_scales, r)
         nc.sync.dma_start(out=bias[:], in_=b.rearrange("(h p) e -> p h e", h=2))
+        load_w8_whole(0, WHOLE, raw_words("w8_whole", "w8_whole", 2 * N * WHOLE))
         load_w8_half(0, WHOLE, E, raw_words("w8_early", "w8_early", 2 * P * (E - WHOLE)))
         nc.sync.dma_start(pos1_sb[:], pos1)
         nc.sync.dma_start(pos2_sb[:], pos2)

@@ -32,15 +32,14 @@ LIVE_ROWS = 100
 MOVE_CUTS = ((0, 64), (64, 4), (96, 4))
 W8_ROW = 8
 
-WORD_WIDTH = (1216, 1216, 704, 896)
+WORD_WIDTH = (1216, 1216, 704, 704)
 WORD_COLUMN = (3 * T, 2 * T, T, 0)
 WINDOW_512 = 704
 
 VECTOR_TOKENS = 336
 VECTOR_TOKENS_1 = 112
 WHOLE = 3
-EARLY_SUMS = 2
-LATE_CUTS = (WHOLE, 5, 7, E)
+LATE_LOADS = ((4, 6), (6, E), (WHOLE, 4))
 W4_EARLY = 4
 
 GATE_RUNS = 2 * T // P
@@ -274,45 +273,50 @@ def tile_moe_pln_lin_silu_kernel(
         load_w4(W4_EARLY, E, raw_words("w4_second", "w4_second", N * (E - W4_EARLY)))
         gather_and_move_scales(1)
         late = raw_words("late", "plane", 2 * P * (E - WHOLE))
-        for lo, hi in zip(LATE_CUTS, LATE_CUTS[1:]):
+        for lo, hi in LATE_LOADS:
             load_w8_half(1, lo, hi, late[:, 2 * P * (lo - WHOLE) : 2 * P * (hi - WHOLE)])
 
-        gather_words(3, 0, GROUP + 1, WORD_WIDTH[3], slot_tile(GROUP + 1, "slots3_first"))
+        gather_words(3, 0, GROUP, WORD_WIDTH[3], slot_tile(GROUP, "slots3_first"))
         gather_words(2, GROUP + 1, E, T, slot_tile(GROUP - 1, "xb3"))
-        gather_words(3, GROUP + 1, E - 1, T, slot_tile(2, "slots3_second"))
+        gather_words(3, GROUP, E - 2, T, slot_tile(2, "slots3_second"))
+        gather_words(3, E - 2, E - 1, T, slot_tile(1, "slots3_third"))
         gather_words(3, E - 1, E, T, slot_tile(1, "slots3_last"))
 
         e4m3_passes, e2m1_passes = (0, 1), (2, 3)
-        first_eight = [(0, e) for e in range(GROUP)] + [(1, e) for e in range(EARLY_SUMS)]
-        first_eight = first_eight + [(0, e) for e in range(GROUP, E - EARLY_SUMS)]
-        for bank, (h, e) in enumerate(first_eight):
-            open_sum(h, e, e4m3_passes, bank)
-        for h, e in first_eight[: GROUP + EARLY_SUMS]:
-            multiply(h, e, 2, False, False)
-        for h, e in first_eight[: GROUP + EARLY_SUMS]:
-            multiply(h, e, 3, False, True)
-            activate(h, e)
-        for bank, e in enumerate(range(E - EARLY_SUMS, E)):
-            open_sum(0, e, e4m3_passes, bank)
+        for e in range(E):
+            open_sum(0, e, e4m3_passes, e)
+        for e in range(GROUP):
+            multiply(0, e, 2, False, False)
+        for e in range(GROUP):
+            multiply(0, e, 3, False, True)
+            activate(0, e)
         for e in range(GROUP, E):
             multiply(0, e, 2, False, False)
         for e in range(GROUP, E):
-            multiply(0, e, 3, False, True)
-            activate(0, e)
+            sums[1, e] = in_bank(e - GROUP, [P, C], "sum")
+            multiply(1, e, 2, True, False)
+        for experts in ((4, 5), (6,), (7,)):
+            for e in experts:
+                multiply(0, e, 3, False, True)
+                activate(0, e)
+            for e in experts:
+                multiply(1, e, 3, False, False)
+        for e in (4, 5):
+            close_sum(1, e, e4m3_passes)
+        for e in (0, 1):
+            open_sum(1, e, e4m3_passes, GROUP + e)
+            close_sum(1, e, e2m1_passes)
+        for e in (6, 7):
+            close_sum(1, e, e4m3_passes)
         open_sum(1, 2, e4m3_passes, 6)
         close_sum(1, 2, e2m1_passes)
-        for e, bank in ((5, 7), (6, 0), (7, 1)):
-            open_sum(1, e, e2m1_passes, bank)
-        for e in (3, 4):
-            open_sum(1, e, e4m3_passes, e - 1)
-            close_sum(1, e, e2m1_passes)
-        for e in range(5, E):
-            close_sum(1, e, e4m3_passes)
+        open_sum(1, 3, e2m1_passes, 7)
+        close_sum(1, 3, e4m3_passes)
 
         fetch_half(0)
-        added = [add_turned(0, 0), add_turned(HALF_T, 1)]
-        turn_back_and_store(added[0], 0, 2)
-        turn_back_and_store(added[1], HALF_T, 3)
+        added = [add_turned(0, 6), add_turned(HALF_T, 7)]
+        turn_back_and_store(added[0], 0, 0)
+        turn_back_and_store(added[1], HALF_T, 1)
         fetch_half(1)
         add_and_store(0, HALF_T)
         add_and_store(HALF_T, T)

@@ -101,6 +101,7 @@ def tile_moe_pln_lin_silu_kernel(
         def load_w8_whole(lo, hi, into):
             into = into.rearrange("p (m n) -> p m n", n=N)
             nc.sync.dma_start(out=into, in_=w8_rows[2 * lo : 2 * hi].rearrange("m p n -> p m n"))
+            w8["pair"] = into[:, 0:2, :].rearrange("p m n -> p (m n)")
             for m in range(2 * lo, 2 * hi):
                 for h in range(2):
                     w8[h, m] = into[:, m - 2 * lo, P * h : P * (h + 1)]
@@ -281,6 +282,18 @@ def tile_moe_pln_lin_silu_kernel(
         gather_words(3, GROUP, E - 2, T, slot_tile(2, "slots3_second"))
         gather_words(3, E - 2, E - 1, T, slot_tile(1, "slots3_third"))
         gather_words(3, E - 1, E, T, slot_tile(1, "slots3_last"))
+
+        warm_up = in_bank(0, [P, 2 * N], "warm_up")
+        for step in range(3):
+            nc.tensor.matmul_mx(
+                out=warm_up[:],
+                lhsT=w8[0, 0].bitcast(E4M3),
+                lhsT_scale=w_plane[W8_ROW:P, 0:P],
+                rhs=w8["pair"].bitcast(E4M3),
+                rhs_scale=w_plane[W8_ROW:P, 0 : 2 * N],
+                start=True,
+                stop=True,
+            )
 
         e4m3_passes, e2m1_passes = (0, 1), (2, 3)
         for e in range(E):

@@ -32,15 +32,15 @@ LIVE_ROWS = 100
 MOVE_CUTS = ((0, 64), (64, 4), (96, 4))
 W8_ROW = 8
 
-WORD_WIDTH = (1216, 1216, 704, 704)
+WORD_WIDTH = (1216, 1216, 704, 896)
 WORD_COLUMN = (3 * T, 2 * T, T, 0)
-WINDOW_512 = 704
+PLANE_WIDTH = 1408
 
 VECTOR_TOKENS = 336
 VECTOR_TOKENS_1 = 112
 WHOLE = 3
 LATE_LOADS = ((4, 6), (6, E), (WHOLE, 4))
-W4_EARLY = 4
+W4_EARLY = 5
 
 GATE_RUNS = 2 * T // P
 GATE_STEP = N * T // 4 - P
@@ -71,9 +71,9 @@ def tile_moe_pln_lin_silu_kernel(
         x = x + [shared.tile([P, 4, T], F32, name="x3", align_bytes=256, offset=0)]
         xb = [keep.tile([P, T, 4], BF16, name="xb%d" % g, align_bytes=256) for g in range(PASSES)]
         words = keep.tile([P, WORD_COLUMN[0] + WORD_WIDTH[0]], I32, name="words", align_bytes=256)
-        plane = keep.tile([P, WINDOW_512], U8, name="plane", align_bytes=256)
-        slot_plane = [keep.tile([P, GROUP_SLOTS], U8, name="slot_plane%d" % u, align_bytes=256) for u in range(2)]
-        moved = [keep.tile([P, GROUP_SLOTS], U8, name="moved%d" % u, align_bytes=256) for u in range(2)]
+        plane = keep.tile([P, PLANE_WIDTH], U8, name="plane", align_bytes=256)
+        slot_plane = keep.tile([P, SLOTS], U8, name="slot_plane", align_bytes=256)
+        moved = keep.tile([P, SLOTS], U8, name="moved", align_bytes=256)
         ident = keep.tile([P, P], F32, name="ident", align_bytes=256)
         gate_rows = keep.tile([P, P], F32, name="gate_rows")
         w_plane = keep.tile([P, E * 2 * N], U8, name="w_plane", align_bytes=256)
@@ -141,19 +141,18 @@ def tile_moe_pln_lin_silu_kernel(
             for e in range(lo, hi):
                 slot_words[g, e] = into[:, C * (e - lo) : C * (e - lo + 1)]
 
-        def gather_and_move_scales(u):
-            entries = offs_sb[:, GROUP_SLOTS * u // 16 : GROUP_SLOTS * (u + 1) // 16]
-            nc.vector.tensor_copy(slot_plane[u][:], plane[:].indirect(entries))
+        def gather_and_move_scales():
+            nc.vector.tensor_copy(slot_plane[:], plane[:].indirect(offs_sb[:]))
             row = TOKEN_ROW[MOVED_PASS]
             for lo, count in MOVE_CUTS:
                 nc.sync.dma_start(
-                    out=moved[u][lo : lo + count, :].bitcast(I32),
-                    in_=slot_plane[u][row + lo : row + lo + count, :].bitcast(I32),
+                    out=moved[lo : lo + count, :].bitcast(I32),
+                    in_=slot_plane[row + lo : row + lo + count, :].bitcast(I32),
                 )
 
         def multiply(h, e, g, start, stop):
-            u, m = e // GROUP, 2 * e + g % 2
-            slots = slice(C * (e % GROUP), C * (e % GROUP + 1))
+            m = 2 * e + g % 2
+            slots = slice(C * e, C * (e + 1))
             if g < 2:
                 w_row, weights = W8_ROW, w8[h, m].bitcast(E4M3)
             else:
@@ -163,7 +162,7 @@ def tile_moe_pln_lin_silu_kernel(
                 lhsT=weights,
                 lhsT_scale=w_plane[w_row:P, N * m + P * h : N * m + P * (h + 1)],
                 rhs=slot_words[g, e].bitcast(E4M3),
-                rhs_scale=moved[u][:, slots] if g == MOVED_PASS else slot_plane[u][TOKEN_ROW[g] : P, slots],
+                rhs_scale=moved[:, slots] if g == MOVED_PASS else slot_plane[TOKEN_ROW[g] : P, slots],
                 start=start,
                 stop=stop,
             )
@@ -215,8 +214,7 @@ def tile_moe_pln_lin_silu_kernel(
         nc.vector.memset(w_plane[:].bitcast(I32), 0)
         nc.vector.memset(plane[:].bitcast(I32), 0)
         nc.vector.memset(words[:, WORD_COLUMN[0] + T :], 0)
-        for u in range(2):
-            nc.vector.memset(moved[u][:].bitcast(I32), 0)
+        nc.vector.memset(moved[:].bitcast(I32), 0)
         make_identity(nc, ident[:])
 
         load_x(0)
@@ -231,10 +229,12 @@ def tile_moe_pln_lin_silu_kernel(
             load_scales(0, w4_scales, r)
         nc.sync.dma_start(out=bias[:], in_=b.rearrange("(h p) e -> p h e", h=2))
         load_w8_whole(0, WHOLE, raw_words("w8_whole", "w8_whole", 2 * N * WHOLE))
-        load_w8_half(0, WHOLE, E, raw_words("w8_early", "w8_early", 2 * P * (E - WHOLE)))
+        load_w8_half(0, WHOLE, 5, raw_words("w8_early", "w8_early", 2 * P * (5 - WHOLE)))
+        load_w8_half(0, 5, E, raw_words("w8_next", "w8_next", 2 * P * (E - 5)))
         nc.sync.dma_start(pos1_sb[:], pos1)
         nc.sync.dma_start(pos2_sb[:], pos2)
-        load_w4(0, W4_EARLY, raw_words("w4_first", "w4_first", N * W4_EARLY))
+        for lo, hi in ((0, 3), (3, 5), (5, E)):
+            load_w4(lo, hi, raw_words("w4_%d" % lo, "w4_%d" % lo, N * (hi - lo)))
 
         round_and_interleave(nc.scalar.copy, 0, VECTOR_TOKENS, T)
         round_and_interleave(nc.vector.tensor_copy, 0, 0, HALF_T)
@@ -270,17 +270,14 @@ def tile_moe_pln_lin_silu_kernel(
         quantize(3, 0, T)
         gather_words(2, GROUP, GROUP + 1, T, shared.tile([P, C], U32, name="slot_words_x3", align_bytes=256, offset=4096))
 
-        gather_and_move_scales(0)
-        load_w4(W4_EARLY, E, raw_words("w4_second", "w4_second", N * (E - W4_EARLY)))
-        gather_and_move_scales(1)
+        gather_and_move_scales()
         late = raw_words("late", "plane", 2 * P * (E - WHOLE))
         for lo, hi in LATE_LOADS:
             load_w8_half(1, lo, hi, late[:, 2 * P * (lo - WHOLE) : 2 * P * (hi - WHOLE)])
 
-        gather_words(3, 0, GROUP, WORD_WIDTH[3], slot_tile(GROUP, "slots3_first"))
+        gather_words(3, 0, GROUP + 1, WORD_WIDTH[3], slot_tile(GROUP + 1, "slots3_first"))
         gather_words(2, GROUP + 1, E, T, slot_tile(GROUP - 1, "xb3"))
-        gather_words(3, GROUP, E - 2, T, slot_tile(2, "slots3_second"))
-        gather_words(3, E - 2, E - 1, T, slot_tile(1, "slots3_third"))
+        gather_words(3, GROUP + 1, E - 1, T, slot_tile(2, "slots3_second"))
         gather_words(3, E - 1, E, T, slot_tile(1, "slots3_last"))
 
         warm_up = in_bank(0, [P, 2 * N], "warm_up")
@@ -298,22 +295,21 @@ def tile_moe_pln_lin_silu_kernel(
         e4m3_passes, e2m1_passes = (0, 1), (2, 3)
         for e in range(E):
             open_sum(0, e, e4m3_passes, e)
-        for e in range(GROUP):
+        for e in range(5):
+            multiply(0, e, 3, False, False)
+        for e in range(5):
+            multiply(0, e, 2, False, True)
+            activate(0, e)
+        for e in range(5, E):
             multiply(0, e, 2, False, False)
-        for e in range(GROUP):
+        for e in (5, 6):
             multiply(0, e, 3, False, True)
             activate(0, e)
-        for e in range(GROUP, E):
-            multiply(0, e, 2, False, False)
-        for e in range(GROUP, E):
-            sums[1, e] = in_bank(e - GROUP, [P, C], "sum")
-            multiply(1, e, 2, True, False)
-        for experts in ((4, 5), (6,), (7,)):
-            for e in experts:
-                multiply(0, e, 3, False, True)
-                activate(0, e)
-            for e in experts:
-                multiply(1, e, 3, False, False)
+        open_sum(1, 4, e2m1_passes, 0)
+        multiply(0, 7, 3, False, True)
+        activate(0, 7)
+        for e in (5, 6, 7):
+            open_sum(1, e, e2m1_passes, e - GROUP)
         for e in (4, 5):
             close_sum(1, e, e4m3_passes)
         for e in (0, 1):

@@ -101,7 +101,6 @@ def tile_moe_pln_lin_silu_kernel(
         def load_w8_whole(lo, hi, into):
             into = into.rearrange("p (m n) -> p m n", n=N)
             nc.sync.dma_start(out=into, in_=w8_rows[2 * lo : 2 * hi].rearrange("m p n -> p m n"))
-            w8["pair"] = into[:, 0:2, :].rearrange("p m n -> p (m n)")
             for m in range(2 * lo, 2 * hi):
                 for h in range(2):
                     w8[h, m] = into[:, m - 2 * lo, P * h : P * (h + 1)]
@@ -228,9 +227,12 @@ def tile_moe_pln_lin_silu_kernel(
             load_scales(W8_ROW, w8_scales, r)
             load_scales(0, w4_scales, r)
         nc.sync.dma_start(out=bias[:], in_=b.rearrange("(h p) e -> p h e", h=2))
-        load_w8_whole(0, WHOLE, raw_words("w8_whole", "w8_whole", 2 * N * WHOLE))
-        load_w8_half(0, WHOLE, 5, raw_words("w8_early", "w8_early", 2 * P * (5 - WHOLE)))
-        load_w8_half(0, 5, E, raw_words("w8_next", "w8_next", 2 * P * (E - 5)))
+        w8_whole = raw_words("w8_whole", "w8_whole", 2 * N * WHOLE)
+        w8_early = raw_words("w8_early", "w8_early", 2 * P * (5 - WHOLE))
+        w8_next = raw_words("w8_next", "w8_next", 2 * P * (E - 5))
+        load_w8_whole(0, WHOLE, w8_whole)
+        load_w8_half(0, WHOLE, 5, w8_early)
+        load_w8_half(0, 5, E, w8_next)
         nc.sync.dma_start(pos1_sb[:], pos1)
         nc.sync.dma_start(pos2_sb[:], pos2)
         for lo, hi in ((0, 3), (3, 5), (5, E)):
@@ -281,12 +283,12 @@ def tile_moe_pln_lin_silu_kernel(
         gather_words(3, E - 1, E, T, slot_tile(1, "slots3_last"))
 
         warm_up = in_bank(0, [P, 2 * N], "warm_up")
-        for step in range(3):
+        for landed in (w8_whole, w8_whole, w8_early, w8_next):
             nc.tensor.matmul_mx(
                 out=warm_up[:],
                 lhsT=w8[0, 0].bitcast(E4M3),
                 lhsT_scale=w_plane[W8_ROW:P, 0:P],
-                rhs=w8["pair"].bitcast(E4M3),
+                rhs=landed[:, 0 : 2 * N].bitcast(E4M3),
                 rhs_scale=w_plane[W8_ROW:P, 0 : 2 * N],
                 start=True,
                 stop=True,

@@ -37,8 +37,8 @@ WORD_COLUMN = (3 * T, 2 * T, T, 0)
 PLANE_WIDTH = 1408
 
 VECTOR_TOKENS = 336
-VECTOR_TOKENS_1 = 112
-WHOLE = 3
+VECTOR_TOKENS_1 = 128
+WHOLE = 2
 LATE_LOADS = ((4, 6), (6, E), (WHOLE, 4))
 W4_EARLY = 5
 
@@ -283,7 +283,7 @@ def tile_moe_pln_lin_silu_kernel(
         gather_words(3, E - 1, E, T, slot_tile(1, "slots3_last"))
 
         warm_up = in_bank(0, [P, 2 * N], "warm_up")
-        for landed in (w8_whole, w8_whole, w8_early, w8_next):
+        for landed in (w8_early, w8_early, w8_next, w8_next):
             nc.tensor.matmul_mx(
                 out=warm_up[:],
                 lhsT=w8[0, 0].bitcast(E4M3),
@@ -319,10 +319,10 @@ def tile_moe_pln_lin_silu_kernel(
             close_sum(1, e, e2m1_passes)
         for e in (6, 7):
             close_sum(1, e, e4m3_passes)
-        open_sum(1, 2, e4m3_passes, 6)
-        close_sum(1, 2, e2m1_passes)
-        open_sum(1, 3, e2m1_passes, 7)
-        close_sum(1, 3, e4m3_passes)
+        for e in (2, 3):
+            open_sum(1, e, e2m1_passes, GROUP + e)
+        for e in (2, 3):
+            close_sum(1, e, e4m3_passes)
 
         fetch_half(0)
         added = [add_turned(0, 6), add_turned(HALF_T, 7)]

@@ -282,17 +282,18 @@ def tile_moe_pln_lin_silu_kernel(
         gather_words(3, GROUP + 1, E - 1, T, slot_tile(2, "slots3_second"))
         gather_words(3, E - 1, E, T, slot_tile(1, "slots3_last"))
 
-        warm_up = in_bank(0, [P, 2 * N], "warm_up")
-        for landed in (w8_early, w8_early, w8_next, w8_next):
-            nc.tensor.matmul_mx(
-                out=warm_up[:],
-                lhsT=w8[0, 0].bitcast(E4M3),
-                lhsT_scale=w_plane[W8_ROW:P, 0:P],
-                rhs=landed[:, 0 : 2 * N].bitcast(E4M3),
-                rhs_scale=w_plane[W8_ROW:P, 0 : 2 * N],
-                start=True,
-                stop=True,
-            )
+        for bank in (0, 6):
+            warm_up = in_bank(bank, [P, 2 * N], "warm_up")
+            for step in range(2):
+                nc.tensor.matmul_mx(
+                    out=warm_up[:],
+                    lhsT=w8[0, 0].bitcast(E4M3),
+                    lhsT_scale=w_plane[W8_ROW:P, 0:P],
+                    rhs=w8_whole[:, 0 : 2 * N].bitcast(E4M3),
+                    rhs_scale=w_plane[W8_ROW:P, 0 : 2 * N],
+                    start=True,
+                    stop=True,
+                )
 
         e4m3_passes, e2m1_passes = (0, 1), (2, 3)
         for e in range(E):

@@ -23,24 +23,24 @@ P = 128
 PASSES = 4
 K_PASS = K // PASSES
 HALF_T = T // 2
-GROUP = E // 2
-GROUP_SLOTS = GROUP * C
+BANKS = 8
+ALIGN = 256
 
 TOKEN_ROW = (4, 8, 12, 0)
 MOVED_PASS = 2
-LIVE_ROWS = 100
-MOVE_CUTS = ((0, 64), (64, 4), (96, 4))
+MOVES = ((0, 64), (64, 4), (96, 4))
 W8_ROW = 8
 
-WORD_WIDTH = (1216, 1216, 704, 896)
-WORD_COLUMN = (3 * T, 2 * T, T, 0)
-PLANE_WIDTH = 1408
+VECTOR_TOKENS = (336, 128)
+AHEAD = 4
+FIRST = 5
 
-VECTOR_TOKENS = 336
-VECTOR_TOKENS_1 = 128
-WHOLE = 2
-LATE_LOADS = ((4, 6), (6, E), (WHOLE, 4))
-W4_EARLY = 5
+WORD_COLUMN = (3 * T, 2 * T, T, 0)
+
+
+def window_width(entries):
+    return max(T, -(-4 * entries // 192) * 64)
+
 
 GATE_RUNS = 2 * T // P
 GATE_STEP = N * T // 4 - P
@@ -60,30 +60,33 @@ def tile_moe_pln_lin_silu_kernel(
         def in_bank(bank, shape, name):
             return psum.tile(shape, F32, name=name, tag="bank%d" % bank)
 
-        def raw_words(name, tag, width):
-            return keep.tile([P, width], I32, name=name, tag=tag, align_bytes=256)[:]
+        def large(name, shape, dtype, tag=None):
+            return keep.tile(shape, dtype, name=name, tag=tag or name, align_bytes=ALIGN)
+
+        def on_last_x(name, shape, dtype, offset):
+            return shared.tile(shape, dtype, name=name, align_bytes=ALIGN, offset=offset)
 
         offs_sb = lists.tile([P, SLOTS // 16], U16, name="offs_sb")
         pos1_sb = lists.tile([P, T // 16], U16, name="pos1_sb")
         pos2_sb = lists.tile([P, T // 16], U16, name="pos2_sb")
 
-        x = [keep.tile([P, 4, T], F32, name="x%d" % g, align_bytes=256) for g in range(PASSES - 1)]
-        x = x + [shared.tile([P, 4, T], F32, name="x3", align_bytes=256, offset=0)]
-        xb = [keep.tile([P, T, 4], BF16, name="xb%d" % g, align_bytes=256) for g in range(PASSES)]
-        words = keep.tile([P, WORD_COLUMN[0] + WORD_WIDTH[0]], I32, name="words", align_bytes=256)
-        plane = keep.tile([P, PLANE_WIDTH], U8, name="plane", align_bytes=256)
-        slot_plane = keep.tile([P, SLOTS], U8, name="slot_plane", align_bytes=256)
-        moved = keep.tile([P, SLOTS], U8, name="moved", align_bytes=256)
-        ident = keep.tile([P, P], F32, name="ident", align_bytes=256)
-        gate_rows = keep.tile([P, P], F32, name="gate_rows")
-        w_plane = keep.tile([P, E * 2 * N], U8, name="w_plane", align_bytes=256)
-        bias = keep.tile([P, 2, E], F32, name="bias")
-        y = [keep.tile([P, SLOTS], F32, name="y%d" % h, align_bytes=256) for h in range(2)]
-        first = [keep.tile([P, T], F32, name="first%d" % h, align_bytes=256) for h in range(2)]
-        second = [keep.tile([P, T], F32, name="second%d" % h, align_bytes=256) for h in range(2)]
-        result = [keep.tile([P, T], F32, name="result%d" % h, align_bytes=256) for h in range(2)]
+        x = [large("x%d" % g, [P, 4, T], F32) for g in range(PASSES - 1)] + [on_last_x("x3", [P, 4, T], F32, 0)]
+        xb = [large("xb%d" % g, [P, T, 4], BF16) for g in range(PASSES)]
+        words = large("words", [P, WORD_COLUMN[0] + window_width(SLOTS - C)], I32)
+        plane = large("plane", [P, window_width(SLOTS)], U8)
+        slot_plane = large("slot_plane", [P, SLOTS], U8)
+        moved = large("moved", [P, SLOTS], U8)
+        ident = large("ident", [P, P], F32)
+        gate_rows = large("gate_rows", [P, P], F32)
+        w_plane = large("w_plane", [P, E * 2 * N], U8)
+        bias = large("bias", [P, 2, E], F32)
+        y = [large("y%d" % h, [P, SLOTS], F32) for h in range(2)]
+        first = [large("first%d" % h, [P, T], F32) for h in range(2)]
+        second = [large("second%d" % h, [P, T], F32) for h in range(2)]
+        result = [large("result%d" % h, [P, T], F32) for h in range(2)]
+        w8_early = large("w8_early", [P, 2 * E, P], I32)
+        w4 = large("w4", [P, 2 * E, N // 2], I32)
         slot_words = {}
-        w8, w4 = {}, {}
         sums = {}
 
         def load_x(g):
@@ -95,28 +98,14 @@ def tile_moe_pln_lin_silu_kernel(
             plane_rows = w_plane[:].bitcast(I32).rearrange("p (m n) -> p m n", m=2 * E)
             nc.sync.dma_start(out=plane_rows[first_row + r : P : 32], in_=rows[r:16:4])
 
-        w8_rows = w8_words.rearrange("e a p n t -> (e a) p (n t)").bitcast(I32)
-        w4_rows = w4_words.rearrange("e a p n -> (e a) p n").bitcast(I32)
+        w8_rows = w8_words.rearrange("e a p n t -> p (e a) (n t)").bitcast(I32)
+        w4_rows = w4_words.rearrange("e a p n -> p (e a) n").bitcast(I32)
 
-        def load_w8_whole(lo, hi, into):
-            into = into.rearrange("p (m n) -> p m n", n=N)
-            nc.sync.dma_start(out=into, in_=w8_rows[2 * lo : 2 * hi].rearrange("m p n -> p m n"))
-            for m in range(2 * lo, 2 * hi):
-                for h in range(2):
-                    w8[h, m] = into[:, m - 2 * lo, P * h : P * (h + 1)]
+        def load_w8(into, h, lo, hi):
+            nc.sync.dma_start(out=into[:, 2 * lo : 2 * hi, :], in_=w8_rows[:, 2 * lo : 2 * hi, P * h : P * (h + 1)])
 
-        def load_w8_half(h, lo, hi, into):
-            into = into.rearrange("p (m n) -> p m n", n=P)
-            rows = w8_rows[2 * lo : 2 * hi, :, P * h : P * (h + 1)]
-            nc.sync.dma_start(out=into, in_=rows.rearrange("m p n -> p m n"))
-            for m in range(2 * lo, 2 * hi):
-                w8[h, m] = into[:, m - 2 * lo, :]
-
-        def load_w4(lo, hi, into):
-            into = into.rearrange("p (m n) -> p m n", n=N // 2)
-            nc.sync.dma_start(out=into, in_=w4_rows[2 * lo : 2 * hi].rearrange("m p n -> p m n"))
-            for m in range(2 * lo, 2 * hi):
-                w4[m] = into[:, m - 2 * lo, :]
+        def load_w4(lo, hi):
+            nc.sync.dma_start(out=w4[:, 2 * lo : 2 * hi, :], in_=w4_rows[:, 2 * lo : 2 * hi, :])
 
         def round_and_interleave(engine_copy, g, lo, hi):
             engine_copy(
@@ -131,31 +120,21 @@ def tile_moe_pln_lin_silu_kernel(
                 in_=xb[g][:, lo:hi, :].rearrange("p t j -> p (t j)"),
             )
 
-        def slot_tile(experts, tag):
-            return keep.tile([P, C * experts], U32, name="slot_words", tag=tag, align_bytes=256)
-
-        def gather_words(g, lo, hi, width, into):
-            window = words[:, WORD_COLUMN[g] : WORD_COLUMN[g] + width].bitcast(U32)
+        def gather_words(g, lo, hi, tag=None, into=None):
+            entries = C * (hi - lo)
+            if into is None:
+                into = large("slot_words%d_%d" % (g, lo), [P, entries], U32, tag)
+            window = words[:, WORD_COLUMN[g] : WORD_COLUMN[g] + window_width(entries)].bitcast(U32)
             nc.vector.tensor_copy(into[:], window.indirect(offs_sb[:, C * lo // 16 : C * hi // 16]))
             for e in range(lo, hi):
                 slot_words[g, e] = into[:, C * (e - lo) : C * (e - lo + 1)]
 
-        def gather_and_move_scales():
-            nc.vector.tensor_copy(slot_plane[:], plane[:].indirect(offs_sb[:]))
-            row = TOKEN_ROW[MOVED_PASS]
-            for lo, count in MOVE_CUTS:
-                nc.sync.dma_start(
-                    out=moved[lo : lo + count, :].bitcast(I32),
-                    in_=slot_plane[row + lo : row + lo + count, :].bitcast(I32),
-                )
-
-        def multiply(h, e, g, start, stop):
-            m = 2 * e + g % 2
-            slots = slice(C * e, C * (e + 1))
+        def multiply(h, e, g, start=False, stop=False):
+            m, slots = 2 * e + g % 2, slice(C * e, C * (e + 1))
             if g < 2:
-                w_row, weights = W8_ROW, w8[h, m].bitcast(E4M3)
+                w_row, weights = W8_ROW, w8[h][:, m, :].bitcast(E4M3)
             else:
-                w_row, weights = 0, w4[m][:, P // 2 * h : P // 2 * (h + 1)].bitcast(U8).bitcast(E2M1)
+                w_row, weights = 0, w4[:, m, P // 2 * h : P // 2 * (h + 1)].bitcast(U8).bitcast(E2M1)
             nc.tensor.matmul_mx(
                 out=sums[h, e][:],
                 lhsT=weights,
@@ -168,15 +147,11 @@ def tile_moe_pln_lin_silu_kernel(
 
         def open_sum(h, e, passes, bank):
             sums[h, e] = in_bank(bank, [P, C], "sum")
-            multiply(h, e, passes[0], True, False)
-            multiply(h, e, passes[1], False, False)
+            multiply(h, e, passes[0], start=True)
+            multiply(h, e, passes[1])
 
-        def close_sum(h, e, passes):
-            multiply(h, e, passes[0], False, False)
-            multiply(h, e, passes[1], False, True)
-            activate(h, e)
-
-        def activate(h, e):
+        def close_sum(h, e, g):
+            multiply(h, e, g, stop=True)
             nc.scalar.activation(y[h][:, C * e : C * (e + 1)], sums[h, e][:], SILU, bias=bias[:, h, e : e + 1])
 
         def fetch(into, h, i, lo, hi):
@@ -194,7 +169,7 @@ def tile_moe_pln_lin_silu_kernel(
                 cols = slice(lo + P * i, lo + P * (i + 1))
                 nc.tensor.matmul(turned[:, i, :], first[0][:, cols], ident[:], start=True, stop=False, is_transpose=True)
                 nc.tensor.matmul(turned[:, i, :], second[0][:, cols], ident[:], start=False, stop=True, is_transpose=True)
-            added = keep.tile([P, 2, P], F32, name="added%d" % lo, align_bytes=256)
+            added = large("added%d" % lo, [P, 2, P], F32)
             nc.scalar.copy(out=added[:], in_=turned[:])
             return added
 
@@ -216,43 +191,38 @@ def tile_moe_pln_lin_silu_kernel(
         nc.vector.memset(moved[:].bitcast(I32), 0)
         make_identity(nc, ident[:])
 
-        load_x(0)
         gate_flat = gate.rearrange("i n t -> (i n t)")[GATE_START : GATE_START + GATE_RUNS * GATE_STEP]
         nc.gpsimd.dma_start(out=gate_rows[0:GATE_RUNS, :], in_=gate_flat.rearrange("(s c) -> s c", c=GATE_STEP)[:, 0:P])
+        load_x(0)
         nc.sync.dma_start(offs_sb[:], offs)
-        load_x(1)
-        load_x(2)
-        load_x(3)
+        for g in range(1, PASSES):
+            load_x(g)
         for r in range(4):
             load_scales(W8_ROW, w8_scales, r)
             load_scales(0, w4_scales, r)
         nc.sync.dma_start(out=bias[:], in_=b.rearrange("(h p) e -> p h e", h=2))
-        w8_whole = raw_words("w8_whole", "w8_whole", 2 * N * WHOLE)
-        w8_early = raw_words("w8_early", "w8_early", 2 * P * (5 - WHOLE))
-        w8_next = raw_words("w8_next", "w8_next", 2 * P * (E - 5))
-        load_w8_whole(0, WHOLE, w8_whole)
-        load_w8_half(0, WHOLE, 5, w8_early)
-        load_w8_half(0, 5, E, w8_next)
+        for e in range(0, E, 2):
+            load_w8(w8_early, 0, e, e + 2)
         nc.sync.dma_start(pos1_sb[:], pos1)
         nc.sync.dma_start(pos2_sb[:], pos2)
-        for lo, hi in ((0, 3), (3, 5), (5, E)):
-            load_w4(lo, hi, raw_words("w4_%d" % lo, "w4_%d" % lo, N * (hi - lo)))
+        load_w4(0, FIRST)
+        load_w4(FIRST, E)
 
-        round_and_interleave(nc.scalar.copy, 0, VECTOR_TOKENS, T)
+        round_and_interleave(nc.scalar.copy, 0, VECTOR_TOKENS[0], T)
         round_and_interleave(nc.vector.tensor_copy, 0, 0, HALF_T)
-        round_and_interleave(nc.vector.tensor_copy, 0, HALF_T, VECTOR_TOKENS)
+        round_and_interleave(nc.vector.tensor_copy, 0, HALF_T, VECTOR_TOKENS[0])
         quantize(0, 0, HALF_T)
         quantize(0, HALF_T, T)
         round_and_interleave(nc.scalar.copy, 1, 0, HALF_T)
-        round_and_interleave(nc.scalar.copy, 1, HALF_T, T - VECTOR_TOKENS_1)
+        round_and_interleave(nc.scalar.copy, 1, HALF_T, T - VECTOR_TOKENS[1])
         round_and_interleave(nc.scalar.copy, 2, 0, T)
         round_and_interleave(nc.scalar.copy, 3, 0, T)
 
         gate_turned = in_bank(5, [P, P], "gate_turned")
         nc.tensor.transpose(gate_turned[:], gate_rows[:], ident[:])
-        gate_columns = shared.tile([P, GATE_RUNS], F32, name="gate_columns", offset=4608)
+        gates = on_last_x("gates", [P, 2, T], F32, 0)
+        gate_columns = on_last_x("gate_columns", [P, GATE_RUNS], F32, 4 * (2 * T + C))
         nc.scalar.copy(out=gate_columns[:], in_=gate_turned[:, 0:GATE_RUNS])
-        gates = shared.tile([P, 2, T], F32, name="gates", offset=0)
         for i in range(2):
             spread = in_bank(6 + i, [P, 4, P], "spread")
             for r in range(4):
@@ -260,73 +230,67 @@ def tile_moe_pln_lin_silu_kernel(
                 nc.tensor.transpose(spread[:, r, :], gate_columns[:, s : s + 1].to_broadcast([P, P]), ident[:])
             nc.scalar.copy(out=gates[:, i, :], in_=spread[:].rearrange("p r t -> p (r t)"))
 
-        gather_words(0, 0, E - 1, WORD_WIDTH[0], slot_tile(E - 1, "slots0"))
-        round_and_interleave(nc.vector.tensor_copy, 1, T - VECTOR_TOKENS_1, T)
+        gather_words(0, 0, E - 1)
+        round_and_interleave(nc.vector.tensor_copy, 1, T - VECTOR_TOKENS[1], T)
         quantize(1, 0, HALF_T)
         quantize(1, HALF_T, T)
-        gather_words(0, E - 1, E, T, slot_tile(1, "x1"))
-        gather_words(1, 0, E - 1, WORD_WIDTH[1], slot_tile(E - 1, "slots1"))
+        gather_words(0, E - 1, E, tag="x1")
+        gather_words(1, 0, E - 1)
         quantize(2, 0, T)
-        gather_words(1, E - 1, E, T, slot_tile(1, "x2"))
-        gather_words(2, 0, GROUP, WORD_WIDTH[2], slot_tile(GROUP, "slots2_first"))
+        gather_words(1, E - 1, E, tag="x2")
+        gather_words(2, 0, AHEAD)
         quantize(3, 0, T)
-        gather_words(2, GROUP, GROUP + 1, T, shared.tile([P, C], U32, name="slot_words_x3", align_bytes=256, offset=4096))
+        gather_words(2, AHEAD, AHEAD + 1, into=on_last_x("slot_words2", [P, C], U32, 4 * 2 * T))
 
-        gather_and_move_scales()
-        late = raw_words("late", "plane", 2 * P * (E - WHOLE))
-        for lo, hi in LATE_LOADS:
-            load_w8_half(1, lo, hi, late[:, 2 * P * (lo - WHOLE) : 2 * P * (hi - WHOLE)])
+        nc.vector.tensor_copy(slot_plane[:], plane[:].indirect(offs_sb[:]))
+        row = TOKEN_ROW[MOVED_PASS]
+        for lo, count in MOVES:
+            nc.sync.dma_start(
+                out=moved[lo : lo + count, :].bitcast(I32), in_=slot_plane[row + lo : row + lo + count, :].bitcast(I32)
+            )
+        w8 = (w8_early, large("w8_late", [P, 2 * E, P], I32, "plane"))
+        late_order = [(e + BANKS // 2) % E for e in range(E)]
+        for e in late_order[::2]:
+            load_w8(w8[1], 1, e, e + 2)
 
-        gather_words(3, 0, GROUP + 1, WORD_WIDTH[3], slot_tile(GROUP + 1, "slots3_first"))
-        gather_words(2, GROUP + 1, E, T, slot_tile(GROUP - 1, "xb3"))
-        gather_words(3, GROUP + 1, E - 1, T, slot_tile(2, "slots3_second"))
-        gather_words(3, E - 1, E, T, slot_tile(1, "slots3_last"))
+        gather_words(3, 0, FIRST)
+        gather_words(2, AHEAD + 1, E, tag="xb3")
+        gather_words(3, FIRST, E - 1)
+        gather_words(3, E - 1, E)
 
         for bank in (0, 6):
-            warm_up = in_bank(bank, [P, 2 * N], "warm_up")
+            warm_up = in_bank(bank, [P, 4 * P], "warm_up")
             for step in range(2):
                 nc.tensor.matmul_mx(
                     out=warm_up[:],
-                    lhsT=w8[0, 0].bitcast(E4M3),
+                    lhsT=w8_early[:, 0, :].bitcast(E4M3),
                     lhsT_scale=w_plane[W8_ROW:P, 0:P],
-                    rhs=w8_whole[:, 0 : 2 * N].bitcast(E4M3),
-                    rhs_scale=w_plane[W8_ROW:P, 0 : 2 * N],
+                    rhs=w8_early[:, 0:4, :].rearrange("p m n -> p (m n)").bitcast(E4M3),
+                    rhs_scale=w_plane[W8_ROW:P, 0 : 4 * P],
                     start=True,
                     stop=True,
                 )
 
-        e4m3_passes, e2m1_passes = (0, 1), (2, 3)
         for e in range(E):
-            open_sum(0, e, e4m3_passes, e)
-        for e in range(5):
-            multiply(0, e, 3, False, False)
-        for e in range(5):
-            multiply(0, e, 2, False, True)
-            activate(0, e)
-        for e in range(5, E):
-            multiply(0, e, 2, False, False)
-        for e in (5, 6):
-            multiply(0, e, 3, False, True)
-            activate(0, e)
-        open_sum(1, 4, e2m1_passes, 0)
-        multiply(0, 7, 3, False, True)
-        activate(0, 7)
-        for e in (5, 6, 7):
-            open_sum(1, e, e2m1_passes, e - GROUP)
-        for e in (4, 5):
-            close_sum(1, e, e4m3_passes)
-        for e in (0, 1):
-            open_sum(1, e, e4m3_passes, GROUP + e)
-            close_sum(1, e, e2m1_passes)
-        for e in (6, 7):
-            close_sum(1, e, e4m3_passes)
-        for e in (2, 3):
-            open_sum(1, e, e2m1_passes, GROUP + e)
-        for e in (2, 3):
-            close_sum(1, e, e4m3_passes)
+            open_sum(0, e, (0, 1), e)
+        for e in range(FIRST):
+            multiply(0, e, 3)
+        for e in range(FIRST):
+            close_sum(0, e, MOVED_PASS)
+        for e in range(FIRST, E):
+            multiply(0, e, MOVED_PASS)
+        for e in range(FIRST, E - 1):
+            close_sum(0, e, 3)
+        open_sum(1, late_order[0], (2, 3), 0)
+        close_sum(0, E - 1, 3)
+        for bank, e in list(enumerate(late_order))[1:]:
+            open_sum(1, e, (2, 3), bank)
+        for e in late_order:
+            multiply(1, e, 0)
+            close_sum(1, e, 1)
 
         fetch_half(0)
-        added = [add_turned(0, 6), add_turned(HALF_T, 7)]
+        added = [add_turned(0, BANKS - 2), add_turned(HALF_T, BANKS - 1)]
         turn_back_and_store(added[0], 0, 0)
         turn_back_and_store(added[1], HALF_T, 1)
         fetch_half(1)

@@ -33,6 +33,7 @@ W8_ROW = 8
 
 VECTOR_TOKENS = (336, 128)
 AHEAD = 4
+WHOLE = 2
 FIRST = 5
 
 WORD_COLUMN = (3 * T, 2 * T, T, 0)
@@ -84,7 +85,8 @@ def tile_moe_pln_lin_silu_kernel(
         first = [large("first%d" % h, [P, T], F32) for h in range(2)]
         second = [large("second%d" % h, [P, T], F32) for h in range(2)]
         result = [large("result%d" % h, [P, T], F32) for h in range(2)]
-        w8_early = large("w8_early", [P, 2 * E, P], I32)
+        w8_whole = large("w8_whole", [P, 2 * WHOLE, N], I32)
+        w8_early = large("w8_early", [P, 2 * (E - WHOLE), P], I32)
         w4 = large("w4", [P, 2 * E, N // 2], I32)
         slot_words = {}
         sums = {}
@@ -101,8 +103,9 @@ def tile_moe_pln_lin_silu_kernel(
         w8_rows = w8_words.rearrange("e a p n t -> p (e a) (n t)").bitcast(I32)
         w4_rows = w4_words.rearrange("e a p n -> p (e a) n").bitcast(I32)
 
-        def load_w8(into, h, lo, hi):
-            nc.sync.dma_start(out=into[:, 2 * lo : 2 * hi, :], in_=w8_rows[:, 2 * lo : 2 * hi, P * h : P * (h + 1)])
+        def load_w8_half(into, h, lo, hi):
+            matrices = into[:, 2 * (lo - WHOLE) : 2 * (hi - WHOLE), :]
+            nc.sync.dma_start(out=matrices, in_=w8_rows[:, 2 * lo : 2 * hi, P * h : P * (h + 1)])
 
         def load_w4(lo, hi):
             nc.sync.dma_start(out=w4[:, 2 * lo : 2 * hi, :], in_=w4_rows[:, 2 * lo : 2 * hi, :])
@@ -131,8 +134,10 @@ def tile_moe_pln_lin_silu_kernel(
 
         def multiply(h, e, g, start=False, stop=False):
             m, slots = 2 * e + g % 2, slice(C * e, C * (e + 1))
-            if g < 2:
-                w_row, weights = W8_ROW, w8[h][:, m, :].bitcast(E4M3)
+            if g < 2 and e < WHOLE:
+                w_row, weights = W8_ROW, w8_whole[:, m, P * h : P * (h + 1)].bitcast(E4M3)
+            elif g < 2:
+                w_row, weights = W8_ROW, (w8_early, w8_late)[h][:, m - 2 * WHOLE, :].bitcast(E4M3)
             else:
                 w_row, weights = 0, w4[:, m, P // 2 * h : P // 2 * (h + 1)].bitcast(U8).bitcast(E2M1)
             nc.tensor.matmul_mx(
@@ -153,6 +158,10 @@ def tile_moe_pln_lin_silu_kernel(
         def close_sum(h, e, g):
             multiply(h, e, g, stop=True)
             nc.scalar.activation(y[h][:, C * e : C * (e + 1)], sums[h, e][:], SILU, bias=bias[:, h, e : e + 1])
+
+        def close_two(e, passes):
+            multiply(1, e, passes[0])
+            close_sum(1, e, passes[1])
 
         def fetch(into, h, i, lo, hi):
             places = (pos1_sb, pos2_sb)[i][:, lo // 16 : hi // 16]
@@ -201,12 +210,13 @@ def tile_moe_pln_lin_silu_kernel(
             load_scales(W8_ROW, w8_scales, r)
             load_scales(0, w4_scales, r)
         nc.sync.dma_start(out=bias[:], in_=b.rearrange("(h p) e -> p h e", h=2))
-        for e in range(0, E, 2):
-            load_w8(w8_early, 0, e, e + 2)
+        nc.sync.dma_start(out=w8_whole[:], in_=w8_rows[:, 0 : 2 * WHOLE, :])
+        load_w8_half(w8_early, 0, WHOLE, FIRST)
+        load_w8_half(w8_early, 0, FIRST, E)
         nc.sync.dma_start(pos1_sb[:], pos1)
         nc.sync.dma_start(pos2_sb[:], pos2)
-        load_w4(0, FIRST)
-        load_w4(FIRST, E)
+        for lo, hi in ((0, WHOLE), (WHOLE, FIRST), (FIRST, E)):
+            load_w4(lo, hi)
 
         round_and_interleave(nc.scalar.copy, 0, VECTOR_TOKENS[0], T)
         round_and_interleave(nc.vector.tensor_copy, 0, 0, HALF_T)
@@ -248,10 +258,9 @@ def tile_moe_pln_lin_silu_kernel(
             nc.sync.dma_start(
                 out=moved[lo : lo + count, :].bitcast(I32), in_=slot_plane[row + lo : row + lo + count, :].bitcast(I32)
             )
-        w8 = (w8_early, large("w8_late", [P, 2 * E, P], I32, "plane"))
-        late_order = [(e + BANKS // 2) % E for e in range(E)]
-        for e in late_order[::2]:
-            load_w8(w8[1], 1, e, e + 2)
+        w8_late = large("w8_late", [P, 2 * (E - WHOLE), P], I32, "plane")
+        for e in (4, 6, 2):
+            load_w8_half(w8_late, 1, e, e + 2)
 
         gather_words(3, 0, FIRST)
         gather_words(2, AHEAD + 1, E, tag="xb3")
@@ -263,9 +272,9 @@ def tile_moe_pln_lin_silu_kernel(
             for step in range(2):
                 nc.tensor.matmul_mx(
                     out=warm_up[:],
-                    lhsT=w8_early[:, 0, :].bitcast(E4M3),
+                    lhsT=w8_whole[:, 0, 0:P].bitcast(E4M3),
                     lhsT_scale=w_plane[W8_ROW:P, 0:P],
-                    rhs=w8_early[:, 0:4, :].rearrange("p m n -> p (m n)").bitcast(E4M3),
+                    rhs=w8_whole[:, 0:2, :].rearrange("p m n -> p (m n)").bitcast(E4M3),
                     rhs_scale=w_plane[W8_ROW:P, 0 : 4 * P],
                     start=True,
                     stop=True,
@@ -281,13 +290,21 @@ def tile_moe_pln_lin_silu_kernel(
             multiply(0, e, MOVED_PASS)
         for e in range(FIRST, E - 1):
             close_sum(0, e, 3)
-        open_sum(1, late_order[0], (2, 3), 0)
+        open_sum(1, 4, (2, 3), 0)
         close_sum(0, E - 1, 3)
-        for bank, e in list(enumerate(late_order))[1:]:
-            open_sum(1, e, (2, 3), bank)
-        for e in late_order:
-            multiply(1, e, 0)
-            close_sum(1, e, 1)
+        for e in (5, 6, 7):
+            open_sum(1, e, (2, 3), e - 4)
+        for e in (4, 5):
+            close_two(e, (0, 1))
+        for e in range(WHOLE):
+            open_sum(1, e, (0, 1), e + 4)
+            close_two(e, (2, 3))
+        for e in (6, 7):
+            close_two(e, (0, 1))
+        for e in (2, 3):
+            open_sum(1, e, (2, 3), e + 4)
+        for e in (2, 3):
+            close_two(e, (0, 1))
 
         fetch_half(0)
         added = [add_turned(0, BANKS - 2), add_turned(HALF_T, BANKS - 1)]

@@ -267,19 +267,6 @@ def tile_moe_pln_lin_silu_kernel(
         gather_words(3, FIRST, E - 1)
         gather_words(3, E - 1, E)
 
-        for bank in (0, 6):
-            warm_up = in_bank(bank, [P, 4 * P], "warm_up")
-            for step in range(2):
-                nc.tensor.matmul_mx(
-                    out=warm_up[:],
-                    lhsT=w8_whole[:, 0, 0:P].bitcast(E4M3),
-                    lhsT_scale=w_plane[W8_ROW:P, 0:P],
-                    rhs=w8_whole[:, 0:2, :].rearrange("p m n -> p (m n)").bitcast(E4M3),
-                    rhs_scale=w_plane[W8_ROW:P, 0 : 4 * P],
-                    start=True,
-                    stop=True,
-                )
-
         for e in range(E):
             open_sum(0, e, (0, 1), e)
         for e in range(FIRST):

@@ -200,8 +200,6 @@ def tile_moe_pln_lin_silu_kernel(
         nc.vector.memset(moved[:].bitcast(I32), 0)
         make_identity(nc, ident[:])
 
-        gate_flat = gate.rearrange("i n t -> (i n t)")[GATE_START : GATE_START + GATE_RUNS * GATE_STEP]
-        nc.gpsimd.dma_start(out=gate_rows[0:GATE_RUNS, :], in_=gate_flat.rearrange("(s c) -> s c", c=GATE_STEP)[:, 0:P])
         load_x(0)
         nc.sync.dma_start(offs_sb[:], offs)
         for g in range(1, PASSES):
@@ -210,13 +208,15 @@ def tile_moe_pln_lin_silu_kernel(
             load_scales(W8_ROW, w8_scales, r)
             load_scales(0, w4_scales, r)
         nc.sync.dma_start(out=bias[:], in_=b.rearrange("(h p) e -> p h e", h=2))
+        gate_flat = gate.rearrange("i n t -> (i n t)")[GATE_START : GATE_START + GATE_RUNS * GATE_STEP]
+        nc.sync.dma_start(out=gate_rows[0:GATE_RUNS, :], in_=gate_flat.rearrange("(s c) -> s c", c=GATE_STEP)[:, 0:P])
         nc.sync.dma_start(out=w8_whole[:], in_=w8_rows[:, 0 : 2 * WHOLE, :])
         load_w8_half(w8_early, 0, WHOLE, FIRST)
         load_w8_half(w8_early, 0, FIRST, E)
         nc.sync.dma_start(pos1_sb[:], pos1)
         nc.sync.dma_start(pos2_sb[:], pos2)
-        for lo, hi in ((0, WHOLE), (WHOLE, FIRST), (FIRST, E)):
-            load_w4(lo, hi)
+        load_w4(0, FIRST)
+        load_w4(FIRST, E)
 
         round_and_interleave(nc.scalar.copy, 0, VECTOR_TOKENS[0], T)
         round_and_interleave(nc.vector.tensor_copy, 0, 0, HALF_T)

@@ -33,7 +33,6 @@ W8_ROW = 8
 
 VECTOR_TOKENS = (336, 128)
 AHEAD = 4
-WHOLE = 2
 FIRST = 5
 
 WORD_COLUMN = (3 * T, 2 * T, T, 0)
@@ -55,7 +54,6 @@ def tile_moe_pln_lin_silu_kernel(
     with ExitStack() as ctx:
         lists = ctx.enter_context(tc.tile_pool(name="lists", bufs=1))
         keep = ctx.enter_context(tc.tile_pool(name="keep", bufs=1))
-        shared = ctx.enter_context(tc.tile_pool(name="shared", bufs=1))
         psum = ctx.enter_context(tc.psum_pool(name="psum", bufs=1))
 
         def in_bank(bank, shape, name):
@@ -64,14 +62,11 @@ def tile_moe_pln_lin_silu_kernel(
         def large(name, shape, dtype, tag=None):
             return keep.tile(shape, dtype, name=name, tag=tag or name, align_bytes=ALIGN)
 
-        def on_last_x(name, shape, dtype, offset):
-            return shared.tile(shape, dtype, name=name, align_bytes=ALIGN, offset=offset)
-
         offs_sb = lists.tile([P, SLOTS // 16], U16, name="offs_sb")
         pos1_sb = lists.tile([P, T // 16], U16, name="pos1_sb")
         pos2_sb = lists.tile([P, T // 16], U16, name="pos2_sb")
 
-        x = [large("x%d" % g, [P, 4, T], F32) for g in range(PASSES - 1)] + [on_last_x("x3", [P, 4, T], F32, 0)]
+        x = [large("x%d" % g, [P, 4, T], F32) for g in range(PASSES)]
         xb = [large("xb%d" % g, [P, T, 4], BF16) for g in range(PASSES)]
         words = large("words", [P, WORD_COLUMN[0] + window_width(SLOTS - C)], I32)
         plane = large("plane", [P, window_width(SLOTS)], U8)
@@ -85,8 +80,7 @@ def tile_moe_pln_lin_silu_kernel(
         first = [large("first%d" % h, [P, T], F32) for h in range(2)]
         second = [large("second%d" % h, [P, T], F32) for h in range(2)]
         result = [large("result%d" % h, [P, T], F32) for h in range(2)]
-        w8_whole = large("w8_whole", [P, 2 * WHOLE, N], I32)
-        w8_early = large("w8_early", [P, 2 * (E - WHOLE), P], I32)
+        w8_early = large("w8_early", [P, 2 * E, P], I32)
         w4 = large("w4", [P, 2 * E, N // 2], I32)
         slot_words = {}
         sums = {}
@@ -104,7 +98,7 @@ def tile_moe_pln_lin_silu_kernel(
         w4_rows = w4_words.rearrange("e a p n -> p (e a) n").bitcast(I32)
 
         def load_w8_half(into, h, lo, hi):
-            matrices = into[:, 2 * (lo - WHOLE) : 2 * (hi - WHOLE), :]
+            matrices = into[:, 2 * lo : 2 * hi, :]
             nc.sync.dma_start(out=matrices, in_=w8_rows[:, 2 * lo : 2 * hi, P * h : P * (h + 1)])
 
         def load_w4(lo, hi):
@@ -123,10 +117,9 @@ def tile_moe_pln_lin_silu_kernel(
                 in_=xb[g][:, lo:hi, :].rearrange("p t j -> p (t j)"),
             )
 
-        def gather_words(g, lo, hi, tag=None, into=None):
+        def gather_words(g, lo, hi, tag=None):
             entries = C * (hi - lo)
-            if into is None:
-                into = large("slot_words%d_%d" % (g, lo), [P, entries], U32, tag)
+            into = large("slot_words%d_%d" % (g, lo), [P, entries], U32, tag)
             window = words[:, WORD_COLUMN[g] : WORD_COLUMN[g] + window_width(entries)].bitcast(U32)
             nc.vector.tensor_copy(into[:], window.indirect(offs_sb[:, C * lo // 16 : C * hi // 16]))
             for e in range(lo, hi):
@@ -134,10 +127,8 @@ def tile_moe_pln_lin_silu_kernel(
 
         def multiply(h, e, g, start=False, stop=False):
             m, slots = 2 * e + g % 2, slice(C * e, C * (e + 1))
-            if g < 2 and e < WHOLE:
-                w_row, weights = W8_ROW, w8_whole[:, m, P * h : P * (h + 1)].bitcast(E4M3)
-            elif g < 2:
-                w_row, weights = W8_ROW, (w8_early, w8_late)[h][:, m - 2 * WHOLE, :].bitcast(E4M3)
+            if g < 2:
+                w_row, weights = W8_ROW, (w8_early, w8_late)[h][:, m, :].bitcast(E4M3)
             else:
                 w_row, weights = 0, w4[:, m, P // 2 * h : P // 2 * (h + 1)].bitcast(U8).bitcast(E2M1)
             nc.tensor.matmul_mx(
@@ -201,44 +192,45 @@ def tile_moe_pln_lin_silu_kernel(
         make_identity(nc, ident[:])
 
         load_x(0)
+        gate_flat = gate.rearrange("i n t -> (i n t)")[GATE_START : GATE_START + GATE_RUNS * GATE_STEP]
+        nc.scalar.dma_start(out=gate_rows[0:GATE_RUNS, :], in_=gate_flat.rearrange("(s c) -> s c", c=GATE_STEP)[:, 0:P])
         nc.sync.dma_start(offs_sb[:], offs)
         for g in range(1, PASSES):
             load_x(g)
         for r in range(4):
             load_scales(W8_ROW, w8_scales, r)
             load_scales(0, w4_scales, r)
+        load_w8_half(w8_early, 0, 0, E // 2)
         nc.sync.dma_start(out=bias[:], in_=b.rearrange("(h p) e -> p h e", h=2))
-        gate_flat = gate.rearrange("i n t -> (i n t)")[GATE_START : GATE_START + GATE_RUNS * GATE_STEP]
-        nc.sync.dma_start(out=gate_rows[0:GATE_RUNS, :], in_=gate_flat.rearrange("(s c) -> s c", c=GATE_STEP)[:, 0:P])
-        nc.sync.dma_start(out=w8_whole[:], in_=w8_rows[:, 0 : 2 * WHOLE, :])
-        load_w8_half(w8_early, 0, WHOLE, FIRST)
-        load_w8_half(w8_early, 0, FIRST, E)
+        load_w8_half(w8_early, 0, E // 2, E)
         nc.sync.dma_start(pos1_sb[:], pos1)
         nc.sync.dma_start(pos2_sb[:], pos2)
         load_w4(0, FIRST)
         load_w4(FIRST, E)
+
+        gate_turned = in_bank(5, [P, P], "gate_turned")
+        nc.tensor.transpose(gate_turned[:], gate_rows[:], ident[:])
+        gate_columns = large("gate_columns", [P, GATE_RUNS], F32)
+        nc.scalar.copy(out=gate_columns[:], in_=gate_turned[:, 0:GATE_RUNS])
+        spread = [in_bank(6 + i, [P, 4, P], "spread") for i in range(2)]
+        for i in range(2):
+            for r in range(4):
+                s = 4 * i + 3 - r
+                nc.tensor.transpose(spread[i][:, r, :], gate_columns[:, s : s + 1].to_broadcast([P, P]), ident[:])
 
         round_and_interleave(nc.scalar.copy, 0, VECTOR_TOKENS[0], T)
         round_and_interleave(nc.vector.tensor_copy, 0, 0, HALF_T)
         round_and_interleave(nc.vector.tensor_copy, 0, HALF_T, VECTOR_TOKENS[0])
         quantize(0, 0, HALF_T)
         quantize(0, HALF_T, T)
+        gates = large("gates", [P, 2, T], F32, "x0")
+        for i in range(2):
+            nc.scalar.copy(out=gates[:, i, :], in_=spread[i][:].rearrange("p r t -> p (r t)"))
         round_and_interleave(nc.scalar.copy, 1, 0, HALF_T)
         round_and_interleave(nc.scalar.copy, 1, HALF_T, T - VECTOR_TOKENS[1])
-        round_and_interleave(nc.scalar.copy, 2, 0, T)
-        round_and_interleave(nc.scalar.copy, 3, 0, T)
-
-        gate_turned = in_bank(5, [P, P], "gate_turned")
-        nc.tensor.transpose(gate_turned[:], gate_rows[:], ident[:])
-        gates = on_last_x("gates", [P, 2, T], F32, 0)
-        gate_columns = on_last_x("gate_columns", [P, GATE_RUNS], F32, 4 * (2 * T + C))
-        nc.scalar.copy(out=gate_columns[:], in_=gate_turned[:, 0:GATE_RUNS])
-        for i in range(2):
-            spread = in_bank(6 + i, [P, 4, P], "spread")
-            for r in range(4):
-                s = 4 * i + 3 - r
-                nc.tensor.transpose(spread[:, r, :], gate_columns[:, s : s + 1].to_broadcast([P, P]), ident[:])
-            nc.scalar.copy(out=gates[:, i, :], in_=spread[:].rearrange("p r t -> p (r t)"))
+        for g in (2, 3):
+            round_and_interleave(nc.scalar.copy, g, 0, HALF_T)
+            round_and_interleave(nc.scalar.copy, g, HALF_T, T)
 
         gather_words(0, 0, E - 1)
         round_and_interleave(nc.vector.tensor_copy, 1, T - VECTOR_TOKENS[1], T)
@@ -246,11 +238,13 @@ def tile_moe_pln_lin_silu_kernel(
         quantize(1, HALF_T, T)
         gather_words(0, E - 1, E, tag="x1")
         gather_words(1, 0, E - 1)
-        quantize(2, 0, T)
+        quantize(2, 0, HALF_T)
+        quantize(2, HALF_T, T)
         gather_words(1, E - 1, E, tag="x2")
         gather_words(2, 0, AHEAD)
-        quantize(3, 0, T)
-        gather_words(2, AHEAD, AHEAD + 1, into=on_last_x("slot_words2", [P, C], U32, 4 * 2 * T))
+        quantize(3, 0, HALF_T)
+        quantize(3, HALF_T, T)
+        gather_words(2, AHEAD, AHEAD + 1, tag="x3")
 
         nc.vector.tensor_copy(slot_plane[:], plane[:].indirect(offs_sb[:]))
         row = TOKEN_ROW[MOVED_PASS]
@@ -258,8 +252,8 @@ def tile_moe_pln_lin_silu_kernel(
             nc.sync.dma_start(
                 out=moved[lo : lo + count, :].bitcast(I32), in_=slot_plane[row + lo : row + lo + count, :].bitcast(I32)
             )
-        w8_late = large("w8_late", [P, 2 * (E - WHOLE), P], I32, "plane")
-        for e in (4, 6, 2):
+        w8_late = large("w8_late", [P, 2 * E, P], I32, "plane")
+        for e in range(0, E, 2):
             load_w8_half(w8_late, 1, e, e + 2)
 
         gather_words(3, 0, FIRST)
@@ -267,6 +261,17 @@ def tile_moe_pln_lin_silu_kernel(
         gather_words(3, FIRST, E - 1)
         gather_words(3, E - 1, E)
 
+        warm = in_bank(BANKS - 1, [P, T], "warm")
+        for i in range(4):
+            nc.tensor.matmul_mx(
+                out=warm[:],
+                lhsT=w8_early[:, i, :].bitcast(E4M3),
+                lhsT_scale=w_plane[W8_ROW:P, 0:P],
+                rhs=w8_early[:, 0:4, :].rearrange("p m n -> p (m n)").bitcast(E4M3),
+                rhs_scale=w_plane[W8_ROW:P, 0:T],
+                start=i == 0,
+                stop=i == 3,
+            )
         for e in range(E):
             open_sum(0, e, (0, 1), e)
         for e in range(FIRST):
@@ -277,20 +282,11 @@ def tile_moe_pln_lin_silu_kernel(
             multiply(0, e, MOVED_PASS)
         for e in range(FIRST, E - 1):
             close_sum(0, e, 3)
-        open_sum(1, 4, (2, 3), 0)
+        open_sum(1, 0, (2, 3), 0)
         close_sum(0, E - 1, 3)
-        for e in (5, 6, 7):
-            open_sum(1, e, (2, 3), e - 4)
-        for e in (4, 5):
-            close_two(e, (0, 1))
-        for e in range(WHOLE):
-            open_sum(1, e, (0, 1), e + 4)
-            close_two(e, (2, 3))
-        for e in (6, 7):
-            close_two(e, (0, 1))
-        for e in (2, 3):
-            open_sum(1, e, (2, 3), e + 4)
-        for e in (2, 3):
+        close_two(0, (0, 1))
+        for e in range(1, E):
+            open_sum(1, e, (2, 3), e)
             close_two(e, (0, 1))
 
         fetch_half(0)

@@ -54,6 +54,7 @@ def tile_moe_pln_lin_silu_kernel(
     with ExitStack() as ctx:
         lists = ctx.enter_context(tc.tile_pool(name="lists", bufs=1))
         keep = ctx.enter_context(tc.tile_pool(name="keep", bufs=1))
+        shared = ctx.enter_context(tc.tile_pool(name="shared", bufs=1))
         psum = ctx.enter_context(tc.psum_pool(name="psum", bufs=1))
 
         def in_bank(bank, shape, name):
@@ -62,11 +63,14 @@ def tile_moe_pln_lin_silu_kernel(
         def large(name, shape, dtype, tag=None):
             return keep.tile(shape, dtype, name=name, tag=tag or name, align_bytes=ALIGN)
 
+        def on_last_x(name, shape, dtype, offset):
+            return shared.tile(shape, dtype, name=name, align_bytes=ALIGN, offset=offset)
+
         offs_sb = lists.tile([P, SLOTS // 16], U16, name="offs_sb")
         pos1_sb = lists.tile([P, T // 16], U16, name="pos1_sb")
         pos2_sb = lists.tile([P, T // 16], U16, name="pos2_sb")
 
-        x = [large("x%d" % g, [P, 4, T], F32) for g in range(PASSES)]
+        x = [large("x%d" % g, [P, 4, T], F32) for g in range(PASSES - 1)] + [on_last_x("x3", [P, 4, T], F32, 0)]
         xb = [large("xb%d" % g, [P, T, 4], BF16) for g in range(PASSES)]
         words = large("words", [P, WORD_COLUMN[0] + window_width(SLOTS - C)], I32)
         plane = large("plane", [P, window_width(SLOTS)], U8)
@@ -117,9 +121,10 @@ def tile_moe_pln_lin_silu_kernel(
                 in_=xb[g][:, lo:hi, :].rearrange("p t j -> p (t j)"),
             )
 
-        def gather_words(g, lo, hi, tag=None):
+        def gather_words(g, lo, hi, tag=None, into=None):
             entries = C * (hi - lo)
-            into = large("slot_words%d_%d" % (g, lo), [P, entries], U32, tag)
+            if into is None:
+                into = large("slot_words%d_%d" % (g, lo), [P, entries], U32, tag)
             window = words[:, WORD_COLUMN[g] : WORD_COLUMN[g] + window_width(entries)].bitcast(U32)
             nc.vector.tensor_copy(into[:], window.indirect(offs_sb[:, C * lo // 16 : C * hi // 16]))
             for e in range(lo, hi):
@@ -192,11 +197,12 @@ def tile_moe_pln_lin_silu_kernel(
         make_identity(nc, ident[:])
 
         load_x(0)
-        gate_flat = gate.rearrange("i n t -> (i n t)")[GATE_START : GATE_START + GATE_RUNS * GATE_STEP]
-        nc.scalar.dma_start(out=gate_rows[0:GATE_RUNS, :], in_=gate_flat.rearrange("(s c) -> s c", c=GATE_STEP)[:, 0:P])
         nc.sync.dma_start(offs_sb[:], offs)
-        for g in range(1, PASSES):
-            load_x(g)
+        load_x(1)
+        gate_flat = gate.rearrange("i n t -> (i n t)")[GATE_START : GATE_START + GATE_RUNS * GATE_STEP]
+        nc.sync.dma_start(out=gate_rows[0:GATE_RUNS, :], in_=gate_flat.rearrange("(s c) -> s c", c=GATE_STEP)[:, 0:P])
+        load_x(2)
+        load_x(3)
         for r in range(4):
             load_scales(W8_ROW, w8_scales, r)
             load_scales(0, w4_scales, r)
@@ -208,6 +214,14 @@ def tile_moe_pln_lin_silu_kernel(
         load_w4(0, FIRST)
         load_w4(FIRST, E)
 
+        round_and_interleave(nc.scalar.copy, 0, VECTOR_TOKENS[0], T)
+        round_and_interleave(nc.vector.tensor_copy, 0, 0, HALF_T)
+        round_and_interleave(nc.vector.tensor_copy, 0, HALF_T, VECTOR_TOKENS[0])
+        quantize(0, 0, HALF_T)
+        quantize(0, HALF_T, T)
+        round_and_interleave(nc.scalar.copy, 1, 0, HALF_T)
+        round_and_interleave(nc.scalar.copy, 1, HALF_T, T - VECTOR_TOKENS[1])
+
         gate_turned = in_bank(5, [P, P], "gate_turned")
         nc.tensor.transpose(gate_turned[:], gate_rows[:], ident[:])
         gate_columns = large("gate_columns", [P, GATE_RUNS], F32)
@@ -218,19 +232,12 @@ def tile_moe_pln_lin_silu_kernel(
                 s = 4 * i + 3 - r
                 nc.tensor.transpose(spread[i][:, r, :], gate_columns[:, s : s + 1].to_broadcast([P, P]), ident[:])
 
-        round_and_interleave(nc.scalar.copy, 0, VECTOR_TOKENS[0], T)
-        round_and_interleave(nc.vector.tensor_copy, 0, 0, HALF_T)
-        round_and_interleave(nc.vector.tensor_copy, 0, HALF_T, VECTOR_TOKENS[0])
-        quantize(0, 0, HALF_T)
-        quantize(0, HALF_T, T)
-        gates = large("gates", [P, 2, T], F32, "x0")
-        for i in range(2):
-            nc.scalar.copy(out=gates[:, i, :], in_=spread[i][:].rearrange("p r t -> p (r t)"))
-        round_and_interleave(nc.scalar.copy, 1, 0, HALF_T)
-        round_and_interleave(nc.scalar.copy, 1, HALF_T, T - VECTOR_TOKENS[1])
         for g in (2, 3):
             round_and_interleave(nc.scalar.copy, g, 0, HALF_T)
             round_and_interleave(nc.scalar.copy, g, HALF_T, T)
+        gates = on_last_x("gates", [P, 2, T], F32, 0)
+        for i in range(2):
+            nc.scalar.copy(out=gates[:, i, :], in_=spread[i][:].rearrange("p r t -> p (r t)"))
 
         gather_words(0, 0, E - 1)
         round_and_interleave(nc.vector.tensor_copy, 1, T - VECTOR_TOKENS[1], T)
@@ -244,7 +251,7 @@ def tile_moe_pln_lin_silu_kernel(
         gather_words(2, 0, AHEAD)
         quantize(3, 0, HALF_T)
         quantize(3, HALF_T, T)
-        gather_words(2, AHEAD, AHEAD + 1, tag="x3")
+        gather_words(2, AHEAD, AHEAD + 1, into=on_last_x("slot_words2", [P, C], U32, 4 * 2 * T))
 
         nc.vector.tensor_copy(slot_plane[:], plane[:].indirect(offs_sb[:]))
         row = TOKEN_ROW[MOVED_PASS]
@@ -261,7 +268,7 @@ def tile_moe_pln_lin_silu_kernel(
         gather_words(3, FIRST, E - 1)
         gather_words(3, E - 1, E)
 
-        warm = in_bank(BANKS - 1, [P, T], "warm")
+        warm = in_bank(5, [P, T], "warm")
         for i in range(4):
             nc.tensor.matmul_mx(
                 out=warm[:],

@@ -34,6 +34,7 @@ W8_ROW = 8
 VECTOR_TOKENS = (336, 128)
 AHEAD = 4
 FIRST = 5
+EARLY = 2
 
 WORD_COLUMN = (3 * T, 2 * T, T, 0)
 
@@ -73,7 +74,7 @@ def tile_moe_pln_lin_silu_kernel(
         x = [large("x%d" % g, [P, 4, T], F32) for g in range(PASSES - 1)] + [on_last_x("x3", [P, 4, T], F32, 0)]
         xb = [large("xb%d" % g, [P, T, 4], BF16) for g in range(PASSES)]
         words = large("words", [P, WORD_COLUMN[0] + window_width(SLOTS - C)], I32)
-        plane = large("plane", [P, window_width(SLOTS)], U8)
+        plane = large("plane", [P, window_width(C * FIRST)], U8)
         slot_plane = large("slot_plane", [P, SLOTS], U8)
         moved = large("moved", [P, SLOTS], U8)
         ident = large("ident", [P, P], F32)
@@ -129,6 +130,17 @@ def tile_moe_pln_lin_silu_kernel(
             nc.vector.tensor_copy(into[:], window.indirect(offs_sb[:, C * lo // 16 : C * hi // 16]))
             for e in range(lo, hi):
                 slot_words[g, e] = into[:, C * (e - lo) : C * (e - lo + 1)]
+
+        def gather_and_move_scales(lo, hi):
+            slots = slice(C * lo, C * hi)
+            window = plane[:, 0 : window_width(C * (hi - lo))]
+            nc.vector.tensor_copy(slot_plane[:, slots], window.indirect(offs_sb[:, C * lo // 16 : C * hi // 16]))
+            row = TOKEN_ROW[MOVED_PASS]
+            for first_row, count in MOVES:
+                nc.sync.dma_start(
+                    out=moved[first_row : first_row + count, slots].bitcast(I32),
+                    in_=slot_plane[row + first_row : row + first_row + count, slots].bitcast(I32),
+                )
 
         def multiply(h, e, g, start=False, stop=False):
             m, slots = 2 * e + g % 2, slice(C * e, C * (e + 1))
@@ -212,7 +224,6 @@ def tile_moe_pln_lin_silu_kernel(
         nc.sync.dma_start(pos1_sb[:], pos1)
         nc.sync.dma_start(pos2_sb[:], pos2)
         load_w4(0, FIRST)
-        load_w4(FIRST, E)
 
         round_and_interleave(nc.scalar.copy, 0, VECTOR_TOKENS[0], T)
         round_and_interleave(nc.vector.tensor_copy, 0, 0, HALF_T)
@@ -253,15 +264,12 @@ def tile_moe_pln_lin_silu_kernel(
         quantize(3, HALF_T, T)
         gather_words(2, AHEAD, AHEAD + 1, into=on_last_x("slot_words2", [P, C], U32, 4 * 2 * T))
 
-        nc.vector.tensor_copy(slot_plane[:], plane[:].indirect(offs_sb[:]))
-        row = TOKEN_ROW[MOVED_PASS]
-        for lo, count in MOVES:
-            nc.sync.dma_start(
-                out=moved[lo : lo + count, :].bitcast(I32), in_=slot_plane[row + lo : row + lo + count, :].bitcast(I32)
-            )
+        gather_and_move_scales(0, FIRST)
+        load_w4(FIRST, E)
+        gather_and_move_scales(FIRST, E)
         w8_late = large("w8_late", [P, 2 * E, P], I32, "plane")
-        for e in range(0, E, 2):
-            load_w8_half(w8_late, 1, e, e + 2)
+        load_w8_half(w8_late, 1, 0, FIRST)
+        load_w8_half(w8_late, 1, FIRST, E)
 
         gather_words(3, 0, FIRST)
         gather_words(2, AHEAD + 1, E, tag="xb3")
@@ -282,19 +290,20 @@ def tile_moe_pln_lin_silu_kernel(
         for e in range(E):
             open_sum(0, e, (0, 1), e)
         for e in range(FIRST):
-            multiply(0, e, 3)
+            multiply(0, e, MOVED_PASS)
         for e in range(FIRST):
-            close_sum(0, e, MOVED_PASS)
+            close_sum(0, e, 3)
+        for e in range(EARLY):
+            open_sum(1, e, (2, 3), e)
         for e in range(FIRST, E):
             multiply(0, e, MOVED_PASS)
-        for e in range(FIRST, E - 1):
+        for e in range(FIRST, E):
             close_sum(0, e, 3)
-        open_sum(1, 0, (2, 3), 0)
-        close_sum(0, E - 1, 3)
-        close_two(0, (0, 1))
-        for e in range(1, E):
-            open_sum(1, e, (2, 3), e)
+        for e in range(EARLY):
             close_two(e, (0, 1))
+        for e in range(EARLY, E):
+            open_sum(1, e, (0, 1), e)
+            close_two(e, (2, 3))
 
         fetch_half(0)
         added = [add_turned(0, BANKS - 2), add_turned(HALF_T, BANKS - 1)]

@@ -71,7 +71,10 @@ def tile_moe_pln_lin_silu_kernel(
         pos1_sb = lists.tile([P, T // 16], U16, name="pos1_sb")
         pos2_sb = lists.tile([P, T // 16], U16, name="pos2_sb")
 
-        x = [large("x%d" % g, [P, 4, T], F32) for g in range(PASSES - 1)] + [on_last_x("x3", [P, 4, T], F32, 0)]
+        x0 = large("x0", [P, 4, T], F32)
+        x = {(g, u): large("x%d_%d" % (g, u), [P, 4, HALF_T], F32) for g in (1, 2) for u in range(2)}
+        for u in range(2):
+            x[3, u] = on_last_x("x3_%d" % u, [P, 4, HALF_T], F32, 16 * HALF_T * u)
         xb = [large("xb%d" % g, [P, T, 4], BF16) for g in range(PASSES)]
         words = large("words", [P, WORD_COLUMN[0] + window_width(SLOTS - C)], I32)
         plane = large("plane", [P, window_width(C * FIRST)], U8)
@@ -92,7 +95,12 @@ def tile_moe_pln_lin_silu_kernel(
 
         def load_x(g):
             rows = xT[K_PASS * g : K_PASS * (g + 1), :]
-            nc.sync.dma_start(out=x[g][:], in_=rows.rearrange("(p j) t -> p j t", j=4))
+            rows = rows.rearrange("(p j) t -> p j t", j=4)
+            if g == 0:
+                nc.sync.dma_start(out=x0[:], in_=rows)
+            else:
+                for u in range(2):
+                    nc.sync.dma_start(out=x[g, u][:], in_=rows[:, :, HALF_T * u : HALF_T * (u + 1)])
 
         def load_scales(first_row, scales, r):
             rows = scales.bitcast(I32).rearrange("e a q n -> q (e a) n")
@@ -110,9 +118,10 @@ def tile_moe_pln_lin_silu_kernel(
             nc.sync.dma_start(out=w4[:, 2 * lo : 2 * hi, :], in_=w4_rows[:, 2 * lo : 2 * hi, :])
 
         def round_and_interleave(engine_copy, g, lo, hi):
+            values = x0[:, :, lo:hi] if g == 0 else x[g, lo // HALF_T][:]
             engine_copy(
                 out=xb[g][:, lo:hi, :].rearrange("p (c i) j -> p c j i", i=4),
-                in_=x[g][:, :, lo:hi].rearrange("p j (c i) -> p c j i", i=4),
+                in_=values.rearrange("p j (c i) -> p c j i", i=4),
             )
 
         def quantize(g, lo, hi):
@@ -231,7 +240,7 @@ def tile_moe_pln_lin_silu_kernel(
         quantize(0, 0, HALF_T)
         quantize(0, HALF_T, T)
         round_and_interleave(nc.scalar.copy, 1, 0, HALF_T)
-        round_and_interleave(nc.scalar.copy, 1, HALF_T, T - VECTOR_TOKENS[1])
+        round_and_interleave(nc.scalar.copy, 1, HALF_T, T)
 
         gate_turned = in_bank(5, [P, P], "gate_turned")
         nc.tensor.transpose(gate_turned[:], gate_rows[:], ident[:])
@@ -246,30 +255,29 @@ def tile_moe_pln_lin_silu_kernel(
         for g in (2, 3):
             round_and_interleave(nc.scalar.copy, g, 0, HALF_T)
             round_and_interleave(nc.scalar.copy, g, HALF_T, T)
-        gates = on_last_x("gates", [P, 2, T], F32, 0)
+        gates = on_last_x("gates", [P, 2, T], F32, 4 * T)
         for i in range(2):
             nc.scalar.copy(out=gates[:, i, :], in_=spread[i][:].rearrange("p r t -> p (r t)"))
 
         gather_words(0, 0, E - 1)
-        round_and_interleave(nc.vector.tensor_copy, 1, T - VECTOR_TOKENS[1], T)
         quantize(1, 0, HALF_T)
         quantize(1, HALF_T, T)
-        gather_words(0, E - 1, E, tag="x1")
+        gather_words(0, E - 1, E, tag="x1_1")
         gather_words(1, 0, E - 1)
         quantize(2, 0, HALF_T)
         quantize(2, HALF_T, T)
-        gather_words(1, E - 1, E, tag="x2")
+        gather_words(1, E - 1, E, tag="x2_1")
         gather_words(2, 0, AHEAD)
         quantize(3, 0, HALF_T)
         quantize(3, HALF_T, T)
-        gather_words(2, AHEAD, AHEAD + 1, into=on_last_x("slot_words2", [P, C], U32, 4 * 2 * T))
+        gather_words(2, AHEAD, AHEAD + 1, into=on_last_x("slot_words2", [P, C], U32, 4 * 3 * T))
 
         gather_and_move_scales(0, FIRST)
         load_w4(FIRST, E)
         gather_and_move_scales(FIRST, E)
         w8_late = large("w8_late", [P, 2 * E, P], I32, "plane")
-        load_w8_half(w8_late, 1, 0, FIRST)
-        load_w8_half(w8_late, 1, FIRST, E)
+        for lo, hi in ((0, 3), (3, 5), (5, 7), (7, 8)):
+            load_w8_half(w8_late, 1, lo, hi)
 
         gather_words(3, 0, FIRST)
         gather_words(2, AHEAD + 1, E, tag="xb3")
@@ -311,4 +319,5 @@ def tile_moe_pln_lin_silu_kernel(
         turn_back_and_store(added[1], HALF_T, 1)
         fetch_half(1)
         add_and_store(0, HALF_T)
-        add_and_store(HALF_T, T)
+        add_and_store(HALF_T, HALF_T + P)
+        add_and_store(HALF_T + P, T)

@@ -34,7 +34,6 @@ W8_ROW = 8
 VECTOR_TOKENS = (336, 128)
 AHEAD = 4
 FIRST = 5
-EARLY = 2
 
 WORD_COLUMN = (3 * T, 2 * T, T, 0)
 
@@ -276,7 +275,7 @@ def tile_moe_pln_lin_silu_kernel(
         load_w4(FIRST, E)
         gather_and_move_scales(FIRST, E)
         w8_late = large("w8_late", [P, 2 * E, P], I32, "plane")
-        for lo, hi in ((0, 3), (3, 5), (5, 7), (7, 8)):
+        for lo, hi in ((5, 8), (0, 2), (2, 4), (4, 5)):
             load_w8_half(w8_late, 1, lo, hi)
 
         gather_words(3, 0, FIRST)
@@ -301,16 +300,18 @@ def tile_moe_pln_lin_silu_kernel(
             multiply(0, e, MOVED_PASS)
         for e in range(FIRST):
             close_sum(0, e, 3)
-        for e in range(EARLY):
-            open_sum(1, e, (2, 3), e)
         for e in range(FIRST, E):
             multiply(0, e, MOVED_PASS)
-        for e in range(FIRST, E):
+        for e in range(FIRST, E - 1):
             close_sum(0, e, 3)
-        for e in range(EARLY):
+        open_sum(1, FIRST, (2, 3), 0)
+        close_sum(0, E - 1, 3)
+        for e in range(FIRST + 1, E):
+            open_sum(1, e, (2, 3), e - FIRST)
+        for e in range(FIRST, E):
             close_two(e, (0, 1))
-        for e in range(EARLY, E):
-            open_sum(1, e, (0, 1), e)
+        for e in range(FIRST):
+            open_sum(1, e, (0, 1), e + E - FIRST)
             close_two(e, (2, 3))
 
         fetch_half(0)

@@ -31,7 +31,8 @@ MOVED_PASS = 2
 MOVES = ((0, 64), (64, 4), (96, 4))
 W8_ROW = 8
 
-VECTOR_TOKENS = (336, 128)
+VECTOR_TOKENS = (256, 64)
+CUTS = ((0, 384, T), (0, HALF_T, T), (0, HALF_T, T), (0, HALF_T, T))
 AHEAD = 4
 FIRST = 5
 
@@ -70,8 +71,7 @@ def tile_moe_pln_lin_silu_kernel(
         pos1_sb = lists.tile([P, T // 16], U16, name="pos1_sb")
         pos2_sb = lists.tile([P, T // 16], U16, name="pos2_sb")
 
-        x0 = large("x0", [P, 4, T], F32)
-        x = {(g, u): large("x%d_%d" % (g, u), [P, 4, HALF_T], F32) for g in (1, 2) for u in range(2)}
+        x = {(g, u): large("x%d_%d" % (g, u), [P, 4, CUTS[g][u + 1] - CUTS[g][u]], F32) for g in range(3) for u in range(2)}
         for u in range(2):
             x[3, u] = on_last_x("x3_%d" % u, [P, 4, HALF_T], F32, 16 * HALF_T * u)
         xb = [large("xb%d" % g, [P, T, 4], BF16) for g in range(PASSES)]
@@ -95,11 +95,8 @@ def tile_moe_pln_lin_silu_kernel(
         def load_x(g):
             rows = xT[K_PASS * g : K_PASS * (g + 1), :]
             rows = rows.rearrange("(p j) t -> p j t", j=4)
-            if g == 0:
-                nc.sync.dma_start(out=x0[:], in_=rows)
-            else:
-                for u in range(2):
-                    nc.sync.dma_start(out=x[g, u][:], in_=rows[:, :, HALF_T * u : HALF_T * (u + 1)])
+            for u in range(2):
+                nc.sync.dma_start(out=x[g, u][:], in_=rows[:, :, CUTS[g][u] : CUTS[g][u + 1]])
 
         def load_scales(first_row, scales, r):
             rows = scales.bitcast(I32).rearrange("e a q n -> q (e a) n")
@@ -117,7 +114,8 @@ def tile_moe_pln_lin_silu_kernel(
             nc.sync.dma_start(out=w4[:, 2 * lo : 2 * hi, :], in_=w4_rows[:, 2 * lo : 2 * hi, :])
 
         def round_and_interleave(engine_copy, g, lo, hi):
-            values = x0[:, :, lo:hi] if g == 0 else x[g, lo // HALF_T][:]
+            u = 0 if lo < CUTS[g][1] else 1
+            values = x[g, u][:, :, lo - CUTS[g][u] : hi - CUTS[g][u]]
             engine_copy(
                 out=xb[g][:, lo:hi, :].rearrange("p (c i) j -> p c j i", i=4),
                 in_=values.rearrange("p j (c i) -> p c j i", i=4),
@@ -233,13 +231,14 @@ def tile_moe_pln_lin_silu_kernel(
         nc.sync.dma_start(pos2_sb[:], pos2)
         load_w4(0, FIRST)
 
-        round_and_interleave(nc.scalar.copy, 0, VECTOR_TOKENS[0], T)
+        round_and_interleave(nc.scalar.copy, 0, HALF_T, CUTS[0][1])
         round_and_interleave(nc.vector.tensor_copy, 0, 0, HALF_T)
-        round_and_interleave(nc.vector.tensor_copy, 0, HALF_T, VECTOR_TOKENS[0])
+        round_and_interleave(nc.scalar.copy, 0, CUTS[0][1], T)
         quantize(0, 0, HALF_T)
-        quantize(0, HALF_T, T)
+        quantize(0, HALF_T, CUTS[0][1])
+        quantize(0, CUTS[0][1], T)
         round_and_interleave(nc.scalar.copy, 1, 0, HALF_T)
-        round_and_interleave(nc.scalar.copy, 1, HALF_T, T)
+        round_and_interleave(nc.scalar.copy, 1, HALF_T, T - VECTOR_TOKENS[1])
 
         gate_turned = in_bank(5, [P, P], "gate_turned")
         nc.tensor.transpose(gate_turned[:], gate_rows[:], ident[:])
@@ -259,6 +258,7 @@ def tile_moe_pln_lin_silu_kernel(
             nc.scalar.copy(out=gates[:, i, :], in_=spread[i][:].rearrange("p r t -> p (r t)"))
 
         gather_words(0, 0, E - 1)
+        round_and_interleave(nc.vector.tensor_copy, 1, T - VECTOR_TOKENS[1], T)
         quantize(1, 0, HALF_T)
         quantize(1, HALF_T, T)
         gather_words(0, E - 1, E, tag="x1_1")
@@ -275,7 +275,7 @@ def tile_moe_pln_lin_silu_kernel(
         load_w4(FIRST, E)
         gather_and_move_scales(FIRST, E)
         w8_late = large("w8_late", [P, 2 * E, P], I32, "plane")
-        for lo, hi in ((5, 8), (0, 2), (2, 4), (4, 5)):
+        for lo, hi in ((5, 8), (0, 4), (4, 5)):
             load_w8_half(w8_late, 1, lo, hi)
 
         gather_words(3, 0, FIRST)

@@ -31,7 +31,7 @@ MOVED_PASS = 2
 MOVES = ((0, 64), (64, 4), (96, 4))
 W8_ROW = 8
 
-VECTOR_TOKENS = (256, 64)
+VECTOR_TOKENS = (256, 32)
 CUTS = ((0, 384, T), (0, HALF_T, T), (0, HALF_T, T), (0, HALF_T, T))
 AHEAD = 4
 FIRST = 5
@@ -186,21 +186,23 @@ def tile_moe_pln_lin_silu_kernel(
             fetch(second, h, 1, 0, HALF_T)
             fetch(second, h, 1, HALF_T, T)
 
-        def add_turned(lo, bank):
-            turned = in_bank(bank, [P, 2, P], "turned")
-            for i in range(2):
+        def add_turned(lo, bank, pieces=2):
+            turned = in_bank(bank, [P, pieces, P], "turned")
+            for i in range(pieces):
                 cols = slice(lo + P * i, lo + P * (i + 1))
                 nc.tensor.matmul(turned[:, i, :], first[0][:, cols], ident[:], start=True, stop=False, is_transpose=True)
                 nc.tensor.matmul(turned[:, i, :], second[0][:, cols], ident[:], start=False, stop=True, is_transpose=True)
-            added = large("added%d" % lo, [P, 2, P], F32)
+            added = large("added%d" % lo, [P, pieces, P], F32)
             nc.scalar.copy(out=added[:], in_=turned[:])
             return added
 
-        def turn_back_and_store(added, lo, bank):
-            back = in_bank(bank, [P, 2, P], "back")
-            for i in range(2):
+        def turn_back(added, lo, bank, pieces=2):
+            back = in_bank(bank, [P, pieces, P], "back")
+            for i in range(pieces):
                 nc.tensor.transpose(back[:, i, :], added[:, i, :], ident[:])
-            nc.scalar.copy(out=result[0][:, lo : lo + HALF_T], in_=back[:].rearrange("p i t -> p (i t)"))
+            nc.scalar.copy(out=result[0][:, lo : lo + pieces * P], in_=back[:].rearrange("p i t -> p (i t)"))
+
+        def store_first_half(lo):
             nc.scalar.dma_start(out=out[0:P, lo : lo + HALF_T], in_=result[0][:, lo : lo + HALF_T])
 
         def add_and_store(lo, hi):
@@ -233,7 +235,8 @@ def tile_moe_pln_lin_silu_kernel(
 
         round_and_interleave(nc.scalar.copy, 0, HALF_T, CUTS[0][1])
         round_and_interleave(nc.vector.tensor_copy, 0, 0, HALF_T)
-        round_and_interleave(nc.scalar.copy, 0, CUTS[0][1], T)
+        round_and_interleave(nc.scalar.copy, 0, CUTS[0][1], T - 64)
+        round_and_interleave(nc.vector.tensor_copy, 0, T - 64, T)
         quantize(0, 0, HALF_T)
         quantize(0, HALF_T, CUTS[0][1])
         quantize(0, CUTS[0][1], T)
@@ -263,19 +266,17 @@ def tile_moe_pln_lin_silu_kernel(
         quantize(1, HALF_T, T)
         gather_words(0, E - 1, E, tag="x1_1")
         gather_words(1, 0, E - 1)
-        quantize(2, 0, HALF_T)
-        quantize(2, HALF_T, T)
+        quantize(2, 0, T)
         gather_words(1, E - 1, E, tag="x2_1")
         gather_words(2, 0, AHEAD)
-        quantize(3, 0, HALF_T)
-        quantize(3, HALF_T, T)
+        quantize(3, 0, T)
         gather_words(2, AHEAD, AHEAD + 1, into=on_last_x("slot_words2", [P, C], U32, 4 * 3 * T))
 
         gather_and_move_scales(0, FIRST)
         load_w4(FIRST, E)
         gather_and_move_scales(FIRST, E)
         w8_late = large("w8_late", [P, 2 * E, P], I32, "plane")
-        for lo, hi in ((5, 8), (0, 4), (4, 5)):
+        for lo, hi in ((5, 8), (0, 2), (2, 4), (4, 5)):
             load_w8_half(w8_late, 1, lo, hi)
 
         gather_words(3, 0, FIRST)
@@ -315,9 +316,12 @@ def tile_moe_pln_lin_silu_kernel(
             close_two(e, (2, 3))
 
         fetch_half(0)
-        added = [add_turned(0, BANKS - 2), add_turned(HALF_T, BANKS - 1)]
-        turn_back_and_store(added[0], 0, 0)
-        turn_back_and_store(added[1], HALF_T, 1)
+        added = [add_turned(0, BANKS - 2), add_turned(HALF_T, BANKS - 1, 1), add_turned(HALF_T + P, BANKS - 2, 1)]
+        turn_back(added[0], 0, 0)
+        store_first_half(0)
+        turn_back(added[1], HALF_T, 1, 1)
+        turn_back(added[2], HALF_T + P, 2, 1)
+        store_first_half(HALF_T)
         fetch_half(1)
         add_and_store(0, HALF_T)
         add_and_store(HALF_T, HALF_T + P)

@@ -133,7 +133,7 @@ def tile_moe_pln_lin_silu_kernel(
             if into is None:
                 into = large("slot_words%d_%d" % (g, lo), [P, entries], U32, tag)
             window = words[:, WORD_COLUMN[g] : WORD_COLUMN[g] + window_width(entries)].bitcast(U32)
-            nc.vector.tensor_copy(into[:], window.indirect(offs_sb[:, C * lo // 16 : C * hi // 16]))
+            nc.vector.tensor_copy(into[:, :], window.indirect(offs_sb[:, C * lo // 16 : C * hi // 16]))
             for e in range(lo, hi):
                 slot_words[g, e] = into[:, C * (e - lo) : C * (e - lo + 1)]
 
@@ -276,13 +276,13 @@ def tile_moe_pln_lin_silu_kernel(
         load_w4(FIRST, E)
         gather_and_move_scales(FIRST, E)
         w8_late = large("w8_late", [P, 2 * E, P], I32, "plane")
-        for lo, hi in ((5, 8), (0, 2), (2, 4), (4, 5)):
+        for lo, hi in ((5, 8), (0, 2), (2, 5)):
             load_w8_half(w8_late, 1, lo, hi)
 
-        gather_words(3, 0, FIRST)
-        gather_words(2, AHEAD + 1, E, tag="xb3")
-        gather_words(3, FIRST, E - 1)
-        gather_words(3, E - 1, E)
+        gather_words(3, 0, E)
+        rest = large("rest", [P, C * (E - AHEAD - 1)], U32, "xb3")
+        gather_words(2, AHEAD + 1, E - 1, into=rest[:, 0 : C * (E - AHEAD - 2)])
+        gather_words(2, E - 1, E, into=rest[:, C * (E - AHEAD - 2) :])
 
         warm = in_bank(5, [P, T], "warm")
         for i in range(4):
@@ -302,11 +302,11 @@ def tile_moe_pln_lin_silu_kernel(
         for e in range(FIRST):
             close_sum(0, e, 3)
         for e in range(FIRST, E):
-            multiply(0, e, MOVED_PASS)
+            multiply(0, e, 3)
         for e in range(FIRST, E - 1):
-            close_sum(0, e, 3)
+            close_sum(0, e, MOVED_PASS)
         open_sum(1, FIRST, (2, 3), 0)
-        close_sum(0, E - 1, 3)
+        close_sum(0, E - 1, MOVED_PASS)
         for e in range(FIRST + 1, E):
             open_sum(1, e, (2, 3), e - FIRST)
         for e in range(FIRST, E):
@@ -316,7 +316,7 @@ def tile_moe_pln_lin_silu_kernel(
             close_two(e, (2, 3))
 
         fetch_half(0)
-        added = [add_turned(0, BANKS - 2), add_turned(HALF_T, BANKS - 1, 1), add_turned(HALF_T + P, BANKS - 2, 1)]
+        added = [add_turned(0, BANKS - 3), add_turned(HALF_T, BANKS - 2, 1), add_turned(HALF_T + P, BANKS - 1, 1)]
         turn_back(added[0], 0, 0)
         store_first_half(0)
         turn_back(added[1], HALF_T, 1, 1)

@@ -26,13 +26,13 @@ HALF_T = T // 2
 BANKS = 8
 ALIGN = 256
 
-TOKEN_ROW = (4, 8, 12, 0)
-MOVED_PASS = 2
+TOKEN_ROW = (4, 8, 0, 12)
+MOVED_PASS = 3
 MOVES = ((0, 64), (64, 4), (96, 4))
 W8_ROW = 8
 
-VECTOR_TOKENS = (256, 32)
-CUTS = ((0, 384, T), (0, HALF_T, T), (0, HALF_T, T), (0, HALF_T, T))
+VECTOR_TOKENS = (256, 64)
+CUTS = ((0, HALF_T, 384, T), (0, HALF_T, T), (0, HALF_T, T), (0, HALF_T, T))
 AHEAD = 4
 FIRST = 5
 
@@ -71,12 +71,12 @@ def tile_moe_pln_lin_silu_kernel(
         pos1_sb = lists.tile([P, T // 16], U16, name="pos1_sb")
         pos2_sb = lists.tile([P, T // 16], U16, name="pos2_sb")
 
-        x = {(g, u): large("x%d_%d" % (g, u), [P, 4, CUTS[g][u + 1] - CUTS[g][u]], F32) for g in range(3) for u in range(2)}
+        x = {(g, u): large("x%d_%d" % (g, u), [P, 4, CUTS[g][u + 1] - CUTS[g][u]], F32) for g in range(3) for u in range(len(CUTS[g]) - 1)}
         for u in range(2):
             x[3, u] = on_last_x("x3_%d" % u, [P, 4, HALF_T], F32, 16 * HALF_T * u)
         xb = [large("xb%d" % g, [P, T, 4], BF16) for g in range(PASSES)]
         words = large("words", [P, WORD_COLUMN[0] + window_width(SLOTS - C)], I32)
-        plane = large("plane", [P, window_width(C * FIRST)], U8)
+        plane = large("plane", [P, window_width(SLOTS)], U8)
         slot_plane = large("slot_plane", [P, SLOTS], U8)
         moved = large("moved", [P, SLOTS], U8)
         ident = large("ident", [P, P], F32)
@@ -95,7 +95,7 @@ def tile_moe_pln_lin_silu_kernel(
         def load_x(g):
             rows = xT[K_PASS * g : K_PASS * (g + 1), :]
             rows = rows.rearrange("(p j) t -> p j t", j=4)
-            for u in range(2):
+            for u in range(len(CUTS[g]) - 1):
                 nc.sync.dma_start(out=x[g, u][:], in_=rows[:, :, CUTS[g][u] : CUTS[g][u + 1]])
 
         def load_scales(first_row, scales, r):
@@ -114,7 +114,7 @@ def tile_moe_pln_lin_silu_kernel(
             nc.sync.dma_start(out=w4[:, 2 * lo : 2 * hi, :], in_=w4_rows[:, 2 * lo : 2 * hi, :])
 
         def round_and_interleave(engine_copy, g, lo, hi):
-            u = 0 if lo < CUTS[g][1] else 1
+            u = len([c for c in CUTS[g][1:] if c <= lo])
             values = x[g, u][:, :, lo - CUTS[g][u] : hi - CUTS[g][u]]
             engine_copy(
                 out=xb[g][:, lo:hi, :].rearrange("p (c i) j -> p c j i", i=4),
@@ -228,18 +228,21 @@ def tile_moe_pln_lin_silu_kernel(
             load_scales(0, w4_scales, r)
         load_w8_half(w8_early, 0, 0, E // 2)
         nc.sync.dma_start(out=bias[:], in_=b.rearrange("(h p) e -> p h e", h=2))
-        load_w8_half(w8_early, 0, E // 2, E)
+        load_w8_half(w8_early, 0, 4, 6)
+        load_w8_half(w8_early, 0, 6, E)
         nc.sync.dma_start(pos1_sb[:], pos1)
         nc.sync.dma_start(pos2_sb[:], pos2)
-        load_w4(0, FIRST)
+        load_w4(0, 3)
+        load_w4(3, 6)
 
-        round_and_interleave(nc.scalar.copy, 0, HALF_T, CUTS[0][1])
-        round_and_interleave(nc.vector.tensor_copy, 0, 0, HALF_T)
-        round_and_interleave(nc.scalar.copy, 0, CUTS[0][1], T - 64)
-        round_and_interleave(nc.vector.tensor_copy, 0, T - 64, T)
+        round_and_interleave(nc.scalar.copy, 0, 176, HALF_T)
+        round_and_interleave(nc.vector.tensor_copy, 0, 0, 176)
         quantize(0, 0, HALF_T)
-        quantize(0, HALF_T, CUTS[0][1])
-        quantize(0, CUTS[0][1], T)
+        round_and_interleave(nc.scalar.copy, 0, HALF_T, 384)
+        round_and_interleave(nc.scalar.copy, 0, 384 + 88, T)
+        round_and_interleave(nc.vector.tensor_copy, 0, 384, 384 + 88)
+        quantize(0, HALF_T, 384)
+        quantize(0, 384, T)
         round_and_interleave(nc.scalar.copy, 1, 0, HALF_T)
         round_and_interleave(nc.scalar.copy, 1, HALF_T, T - VECTOR_TOKENS[1])
 
@@ -272,9 +275,8 @@ def tile_moe_pln_lin_silu_kernel(
         quantize(3, 0, T)
         gather_words(2, AHEAD, AHEAD + 1, into=on_last_x("slot_words2", [P, C], U32, 4 * 3 * T))
 
-        gather_and_move_scales(0, FIRST)
-        load_w4(FIRST, E)
-        gather_and_move_scales(FIRST, E)
+        gather_and_move_scales(0, E)
+        load_w4(6, E)
         w8_late = large("w8_late", [P, 2 * E, P], I32, "plane")
         for lo, hi in ((5, 8), (0, 2), (2, 5)):
             load_w8_half(w8_late, 1, lo, hi)
@@ -298,15 +300,15 @@ def tile_moe_pln_lin_silu_kernel(
         for e in range(E):
             open_sum(0, e, (0, 1), e)
         for e in range(FIRST):
-            multiply(0, e, MOVED_PASS)
+            multiply(0, e, 2)
         for e in range(FIRST):
             close_sum(0, e, 3)
         for e in range(FIRST, E):
             multiply(0, e, 3)
         for e in range(FIRST, E - 1):
-            close_sum(0, e, MOVED_PASS)
+            close_sum(0, e, 2)
         open_sum(1, FIRST, (2, 3), 0)
-        close_sum(0, E - 1, MOVED_PASS)
+        close_sum(0, E - 1, 2)
         for e in range(FIRST + 1, E):
             open_sum(1, e, (2, 3), e - FIRST)
         for e in range(FIRST, E):

@@ -230,10 +230,8 @@ def tile_moe_pln_lin_silu_kernel(
         nc.sync.dma_start(out=bias[:], in_=b.rearrange("(h p) e -> p h e", h=2))
         load_w8_half(w8_early, 0, 4, 6)
         load_w8_half(w8_early, 0, 6, E)
-        nc.sync.dma_start(pos1_sb[:], pos1)
-        nc.sync.dma_start(pos2_sb[:], pos2)
-        load_w4(0, 3)
-        load_w4(3, 6)
+        load_w4(0, 4)
+        load_w4(4, 7)
 
         round_and_interleave(nc.scalar.copy, 0, 176, HALF_T)
         round_and_interleave(nc.vector.tensor_copy, 0, 0, 176)
@@ -276,7 +274,9 @@ def tile_moe_pln_lin_silu_kernel(
         gather_words(2, AHEAD, AHEAD + 1, into=on_last_x("slot_words2", [P, C], U32, 4 * 3 * T))
 
         gather_and_move_scales(0, E)
-        load_w4(6, E)
+        load_w4(7, E)
+        nc.sync.dma_start(pos1_sb[:], pos1)
+        nc.sync.dma_start(pos2_sb[:], pos2)
         w8_late = large("w8_late", [P, 2 * E, P], I32, "plane")
         for lo, hi in ((5, 8), (0, 2), (2, 5)):
             load_w8_half(w8_late, 1, lo, hi)

@@ -230,7 +230,8 @@ def tile_moe_pln_lin_silu_kernel(
         nc.sync.dma_start(out=bias[:], in_=b.rearrange("(h p) e -> p h e", h=2))
         load_w8_half(w8_early, 0, 4, 6)
         load_w8_half(w8_early, 0, 6, E)
-        load_w4(0, 4)
+        load_w4(0, 2)
+        load_w4(2, 4)
         load_w4(4, 7)
 
         round_and_interleave(nc.scalar.copy, 0, 176, HALF_T)

@@ -327,5 +327,4 @@ def tile_moe_pln_lin_silu_kernel(
         store_first_half(HALF_T)
         fetch_half(1)
         add_and_store(0, HALF_T)
-        add_and_store(HALF_T, HALF_T + P)
-        add_and_store(HALF_T + P, T)
+        add_and_store(HALF_T, T)

@@ -282,10 +282,9 @@ def tile_moe_pln_lin_silu_kernel(
         for lo, hi in ((5, 8), (0, 2), (2, 5)):
             load_w8_half(w8_late, 1, lo, hi)
 
-        gather_words(3, 0, E)
-        rest = large("rest", [P, C * (E - AHEAD - 1)], U32, "xb3")
-        gather_words(2, AHEAD + 1, E - 1, into=rest[:, 0 : C * (E - AHEAD - 2)])
-        gather_words(2, E - 1, E, into=rest[:, C * (E - AHEAD - 2) :])
+        gather_words(3, 0, E - 1)
+        gather_words(2, AHEAD + 1, E, tag="xb3")
+        gather_words(3, E - 1, E)
 
         warm = in_bank(5, [P, T], "warm")
         for i in range(4):
@@ -304,12 +303,13 @@ def tile_moe_pln_lin_silu_kernel(
             multiply(0, e, 2)
         for e in range(FIRST):
             close_sum(0, e, 3)
-        for e in range(FIRST, E):
+        for e in range(FIRST, E - 1):
             multiply(0, e, 3)
         for e in range(FIRST, E - 1):
             close_sum(0, e, 2)
+        multiply(0, E - 1, 2)
         open_sum(1, FIRST, (2, 3), 0)
-        close_sum(0, E - 1, 2)
+        close_sum(0, E - 1, 3)
         for e in range(FIRST + 1, E):
             open_sum(1, e, (2, 3), e - FIRST)
         for e in range(FIRST, E):

@@ -23,7 +23,9 @@ P = 128
 PASSES = 4
 K_PASS = K // PASSES
 HALF_T = T // 2
+LAST_QUARTER = T - T // 4
 BANKS = 8
+LAST = E - 1
 ALIGN = 256
 
 TOKEN_ROW = (4, 8, 0, 12)
@@ -31,10 +33,11 @@ MOVED_PASS = 3
 MOVES = ((0, 64), (64, 4), (96, 4))
 W8_ROW = 8
 
-VECTOR_TOKENS = (256, 64)
-CUTS = ((0, HALF_T, 384, T), (0, HALF_T, T), (0, HALF_T, T), (0, HALF_T, T))
+CUTS = ((0, HALF_T, LAST_QUARTER, T), (0, HALF_T, T), (0, HALF_T, T), (0, HALF_T, T))
+VECTOR_FIRST_PIECE, VECTOR_LAST_PIECE, VECTOR_PASS_1 = 176, 88, 64
 AHEAD = 4
-FIRST = 5
+EARLY = AHEAD + 1
+ADD_RUNS = ((0, 2), (2, 1), (3, 1))
 
 WORD_COLUMN = (3 * T, 2 * T, T, 0)
 
@@ -71,9 +74,13 @@ def tile_moe_pln_lin_silu_kernel(
         pos1_sb = lists.tile([P, T // 16], U16, name="pos1_sb")
         pos2_sb = lists.tile([P, T // 16], U16, name="pos2_sb")
 
-        x = {(g, u): large("x%d_%d" % (g, u), [P, 4, CUTS[g][u + 1] - CUTS[g][u]], F32) for g in range(3) for u in range(len(CUTS[g]) - 1)}
+        x = {}
+        for g in range(PASSES - 1):
+            for u in range(len(CUTS[g]) - 1):
+                x[g, u] = large("x%d_%d" % (g, u), [P, 4, CUTS[g][u + 1] - CUTS[g][u]], F32)
+        piece_bytes = 4 * 4 * HALF_T
         for u in range(2):
-            x[3, u] = on_last_x("x3_%d" % u, [P, 4, HALF_T], F32, 16 * HALF_T * u)
+            x[3, u] = on_last_x("x3_%d" % u, [P, 4, HALF_T], F32, piece_bytes * u)
         xb = [large("xb%d" % g, [P, T, 4], BF16) for g in range(PASSES)]
         words = large("words", [P, WORD_COLUMN[0] + window_width(SLOTS - C)], I32)
         plane = large("plane", [P, window_width(SLOTS)], U8)
@@ -93,8 +100,7 @@ def tile_moe_pln_lin_silu_kernel(
         sums = {}
 
         def load_x(g):
-            rows = xT[K_PASS * g : K_PASS * (g + 1), :]
-            rows = rows.rearrange("(p j) t -> p j t", j=4)
+            rows = xT[K_PASS * g : K_PASS * (g + 1), :].rearrange("(p j) t -> p j t", j=4)
             for u in range(len(CUTS[g]) - 1):
                 nc.sync.dma_start(out=x[g, u][:], in_=rows[:, :, CUTS[g][u] : CUTS[g][u + 1]])
 
@@ -107,18 +113,16 @@ def tile_moe_pln_lin_silu_kernel(
         w4_rows = w4_words.rearrange("e a p n -> p (e a) n").bitcast(I32)
 
         def load_w8_half(into, h, lo, hi):
-            matrices = into[:, 2 * lo : 2 * hi, :]
-            nc.sync.dma_start(out=matrices, in_=w8_rows[:, 2 * lo : 2 * hi, P * h : P * (h + 1)])
+            nc.sync.dma_start(out=into[:, 2 * lo : 2 * hi, :], in_=w8_rows[:, 2 * lo : 2 * hi, P * h : P * (h + 1)])
 
         def load_w4(lo, hi):
             nc.sync.dma_start(out=w4[:, 2 * lo : 2 * hi, :], in_=w4_rows[:, 2 * lo : 2 * hi, :])
 
         def round_and_interleave(engine_copy, g, lo, hi):
-            u = len([c for c in CUTS[g][1:] if c <= lo])
-            values = x[g, u][:, :, lo - CUTS[g][u] : hi - CUTS[g][u]]
+            u = len([cut for cut in CUTS[g][1:] if cut <= lo])
             engine_copy(
                 out=xb[g][:, lo:hi, :].rearrange("p (c i) j -> p c j i", i=4),
-                in_=values.rearrange("p j (c i) -> p c j i", i=4),
+                in_=x[g, u][:, :, lo - CUTS[g][u] : hi - CUTS[g][u]].rearrange("p j (c i) -> p c j i", i=4),
             )
 
         def quantize(g, lo, hi):
@@ -133,20 +137,9 @@ def tile_moe_pln_lin_silu_kernel(
             if into is None:
                 into = large("slot_words%d_%d" % (g, lo), [P, entries], U32, tag)
             window = words[:, WORD_COLUMN[g] : WORD_COLUMN[g] + window_width(entries)].bitcast(U32)
-            nc.vector.tensor_copy(into[:, :], window.indirect(offs_sb[:, C * lo // 16 : C * hi // 16]))
+            nc.vector.tensor_copy(into[:], window.indirect(offs_sb[:, C * lo // 16 : C * hi // 16]))
             for e in range(lo, hi):
                 slot_words[g, e] = into[:, C * (e - lo) : C * (e - lo + 1)]
-
-        def gather_and_move_scales(lo, hi):
-            slots = slice(C * lo, C * hi)
-            window = plane[:, 0 : window_width(C * (hi - lo))]
-            nc.vector.tensor_copy(slot_plane[:, slots], window.indirect(offs_sb[:, C * lo // 16 : C * hi // 16]))
-            row = TOKEN_ROW[MOVED_PASS]
-            for first_row, count in MOVES:
-                nc.sync.dma_start(
-                    out=moved[first_row : first_row + count, slots].bitcast(I32),
-                    in_=slot_plane[row + first_row : row + first_row + count, slots].bitcast(I32),
-                )
 
         def multiply(h, e, g, start=False, stop=False):
             m, slots = 2 * e + g % 2, slice(C * e, C * (e + 1))
@@ -173,7 +166,7 @@ def tile_moe_pln_lin_silu_kernel(
             multiply(h, e, g, stop=True)
             nc.scalar.activation(y[h][:, C * e : C * (e + 1)], sums[h, e][:], SILU, bias=bias[:, h, e : e + 1])
 
-        def close_two(e, passes):
+        def close_second_half(e, passes):
             multiply(1, e, passes[0])
             close_sum(1, e, passes[1])
 
@@ -186,28 +179,21 @@ def tile_moe_pln_lin_silu_kernel(
             fetch(second, h, 1, 0, HALF_T)
             fetch(second, h, 1, HALF_T, T)
 
-        def add_turned(lo, bank, pieces=2):
-            turned = in_bank(bank, [P, pieces, P], "turned")
-            for i in range(pieces):
-                cols = slice(lo + P * i, lo + P * (i + 1))
+        def add_turned(block, blocks, bank):
+            turned = in_bank(bank, [P, blocks, P], "turned")
+            for i in range(blocks):
+                cols = slice(P * (block + i), P * (block + i + 1))
                 nc.tensor.matmul(turned[:, i, :], first[0][:, cols], ident[:], start=True, stop=False, is_transpose=True)
                 nc.tensor.matmul(turned[:, i, :], second[0][:, cols], ident[:], start=False, stop=True, is_transpose=True)
-            added = large("added%d" % lo, [P, pieces, P], F32)
+            added = large("added%d" % block, [P, blocks, P], F32)
             nc.scalar.copy(out=added[:], in_=turned[:])
             return added
 
-        def turn_back(added, lo, bank, pieces=2):
-            back = in_bank(bank, [P, pieces, P], "back")
-            for i in range(pieces):
+        def turn_back(added, block, blocks, bank):
+            back = in_bank(bank, [P, blocks, P], "back")
+            for i in range(blocks):
                 nc.tensor.transpose(back[:, i, :], added[:, i, :], ident[:])
-            nc.scalar.copy(out=result[0][:, lo : lo + pieces * P], in_=back[:].rearrange("p i t -> p (i t)"))
-
-        def store_first_half(lo):
-            nc.scalar.dma_start(out=out[0:P, lo : lo + HALF_T], in_=result[0][:, lo : lo + HALF_T])
-
-        def add_and_store(lo, hi):
-            nc.vector.tensor_add(result[1][:, lo:hi], first[1][:, lo:hi], second[1][:, lo:hi])
-            nc.sync.dma_start(out=out[P:N, lo:hi], in_=result[1][:, lo:hi])
+            nc.scalar.copy(out=result[0][:, P * block : P * (block + blocks)], in_=back[:].rearrange("p i t -> p (i t)"))
 
         nc.vector.memset(gate_rows[:], 0.0)
         nc.vector.memset(w_plane[:].bitcast(I32), 0)
@@ -226,30 +212,30 @@ def tile_moe_pln_lin_silu_kernel(
         for r in range(4):
             load_scales(W8_ROW, w8_scales, r)
             load_scales(0, w4_scales, r)
-        load_w8_half(w8_early, 0, 0, E // 2)
+        load_w8_half(w8_early, 0, 0, 4)
         nc.sync.dma_start(out=bias[:], in_=b.rearrange("(h p) e -> p h e", h=2))
         load_w8_half(w8_early, 0, 4, 6)
         load_w8_half(w8_early, 0, 6, E)
         load_w4(0, 2)
         load_w4(2, 4)
-        load_w4(4, 7)
+        load_w4(4, LAST)
 
-        round_and_interleave(nc.scalar.copy, 0, 176, HALF_T)
-        round_and_interleave(nc.vector.tensor_copy, 0, 0, 176)
+        round_and_interleave(nc.scalar.copy, 0, VECTOR_FIRST_PIECE, HALF_T)
+        round_and_interleave(nc.vector.tensor_copy, 0, 0, VECTOR_FIRST_PIECE)
         quantize(0, 0, HALF_T)
-        round_and_interleave(nc.scalar.copy, 0, HALF_T, 384)
-        round_and_interleave(nc.scalar.copy, 0, 384 + 88, T)
-        round_and_interleave(nc.vector.tensor_copy, 0, 384, 384 + 88)
-        quantize(0, HALF_T, 384)
-        quantize(0, 384, T)
+        round_and_interleave(nc.scalar.copy, 0, HALF_T, LAST_QUARTER)
+        round_and_interleave(nc.scalar.copy, 0, LAST_QUARTER + VECTOR_LAST_PIECE, T)
+        round_and_interleave(nc.vector.tensor_copy, 0, LAST_QUARTER, LAST_QUARTER + VECTOR_LAST_PIECE)
+        quantize(0, HALF_T, LAST_QUARTER)
+        quantize(0, LAST_QUARTER, T)
         round_and_interleave(nc.scalar.copy, 1, 0, HALF_T)
-        round_and_interleave(nc.scalar.copy, 1, HALF_T, T - VECTOR_TOKENS[1])
+        round_and_interleave(nc.scalar.copy, 1, HALF_T, T - VECTOR_PASS_1)
 
-        gate_turned = in_bank(5, [P, P], "gate_turned")
+        gate_turned = in_bank(BANKS - 3, [P, P], "gate_turned")
         nc.tensor.transpose(gate_turned[:], gate_rows[:], ident[:])
         gate_columns = large("gate_columns", [P, GATE_RUNS], F32)
         nc.scalar.copy(out=gate_columns[:], in_=gate_turned[:, 0:GATE_RUNS])
-        spread = [in_bank(6 + i, [P, 4, P], "spread") for i in range(2)]
+        spread = [in_bank(BANKS - 2 + i, [P, 4, P], "spread") for i in range(2)]
         for i in range(2):
             for r in range(4):
                 s = 4 * i + 3 - r
@@ -258,73 +244,70 @@ def tile_moe_pln_lin_silu_kernel(
         for g in (2, 3):
             round_and_interleave(nc.scalar.copy, g, 0, HALF_T)
             round_and_interleave(nc.scalar.copy, g, HALF_T, T)
-        gates = on_last_x("gates", [P, 2, T], F32, 4 * T)
+        gates = on_last_x("gates", [P, 2, T], F32, piece_bytes // 2)
         for i in range(2):
             nc.scalar.copy(out=gates[:, i, :], in_=spread[i][:].rearrange("p r t -> p (r t)"))
 
-        gather_words(0, 0, E - 1)
-        round_and_interleave(nc.vector.tensor_copy, 1, T - VECTOR_TOKENS[1], T)
+        gather_words(0, 0, LAST)
+        round_and_interleave(nc.vector.tensor_copy, 1, T - VECTOR_PASS_1, T)
         quantize(1, 0, HALF_T)
         quantize(1, HALF_T, T)
-        gather_words(0, E - 1, E, tag="x1_1")
-        gather_words(1, 0, E - 1)
+        gather_words(0, LAST, E, tag="x1_1")
+        gather_words(1, 0, LAST)
         quantize(2, 0, T)
-        gather_words(1, E - 1, E, tag="x2_1")
+        gather_words(1, LAST, E, tag="x2_1")
         gather_words(2, 0, AHEAD)
         quantize(3, 0, T)
-        gather_words(2, AHEAD, AHEAD + 1, into=on_last_x("slot_words2", [P, C], U32, 4 * 3 * T))
+        gather_words(2, AHEAD, EARLY, into=on_last_x("slot_words2", [P, C], U32, 3 * piece_bytes // 2))
 
-        gather_and_move_scales(0, E)
-        load_w4(7, E)
+        nc.vector.tensor_copy(slot_plane[:], plane[:].indirect(offs_sb[:]))
+        row = TOKEN_ROW[MOVED_PASS]
+        for lo, count in MOVES:
+            nc.sync.dma_start(
+                out=moved[lo : lo + count, :].bitcast(I32), in_=slot_plane[row + lo : row + lo + count, :].bitcast(I32)
+            )
+        load_w4(LAST, E)
         nc.sync.dma_start(pos1_sb[:], pos1)
         nc.sync.dma_start(pos2_sb[:], pos2)
         w8_late = large("w8_late", [P, 2 * E, P], I32, "plane")
-        for lo, hi in ((5, 8), (0, 2), (2, 5)):
-            load_w8_half(w8_late, 1, lo, hi)
+        load_w8_half(w8_late, 1, EARLY, E)
+        load_w8_half(w8_late, 1, 0, EARLY - len(ADD_RUNS))
+        load_w8_half(w8_late, 1, EARLY - len(ADD_RUNS), EARLY)
 
-        gather_words(3, 0, E - 1)
-        gather_words(2, AHEAD + 1, E, tag="xb3")
-        gather_words(3, E - 1, E)
+        gather_words(3, 0, LAST)
+        gather_words(2, EARLY, E, tag="xb3")
+        gather_words(3, LAST, E)
 
-        warm = in_bank(5, [P, T], "warm")
-        for i in range(4):
-            nc.tensor.matmul_mx(
-                out=warm[:],
-                lhsT=w8_early[:, i, :].bitcast(E4M3),
-                lhsT_scale=w_plane[W8_ROW:P, 0:P],
-                rhs=w8_early[:, 0:4, :].rearrange("p m n -> p (m n)").bitcast(E4M3),
-                rhs_scale=w_plane[W8_ROW:P, 0:T],
-                start=i == 0,
-                stop=i == 3,
-            )
         for e in range(E):
             open_sum(0, e, (0, 1), e)
-        for e in range(FIRST):
+        for e in range(EARLY):
             multiply(0, e, 2)
-        for e in range(FIRST):
+        for e in range(EARLY):
             close_sum(0, e, 3)
-        for e in range(FIRST, E - 1):
+        for e in range(EARLY, LAST):
             multiply(0, e, 3)
-        for e in range(FIRST, E - 1):
+        for e in range(EARLY, LAST):
             close_sum(0, e, 2)
-        multiply(0, E - 1, 2)
-        open_sum(1, FIRST, (2, 3), 0)
-        close_sum(0, E - 1, 3)
-        for e in range(FIRST + 1, E):
-            open_sum(1, e, (2, 3), e - FIRST)
-        for e in range(FIRST, E):
-            close_two(e, (0, 1))
-        for e in range(FIRST):
-            open_sum(1, e, (0, 1), e + E - FIRST)
-            close_two(e, (2, 3))
+        multiply(0, LAST, 2)
+        open_sum(1, EARLY, (2, 3), 0)
+        close_sum(0, LAST, 3)
+        for e in range(EARLY + 1, E):
+            open_sum(1, e, (2, 3), e - EARLY)
+        for e in range(EARLY, E):
+            close_second_half(e, (0, 1))
+        for e in range(EARLY):
+            open_sum(1, e, (0, 1), e + E - EARLY)
+            close_second_half(e, (2, 3))
 
         fetch_half(0)
-        added = [add_turned(0, BANKS - 3), add_turned(HALF_T, BANKS - 2, 1), add_turned(HALF_T + P, BANKS - 1, 1)]
-        turn_back(added[0], 0, 0)
-        store_first_half(0)
-        turn_back(added[1], HALF_T, 1, 1)
-        turn_back(added[2], HALF_T + P, 2, 1)
-        store_first_half(HALF_T)
+        added = [add_turned(block, blocks, BANKS - 3 + i) for i, (block, blocks) in enumerate(ADD_RUNS)]
+        for i, (block, blocks) in enumerate(ADD_RUNS):
+            turn_back(added[i], block, blocks, i)
+            end = P * (block + blocks)
+            if end % HALF_T == 0:
+                nc.scalar.dma_start(out=out[0:P, end - HALF_T : end], in_=result[0][:, end - HALF_T : end])
         fetch_half(1)
-        add_and_store(0, HALF_T)
-        add_and_store(HALF_T, T)
+        for lo in (0, HALF_T):
+            tokens = slice(lo, lo + HALF_T)
+            nc.vector.tensor_add(result[1][:, tokens], first[1][:, tokens], second[1][:, tokens])
+            nc.sync.dma_start(out=out[P:N, tokens], in_=result[1][:, tokens])

@@ -289,9 +289,8 @@ def tile_moe_pln_lin_silu_kernel(
         for e in range(EARLY, LAST):
             close_sum(0, e, 2)
         multiply(0, LAST, 2)
-        open_sum(1, EARLY, (2, 3), 0)
         close_sum(0, LAST, 3)
-        for e in range(EARLY + 1, E):
+        for e in range(EARLY, E):
             open_sum(1, e, (2, 3), e - EARLY)
         for e in range(EARLY, E):
             close_second_half(e, (0, 1))

@@ -83,7 +83,7 @@ def tile_moe_pln_lin_silu_kernel(
             x[3, u] = on_last_x("x3_%d" % u, [P, 4, HALF_T], F32, piece_bytes * u)
         xb = [large("xb%d" % g, [P, T, 4], BF16) for g in range(PASSES)]
         words = large("words", [P, WORD_COLUMN[0] + window_width(SLOTS - C)], I32)
-        plane = large("plane", [P, window_width(SLOTS)], U8)
+        plane = large("plane", [P, window_width(SLOTS // 2)], U8)
         slot_plane = large("slot_plane", [P, SLOTS], U8)
         moved = large("moved", [P, SLOTS], U8)
         ident = large("ident", [P, P], F32)
@@ -260,7 +260,9 @@ def tile_moe_pln_lin_silu_kernel(
         quantize(3, 0, T)
         gather_words(2, AHEAD, EARLY, into=on_last_x("slot_words2", [P, C], U32, 3 * piece_bytes // 2))
 
-        nc.vector.tensor_copy(slot_plane[:], plane[:].indirect(offs_sb[:]))
+        for lo in (0, SLOTS // 2):
+            places = offs_sb[:, lo // 16 : (lo + SLOTS // 2) // 16]
+            nc.vector.tensor_copy(slot_plane[:, lo : lo + SLOTS // 2], plane[:].indirect(places))
         row = TOKEN_ROW[MOVED_PASS]
         for lo, count in MOVES:
             nc.sync.dma_start(

@@ -34,10 +34,11 @@ MOVES = ((0, 64), (64, 4), (96, 4))
 W8_ROW = 8
 
 CUTS = ((0, HALF_T, LAST_QUARTER, T), (0, HALF_T, T), (0, HALF_T, T), (0, HALF_T, T))
-VECTOR_FIRST_PIECE, VECTOR_LAST_PIECE, VECTOR_PASS_1 = 176, 88, 64
+VECTOR_FIRST_PIECE, VECTOR_LAST_PIECE = 176, 88
 AHEAD = 4
 EARLY = AHEAD + 1
 ADD_RUNS = ((0, 2), (2, 1), (3, 1))
+LATE_CUTS = (0, 2, E - len(ADD_RUNS), E)
 
 WORD_COLUMN = (3 * T, 2 * T, T, 0)
 
@@ -82,7 +83,7 @@ def tile_moe_pln_lin_silu_kernel(
         for u in range(2):
             x[3, u] = on_last_x("x3_%d" % u, [P, 4, HALF_T], F32, piece_bytes * u)
         xb = [large("xb%d" % g, [P, T, 4], BF16) for g in range(PASSES)]
-        words = large("words", [P, WORD_COLUMN[0] + window_width(SLOTS - C)], I32)
+        words = large("words", [P, WORD_COLUMN[0] + window_width(SLOTS)], I32)
         plane = large("plane", [P, window_width(SLOTS // 2)], U8)
         slot_plane = large("slot_plane", [P, SLOTS], U8)
         moved = large("moved", [P, SLOTS], U8)
@@ -212,13 +213,13 @@ def tile_moe_pln_lin_silu_kernel(
         for r in range(4):
             load_scales(W8_ROW, w8_scales, r)
             load_scales(0, w4_scales, r)
-        load_w8_half(w8_early, 0, 0, 4)
+        load_w8_half(w8_early, 0, 0, E // 2)
         nc.sync.dma_start(out=bias[:], in_=b.rearrange("(h p) e -> p h e", h=2))
-        load_w8_half(w8_early, 0, 4, 6)
-        load_w8_half(w8_early, 0, 6, E)
-        load_w4(0, 2)
-        load_w4(2, 4)
-        load_w4(4, LAST)
+        for e in range(E // 2, E, 2):
+            load_w8_half(w8_early, 0, e, e + 2)
+        for e in range(0, E // 2, 2):
+            load_w4(e, e + 2)
+        load_w4(E // 2, LAST)
 
         round_and_interleave(nc.scalar.copy, 0, VECTOR_FIRST_PIECE, HALF_T)
         round_and_interleave(nc.vector.tensor_copy, 0, 0, VECTOR_FIRST_PIECE)
@@ -229,7 +230,7 @@ def tile_moe_pln_lin_silu_kernel(
         quantize(0, HALF_T, LAST_QUARTER)
         quantize(0, LAST_QUARTER, T)
         round_and_interleave(nc.scalar.copy, 1, 0, HALF_T)
-        round_and_interleave(nc.scalar.copy, 1, HALF_T, T - VECTOR_PASS_1)
+        round_and_interleave(nc.scalar.copy, 1, HALF_T, T)
 
         gate_turned = in_bank(BANKS - 3, [P, P], "gate_turned")
         nc.tensor.transpose(gate_turned[:], gate_rows[:], ident[:])
@@ -248,11 +249,9 @@ def tile_moe_pln_lin_silu_kernel(
         for i in range(2):
             nc.scalar.copy(out=gates[:, i, :], in_=spread[i][:].rearrange("p r t -> p (r t)"))
 
-        gather_words(0, 0, LAST)
-        round_and_interleave(nc.vector.tensor_copy, 1, T - VECTOR_PASS_1, T)
+        gather_words(0, 0, E)
         quantize(1, 0, HALF_T)
         quantize(1, HALF_T, T)
-        gather_words(0, LAST, E, tag="x1_1")
         gather_words(1, 0, LAST)
         quantize(2, 0, T)
         gather_words(1, LAST, E, tag="x2_1")
@@ -272,9 +271,8 @@ def tile_moe_pln_lin_silu_kernel(
         nc.sync.dma_start(pos1_sb[:], pos1)
         nc.sync.dma_start(pos2_sb[:], pos2)
         w8_late = large("w8_late", [P, 2 * E, P], I32, "plane")
-        load_w8_half(w8_late, 1, EARLY, E)
-        load_w8_half(w8_late, 1, 0, EARLY - len(ADD_RUNS))
-        load_w8_half(w8_late, 1, EARLY - len(ADD_RUNS), EARLY)
+        for lo, hi in zip(LATE_CUTS, LATE_CUTS[1:]):
+            load_w8_half(w8_late, 1, lo, hi)
 
         gather_words(3, 0, LAST)
         gather_words(2, EARLY, E, tag="xb3")
@@ -292,13 +290,11 @@ def tile_moe_pln_lin_silu_kernel(
             close_sum(0, e, 2)
         multiply(0, LAST, 2)
         close_sum(0, LAST, 3)
-        for e in range(EARLY, E):
-            open_sum(1, e, (2, 3), e - EARLY)
-        for e in range(EARLY, E):
+
+        for e in range(E):
+            open_sum(1, e, (2, 3), e)
+        for e in range(E):
             close_second_half(e, (0, 1))
-        for e in range(EARLY):
-            open_sum(1, e, (0, 1), e + E - EARLY)
-            close_second_half(e, (2, 3))
 
         fetch_half(0)
         added = [add_turned(block, blocks, BANKS - 3 + i) for i, (block, blocks) in enumerate(ADD_RUNS)]

@@ -35,6 +35,7 @@ W8_ROW = 8
 
 CUTS = ((0, HALF_T, LAST_QUARTER, T), (0, HALF_T, T), (0, HALF_T, T), (0, HALF_T, T))
 VECTOR_FIRST_PIECE, VECTOR_LAST_PIECE = 176, 88
+GPSIMD_TOKENS = 64
 AHEAD = 4
 EARLY = AHEAD + 1
 ADD_RUNS = ((0, 2), (2, 1), (3, 1))
@@ -125,6 +126,11 @@ def tile_moe_pln_lin_silu_kernel(
                 out=xb[g][:, lo:hi, :].rearrange("p (c i) j -> p c j i", i=4),
                 in_=x[g, u][:, :, lo - CUTS[g][u] : hi - CUTS[g][u]].rearrange("p j (c i) -> p c j i", i=4),
             )
+
+        def round_pass(g):
+            round_and_interleave(nc.scalar.copy, g, 0, HALF_T)
+            round_and_interleave(nc.scalar.copy, g, HALF_T, T - GPSIMD_TOKENS)
+            round_and_interleave(nc.gpsimd.tensor_copy, g, T - GPSIMD_TOKENS, T)
 
         def quantize(g, lo, hi):
             nc.vector.quantize_mx(
@@ -229,8 +235,7 @@ def tile_moe_pln_lin_silu_kernel(
         round_and_interleave(nc.vector.tensor_copy, 0, LAST_QUARTER, LAST_QUARTER + VECTOR_LAST_PIECE)
         quantize(0, HALF_T, LAST_QUARTER)
         quantize(0, LAST_QUARTER, T)
-        round_and_interleave(nc.scalar.copy, 1, 0, HALF_T)
-        round_and_interleave(nc.scalar.copy, 1, HALF_T, T)
+        round_pass(1)
 
         gate_turned = in_bank(BANKS - 3, [P, P], "gate_turned")
         nc.tensor.transpose(gate_turned[:], gate_rows[:], ident[:])
@@ -242,9 +247,8 @@ def tile_moe_pln_lin_silu_kernel(
                 s = 4 * i + 3 - r
                 nc.tensor.transpose(spread[i][:, r, :], gate_columns[:, s : s + 1].to_broadcast([P, P]), ident[:])
 
-        for g in (2, 3):
-            round_and_interleave(nc.scalar.copy, g, 0, HALF_T)
-            round_and_interleave(nc.scalar.copy, g, HALF_T, T)
+        round_pass(2)
+        round_pass(3)
         gates = on_last_x("gates", [P, 2, T], F32, piece_bytes // 2)
         for i in range(2):
             nc.scalar.copy(out=gates[:, i, :], in_=spread[i][:].rearrange("p r t -> p (r t)"))

@@ -35,7 +35,7 @@ W8_ROW = 8
 
 CUTS = ((0, HALF_T, LAST_QUARTER, T), (0, HALF_T, T), (0, HALF_T, T), (0, HALF_T, T))
 VECTOR_FIRST_PIECE, VECTOR_LAST_PIECE = 176, 88
-GPSIMD_TOKENS = 64
+GPSIMD_TOKENS = 128
 AHEAD = 4
 EARLY = AHEAD + 1
 ADD_RUNS = ((0, 2), (2, 1), (3, 1))
@@ -130,7 +130,10 @@ def tile_moe_pln_lin_silu_kernel(
         def round_pass(g):
             round_and_interleave(nc.scalar.copy, g, 0, HALF_T)
             round_and_interleave(nc.scalar.copy, g, HALF_T, T - GPSIMD_TOKENS)
-            round_and_interleave(nc.gpsimd.tensor_copy, g, T - GPSIMD_TOKENS, T)
+            nc.gpsimd.tensor_copy(
+                out=xb[g][:, T - GPSIMD_TOKENS : T, :],
+                in_=x[g, 1][:, :, HALF_T - GPSIMD_TOKENS : HALF_T].rearrange("p j t -> p t j"),
+            )
 
         def quantize(g, lo, hi):
             nc.vector.quantize_mx(
@@ -253,9 +256,10 @@ def tile_moe_pln_lin_silu_kernel(
         for i in range(2):
             nc.scalar.copy(out=gates[:, i, :], in_=spread[i][:].rearrange("p r t -> p (r t)"))
 
-        gather_words(0, 0, E)
+        gather_words(0, 0, LAST)
         quantize(1, 0, HALF_T)
         quantize(1, HALF_T, T)
+        gather_words(0, LAST, E, tag="x1_1")
         gather_words(1, 0, LAST)
         quantize(2, 0, T)
         gather_words(1, LAST, E, tag="x2_1")

@@ -31,6 +31,7 @@ ALIGN = 256
 TOKEN_ROW = (4, 8, 0, 12)
 MOVED_PASS = 3
 MOVES = ((0, 64), (64, 4), (96, 4))
+PAIRS = ((0, 1), (2, 3))
 W8_ROW = 8
 
 CUTS = ((0, HALF_T, LAST_QUARTER, T), (0, HALF_T, T), (0, HALF_T, T), (0, HALF_T, T))
@@ -158,7 +159,7 @@ def tile_moe_pln_lin_silu_kernel(
             else:
                 w_row, weights = 0, w4[:, m, P // 2 * h : P // 2 * (h + 1)].bitcast(U8).bitcast(E2M1)
             nc.tensor.matmul_mx(
-                out=sums[h, e][:],
+                out=sums[h, e],
                 lhsT=weights,
                 lhsT_scale=w_plane[w_row:P, N * m + P * h : N * m + P * (h + 1)],
                 rhs=slot_words[g, e].bitcast(E4M3),
@@ -167,18 +168,19 @@ def tile_moe_pln_lin_silu_kernel(
                 stop=stop,
             )
 
-        def open_sum(h, e, passes, bank):
-            sums[h, e] = in_bank(bank, [P, C], "sum")
-            multiply(h, e, passes[0], start=True)
-            multiply(h, e, passes[1])
+        def open_bank(h, experts, passes, bank):
+            tile = in_bank(bank, [P, len(experts), C], "sums")
+            for i, e in enumerate(experts):
+                sums[h, e] = tile[:, i, :]
+                for g in passes:
+                    multiply(h, e, g, start=(e, g) == (experts[0], passes[0]))
 
-        def close_sum(h, e, g):
-            multiply(h, e, g, stop=True)
-            nc.scalar.activation(y[h][:, C * e : C * (e + 1)], sums[h, e][:], SILU, bias=bias[:, h, e : e + 1])
-
-        def close_second_half(e, passes):
-            multiply(1, e, passes[0])
-            close_sum(1, e, passes[1])
+        def close_bank(h, experts, passes):
+            for e in experts:
+                for g in passes:
+                    multiply(h, e, g, stop=(e, g) == (experts[-1], passes[-1]))
+            for e in experts:
+                nc.scalar.activation(y[h][:, C * e : C * (e + 1)], sums[h, e], SILU, bias=bias[:, h, e : e + 1])
 
         def fetch(into, h, i, lo, hi):
             places = (pos1_sb, pos2_sb)[i][:, lo // 16 : hi // 16]
@@ -286,23 +288,33 @@ def tile_moe_pln_lin_silu_kernel(
         gather_words(2, EARLY, E, tag="xb3")
         gather_words(3, LAST, E)
 
-        for e in range(E):
-            open_sum(0, e, (0, 1), e)
+        for i, pair in enumerate(PAIRS):
+            open_bank(0, pair, (0, 1), i)
+        for e in range(E // 2, E):
+            open_bank(0, (e,), (0, 1), e)
         for e in range(EARLY):
             multiply(0, e, 2)
-        for e in range(EARLY):
-            close_sum(0, e, 3)
+        for i, pair in enumerate(PAIRS):
+            open_bank(1, pair, (2,), len(PAIRS) + i)
+        for pair in PAIRS:
+            close_bank(0, pair, (3,))
+        for e in range(E // 2, EARLY):
+            close_bank(0, (e,), (3,))
         for e in range(EARLY, LAST):
             multiply(0, e, 3)
         for e in range(EARLY, LAST):
-            close_sum(0, e, 2)
+            close_bank(0, (e,), (2,))
         multiply(0, LAST, 2)
-        close_sum(0, LAST, 3)
+        close_bank(0, (LAST,), (3,))
 
-        for e in range(E):
-            open_sum(1, e, (2, 3), e)
-        for e in range(E):
-            close_second_half(e, (0, 1))
+        for e in range(E // 2):
+            multiply(1, e, 3)
+        for e in range(E // 2, E):
+            open_bank(1, (e,), (2, 3), e)
+        for pair in PAIRS:
+            close_bank(1, pair, (0, 1))
+        for e in range(E // 2, E):
+            close_bank(1, (e,), (0, 1))
 
         fetch_half(0)
         added = [add_turned(block, blocks, BANKS - 3 + i) for i, (block, blocks) in enumerate(ADD_RUNS)]

@@ -26,12 +26,12 @@ HALF_T = T // 2
 LAST_QUARTER = T - T // 4
 BANKS = 8
 LAST = E - 1
+PAIRS = ((0, 1), (2, 3))
 ALIGN = 256
 
 TOKEN_ROW = (4, 8, 0, 12)
 MOVED_PASS = 3
 MOVES = ((0, 64), (64, 4), (96, 4))
-PAIRS = ((0, 1), (2, 3))
 W8_ROW = 8
 
 CUTS = ((0, HALF_T, LAST_QUARTER, T), (0, HALF_T, T), (0, HALF_T, T), (0, HALF_T, T))
@@ -85,7 +85,7 @@ def tile_moe_pln_lin_silu_kernel(
         for u in range(2):
             x[3, u] = on_last_x("x3_%d" % u, [P, 4, HALF_T], F32, piece_bytes * u)
         xb = [large("xb%d" % g, [P, T, 4], BF16) for g in range(PASSES)]
-        words = large("words", [P, WORD_COLUMN[0] + window_width(SLOTS)], I32)
+        words = large("words", [P, WORD_COLUMN[0] + window_width(C * LAST)], I32)
         plane = large("plane", [P, window_width(SLOTS // 2)], U8)
         slot_plane = large("slot_plane", [P, SLOTS], U8)
         moved = large("moved", [P, SLOTS], U8)
@@ -317,7 +317,8 @@ def tile_moe_pln_lin_silu_kernel(
             close_bank(1, (e,), (0, 1))
 
         fetch_half(0)
-        added = [add_turned(block, blocks, BANKS - 3 + i) for i, (block, blocks) in enumerate(ADD_RUNS)]
+        first_bank = BANKS - len(ADD_RUNS)
+        added = [add_turned(block, blocks, first_bank + i) for i, (block, blocks) in enumerate(ADD_RUNS)]
         for i, (block, blocks) in enumerate(ADD_RUNS):
             turn_back(added[i], block, blocks, i)
             end = P * (block + blocks)

@@ -36,7 +36,7 @@ W8_ROW = 8
 
 CUTS = ((0, HALF_T, LAST_QUARTER, T), (0, HALF_T, T), (0, HALF_T, T), (0, HALF_T, T))
 VECTOR_FIRST_PIECE, VECTOR_LAST_PIECE = 176, 88
-GPSIMD_TOKENS = 128
+GPSIMD_TOKENS = 96
 AHEAD = 4
 EARLY = AHEAD + 1
 ADD_RUNS = ((0, 2), (2, 1), (3, 1))

@@ -224,13 +224,11 @@ def tile_moe_pln_lin_silu_kernel(
         for r in range(4):
             load_scales(W8_ROW, w8_scales, r)
             load_scales(0, w4_scales, r)
-        load_w8_half(w8_early, 0, 0, E // 2)
-        nc.sync.dma_start(out=bias[:], in_=b.rearrange("(h p) e -> p h e", h=2))
-        for e in range(E // 2, E, 2):
+        for e in range(0, E, 2):
             load_w8_half(w8_early, 0, e, e + 2)
-        for e in range(0, E // 2, 2):
-            load_w4(e, e + 2)
-        load_w4(E // 2, LAST)
+        nc.sync.dma_start(out=bias[:], in_=b.rearrange("(h p) e -> p h e", h=2))
+        for e in range(0, E, 2):
+            load_w4(e, min(e + 2, LAST))
 
         round_and_interleave(nc.scalar.copy, 0, VECTOR_FIRST_PIECE, HALF_T)
         round_and_interleave(nc.vector.tensor_copy, 0, 0, VECTOR_FIRST_PIECE)

@@ -31,7 +31,6 @@ ALIGN = 256
 
 TOKEN_ROW = (4, 8, 0, 12)
 MOVED_PASS = 3
-MOVES = ((0, 64), (64, 4), (96, 4))
 W8_ROW = 8
 
 CUTS = ((0, HALF_T, LAST_QUARTER, T), (0, HALF_T, T), (0, HALF_T, T), (0, HALF_T, T))
@@ -227,8 +226,9 @@ def tile_moe_pln_lin_silu_kernel(
         for e in range(0, E, 2):
             load_w8_half(w8_early, 0, e, e + 2)
         nc.sync.dma_start(out=bias[:], in_=b.rearrange("(h p) e -> p h e", h=2))
-        for e in range(0, E, 2):
-            load_w4(e, min(e + 2, LAST))
+        for e in range(0, E // 2, 2):
+            load_w4(e, e + 2)
+        load_w4(E // 2, LAST)
 
         round_and_interleave(nc.scalar.copy, 0, VECTOR_FIRST_PIECE, HALF_T)
         round_and_interleave(nc.vector.tensor_copy, 0, 0, VECTOR_FIRST_PIECE)
@@ -271,16 +271,15 @@ def tile_moe_pln_lin_silu_kernel(
             places = offs_sb[:, lo // 16 : (lo + SLOTS // 2) // 16]
             nc.vector.tensor_copy(slot_plane[:, lo : lo + SLOTS // 2], plane[:].indirect(places))
         row = TOKEN_ROW[MOVED_PASS]
-        for lo, count in MOVES:
-            nc.sync.dma_start(
-                out=moved[lo : lo + count, :].bitcast(I32), in_=slot_plane[row + lo : row + lo + count, :].bitcast(I32)
-            )
+        for r in range(4):
+            nc.sync.dma_start(out=moved[:].bitcast(I32)[r:P:32], in_=slot_plane[:].bitcast(I32)[row + r : P : 32])
         load_w4(LAST, E)
         nc.sync.dma_start(pos1_sb[:], pos1)
-        nc.sync.dma_start(pos2_sb[:], pos2)
         w8_late = large("w8_late", [P, 2 * E, P], I32, "plane")
         for lo, hi in zip(LATE_CUTS, LATE_CUTS[1:]):
             load_w8_half(w8_late, 1, lo, hi)
+            if lo == 0:
+                nc.sync.dma_start(pos2_sb[:], pos2)
 
         gather_words(3, 0, LAST)
         gather_words(2, EARLY, E, tag="xb3")

@@ -34,7 +34,7 @@ MOVED_PASS = 3
 W8_ROW = 8
 
 CUTS = ((0, HALF_T, LAST_QUARTER, T), (0, HALF_T, T), (0, HALF_T, T), (0, HALF_T, T))
-VECTOR_FIRST_PIECE, VECTOR_LAST_PIECE = 176, 88
+VECTOR_FIRST_PIECE, VECTOR_LAST_PIECE = 128, 88
 GPSIMD_TOKENS = 96
 AHEAD = 4
 EARLY = AHEAD + 1
@@ -232,7 +232,8 @@ def tile_moe_pln_lin_silu_kernel(
 
         round_and_interleave(nc.scalar.copy, 0, VECTOR_FIRST_PIECE, HALF_T)
         round_and_interleave(nc.vector.tensor_copy, 0, 0, VECTOR_FIRST_PIECE)
-        quantize(0, 0, HALF_T)
+        quantize(0, 0, VECTOR_FIRST_PIECE)
+        quantize(0, VECTOR_FIRST_PIECE, HALF_T)
         round_and_interleave(nc.scalar.copy, 0, HALF_T, LAST_QUARTER)
         round_and_interleave(nc.scalar.copy, 0, LAST_QUARTER + VECTOR_LAST_PIECE, T)
         round_and_interleave(nc.vector.tensor_copy, 0, LAST_QUARTER, LAST_QUARTER + VECTOR_LAST_PIECE)

@@ -17,6 +17,7 @@ U8 = mybir.dt.uint8
 E4M3 = mybir.dt.float8_e4m3fn_x4
 E2M1 = mybir.dt.float4_e2m1fn_x4
 MULT = mybir.AluOpType.mult
+COPY = mybir.ActivationFunctionType.Copy
 SILU = mybir.ActivationFunctionType.Silu
 
 P = 128
@@ -315,6 +316,8 @@ def tile_moe_pln_lin_silu_kernel(
             close_bank(1, (e,), (0, 1))
 
         fetch_half(0)
+        plain = large("plain", [P, HALF_T], F32)
+        nc.scalar.activation(plain[:], y[1][:].indirect(pos2_sb[:, HALF_T // 16 :]), COPY)
         first_bank = BANKS - len(ADD_RUNS)
         added = [add_turned(block, blocks, first_bank + i) for i, (block, blocks) in enumerate(ADD_RUNS)]
         for i, (block, blocks) in enumerate(ADD_RUNS):
@@ -322,7 +325,9 @@ def tile_moe_pln_lin_silu_kernel(
             end = P * (block + blocks)
             if end % HALF_T == 0:
                 nc.scalar.dma_start(out=out[0:P, end - HALF_T : end], in_=result[0][:, end - HALF_T : end])
-        fetch_half(1)
+        fetch(first, 1, 0, 0, T)
+        fetch(second, 1, 1, 0, HALF_T)
+        nc.vector.tensor_mul(second[1][:, HALF_T:T], plain[:], gates[:, 1, HALF_T:T])
         for lo in (0, HALF_T):
             tokens = slice(lo, lo + HALF_T)
             nc.vector.tensor_add(result[1][:, tokens], first[1][:, tokens], second[1][:, tokens])

@@ -96,7 +96,7 @@ def tile_moe_pln_lin_silu_kernel(
         y = [large("y%d" % h, [P, SLOTS], F32) for h in range(2)]
         first = [large("first%d" % h, [P, T], F32) for h in range(2)]
         second = [large("second%d" % h, [P, T], F32) for h in range(2)]
-        result = [large("result%d" % h, [P, T], F32) for h in range(2)]
+        result = [large("result0", [P, T], F32)]
         w8_early = large("w8_early", [P, 2 * E, P], I32)
         w4 = large("w4", [P, 2 * E, N // 2], I32)
         slot_words = {}
@@ -207,11 +207,11 @@ def tile_moe_pln_lin_silu_kernel(
                 nc.tensor.transpose(back[:, i, :], added[:, i, :], ident[:])
             nc.scalar.copy(out=result[0][:, P * block : P * (block + blocks)], in_=back[:].rearrange("p i t -> p (i t)"))
 
-        nc.vector.memset(gate_rows[:], 0.0)
+        nc.gpsimd.memset(gate_rows[:], 0.0)
         nc.vector.memset(w_plane[:].bitcast(I32), 0)
         nc.vector.memset(plane[:].bitcast(I32), 0)
         nc.vector.memset(words[:, WORD_COLUMN[0] + T :], 0)
-        nc.vector.memset(moved[:].bitcast(I32), 0)
+        nc.gpsimd.memset(moved[:].bitcast(I32), 0)
         make_identity(nc, ident[:])
 
         load_x(0)
@@ -224,8 +224,8 @@ def tile_moe_pln_lin_silu_kernel(
         for r in range(4):
             load_scales(W8_ROW, w8_scales, r)
             load_scales(0, w4_scales, r)
-        for e in range(0, E, 2):
-            load_w8_half(w8_early, 0, e, e + 2)
+        for lo, hi in ((0, 2), (2, E // 2), (E // 2, E)):
+            load_w8_half(w8_early, 0, lo, hi)
         nc.sync.dma_start(out=bias[:], in_=b.rearrange("(h p) e -> p h e", h=2))
         for e in range(0, E // 2, 2):
             load_w4(e, e + 2)
@@ -324,7 +324,8 @@ def tile_moe_pln_lin_silu_kernel(
             turn_back(added[i], block, blocks, i)
             end = P * (block + blocks)
             if end % HALF_T == 0:
-                nc.scalar.dma_start(out=out[0:P, end - HALF_T : end], in_=result[0][:, end - HALF_T : end])
+                nc.sync.dma_start(out=out[0:P, end - HALF_T : end], in_=result[0][:, end - HALF_T : end])
+        result.append(large("result1", [P, T], F32, "added%d" % ADD_RUNS[-1][0]))
         fetch(first, 1, 0, 0, T)
         fetch(second, 1, 1, 0, HALF_T)
         nc.vector.tensor_mul(second[1][:, HALF_T:T], plain[:], gates[:, 1, HALF_T:T])

@@ -39,8 +39,8 @@ VECTOR_FIRST_PIECE, VECTOR_LAST_PIECE = 128, 88
 GPSIMD_TOKENS = 96
 AHEAD = 4
 EARLY = AHEAD + 1
-ADD_RUNS = ((0, 2), (2, 1), (3, 1))
-LATE_CUTS = (0, 2, E - len(ADD_RUNS), E)
+ADD_RUNS = ((0, 2), (2, 2))
+LATE_CUTS = (0, 3, E - len(ADD_RUNS), E)
 
 WORD_COLUMN = (3 * T, 2 * T, T, 0)
 

@@ -39,8 +39,7 @@ VECTOR_FIRST_PIECE, VECTOR_LAST_PIECE = 128, 88
 GPSIMD_TOKENS = 96
 AHEAD = 4
 EARLY = AHEAD + 1
-ADD_RUNS = ((0, 2), (2, 2))
-LATE_CUTS = (0, 3, E - len(ADD_RUNS), E)
+LATE_CUTS = (0, 3, 6, E)
 
 WORD_COLUMN = (3 * T, 2 * T, T, 0)
 
@@ -92,11 +91,10 @@ def tile_moe_pln_lin_silu_kernel(
         ident = large("ident", [P, P], F32)
         gate_rows = large("gate_rows", [P, P], F32)
         w_plane = large("w_plane", [P, E * 2 * N], U8)
-        bias = large("bias", [P, 2, E], F32)
+        bias = on_last_x("bias", [P, 2, E], F32, 2 * piece_bytes)
         y = [large("y%d" % h, [P, SLOTS], F32) for h in range(2)]
         first = [large("first%d" % h, [P, T], F32) for h in range(2)]
-        second = [large("second%d" % h, [P, T], F32) for h in range(2)]
-        result = [large("result0", [P, T], F32)]
+        second = [large("second0", [P, T], F32)]
         w8_early = large("w8_early", [P, 2 * E, P], I32)
         w4 = large("w4", [P, 2 * E, N // 2], I32)
         slot_words = {}
@@ -185,27 +183,6 @@ def tile_moe_pln_lin_silu_kernel(
         def fetch(into, h, i, lo, hi):
             places = (pos1_sb, pos2_sb)[i][:, lo // 16 : hi // 16]
             nc.vector.tensor_tensor(into[h][:, lo:hi], y[h][:].indirect(places), gates[:, i, lo:hi], MULT)
-
-        def fetch_half(h):
-            fetch(first, h, 0, 0, T)
-            fetch(second, h, 1, 0, HALF_T)
-            fetch(second, h, 1, HALF_T, T)
-
-        def add_turned(block, blocks, bank):
-            turned = in_bank(bank, [P, blocks, P], "turned")
-            for i in range(blocks):
-                cols = slice(P * (block + i), P * (block + i + 1))
-                nc.tensor.matmul(turned[:, i, :], first[0][:, cols], ident[:], start=True, stop=False, is_transpose=True)
-                nc.tensor.matmul(turned[:, i, :], second[0][:, cols], ident[:], start=False, stop=True, is_transpose=True)
-            added = large("added%d" % block, [P, blocks, P], F32)
-            nc.scalar.copy(out=added[:], in_=turned[:])
-            return added
-
-        def turn_back(added, block, blocks, bank):
-            back = in_bank(bank, [P, blocks, P], "back")
-            for i in range(blocks):
-                nc.tensor.transpose(back[:, i, :], added[:, i, :], ident[:])
-            nc.scalar.copy(out=result[0][:, P * block : P * (block + blocks)], in_=back[:].rearrange("p i t -> p (i t)"))
 
         nc.gpsimd.memset(gate_rows[:], 0.0)
         nc.vector.memset(w_plane[:].bitcast(I32), 0)
@@ -315,21 +292,33 @@ def tile_moe_pln_lin_silu_kernel(
         for e in range(E // 2, E):
             close_bank(1, (e,), (0, 1))
 
-        fetch_half(0)
-        plain = large("plain", [P, HALF_T], F32)
-        nc.scalar.activation(plain[:], y[1][:].indirect(pos2_sb[:, HALF_T // 16 :]), COPY)
-        first_bank = BANKS - len(ADD_RUNS)
-        added = [add_turned(block, blocks, first_bank + i) for i, (block, blocks) in enumerate(ADD_RUNS)]
-        for i, (block, blocks) in enumerate(ADD_RUNS):
-            turn_back(added[i], block, blocks, i)
-            end = P * (block + blocks)
-            if end % HALF_T == 0:
-                nc.sync.dma_start(out=out[0:P, end - HALF_T : end], in_=result[0][:, end - HALF_T : end])
-        result.append(large("result1", [P, T], F32, "added%d" % ADD_RUNS[-1][0]))
-        fetch(first, 1, 0, 0, T)
-        fetch(second, 1, 1, 0, HALF_T)
-        nc.vector.tensor_mul(second[1][:, HALF_T:T], plain[:], gates[:, 1, HALF_T:T])
-        for lo in (0, HALF_T):
-            tokens = slice(lo, lo + HALF_T)
-            nc.vector.tensor_add(result[1][:, tokens], first[1][:, tokens], second[1][:, tokens])
-            nc.sync.dma_start(out=out[P:N, tokens], in_=result[1][:, tokens])
+        fetch(first, 0, 0, 0, T)
+        fetch(second, 0, 1, 0, T)
+        back = []
+        plain = [large("plain%d" % i, [P, HALF_T], F32) for i in range(2)]
+        for i in range(2):
+            nc.scalar.activation(plain[i][:], y[1][:].indirect(pos2_sb[:, HALF_T * i // 16 : HALF_T * (i + 1) // 16]), COPY)
+        weighted = []
+        for i in range(2):
+            turned = in_bank(BANKS - 2 + i, [P, 2, P], "turned")
+            for j in range(2):
+                nc.tensor.transpose(turned[:, j, :], plain[i][:, P * j : P * (j + 1)], ident[:])
+            weighted.append(large("weighted%d" % i, [P, 2, P], F32))
+            for j in range(2):
+                s = GATE_RUNS - 1 - (2 * i + j)
+                nc.scalar.activation(weighted[i][:, j, :], turned[:, j, :], COPY, scale=gate_columns[:, s : s + 1])
+        for i in range(2):
+            back.append(in_bank(i, [P, 2, P], "back"))
+            for j in range(2):
+                nc.tensor.transpose(back[i][:, j, :], weighted[i][:, j, :], ident[:])
+
+        fetch(first, 1, 0, 0, HALF_T)
+        result0 = on_last_x("result0", [P, T], F32, 2 * piece_bytes)
+        nc.vector.tensor_add(result0[:], first[0][:], second[0][:])
+        nc.sync.dma_start(out=out[0:P, :], in_=result0[:])
+        fetch(first, 1, 0, HALF_T, T)
+        result1 = large("result1", [P, T], F32)
+        for i in range(2):
+            tokens = slice(HALF_T * i, HALF_T * (i + 1))
+            nc.vector.tensor_add(result1[:, tokens], first[1][:, tokens], back[i][:].rearrange("p j t -> p (j t)"))
+            nc.sync.dma_start(out=out[P:N, tokens], in_=result1[:, tokens])

@@ -27,19 +27,20 @@ HALF_T = T // 2
 LAST_QUARTER = T - T // 4
 BANKS = 8
 LAST = E - 1
-PAIRS = ((0, 1), (2, 3))
 ALIGN = 256
 
 TOKEN_ROW = (4, 8, 0, 12)
 MOVED_PASS = 3
 W8_ROW = 8
 
-CUTS = ((0, HALF_T, LAST_QUARTER, T), (0, HALF_T, T), (0, HALF_T, T), (0, HALF_T, T))
+CUTS = ((0, HALF_T, LAST_QUARTER, T), (0, HALF_T, T))
+GPSIMD_PAIR_TOKENS = 352
 VECTOR_FIRST_PIECE, VECTOR_LAST_PIECE = 128, 88
 GPSIMD_TOKENS = 96
 AHEAD = 4
 EARLY = AHEAD + 1
-LATE_CUTS = (0, 3, 6, E)
+WHOLE = 2
+LATE_CUTS = (WHOLE, 4, 6, E)
 
 WORD_COLUMN = (3 * T, 2 * T, T, 0)
 
@@ -77,12 +78,13 @@ def tile_moe_pln_lin_silu_kernel(
         pos2_sb = lists.tile([P, T // 16], U16, name="pos2_sb")
 
         x = {}
-        for g in range(PASSES - 1):
+        for g in range(2):
             for u in range(len(CUTS[g]) - 1):
                 x[g, u] = large("x%d_%d" % (g, u), [P, 4, CUTS[g][u + 1] - CUTS[g][u]], F32)
-        piece_bytes = 4 * 4 * HALF_T
+        piece_bytes = 4 * 2 * T
         for u in range(2):
-            x[3, u] = on_last_x("x3_%d" % u, [P, 4, HALF_T], F32, piece_bytes * u)
+            x[2, u] = large("x2_%d" % u, [P, 2, T], F32)
+            x[3, u] = on_last_x("x3_%d" % u, [P, 2, T], F32, piece_bytes * u)
         xb = [large("xb%d" % g, [P, T, 4], BF16) for g in range(PASSES)]
         words = large("words", [P, WORD_COLUMN[0] + window_width(C * LAST)], I32)
         plane = large("plane", [P, window_width(SLOTS // 2)], U8)
@@ -95,15 +97,20 @@ def tile_moe_pln_lin_silu_kernel(
         y = [large("y%d" % h, [P, SLOTS], F32) for h in range(2)]
         first = [large("first%d" % h, [P, T], F32) for h in range(2)]
         second = [large("second0", [P, T], F32)]
-        w8_early = large("w8_early", [P, 2 * E, P], I32)
+        w8_whole = large("w8_whole", [P, 2 * WHOLE, N], I32)
+        w8_early = large("w8_early", [P, 2 * (E - WHOLE), P], I32)
         w4 = large("w4", [P, 2 * E, N // 2], I32)
         slot_words = {}
         sums = {}
 
         def load_x(g):
             rows = xT[K_PASS * g : K_PASS * (g + 1), :].rearrange("(p j) t -> p j t", j=4)
-            for u in range(len(CUTS[g]) - 1):
-                nc.sync.dma_start(out=x[g, u][:], in_=rows[:, :, CUTS[g][u] : CUTS[g][u + 1]])
+            if g < 2:
+                for u in range(len(CUTS[g]) - 1):
+                    nc.sync.dma_start(out=x[g, u][:], in_=rows[:, :, CUTS[g][u] : CUTS[g][u + 1]])
+            else:
+                for u in range(2):
+                    nc.sync.dma_start(out=x[g, u][:], in_=rows[:, 2 * u : 2 * u + 2, :])
 
         def load_scales(first_row, scales, r):
             rows = scales.bitcast(I32).rearrange("e a q n -> q (e a) n")
@@ -114,7 +121,8 @@ def tile_moe_pln_lin_silu_kernel(
         w4_rows = w4_words.rearrange("e a p n -> p (e a) n").bitcast(I32)
 
         def load_w8_half(into, h, lo, hi):
-            nc.sync.dma_start(out=into[:, 2 * lo : 2 * hi, :], in_=w8_rows[:, 2 * lo : 2 * hi, P * h : P * (h + 1)])
+            rows = w8_rows[:, 2 * lo : 2 * hi, P * h : P * (h + 1)]
+            nc.sync.dma_start(out=into[:, 2 * (lo - WHOLE) : 2 * (hi - WHOLE), :], in_=rows)
 
         def load_w4(lo, hi):
             nc.sync.dma_start(out=w4[:, 2 * lo : 2 * hi, :], in_=w4_rows[:, 2 * lo : 2 * hi, :])
@@ -134,6 +142,14 @@ def tile_moe_pln_lin_silu_kernel(
                 in_=x[g, 1][:, :, HALF_T - GPSIMD_TOKENS : HALF_T].rearrange("p j t -> p t j"),
             )
 
+        def round_pairs(g):
+            def copy_pair(engine_copy, u, lo, hi):
+                engine_copy(out=xb[g][:, lo:hi, 2 * u : 2 * u + 2], in_=x[g, u][:, :, lo:hi].rearrange("p j t -> p t j"))
+
+            copy_pair(nc.scalar.copy, 0, 0, T)
+            copy_pair(nc.scalar.copy, 1, 0, T - GPSIMD_PAIR_TOKENS)
+            copy_pair(nc.gpsimd.tensor_copy, 1, T - GPSIMD_PAIR_TOKENS, T)
+
         def quantize(g, lo, hi):
             nc.vector.quantize_mx(
                 out=words[:, WORD_COLUMN[g] + lo : WORD_COLUMN[g] + hi].bitcast(E4M3),
@@ -152,8 +168,10 @@ def tile_moe_pln_lin_silu_kernel(
 
         def multiply(h, e, g, start=False, stop=False):
             m, slots = 2 * e + g % 2, slice(C * e, C * (e + 1))
-            if g < 2:
-                w_row, weights = W8_ROW, (w8_early, w8_late)[h][:, m, :].bitcast(E4M3)
+            if g < 2 and e < WHOLE:
+                w_row, weights = W8_ROW, w8_whole[:, m, P * h : P * (h + 1)].bitcast(E4M3)
+            elif g < 2:
+                w_row, weights = W8_ROW, (w8_early, w8_late)[h][:, m - 2 * WHOLE, :].bitcast(E4M3)
             else:
                 w_row, weights = 0, w4[:, m, P // 2 * h : P // 2 * (h + 1)].bitcast(U8).bitcast(E2M1)
             nc.tensor.matmul_mx(
@@ -165,20 +183,6 @@ def tile_moe_pln_lin_silu_kernel(
                 start=start,
                 stop=stop,
             )
-
-        def open_bank(h, experts, passes, bank):
-            tile = in_bank(bank, [P, len(experts), C], "sums")
-            for i, e in enumerate(experts):
-                sums[h, e] = tile[:, i, :]
-                for g in passes:
-                    multiply(h, e, g, start=(e, g) == (experts[0], passes[0]))
-
-        def close_bank(h, experts, passes):
-            for e in experts:
-                for g in passes:
-                    multiply(h, e, g, stop=(e, g) == (experts[-1], passes[-1]))
-            for e in experts:
-                nc.scalar.activation(y[h][:, C * e : C * (e + 1)], sums[h, e], SILU, bias=bias[:, h, e : e + 1])
 
         def fetch(into, h, i, lo, hi):
             places = (pos1_sb, pos2_sb)[i][:, lo // 16 : hi // 16]
@@ -201,7 +205,8 @@ def tile_moe_pln_lin_silu_kernel(
         for r in range(4):
             load_scales(W8_ROW, w8_scales, r)
             load_scales(0, w4_scales, r)
-        for lo, hi in ((0, 2), (2, E // 2), (E // 2, E)):
+        nc.sync.dma_start(out=w8_whole[:], in_=w8_rows[:, : 2 * WHOLE, :])
+        for lo, hi in ((WHOLE, E // 2), (E // 2, E)):
             load_w8_half(w8_early, 0, lo, hi)
         nc.sync.dma_start(out=bias[:], in_=b.rearrange("(h p) e -> p h e", h=2))
         for e in range(0, E // 2, 2):
@@ -229,8 +234,8 @@ def tile_moe_pln_lin_silu_kernel(
                 s = 4 * i + 3 - r
                 nc.tensor.transpose(spread[i][:, r, :], gate_columns[:, s : s + 1].to_broadcast([P, P]), ident[:])
 
-        round_pass(2)
-        round_pass(3)
+        round_pairs(2)
+        round_pairs(3)
         gates = on_last_x("gates", [P, 2, T], F32, piece_bytes // 2)
         for i in range(2):
             nc.scalar.copy(out=gates[:, i, :], in_=spread[i][:].rearrange("p r t -> p (r t)"))
@@ -254,63 +259,86 @@ def tile_moe_pln_lin_silu_kernel(
             nc.sync.dma_start(out=moved[:].bitcast(I32)[r:P:32], in_=slot_plane[:].bitcast(I32)[row + r : P : 32])
         load_w4(LAST, E)
         nc.sync.dma_start(pos1_sb[:], pos1)
-        w8_late = large("w8_late", [P, 2 * E, P], I32, "plane")
+        w8_late = large("w8_late", [P, 2 * (E - WHOLE), P], I32, "plane")
         for lo, hi in zip(LATE_CUTS, LATE_CUTS[1:]):
             load_w8_half(w8_late, 1, lo, hi)
-            if lo == 0:
+            if lo == WHOLE:
                 nc.sync.dma_start(pos2_sb[:], pos2)
 
         gather_words(3, 0, LAST)
         gather_words(2, EARLY, E, tag="xb3")
         gather_words(3, LAST, E)
 
-        for i, pair in enumerate(PAIRS):
-            open_bank(0, pair, (0, 1), i)
-        for e in range(E // 2, E):
-            open_bank(0, (e,), (0, 1), e)
+        groups = (((0, 1), (2, 3, 4), (5, 6), (LAST,)), ((0, 1), (2, 3), (4, 5), (6, LAST)))
+        def place(h, experts, bank):
+            tile = in_bank(bank, [P, len(experts), C], "sums")
+            for j, e in enumerate(experts):
+                sums[h, e] = tile[:, j, :]
+
+        for h in range(2):
+            for i, experts in enumerate(groups[h]):
+                if (h, i) != (1, 3):
+                    place(h, experts, len(groups[0]) * h + i)
+        firsts = [[experts[0] for experts in groups[h]] for h in range(2)]
+
+        def close(h, experts, passes):
+            for g in passes:
+                for e in experts:
+                    multiply(h, e, g, stop=(g, e) == (passes[-1], experts[-1]))
+            for e in experts:
+                nc.scalar.activation(y[h][:, C * e : C * (e + 1)], sums[h, e], SILU, bias=bias[:, h, e : e + 1])
+
+        for e in range(E):
+            for g in range(2):
+                multiply(0, e, g, start=g == 0 and e in firsts[0])
         for e in range(EARLY):
             multiply(0, e, 2)
-        for i, pair in enumerate(PAIRS):
-            open_bank(1, pair, (2,), len(PAIRS) + i)
-        for pair in PAIRS:
-            close_bank(0, pair, (3,))
-        for e in range(E // 2, EARLY):
-            close_bank(0, (e,), (3,))
-        for e in range(EARLY, LAST):
+        for e in range(EARLY):
+            multiply(1, e, 2, start=e in firsts[1])
+        for e in range(WHOLE):
+            for g in range(2):
+                multiply(1, e, g)
+        for experts in groups[0][:2]:
+            close(0, experts, (3,))
+        for e in groups[0][2]:
             multiply(0, e, 3)
-        for e in range(EARLY, LAST):
-            close_bank(0, (e,), (2,))
+        close(1, groups[1][0], (3,))
+        close(0, groups[0][2], (2,))
         multiply(0, LAST, 2)
-        close_bank(0, (LAST,), (3,))
-
-        for e in range(E // 2):
+        for e in range(WHOLE, EARLY):
             multiply(1, e, 3)
-        for e in range(E // 2, E):
-            open_bank(1, (e,), (2, 3), e)
-        for pair in PAIRS:
-            close_bank(1, pair, (0, 1))
-        for e in range(E // 2, E):
-            close_bank(1, (e,), (0, 1))
+        close(0, groups[0][3], (3,))
+        close(1, groups[1][1], (0, 1))
+        for g in range(2):
+            for e in groups[1][2]:
+                multiply(1, e, g)
+        multiply(1, EARLY, 3)
+        multiply(1, EARLY, 2, stop=True)
+        close(1, groups[1][2], ())
+        place(1, groups[1][3], 0)
+        for g in (3, 2):
+            for e in groups[1][3]:
+                multiply(1, e, g, start=(g, e) == (3, firsts[1][3]))
+        close(1, groups[1][3], (0, 1))
 
         fetch(first, 0, 0, 0, T)
         fetch(second, 0, 1, 0, T)
-        back = []
-        plain = [large("plain%d" % i, [P, HALF_T], F32) for i in range(2)]
-        for i in range(2):
-            nc.scalar.activation(plain[i][:], y[1][:].indirect(pos2_sb[:, HALF_T * i // 16 : HALF_T * (i + 1) // 16]), COPY)
-        weighted = []
-        for i in range(2):
-            turned = in_bank(BANKS - 2 + i, [P, 2, P], "turned")
-            for j in range(2):
-                nc.tensor.transpose(turned[:, j, :], plain[i][:, P * j : P * (j + 1)], ident[:])
-            weighted.append(large("weighted%d" % i, [P, 2, P], F32))
-            for j in range(2):
-                s = GATE_RUNS - 1 - (2 * i + j)
-                nc.scalar.activation(weighted[i][:, j, :], turned[:, j, :], COPY, scale=gate_columns[:, s : s + 1])
-        for i in range(2):
-            back.append(in_bank(i, [P, 2, P], "back"))
-            for j in range(2):
-                nc.tensor.transpose(back[i][:, j, :], weighted[i][:, j, :], ident[:])
+        runs = ((0, 2, BANKS - 1), (2, 1, 1), (3, 1, 2))
+        plain = large("plain", [P, T], F32)
+        weighted = large("weighted", [P, T // P, P], F32)
+        for block, blocks, bank in runs:
+            lo, hi = P * block, P * (block + blocks)
+            nc.scalar.activation(plain[:, lo:hi], y[1][:].indirect(pos2_sb[:, lo // 16 : hi // 16]), COPY)
+        for block, blocks, bank in runs:
+            turned = in_bank(bank, [P, blocks, P], "turned")
+            for j in range(blocks):
+                nc.tensor.transpose(turned[:, j, :], plain[:, P * (block + j) : P * (block + j + 1)], ident[:])
+            for j in range(blocks):
+                s = GATE_RUNS - 1 - (block + j)
+                nc.scalar.activation(weighted[:, block + j, :], turned[:, j, :], COPY, scale=gate_columns[:, s : s + 1])
+        back = [in_bank(3 + i, [P, 2, P], "back") for i in range(2)]
+        for block in range(T // P):
+            nc.tensor.transpose(back[block // 2][:, block % 2, :], weighted[:, block, :], ident[:])
 
         fetch(first, 1, 0, 0, HALF_T)
         result0 = on_last_x("result0", [P, T], F32, 2 * piece_bytes)

@@ -87,7 +87,7 @@ def tile_moe_pln_lin_silu_kernel(
             x[3, u] = on_last_x("x3_%d" % u, [P, 2, T], F32, piece_bytes * u)
         xb = [large("xb%d" % g, [P, T, 4], BF16) for g in range(PASSES)]
         words = large("words", [P, WORD_COLUMN[0] + window_width(C * LAST)], I32)
-        plane = large("plane", [P, window_width(SLOTS // 2)], U8)
+        plane = large("plane", [P, window_width(SLOTS - C * WHOLE)], U8)
         slot_plane = large("slot_plane", [P, SLOTS], U8)
         moved = large("moved", [P, SLOTS], U8)
         ident = large("ident", [P, P], F32)
@@ -206,11 +206,11 @@ def tile_moe_pln_lin_silu_kernel(
             load_scales(W8_ROW, w8_scales, r)
             load_scales(0, w4_scales, r)
         nc.sync.dma_start(out=w8_whole[:], in_=w8_rows[:, : 2 * WHOLE, :])
+        load_w4(0, WHOLE)
         for lo, hi in ((WHOLE, E // 2), (E // 2, E)):
             load_w8_half(w8_early, 0, lo, hi)
         nc.sync.dma_start(out=bias[:], in_=b.rearrange("(h p) e -> p h e", h=2))
-        for e in range(0, E // 2, 2):
-            load_w4(e, e + 2)
+        load_w4(WHOLE, E // 2)
         load_w4(E // 2, LAST)
 
         round_and_interleave(nc.scalar.copy, 0, VECTOR_FIRST_PIECE, HALF_T)
@@ -251,9 +251,8 @@ def tile_moe_pln_lin_silu_kernel(
         quantize(3, 0, T)
         gather_words(2, AHEAD, EARLY, into=on_last_x("slot_words2", [P, C], U32, 3 * piece_bytes // 2))
 
-        for lo in (0, SLOTS // 2):
-            places = offs_sb[:, lo // 16 : (lo + SLOTS // 2) // 16]
-            nc.vector.tensor_copy(slot_plane[:, lo : lo + SLOTS // 2], plane[:].indirect(places))
+        for lo, hi in ((0, C * WHOLE), (C * WHOLE, SLOTS)):
+            nc.vector.tensor_copy(slot_plane[:, lo:hi], plane[:].indirect(offs_sb[:, lo // 16 : hi // 16]))
         row = TOKEN_ROW[MOVED_PASS]
         for r in range(4):
             nc.sync.dma_start(out=moved[:].bitcast(I32)[r:P:32], in_=slot_plane[:].bitcast(I32)[row + r : P : 32])
@@ -288,16 +287,17 @@ def tile_moe_pln_lin_silu_kernel(
             for e in experts:
                 nc.scalar.activation(y[h][:, C * e : C * (e + 1)], sums[h, e], SILU, bias=bias[:, h, e : e + 1])
 
-        for e in range(E):
+        for passes in ((0, 1), (2,)):
+            for h in range(2):
+                for e in range(WHOLE):
+                    for g in passes:
+                        multiply(h, e, g, start=(e, g) == (0, 0))
+        for e in range(WHOLE, E):
             for g in range(2):
                 multiply(0, e, g, start=g == 0 and e in firsts[0])
-        for e in range(EARLY):
-            multiply(0, e, 2)
-        for e in range(EARLY):
-            multiply(1, e, 2, start=e in firsts[1])
-        for e in range(WHOLE):
-            for g in range(2):
-                multiply(1, e, g)
+        for h in range(2):
+            for e in range(WHOLE, EARLY):
+                multiply(h, e, 2, start=h == 1 and e in firsts[1])
         for experts in groups[0][:2]:
             close(0, experts, (3,))
         for e in groups[0][2]:

@@ -40,7 +40,7 @@ GPSIMD_TOKENS = 96
 AHEAD = 4
 EARLY = AHEAD + 1
 WHOLE = 2
-LATE_CUTS = (WHOLE, 4, 6, E)
+LATE_CUTS = (WHOLE, 5, LAST, E)
 
 WORD_COLUMN = (3 * T, 2 * T, T, 0)
 
@@ -93,10 +93,10 @@ def tile_moe_pln_lin_silu_kernel(
         ident = large("ident", [P, P], F32)
         gate_rows = large("gate_rows", [P, P], F32)
         w_plane = large("w_plane", [P, E * 2 * N], U8)
-        bias = on_last_x("bias", [P, 2, E], F32, 2 * piece_bytes)
+        bias = large("bias", [P, 2, E], F32)
         y = [large("y%d" % h, [P, SLOTS], F32) for h in range(2)]
         first = [large("first%d" % h, [P, T], F32) for h in range(2)]
-        second = [large("second0", [P, T], F32)]
+        second = [large("second%d" % h, [P, T], F32) for h in range(2)]
         w8_whole = large("w8_whole", [P, 2 * WHOLE, N], I32)
         w8_early = large("w8_early", [P, 2 * (E - WHOLE), P], I32)
         w4 = large("w4", [P, 2 * E, N // 2], I32)
@@ -268,7 +268,7 @@ def tile_moe_pln_lin_silu_kernel(
         gather_words(2, EARLY, E, tag="xb3")
         gather_words(3, LAST, E)
 
-        groups = (((0, 1), (2, 3, 4), (5, 6), (LAST,)), ((0, 1), (2, 3), (4, 5), (6, LAST)))
+        groups = (((0, 1), (2, 3, 4), (5, 6), (LAST,)), ((0, 1), (2, 3, 4), (5, 6), (LAST,)))
         def place(h, experts, bank):
             tile = in_bank(bank, [P, len(experts), C], "sums")
             for j, e in enumerate(experts):
@@ -276,7 +276,7 @@ def tile_moe_pln_lin_silu_kernel(
 
         for h in range(2):
             for i, experts in enumerate(groups[h]):
-                if (h, i) != (1, 3):
+                if h == 0 or i < 2:
                     place(h, experts, len(groups[0]) * h + i)
         firsts = [[experts[0] for experts in groups[h]] for h in range(2)]
 
@@ -302,51 +302,55 @@ def tile_moe_pln_lin_silu_kernel(
             close(0, experts, (3,))
         for e in groups[0][2]:
             multiply(0, e, 3)
-        close(1, groups[1][0], (3,))
+        multiply(1, 0, 3)
         close(0, groups[0][2], (2,))
         multiply(0, LAST, 2)
         for e in range(WHOLE, EARLY):
             multiply(1, e, 3)
         close(0, groups[0][3], (3,))
+        multiply(1, 1, 3, stop=True)
+        close(1, groups[1][0], ())
         close(1, groups[1][1], (0, 1))
-        for g in range(2):
-            for e in groups[1][2]:
-                multiply(1, e, g)
-        multiply(1, EARLY, 3)
-        multiply(1, EARLY, 2, stop=True)
-        close(1, groups[1][2], ())
-        place(1, groups[1][3], 0)
-        for g in (3, 2):
-            for e in groups[1][3]:
-                multiply(1, e, g, start=(g, e) == (3, firsts[1][3]))
-        close(1, groups[1][3], (0, 1))
+        for i, experts in enumerate(groups[1][2:]):
+            place(1, experts, i)
+            for g in (3, 2):
+                for e in experts:
+                    multiply(1, e, g, start=(g, e) == (3, experts[0]))
+        for experts in groups[1][2:]:
+            close(1, experts, (0, 1))
 
-        fetch(first, 0, 0, 0, T)
-        fetch(second, 0, 1, 0, T)
-        runs = ((0, 2, BANKS - 1), (2, 1, 1), (3, 1, 2))
-        plain = large("plain", [P, T], F32)
-        weighted = large("weighted", [P, T // P, P], F32)
+        runs = ((0, 2, BANKS - 1), (2, 1, BANKS - 2), (3, 1, 4))
+        plain = large("plain", [P, T], F32, "plane")
+        weighted = [large("weighted%d" % h, [P, 2, P], F32) for h in range(2)]
         for block, blocks, bank in runs:
             lo, hi = P * block, P * (block + blocks)
-            nc.scalar.activation(plain[:, lo:hi], y[1][:].indirect(pos2_sb[:, lo // 16 : hi // 16]), COPY)
+            nc.scalar.activation(plain[:, lo:hi], y[block // 2][:].indirect(pos2_sb[:, lo // 16 : hi // 16]), COPY)
         for block, blocks, bank in runs:
             turned = in_bank(bank, [P, blocks, P], "turned")
             for j in range(blocks):
                 nc.tensor.transpose(turned[:, j, :], plain[:, P * (block + j) : P * (block + j + 1)], ident[:])
             for j in range(blocks):
-                s = GATE_RUNS - 1 - (block + j)
-                nc.scalar.activation(weighted[:, block + j, :], turned[:, j, :], COPY, scale=gate_columns[:, s : s + 1])
-        back = [in_bank(3 + i, [P, 2, P], "back") for i in range(2)]
+                s, into = GATE_RUNS - 1 - (block + j), weighted[block // 2][:, (block + j) % 2, :]
+                nc.scalar.activation(into, turned[:, j, :], COPY, scale=gate_columns[:, s : s + 1])
+        back = [in_bank(2 + h, [P, 2, P], "back") for h in range(2)]
         for block in range(T // P):
-            nc.tensor.transpose(back[block // 2][:, block % 2, :], weighted[:, block, :], ident[:])
+            nc.tensor.transpose(back[block // 2][:, block % 2, :], weighted[block // 2][:, block % 2, :], ident[:])
 
-        fetch(first, 1, 0, 0, HALF_T)
-        result0 = on_last_x("result0", [P, T], F32, 2 * piece_bytes)
-        nc.vector.tensor_add(result0[:], first[0][:], second[0][:])
-        nc.sync.dma_start(out=out[0:P, :], in_=result0[:])
-        fetch(first, 1, 0, HALF_T, T)
-        result1 = large("result1", [P, T], F32)
-        for i in range(2):
-            tokens = slice(HALF_T * i, HALF_T * (i + 1))
-            nc.vector.tensor_add(result1[:, tokens], first[1][:, tokens], back[i][:].rearrange("p j t -> p (j t)"))
-            nc.sync.dma_start(out=out[P:N, tokens], in_=result1[:, tokens])
+        low, high = slice(0, HALF_T), slice(HALF_T, T)
+        result = {(h, i): large("result%d_%d" % (h, i), [P, HALF_T], F32) for h, i in ((0, 0), (1, 1))}
+        result[1, 0] = large("result1_0", [P, HALF_T], F32, "weighted0")
+        result[0, 1] = on_last_x("result0_1", [P, HALF_T], F32, piece_bytes // 2)
+
+        def add_and_store(h, i, other):
+            tokens = (low, high)[i]
+            nc.vector.tensor_add(result[h, i][:], first[h][:, tokens], other)
+            nc.sync.dma_start(out=out[P * h : P * (h + 1), tokens], in_=result[h, i][:])
+
+        fetch(first, 0, 0, 0, T)
+        fetch(second, 0, 1, HALF_T, T)
+        fetch(first, 1, 0, 0, T)
+        add_and_store(0, 1, second[0][:, high])
+        fetch(second, 1, 1, 0, HALF_T)
+        add_and_store(0, 0, back[0][:].rearrange("p j t -> p (j t)"))
+        add_and_store(1, 0, second[1][:, low])
+        add_and_store(1, 1, back[1][:].rearrange("p j t -> p (j t)"))

@@ -320,15 +320,17 @@ def tile_moe_pln_lin_silu_kernel(
             close(1, experts, (0, 1))
 
         runs = ((0, 2, BANKS - 1), (2, 1, BANKS - 2), (3, 1, 4))
-        plain = large("plain", [P, T], F32, "plane")
+        plain = [large("plain0", [P, HALF_T], F32, "plane"), large("plain1", [P, HALF_T], F32)]
         weighted = [large("weighted%d" % h, [P, 2, P], F32) for h in range(2)]
         for block, blocks, bank in runs:
             lo, hi = P * block, P * (block + blocks)
-            nc.scalar.activation(plain[:, lo:hi], y[block // 2][:].indirect(pos2_sb[:, lo // 16 : hi // 16]), COPY)
+            into = plain[block // 2][:, lo % HALF_T : lo % HALF_T + hi - lo]
+            nc.scalar.activation(into, y[block // 2][:].indirect(pos2_sb[:, lo // 16 : hi // 16]), COPY)
         for block, blocks, bank in runs:
             turned = in_bank(bank, [P, blocks, P], "turned")
             for j in range(blocks):
-                nc.tensor.transpose(turned[:, j, :], plain[:, P * (block + j) : P * (block + j + 1)], ident[:])
+                lo = P * ((block + j) % 2)
+                nc.tensor.transpose(turned[:, j, :], plain[block // 2][:, lo : lo + P], ident[:])
             for j in range(blocks):
                 s, into = GATE_RUNS - 1 - (block + j), weighted[block // 2][:, (block + j) % 2, :]
                 nc.scalar.activation(into, turned[:, j, :], COPY, scale=gate_columns[:, s : s + 1])
@@ -339,7 +341,7 @@ def tile_moe_pln_lin_silu_kernel(
         low, high = slice(0, HALF_T), slice(HALF_T, T)
         result = {(h, i): large("result%d_%d" % (h, i), [P, HALF_T], F32) for h, i in ((0, 0), (1, 1))}
         result[1, 0] = large("result1_0", [P, HALF_T], F32, "weighted0")
-        result[0, 1] = on_last_x("result0_1", [P, HALF_T], F32, piece_bytes // 2)
+        result[0, 1] = large("result0_1", [P, HALF_T], F32, "plane")
 
         def add_and_store(h, i, other):
             tokens = (low, high)[i]

@@ -39,8 +39,9 @@ VECTOR_FIRST_PIECE, VECTOR_LAST_PIECE = 128, 88
 GPSIMD_TOKENS = 96
 AHEAD = 4
 EARLY = AHEAD + 1
-WHOLE = 2
+WHOLE = 3
 LATE_CUTS = (WHOLE, 5, LAST, E)
+FIRST = 2
 
 WORD_COLUMN = (3 * T, 2 * T, T, 0)
 
@@ -87,7 +88,7 @@ def tile_moe_pln_lin_silu_kernel(
             x[3, u] = on_last_x("x3_%d" % u, [P, 2, T], F32, piece_bytes * u)
         xb = [large("xb%d" % g, [P, T, 4], BF16) for g in range(PASSES)]
         words = large("words", [P, WORD_COLUMN[0] + window_width(C * LAST)], I32)
-        plane = large("plane", [P, window_width(SLOTS - C * WHOLE)], U8)
+        plane = large("plane", [P, window_width(SLOTS - C * FIRST)], U8)
         slot_plane = large("slot_plane", [P, SLOTS], U8)
         moved = large("moved", [P, SLOTS], U8)
         ident = large("ident", [P, P], F32)
@@ -205,13 +206,13 @@ def tile_moe_pln_lin_silu_kernel(
         for r in range(4):
             load_scales(W8_ROW, w8_scales, r)
             load_scales(0, w4_scales, r)
-        nc.sync.dma_start(out=w8_whole[:], in_=w8_rows[:, : 2 * WHOLE, :])
-        load_w4(0, WHOLE)
-        for lo, hi in ((WHOLE, E // 2), (E // 2, E)):
-            load_w8_half(w8_early, 0, lo, hi)
+        nc.sync.dma_start(out=w8_whole[:, : 2 * FIRST, :], in_=w8_rows[:, : 2 * FIRST, :])
+        load_w4(0, FIRST)
+        nc.sync.dma_start(out=w8_whole[:, 2 * FIRST :, :], in_=w8_rows[:, 2 * FIRST : 2 * WHOLE, :])
+        load_w8_half(w8_early, 0, WHOLE, E)
         nc.sync.dma_start(out=bias[:], in_=b.rearrange("(h p) e -> p h e", h=2))
-        load_w4(WHOLE, E // 2)
-        load_w4(E // 2, LAST)
+        load_w4(FIRST, E // 2)
+        load_w4(E // 2, 6)
 
         round_and_interleave(nc.scalar.copy, 0, VECTOR_FIRST_PIECE, HALF_T)
         round_and_interleave(nc.vector.tensor_copy, 0, 0, VECTOR_FIRST_PIECE)
@@ -251,12 +252,12 @@ def tile_moe_pln_lin_silu_kernel(
         quantize(3, 0, T)
         gather_words(2, AHEAD, EARLY, into=on_last_x("slot_words2", [P, C], U32, 3 * piece_bytes // 2))
 
-        for lo, hi in ((0, C * WHOLE), (C * WHOLE, SLOTS)):
+        for lo, hi in ((0, C * FIRST), (C * FIRST, SLOTS)):
             nc.vector.tensor_copy(slot_plane[:, lo:hi], plane[:].indirect(offs_sb[:, lo // 16 : hi // 16]))
         row = TOKEN_ROW[MOVED_PASS]
         for r in range(4):
             nc.sync.dma_start(out=moved[:].bitcast(I32)[r:P:32], in_=slot_plane[:].bitcast(I32)[row + r : P : 32])
-        load_w4(LAST, E)
+        load_w4(6, E)
         nc.sync.dma_start(pos1_sb[:], pos1)
         w8_late = large("w8_late", [P, 2 * (E - WHOLE), P], I32, "plane")
         for lo, hi in zip(LATE_CUTS, LATE_CUTS[1:]):
@@ -268,7 +269,7 @@ def tile_moe_pln_lin_silu_kernel(
         gather_words(2, EARLY, E, tag="xb3")
         gather_words(3, LAST, E)
 
-        groups = (((0, 1), (2, 3, 4), (5, 6), (LAST,)), ((0, 1), (2, 3, 4), (5, 6), (LAST,)))
+        groups = (((0, 1), (2, 3, 4), (5, 6), (LAST,)), ((0, 1, 2), (3, 4), (5, 6), (LAST,)))
         def place(h, experts, bank):
             tile = in_bank(bank, [P, len(experts), C], "sums")
             for j, e in enumerate(experts):
@@ -289,26 +290,27 @@ def tile_moe_pln_lin_silu_kernel(
 
         for passes in ((0, 1), (2,)):
             for h in range(2):
-                for e in range(WHOLE):
+                for e in range(FIRST):
                     for g in passes:
                         multiply(h, e, g, start=(e, g) == (0, 0))
-        for e in range(WHOLE, E):
+        for h, e in [(0, e) for e in range(FIRST, E)] + [(1, e) for e in range(FIRST, WHOLE)]:
             for g in range(2):
-                multiply(0, e, g, start=g == 0 and e in firsts[0])
+                multiply(h, e, g, start=g == 0 and h == 0 and e in firsts[0])
         for h in range(2):
-            for e in range(WHOLE, EARLY):
+            for e in range(FIRST, EARLY):
                 multiply(h, e, 2, start=h == 1 and e in firsts[1])
         for experts in groups[0][:2]:
             close(0, experts, (3,))
         for e in groups[0][2]:
             multiply(0, e, 3)
-        multiply(1, 0, 3)
+        for e in range(WHOLE - 1):
+            multiply(1, e, 3)
         close(0, groups[0][2], (2,))
         multiply(0, LAST, 2)
         for e in range(WHOLE, EARLY):
             multiply(1, e, 3)
         close(0, groups[0][3], (3,))
-        multiply(1, 1, 3, stop=True)
+        multiply(1, WHOLE - 1, 3, stop=True)
         close(1, groups[1][0], ())
         close(1, groups[1][1], (0, 1))
         for i, experts in enumerate(groups[1][2:]):

@@ -36,7 +36,7 @@ W8_ROW = 8
 CUTS = ((0, HALF_T, LAST_QUARTER, T), (0, HALF_T, T))
 GPSIMD_PAIR_TOKENS = 352
 VECTOR_FIRST_PIECE, VECTOR_LAST_PIECE = 128, 88
-GPSIMD_TOKENS = 96
+GPSIMD_TOKENS = 128
 AHEAD = 4
 EARLY = AHEAD + 1
 WHOLE = 3

@@ -207,10 +207,10 @@ def tile_moe_pln_lin_silu_kernel(
             load_scales(W8_ROW, w8_scales, r)
             load_scales(0, w4_scales, r)
         nc.sync.dma_start(out=w8_whole[:, : 2 * FIRST, :], in_=w8_rows[:, : 2 * FIRST, :])
+        nc.sync.dma_start(out=bias[:], in_=b.rearrange("(h p) e -> p h e", h=2))
         load_w4(0, FIRST)
         nc.sync.dma_start(out=w8_whole[:, 2 * FIRST :, :], in_=w8_rows[:, 2 * FIRST : 2 * WHOLE, :])
         load_w8_half(w8_early, 0, WHOLE, E)
-        nc.sync.dma_start(out=bias[:], in_=b.rearrange("(h p) e -> p h e", h=2))
         load_w4(FIRST, E // 2)
         load_w4(E // 2, 6)
 

@@ -39,8 +39,8 @@ VECTOR_FIRST_PIECE, VECTOR_LAST_PIECE = 128, 88
 GPSIMD_TOKENS = 128
 AHEAD = 4
 EARLY = AHEAD + 1
-WHOLE = 3
-LATE_CUTS = (WHOLE, 5, LAST, E)
+WHOLE = 2
+LATE_CUTS = (WHOLE, 4, 6, LAST, E)
 FIRST = 2
 
 WORD_COLUMN = (3 * T, 2 * T, T, 0)
@@ -90,7 +90,6 @@ def tile_moe_pln_lin_silu_kernel(
         words = large("words", [P, WORD_COLUMN[0] + window_width(C * LAST)], I32)
         plane = large("plane", [P, window_width(SLOTS - C * FIRST)], U8)
         slot_plane = large("slot_plane", [P, SLOTS], U8)
-        moved = large("moved", [P, SLOTS], U8)
         ident = large("ident", [P, P], F32)
         gate_rows = large("gate_rows", [P, P], F32)
         w_plane = large("w_plane", [P, E * 2 * N], U8)
@@ -191,9 +190,8 @@ def tile_moe_pln_lin_silu_kernel(
 
         nc.gpsimd.memset(gate_rows[:], 0.0)
         nc.vector.memset(w_plane[:].bitcast(I32), 0)
-        nc.vector.memset(plane[:].bitcast(I32), 0)
+        nc.gpsimd.memset(plane[:].bitcast(I32), 0)
         nc.vector.memset(words[:, WORD_COLUMN[0] + T :], 0)
-        nc.gpsimd.memset(moved[:].bitcast(I32), 0)
         make_identity(nc, ident[:])
 
         load_x(0)
@@ -208,8 +206,8 @@ def tile_moe_pln_lin_silu_kernel(
             load_scales(0, w4_scales, r)
         nc.sync.dma_start(out=w8_whole[:, : 2 * FIRST, :], in_=w8_rows[:, : 2 * FIRST, :])
         nc.sync.dma_start(out=bias[:], in_=b.rearrange("(h p) e -> p h e", h=2))
+        nc.sync.dma_start(pos1_sb[:], pos1)
         load_w4(0, FIRST)
-        nc.sync.dma_start(out=w8_whole[:, 2 * FIRST :, :], in_=w8_rows[:, 2 * FIRST : 2 * WHOLE, :])
         load_w8_half(w8_early, 0, WHOLE, E)
         load_w4(FIRST, E // 2)
         load_w4(E // 2, 6)
@@ -254,72 +252,53 @@ def tile_moe_pln_lin_silu_kernel(
 
         for lo, hi in ((0, C * FIRST), (C * FIRST, SLOTS)):
             nc.vector.tensor_copy(slot_plane[:, lo:hi], plane[:].indirect(offs_sb[:, lo // 16 : hi // 16]))
+        moved = large("moved", [P, SLOTS], U8, "x0_0")
         row = TOKEN_ROW[MOVED_PASS]
         for r in range(4):
             nc.sync.dma_start(out=moved[:].bitcast(I32)[r:P:32], in_=slot_plane[:].bitcast(I32)[row + r : P : 32])
         load_w4(6, E)
-        nc.sync.dma_start(pos1_sb[:], pos1)
         w8_late = large("w8_late", [P, 2 * (E - WHOLE), P], I32, "plane")
         for lo, hi in zip(LATE_CUTS, LATE_CUTS[1:]):
             load_w8_half(w8_late, 1, lo, hi)
-            if lo == WHOLE:
-                nc.sync.dma_start(pos2_sb[:], pos2)
+        nc.sync.dma_start(pos2_sb[:], pos2)
 
         gather_words(3, 0, LAST)
         gather_words(2, EARLY, E, tag="xb3")
         gather_words(3, LAST, E)
 
-        groups = (((0, 1), (2, 3, 4), (5, 6), (LAST,)), ((0, 1, 2), (3, 4), (5, 6), (LAST,)))
-        def place(h, experts, bank):
-            tile = in_bank(bank, [P, len(experts), C], "sums")
-            for j, e in enumerate(experts):
-                sums[h, e] = tile[:, j, :]
+        groups = (((0, 1), (2, 3, 4), (5, 6), (LAST,)), ((0, 1), (2, 3), (4, 5), (6,), (LAST,)))
+        banks = ((0, 1, 2, 3), (4, 5, 6, 0, 1))
 
-        for h in range(2):
-            for i, experts in enumerate(groups[h]):
-                if h == 0 or i < 2:
-                    place(h, experts, len(groups[0]) * h + i)
-        firsts = [[experts[0] for experts in groups[h]] for h in range(2)]
+        def passes(steps, close=False):
+            for step in steps:
+                h, e, g = step
+                i = [e in experts for experts in groups[h]].index(True)
+                start = (h, e) not in sums
+                if start:
+                    tile = in_bank(banks[h][i], [P, len(groups[h][i]), C], "sums")
+                    for j, expert in enumerate(groups[h][i]):
+                        sums[h, expert] = tile[:, j, :]
+                multiply(h, e, g, start=start, stop=close and step == steps[-1])
+            if close:
+                for e in groups[h][i]:
+                    nc.scalar.activation(y[h][:, C * e : C * (e + 1)], sums[h, e], SILU, bias=bias[:, h, e : e + 1])
 
-        def close(h, experts, passes):
-            for g in passes:
-                for e in experts:
-                    multiply(h, e, g, stop=(g, e) == (passes[-1], experts[-1]))
-            for e in experts:
-                nc.scalar.activation(y[h][:, C * e : C * (e + 1)], sums[h, e], SILU, bias=bias[:, h, e : e + 1])
-
-        for passes in ((0, 1), (2,)):
-            for h in range(2):
-                for e in range(FIRST):
-                    for g in passes:
-                        multiply(h, e, g, start=(e, g) == (0, 0))
-        for h, e in [(0, e) for e in range(FIRST, E)] + [(1, e) for e in range(FIRST, WHOLE)]:
-            for g in range(2):
-                multiply(h, e, g, start=g == 0 and h == 0 and e in firsts[0])
-        for h in range(2):
-            for e in range(FIRST, EARLY):
-                multiply(h, e, 2, start=h == 1 and e in firsts[1])
+        passes([(h, e, g) for h in range(2) for e in range(FIRST) for g in range(2)])
+        passes([(h, e, 2) for h in range(2) for e in range(FIRST)])
+        passes([(0, e, g) for e in range(FIRST, E) for g in range(2)])
+        passes([(h, e, 2) for h in range(2) for e in range(FIRST, EARLY)])
         for experts in groups[0][:2]:
-            close(0, experts, (3,))
-        for e in groups[0][2]:
-            multiply(0, e, 3)
-        for e in range(WHOLE - 1):
-            multiply(1, e, 3)
-        close(0, groups[0][2], (2,))
-        multiply(0, LAST, 2)
-        for e in range(WHOLE, EARLY):
-            multiply(1, e, 3)
-        close(0, groups[0][3], (3,))
-        multiply(1, WHOLE - 1, 3, stop=True)
-        close(1, groups[1][0], ())
-        close(1, groups[1][1], (0, 1))
-        for i, experts in enumerate(groups[1][2:]):
-            place(1, experts, i)
-            for g in (3, 2):
-                for e in experts:
-                    multiply(1, e, g, start=(g, e) == (3, experts[0]))
-        for experts in groups[1][2:]:
-            close(1, experts, (0, 1))
+            passes([(0, e, 3) for e in experts], close=True)
+        passes([(0, e, 3) for e in groups[0][2]] + [(1, 0, 3), (1, 2, 3)])
+        passes([(0, e, 2) for e in groups[0][2]], close=True)
+        passes([(0, LAST, 2), (1, 3, 3), (1, 4, 3)])
+        passes([(0, LAST, 3)], close=True)
+        passes([(1, 1, 3)], close=True)
+        passes([(1, e, g) for g in range(2) for e in groups[1][1]], close=True)
+        passes([(1, 5, 3), (1, 5, 2)] + [(1, e, g) for g in range(2) for e in groups[1][2]], close=True)
+        passes([(1, e, g) for e in (6, LAST) for g in (3, 2)])
+        for e in (6, LAST):
+            passes([(1, e, g) for g in range(2)], close=True)
 
         runs = ((0, 2, BANKS - 1), (2, 1, BANKS - 2), (3, 1, 4))
         plain = [large("plain0", [P, HALF_T], F32, "plane"), large("plain1", [P, HALF_T], F32)]

@@ -206,7 +206,6 @@ def tile_moe_pln_lin_silu_kernel(
             load_scales(0, w4_scales, r)
         nc.sync.dma_start(out=w8_whole[:, : 2 * FIRST, :], in_=w8_rows[:, : 2 * FIRST, :])
         nc.sync.dma_start(out=bias[:], in_=b.rearrange("(h p) e -> p h e", h=2))
-        nc.sync.dma_start(pos1_sb[:], pos1)
         load_w4(0, FIRST)
         load_w8_half(w8_early, 0, WHOLE, E)
         load_w4(FIRST, E // 2)
@@ -257,6 +256,7 @@ def tile_moe_pln_lin_silu_kernel(
         for r in range(4):
             nc.sync.dma_start(out=moved[:].bitcast(I32)[r:P:32], in_=slot_plane[:].bitcast(I32)[row + r : P : 32])
         load_w4(6, E)
+        nc.sync.dma_start(pos1_sb[:], pos1)
         w8_late = large("w8_late", [P, 2 * (E - WHOLE), P], I32, "plane")
         for lo, hi in zip(LATE_CUTS, LATE_CUTS[1:]):
             load_w8_half(w8_late, 1, lo, hi)

@@ -39,8 +39,8 @@ VECTOR_FIRST_PIECE, VECTOR_LAST_PIECE = 128, 88
 GPSIMD_TOKENS = 128
 AHEAD = 4
 EARLY = AHEAD + 1
-WHOLE = 2
-LATE_CUTS = (WHOLE, 4, 6, LAST, E)
+WHOLE = 4
+LATE_CUTS = (WHOLE, 6, LAST, E)
 FIRST = 2
 
 WORD_COLUMN = (3 * T, 2 * T, T, 0)
@@ -203,10 +203,12 @@ def tile_moe_pln_lin_silu_kernel(
         load_x(3)
         for r in range(4):
             load_scales(W8_ROW, w8_scales, r)
-            load_scales(0, w4_scales, r)
         nc.sync.dma_start(out=w8_whole[:, : 2 * FIRST, :], in_=w8_rows[:, : 2 * FIRST, :])
-        nc.sync.dma_start(out=bias[:], in_=b.rearrange("(h p) e -> p h e", h=2))
+        for r in range(4):
+            load_scales(0, w4_scales, r)
         load_w4(0, FIRST)
+        nc.sync.dma_start(out=w8_whole[:, 2 * FIRST :, :], in_=w8_rows[:, 2 * FIRST : 2 * WHOLE, :])
+        nc.sync.dma_start(out=bias[:], in_=b.rearrange("(h p) e -> p h e", h=2))
         load_w8_half(w8_early, 0, WHOLE, E)
         load_w4(FIRST, E // 2)
         load_w4(E // 2, 6)
@@ -285,17 +287,18 @@ def tile_moe_pln_lin_silu_kernel(
 
         passes([(h, e, g) for h in range(2) for e in range(FIRST) for g in range(2)])
         passes([(h, e, 2) for h in range(2) for e in range(FIRST)])
-        passes([(0, e, g) for e in range(FIRST, E) for g in range(2)])
+        passes([(h, e, g) for h in range(2) for e in range(FIRST, WHOLE) for g in range(2)])
+        passes([(0, e, g) for e in range(WHOLE, E) for g in range(2)])
         passes([(h, e, 2) for h in range(2) for e in range(FIRST, EARLY)])
         for experts in groups[0][:2]:
             passes([(0, e, 3) for e in experts], close=True)
         passes([(0, e, 3) for e in groups[0][2]] + [(1, 0, 3), (1, 2, 3)])
         passes([(0, e, 2) for e in groups[0][2]], close=True)
-        passes([(0, LAST, 2), (1, 3, 3), (1, 4, 3)])
+        passes([(0, LAST, 2), (1, 4, 3), (1, 5, 3)])
         passes([(0, LAST, 3)], close=True)
         passes([(1, 1, 3)], close=True)
-        passes([(1, e, g) for g in range(2) for e in groups[1][1]], close=True)
-        passes([(1, 5, 3), (1, 5, 2)] + [(1, e, g) for g in range(2) for e in groups[1][2]], close=True)
+        passes([(1, 3, 3)], close=True)
+        passes([(1, 5, 2)] + [(1, e, g) for g in range(2) for e in groups[1][2]], close=True)
         passes([(1, e, g) for e in (6, LAST) for g in (3, 2)])
         for e in (6, LAST):
             passes([(1, e, g) for g in range(2)], close=True)

@@ -203,9 +203,9 @@ def tile_moe_pln_lin_silu_kernel(
         load_x(3)
         for r in range(4):
             load_scales(W8_ROW, w8_scales, r)
-        nc.sync.dma_start(out=w8_whole[:, : 2 * FIRST, :], in_=w8_rows[:, : 2 * FIRST, :])
-        for r in range(4):
             load_scales(0, w4_scales, r)
+            if r == 1:
+                nc.sync.dma_start(out=w8_whole[:, : 2 * FIRST, :], in_=w8_rows[:, : 2 * FIRST, :])
         load_w4(0, FIRST)
         nc.sync.dma_start(out=w8_whole[:, 2 * FIRST :, :], in_=w8_rows[:, 2 * FIRST : 2 * WHOLE, :])
         nc.sync.dma_start(out=bias[:], in_=b.rearrange("(h p) e -> p h e", h=2))

@@ -39,8 +39,8 @@ VECTOR_FIRST_PIECE, VECTOR_LAST_PIECE = 128, 88
 GPSIMD_TOKENS = 128
 AHEAD = 4
 EARLY = AHEAD + 1
-WHOLE = 4
-LATE_CUTS = (WHOLE, 6, LAST, E)
+WHOLE = 3
+LATE_CUTS = (WHOLE, 5, LAST, E)
 FIRST = 2
 
 WORD_COLUMN = (3 * T, 2 * T, T, 0)
@@ -268,8 +268,8 @@ def tile_moe_pln_lin_silu_kernel(
         gather_words(2, EARLY, E, tag="xb3")
         gather_words(3, LAST, E)
 
-        groups = (((0, 1), (2, 3, 4), (5, 6), (LAST,)), ((0, 1), (2, 3), (4, 5), (6,), (LAST,)))
-        banks = ((0, 1, 2, 3), (4, 5, 6, 0, 1))
+        groups = (((0, 1), (2, 3, 4), (5, 6), (LAST,)), ((0, 1, 2), (3, 4), (5, 6), (LAST,)))
+        banks = ((0, 1, 2, 3), (4, 5, 6, 0))
 
         def passes(steps, close=False):
             for step in steps:
@@ -292,16 +292,15 @@ def tile_moe_pln_lin_silu_kernel(
         passes([(h, e, 2) for h in range(2) for e in range(FIRST, EARLY)])
         for experts in groups[0][:2]:
             passes([(0, e, 3) for e in experts], close=True)
-        passes([(0, e, 3) for e in groups[0][2]] + [(1, 0, 3), (1, 2, 3)])
+        passes([(0, e, 3) for e in groups[0][2]] + [(1, 0, 3), (1, 1, 3)])
         passes([(0, e, 2) for e in groups[0][2]], close=True)
-        passes([(0, LAST, 2), (1, 4, 3), (1, 5, 3)])
+        passes([(0, LAST, 2), (1, 3, 3), (1, 4, 3)])
         passes([(0, LAST, 3)], close=True)
-        passes([(1, 1, 3)], close=True)
-        passes([(1, 3, 3)], close=True)
-        passes([(1, 5, 2)] + [(1, e, g) for g in range(2) for e in groups[1][2]], close=True)
-        passes([(1, e, g) for e in (6, LAST) for g in (3, 2)])
-        for e in (6, LAST):
-            passes([(1, e, g) for g in range(2)], close=True)
+        passes([(1, 2, 3)], close=True)
+        passes([(1, e, g) for g in range(2) for e in groups[1][1]], close=True)
+        passes([(1, e, g) for e in (5, 6, LAST) for g in (3, 2)])
+        passes([(1, e, g) for g in range(2) for e in groups[1][2]], close=True)
+        passes([(1, LAST, g) for g in range(2)], close=True)
 
         runs = ((0, 2, BANKS - 1), (2, 1, BANKS - 2), (3, 1, 4))
         plain = [large("plain0", [P, HALF_T], F32, "plane"), large("plain1", [P, HALF_T], F32)]

from contextlib import ExitStack

import concourse.mybir as mybir
from concourse.masks import make_identity

K, T, E, C, N = 2048, 512, 8, 128, 256
SLOTS = E * C
FLOPS = 2 * SLOTS * K * N
BYTES = 4 * K * T + E * N * (1024 + 512) + E * N * K // 32 + 4 * N * E + 4 * 2 * T + 2 * 8 * (SLOTS + 2 * T) + 4 * N * T

F32 = mybir.dt.float32
BF16 = mybir.dt.bfloat16
I32 = mybir.dt.int32
U32 = mybir.dt.uint32
U16 = mybir.dt.uint16
U8 = mybir.dt.uint8
E4M3 = mybir.dt.float8_e4m3fn_x4
E2M1 = mybir.dt.float4_e2m1fn_x4
MULT = mybir.AluOpType.mult
COPY = mybir.ActivationFunctionType.Copy
SILU = mybir.ActivationFunctionType.Silu

P = 128
PASSES = 4
K_PASS = K // PASSES
HALF_T = T // 2
LAST_QUARTER = T - T // 4
BANKS = 8
LAST = E - 1
ALIGN = 256

TOKEN_ROW = (4, 8, 0, 12)
MOVED_PASS = 3
W8_ROW = 8

CUTS = ((0, HALF_T, LAST_QUARTER, T), (0, HALF_T, T))
GPSIMD_PAIR_TOKENS = 352
VECTOR_FIRST_PIECE, VECTOR_LAST_PIECE = 128, 88
GPSIMD_TOKENS = 128
AHEAD = 4
EARLY = AHEAD + 1
WHOLE = 3
LATE_CUTS = (WHOLE, 5, LAST, E)
FIRST = 2

WORD_COLUMN = (3 * T, 2 * T, T, 0)


def window_width(entries):
    return max(T, -(-4 * entries // 192) * 64)


GATE_RUNS = 2 * T // P
GATE_STEP = N * T // 4 - P
GATE_START = T + 3 * P


def tile_moe_pln_lin_silu_kernel(
    tc, xT, w8_words, w8_scales, w4_words, w4_scales, b, gate, offs, pos1, pos2, out
):
    nc = tc.nc
    with ExitStack() as ctx:
        lists = ctx.enter_context(tc.tile_pool(name="lists", bufs=1))
        keep = ctx.enter_context(tc.tile_pool(name="keep", bufs=1))
        shared = ctx.enter_context(tc.tile_pool(name="shared", bufs=1))
        psum = ctx.enter_context(tc.psum_pool(name="psum", bufs=1))

        def in_bank(bank, shape, name):
            return psum.tile(shape, F32, name=name, tag="bank%d" % bank)

        def large(name, shape, dtype, tag=None):
            return keep.tile(shape, dtype, name=name, tag=tag or name, align_bytes=ALIGN)

        def on_last_x(name, shape, dtype, offset):
            return shared.tile(shape, dtype, name=name, align_bytes=ALIGN, offset=offset)

        offs_sb = lists.tile([P, SLOTS // 16], U16, name="offs_sb")
        pos1_sb = lists.tile([P, T // 16], U16, name="pos1_sb")
        pos2_sb = lists.tile([P, T // 16], U16, name="pos2_sb")

        x = {}
        for g in range(2):
            for u in range(len(CUTS[g]) - 1):
                x[g, u] = large("x%d_%d" % (g, u), [P, 4, CUTS[g][u + 1] - CUTS[g][u]], F32)
        piece_bytes = 4 * 2 * T
        for u in range(2):
            x[2, u] = large("x2_%d" % u, [P, 2, T], F32)
            x[3, u] = on_last_x("x3_%d" % u, [P, 2, T], F32, piece_bytes * u)
        xb = [large("xb%d" % g, [P, T, 4], BF16) for g in range(PASSES)]
        words = large("words", [P, WORD_COLUMN[0] + window_width(C * LAST)], I32)
        plane = large("plane", [P, window_width(SLOTS - C * FIRST)], U8)
        slot_plane = large("slot_plane", [P, SLOTS], U8)
        ident = large("ident", [P, P], F32)
        gate_rows = large("gate_rows", [P, P], F32)
        w_plane = large("w_plane", [P, E * 2 * N], U8)
        bias = large("bias", [P, 2, E], F32)
        y = [large("y%d" % h, [P, SLOTS], F32) for h in range(2)]
        first = [large("first%d" % h, [P, T], F32) for h in range(2)]
        second = [large("second%d" % h, [P, T], F32) for h in range(2)]
        w8_whole = large("w8_whole", [P, 2 * WHOLE, N], I32)
        w8_early = large("w8_early", [P, 2 * (E - WHOLE), P], I32)
        w4 = large("w4", [P, 2 * E, N // 2], I32)
        slot_words = {}
        sums = {}

        def load_x(g):
            rows = xT[K_PASS * g : K_PASS * (g + 1), :].rearrange("(p j) t -> p j t", j=4)
            if g < 2:
                for u in range(len(CUTS[g]) - 1):
                    nc.sync.dma_start(out=x[g, u][:], in_=rows[:, :, CUTS[g][u] : CUTS[g][u + 1]])
            else:
                for u in range(2):
                    nc.sync.dma_start(out=x[g, u][:], in_=rows[:, 2 * u : 2 * u + 2, :])

        def load_scales(first_row, scales, r):
            rows = scales.bitcast(I32).rearrange("e a q n -> q (e a) n")
            plane_rows = w_plane[:].bitcast(I32).rearrange("p (m n) -> p m n", m=2 * E)
            nc.sync.dma_start(out=plane_rows[first_row + r : P : 32], in_=rows[r:16:4])

        w8_rows = w8_words.rearrange("e a p n t -> p (e a) (n t)").bitcast(I32)
        w4_rows = w4_words.rearrange("e a p n -> p (e a) n").bitcast(I32)

        def load_w8_half(into, h, lo, hi):
            rows = w8_rows[:, 2 * lo : 2 * hi, P * h : P * (h + 1)]
            nc.sync.dma_start(out=into[:, 2 * (lo - WHOLE) : 2 * (hi - WHOLE), :], in_=rows)

        def load_w4(lo, hi):
            nc.sync.dma_start(out=w4[:, 2 * lo : 2 * hi, :], in_=w4_rows[:, 2 * lo : 2 * hi, :])

        def round_and_interleave(engine_copy, g, lo, hi):
            u = len([cut for cut in CUTS[g][1:] if cut <= lo])
            engine_copy(
                out=xb[g][:, lo:hi, :].rearrange("p (c i) j -> p c j i", i=4),
                in_=x[g, u][:, :, lo - CUTS[g][u] : hi - CUTS[g][u]].rearrange("p j (c i) -> p c j i", i=4),
            )

        def round_pass(g):
            round_and_interleave(nc.scalar.copy, g, 0, HALF_T)
            round_and_interleave(nc.scalar.copy, g, HALF_T, T - GPSIMD_TOKENS)
            nc.gpsimd.tensor_copy(
                out=xb[g][:, T - GPSIMD_TOKENS : T, :],
                in_=x[g, 1][:, :, HALF_T - GPSIMD_TOKENS : HALF_T].rearrange("p j t -> p t j"),
            )

        def round_pairs(g):
            def copy_pair(engine_copy, u, lo, hi):
                engine_copy(out=xb[g][:, lo:hi, 2 * u : 2 * u + 2], in_=x[g, u][:, :, lo:hi].rearrange("p j t -> p t j"))

            copy_pair(nc.scalar.copy, 0, 0, T)
            copy_pair(nc.scalar.copy, 1, 0, T - GPSIMD_PAIR_TOKENS)
            copy_pair(nc.gpsimd.tensor_copy, 1, T - GPSIMD_PAIR_TOKENS, T)

        def quantize(g, lo, hi):
            nc.vector.quantize_mx(
                out=words[:, WORD_COLUMN[g] + lo : WORD_COLUMN[g] + hi].bitcast(E4M3),
                scales=plane[TOKEN_ROW[g] : P, lo:hi],
                in_=xb[g][:, lo:hi, :].rearrange("p t j -> p (t j)"),
            )

        def gather_words(g, lo, hi, tag=None, into=None):
            entries = C * (hi - lo)
            if into is None:
                into = large("slot_words%d_%d" % (g, lo), [P, entries], U32, tag)
            window = words[:, WORD_COLUMN[g] : WORD_COLUMN[g] + window_width(entries)].bitcast(U32)
            nc.vector.tensor_copy(into[:], window.indirect(offs_sb[:, C * lo // 16 : C * hi // 16]))
            for e in range(lo, hi):
                slot_words[g, e] = into[:, C * (e - lo) : C * (e - lo + 1)]

        def multiply(h, e, g, start=False, stop=False):
            m, slots = 2 * e + g % 2, slice(C * e, C * (e + 1))
            if g < 2 and e < WHOLE:
                w_row, weights = W8_ROW, w8_whole[:, m, P * h : P * (h + 1)].bitcast(E4M3)
            elif g < 2:
                w_row, weights = W8_ROW, (w8_early, w8_late)[h][:, m - 2 * WHOLE, :].bitcast(E4M3)
            else:
                w_row, weights = 0, w4[:, m, P // 2 * h : P // 2 * (h + 1)].bitcast(U8).bitcast(E2M1)
            nc.tensor.matmul_mx(
                out=sums[h, e],
                lhsT=weights,
                lhsT_scale=w_plane[w_row:P, N * m + P * h : N * m + P * (h + 1)],
                rhs=slot_words[g, e].bitcast(E4M3),
                rhs_scale=moved[:, slots] if g == MOVED_PASS else slot_plane[TOKEN_ROW[g] : P, slots],
                start=start,
                stop=stop,
            )

        def fetch(into, h, i, lo, hi):
            places = (pos1_sb, pos2_sb)[i][:, lo // 16 : hi // 16]
            nc.vector.tensor_tensor(into[h][:, lo:hi], y[h][:].indirect(places), gates[:, i, lo:hi], MULT)

        nc.gpsimd.memset(gate_rows[:], 0.0)
        nc.vector.memset(w_plane[:].bitcast(I32), 0)
        nc.gpsimd.memset(plane[:].bitcast(I32), 0)
        nc.vector.memset(words[:, WORD_COLUMN[0] + T :], 0)
        make_identity(nc, ident[:])

        load_x(0)
        nc.sync.dma_start(offs_sb[:], offs)
        load_x(1)
        gate_flat = gate.rearrange("i n t -> (i n t)")[GATE_START : GATE_START + GATE_RUNS * GATE_STEP]
        nc.sync.dma_start(out=gate_rows[0:GATE_RUNS, :], in_=gate_flat.rearrange("(s c) -> s c", c=GATE_STEP)[:, 0:P])
        load_x(2)
        load_x(3)
        for r in range(4):
            load_scales(W8_ROW, w8_scales, r)
            load_scales(0, w4_scales, r)
            if r == 1:
                nc.sync.dma_start(out=w8_whole[:, : 2 * FIRST, :], in_=w8_rows[:, : 2 * FIRST, :])
        load_w4(0, FIRST)
        nc.sync.dma_start(out=w8_whole[:, 2 * FIRST :, :], in_=w8_rows[:, 2 * FIRST : 2 * WHOLE, :])
        nc.sync.dma_start(out=bias[:], in_=b.rearrange("(h p) e -> p h e", h=2))
        load_w8_half(w8_early, 0, WHOLE, E)
        load_w4(FIRST, E // 2)
        load_w4(E // 2, 6)

        round_and_interleave(nc.scalar.copy, 0, VECTOR_FIRST_PIECE, HALF_T)
        round_and_interleave(nc.vector.tensor_copy, 0, 0, VECTOR_FIRST_PIECE)
        quantize(0, 0, VECTOR_FIRST_PIECE)
        quantize(0, VECTOR_FIRST_PIECE, HALF_T)
        round_and_interleave(nc.scalar.copy, 0, HALF_T, LAST_QUARTER)
        round_and_interleave(nc.scalar.copy, 0, LAST_QUARTER + VECTOR_LAST_PIECE, T)
        round_and_interleave(nc.vector.tensor_copy, 0, LAST_QUARTER, LAST_QUARTER + VECTOR_LAST_PIECE)
        quantize(0, HALF_T, LAST_QUARTER)
        quantize(0, LAST_QUARTER, T)
        round_pass(1)

        gate_turned = in_bank(BANKS - 3, [P, P], "gate_turned")
        nc.tensor.transpose(gate_turned[:], gate_rows[:], ident[:])
        gate_columns = large("gate_columns", [P, GATE_RUNS], F32)
        nc.scalar.copy(out=gate_columns[:], in_=gate_turned[:, 0:GATE_RUNS])
        spread = [in_bank(BANKS - 2 + i, [P, 4, P], "spread") for i in range(2)]
        for i in range(2):
            for r in range(4):
                s = 4 * i + 3 - r
                nc.tensor.transpose(spread[i][:, r, :], gate_columns[:, s : s + 1].to_broadcast([P, P]), ident[:])

        round_pairs(2)
        round_pairs(3)
        gates = on_last_x("gates", [P, 2, T], F32, piece_bytes // 2)
        for i in range(2):
            nc.scalar.copy(out=gates[:, i, :], in_=spread[i][:].rearrange("p r t -> p (r t)"))

        gather_words(0, 0, LAST)
        quantize(1, 0, HALF_T)
        quantize(1, HALF_T, T)
        gather_words(0, LAST, E, tag="x1_1")
        gather_words(1, 0, LAST)
        quantize(2, 0, T)
        gather_words(1, LAST, E, tag="x2_1")
        gather_words(2, 0, AHEAD)
        quantize(3, 0, T)
        gather_words(2, AHEAD, EARLY, into=on_last_x("slot_words2", [P, C], U32, 3 * piece_bytes // 2))

        for lo, hi in ((0, C * FIRST), (C * FIRST, SLOTS)):
            nc.vector.tensor_copy(slot_plane[:, lo:hi], plane[:].indirect(offs_sb[:, lo // 16 : hi // 16]))
        moved = large("moved", [P, SLOTS], U8, "x0_0")
        row = TOKEN_ROW[MOVED_PASS]
        for r in range(4):
            nc.sync.dma_start(out=moved[:].bitcast(I32)[r:P:32], in_=slot_plane[:].bitcast(I32)[row + r : P : 32])
        load_w4(6, E)
        nc.sync.dma_start(pos1_sb[:], pos1)
        w8_late = large("w8_late", [P, 2 * (E - WHOLE), P], I32, "plane")
        for lo, hi in zip(LATE_CUTS, LATE_CUTS[1:]):
            load_w8_half(w8_late, 1, lo, hi)
        nc.sync.dma_start(pos2_sb[:], pos2)

        gather_words(3, 0, LAST)
        gather_words(2, EARLY, E, tag="xb3")
        gather_words(3, LAST, E)

        groups = (((0, 1), (2, 3, 4), (5, 6), (LAST,)), ((0, 1, 2), (3, 4), (5, 6), (LAST,)))
        banks = ((0, 1, 2, 3), (4, 5, 6, 0))

        def passes(steps, close=False):
            for step in steps:
                h, e, g = step
                i = [e in experts for experts in groups[h]].index(True)
                start = (h, e) not in sums
                if start:
                    tile = in_bank(banks[h][i], [P, len(groups[h][i]), C], "sums")
                    for j, expert in enumerate(groups[h][i]):
                        sums[h, expert] = tile[:, j, :]
                multiply(h, e, g, start=start, stop=close and step == steps[-1])
            if close:
                for e in groups[h][i]:
                    nc.scalar.activation(y[h][:, C * e : C * (e + 1)], sums[h, e], SILU, bias=bias[:, h, e : e + 1])

        passes([(h, e, g) for h in range(2) for e in range(FIRST) for g in range(2)])
        passes([(h, e, 2) for h in range(2) for e in range(FIRST)])
        passes([(h, e, g) for h in range(2) for e in range(FIRST, WHOLE) for g in range(2)])
        passes([(0, e, g) for e in range(WHOLE, E) for g in range(2)])
        passes([(h, e, 2) for h in range(2) for e in range(FIRST, EARLY)])
        for experts in groups[0][:2]:
            passes([(0, e, 3) for e in experts], close=True)
        passes([(0, e, 3) for e in groups[0][2]] + [(1, 0, 3), (1, 1, 3)])
        passes([(0, e, 2) for e in groups[0][2]], close=True)
        passes([(0, LAST, 2), (1, 3, 3), (1, 4, 3)])
        passes([(0, LAST, 3)], close=True)
        passes([(1, 2, 3)], close=True)
        passes([(1, e, g) for g in range(2) for e in groups[1][1]], close=True)
        passes([(1, e, g) for e in (5, 6, LAST) for g in (3, 2)])
        passes([(1, e, g) for g in range(2) for e in groups[1][2]], close=True)
        passes([(1, LAST, g) for g in range(2)], close=True)

        runs = ((0, 2, BANKS - 1), (2, 1, BANKS - 2), (3, 1, 4))
        plain = [large("plain0", [P, HALF_T], F32, "plane"), large("plain1", [P, HALF_T], F32)]
        weighted = [large("weighted%d" % h, [P, 2, P], F32) for h in range(2)]
        for block, blocks, bank in runs:
            lo, hi = P * block, P * (block + blocks)
            into = plain[block // 2][:, lo % HALF_T : lo % HALF_T + hi - lo]
            nc.scalar.activation(into, y[block // 2][:].indirect(pos2_sb[:, lo // 16 : hi // 16]), COPY)
        for block, blocks, bank in runs:
            turned = in_bank(bank, [P, blocks, P], "turned")
            for j in range(blocks):
                lo = P * ((block + j) % 2)
                nc.tensor.transpose(turned[:, j, :], plain[block // 2][:, lo : lo + P], ident[:])
            for j in range(blocks):
                s, into = GATE_RUNS - 1 - (block + j), weighted[block // 2][:, (block + j) % 2, :]
                nc.scalar.activation(into, turned[:, j, :], COPY, scale=gate_columns[:, s : s + 1])
        back = [in_bank(2 + h, [P, 2, P], "back") for h in range(2)]
        for block in range(T // P):
            nc.tensor.transpose(back[block // 2][:, block % 2, :], weighted[block // 2][:, block % 2, :], ident[:])

        low, high = slice(0, HALF_T), slice(HALF_T, T)
        result = {(h, i): large("result%d_%d" % (h, i), [P, HALF_T], F32) for h, i in ((0, 0), (1, 1))}
        result[1, 0] = large("result1_0", [P, HALF_T], F32, "weighted0")
        result[0, 1] = large("result0_1", [P, HALF_T], F32, "plane")

        def add_and_store(h, i, other):
            tokens = (low, high)[i]
            nc.vector.tensor_add(result[h, i][:], first[h][:, tokens], other)
            nc.sync.dma_start(out=out[P * h : P * (h + 1), tokens], in_=result[h, i][:])

        fetch(first, 0, 0, 0, T)
        fetch(second, 0, 1, HALF_T, T)
        fetch(first, 1, 0, 0, T)
        add_and_store(0, 1, second[0][:, high])
        fetch(second, 1, 1, 0, HALF_T)
        add_and_store(0, 0, back[0][:].rearrange("p j t -> p (j t)"))
        add_and_store(1, 0, second[1][:, low])
        add_and_store(1, 1, back[1][:].rearrange("p j t -> p (j t)"))
